import numpy as np
import ml_dtypes


def mxq(x, axis, fmt="e4m3"):
    dtype, down = {"e4m3": (ml_dtypes.float8_e4m3fn, 7), "e5m2": (ml_dtypes.float8_e5m2, 14)}[fmt]
    v = np.moveaxis(np.asarray(x, np.float32).astype(ml_dtypes.bfloat16).astype(np.float64), axis, -1)
    blocks = v.reshape(v.shape[:-1] + (-1, 32))
    amax = np.abs(blocks).max(-1, keepdims=True)
    byte = np.maximum(np.where(amax > 0, np.frexp(amax)[1] - 1 + 127, 0) - down, 1)
    scale = np.exp2(byte - 127.0)
    codes = (blocks / scale).astype(np.float32).astype(dtype).astype(np.float64)
    return np.moveaxis((codes * scale).reshape(v.shape), -1, axis)


WIDE = False


def mx_kscale(k):
    if not WIDE:
        return np.ones(k)
    levels = np.array([10, -10, 5, -5, 0])
    if k % 512:
        return np.exp2(np.random.permutation(np.resize(levels, k // 32))).repeat(32)
    a = np.empty((k // 512, 16))
    for p in range(k // 512):
        a[p, :8] = np.random.permutation(np.resize(levels, 8))
        for g in range(8):
            far = levels[np.abs(levels - a[p, g]) >= 10]
            a[p, g + 8] = far[np.random.randint(len(far))]
    return np.exp2(a.ravel()).repeat(32)


BF16 = ml_dtypes.bfloat16


def bf(x):
    return np.asarray(x, np.float32).astype(BF16)


def f64(x):
    return np.asarray(x).astype(np.float64)


E2M1 = np.array([0.0, 0.5, 1.0, 1.5, 2.0, 3.0, 4.0, 6.0, -0.0, -0.5, -1.0, -1.5, -2.0, -3.0, -4.0, -6.0])


def pack_weight(w, fmt):
    k, n = w.shape
    w = f64(bf(w)).reshape(k // 32, 32, n)
    amax = np.abs(w).max(1)
    if fmt == "e4m3":
        byte = np.frexp(amax)[1] - 1 + 127 - 7
    else:
        mant, ex = np.frexp(amax / 6.0)
        byte = np.where(mant > 0.5, ex, ex - 1) + 127
    byte = np.clip(np.where(amax > 0, byte, 1), 1, 254)
    scaled = (w * np.exp2(127.0 - byte)[:, None, :]).reshape(k, n).astype(np.float32)
    by_word = np.ascontiguousarray(scaled.reshape(k // 512, 128, 4, n).transpose(0, 1, 3, 2))
    if fmt == "e4m3":
        words = by_word.astype(ml_dtypes.float8_e4m3fn).view(np.uint8)
    else:
        c = by_word.astype(ml_dtypes.float4_e2m1fn).view(np.uint8) & 0xF
        words = c[..., 0::2] | (c[..., 1::2] << 4)
    return np.ascontiguousarray(words), np.ascontiguousarray(byte.astype(np.uint8).reshape(k // 512, 16, n))


def unpack_weight(words, scales, fmt):
    g, p, n, _ = words.shape
    if fmt == "e4m3":
        vals = np.ascontiguousarray(words).view(ml_dtypes.float8_e4m3fn).astype(np.float64)
    else:
        nib = np.empty((g, p, n, 4), np.uint8)
        nib[..., 0::2] = words & 0xF
        nib[..., 1::2] = words >> 4
        vals = E2M1[nib]
    vals = vals * np.repeat(np.exp2(scales.astype(np.float64) - 127.0), 8, axis=1)[..., None]
    return vals.transpose(0, 1, 3, 2).reshape(g * 512, n)
def pack4(w):
    words, scales = pack_weight(w, "e2m1")
    return words.reshape(words.shape[0], 128, -1), scales


def unpack4(words, scales):
    return unpack_weight(words.reshape(words.shape[0], 128, -1, 2), scales, "e2m1")


S, N, C, R = 1536, 1024, 512, 512

SHOCK = 0.7
SPREAD = 0.2


def draw0():
    s = mx_kscale(N)
    t = mx_kscale(N)
    u = mx_kscale(S)
    shocks = SHOCK * np.random.standard_normal((S, N))
    inverse = np.random.standard_normal((N, N)) ** 2 / np.sqrt(3 * N)
    baskets = np.random.standard_normal((N, C)) / np.sqrt(N)
    words, scales = pack4(baskets / t[:, None])
    contrasts = np.random.standard_normal((R, S)) / np.sqrt(S)
    return {"shocks": bf(shocks * s),
            "inverse": bf(inverse / s[:, None]),
            "base": bf((1 + SPREAD * np.random.standard_normal(N)) * t),
            "weight": bf((1 + SPREAD * np.random.standard_normal(S)) * u),
            "basket_words": words, "basket_scales": scales,
            "contrasts": bf(contrasts / u)}


def core(shocks, inverse, base, weight, basket_words, basket_scales, contrasts):
    moves = mxq(f64(shocks), 1, "e4m3") @ mxq(f64(inverse), 0, "e4m3")
    rel = np.exp(moves)
    priced = mxq(rel * f64(base)[None, :], 1, "e4m3")
    index = priced @ unpack4(basket_words, basket_scales)
    weighted = mxq(rel * f64(weight)[:, None], 0, "e4m3")
    contrast = mxq(f64(contrasts), 1, "e4m3") @ weighted
    return index, contrast


def e4m3fn_bytes(y):
    return np.clip(np.asarray(y, np.float64), -448.0, 448.0).astype(np.float32).astype(ml_dtypes.float8_e4m3fn).view(np.uint8)


def e4m3fn_values(b):
    return np.asarray(b, np.uint8).view(ml_dtypes.float8_e4m3fn).astype(np.float64)


def setup_inputs():
    d = draw0()
    x0 = np.asarray(d['shocks']).astype(np.float64)
    s = (np.max(np.abs(x0), axis=(0,), keepdims=True) / 448.0).astype(np.float32)
    out = {}
    for k, v in d.items():
        if k == 'shocks':
            out['shocks_bytes'] = e4m3fn_bytes(x0 / s.astype(np.float64))
            out['shocks_scale'] = s
        else:
            out[k] = v
    return out


def reference(shocks_bytes, shocks_scale, inverse, base, weight, basket_words, basket_scales, contrasts):
    return core(e4m3fn_values(shocks_bytes) * shocks_scale.astype(np.float64), inverse, base, weight, basket_words, basket_scales, contrasts)

@@ -1,0 +1,474 @@
+from contextlib import ExitStack
+
+import concourse.mybir as mybir
+from concourse.masks import make_identity
+
+S, N, C, R = 1536, 1024, 512, 512
+FLOPS = 2 * (S * N * N + S * N * C + R * S * N)
+
+F32 = mybir.dt.float32
+BF16 = mybir.dt.bfloat16
+I32 = mybir.dt.int32
+U32 = mybir.dt.uint32
+U8 = mybir.dt.uint8
+FP8 = mybir.dt.float8_e4m3fn
+FP8X4 = mybir.dt.float8_e4m3fn_x4
+FP4X4 = mybir.dt.float4_e2m1fn_x4
+MULT = mybir.AluOpType.mult
+EXP = mybir.ActivationFunctionType.Exp
+
+P = 128
+T = 4
+KP = P * T
+SG = S // KP
+KQ = N // KP
+NJ = N // KP
+
+BLOCKS = ((0, 0), (0, 1), (1, 0), (2, 0), (2, 1), (1, 1))
+
+
+def tile_ghosh_price_push_s8_kernel(
+    tc, shocks_bytes, shocks_scale, inverse, base, weight, basket_words, basket_scales, contrasts, out_0, out_1
+):
+    nc = tc.nc
+    with ExitStack() as ctx:
+        keep = ctx.enter_context(tc.tile_pool(name="keep", bufs=1))
+        work = ctx.enter_context(tc.tile_pool(name="work", bufs=3))
+        psum = ctx.enter_context(tc.psum_pool(name="psum", bufs=2))
+
+        sh_bytes = keep.tile([P, SG * T, N], U8, name="sh_bytes", align_bytes=64)
+        scale_kp = keep.tile([P, KQ, T], F32, name="scale_kp")
+        scale_row = keep.tile([P, N], F32, name="scale_row")
+        inv_raw = keep.tile([P, NJ, KQ, T, KP], BF16, name="inv_raw")
+        base_kp = keep.tile([P, NJ, T], BF16, name="base_kp")
+        weight_kp = keep.tile([P, SG, T], BF16, name="weight_kp")
+        weight_f32 = keep.tile([P, SG, T], F32, name="weight_f32")
+        b_words = keep.tile([P, NJ, 2 * C], U8, name="b_words", align_bytes=64)
+        b_scales = keep.tile([P, NJ, C], U8, name="b_scales", align_bytes=64)
+        con_raw = keep.tile([P, T, S], BF16, name="con_raw")
+
+        sh_codes = keep.tile([P, SG * T, KQ, P], U32, name="sh_codes", align_bytes=64)
+        sh_scales = keep.tile([P, SG * T, KQ, P], U8, name="sh_scales", align_bytes=64)
+        inv_codes = keep.tile([P, NJ, KQ, KP], U32, name="inv_codes", align_bytes=64)
+        inv_scales = keep.tile([P, NJ, KQ, KP], U8, name="inv_scales", align_bytes=64)
+        con_codes = keep.tile([P, SG, R], U32, name="con_codes", align_bytes=64)
+        con_scales = keep.tile([P, SG, R], U8, name="con_scales", align_bytes=64)
+        pr_codes = keep.tile([P, SG, NJ, KP], U32, name="pr_codes", align_bytes=64)
+        pr_scales = keep.tile([P, SG, NJ, KP], U8, name="pr_scales", align_bytes=64)
+        we_codes = keep.tile([P, SG, NJ, KP], U32, name="we_codes", align_bytes=64)
+        we_scales = keep.tile([P, SG, NJ, KP], U8, name="we_scales", align_bytes=64)
+
+        ident = keep.tile([P, P], F32, name="ident")
+        warm = keep.tile([P, 1], F32, name="warm")
+
+        nc.vector.memset(warm[:], 0.0)
+        nc.vector.memset(b_scales[:].rearrange("p j n -> p (j n)").bitcast(I32), 0)
+        nc.scalar.activation(out=warm[:], in_=warm[:], func=EXP)
+        make_identity(nc, ident[:])
+
+        shocks_v = shocks_bytes.rearrange("(g m t) k -> g m t k", m=P, t=T)
+
+        def load_shocks(g, t0, t1):
+            nc.sync.dma_start(out=sh_bytes[:, T * g + t0 : T * g + t1, :], in_=shocks_v[g][:, t0:t1, :])
+
+        inverse_v = inverse.rearrange("(q p t) n -> q p t n", p=P, t=T)
+
+        def load_inverse(j, q):
+            nc.sync.dma_start(out=inv_raw[:, j, q], in_=inverse_v[q][:, :, KP * j : KP * (j + 1)])
+
+        nc.sync.dma_start(out=scale_kp[:], in_=shocks_scale.rearrange("o (q p t) -> p (o q) t", p=P, t=T))
+        load_shocks(0, 0, 2)
+        load_inverse(0, 0)
+        load_inverse(0, 1)
+        load_shocks(0, 2, 4)
+        nc.sync.dma_start(out=scale_row[:], in_=shocks_scale.rearrange("o k -> (o k)").partition_broadcast(P))
+        load_inverse(1, 0)
+        load_inverse(1, 1)
+        nc.sync.dma_start(out=base_kp[:], in_=base.rearrange("(j p t) -> p j t", p=P, t=T))
+        nc.sync.dma_start(out=weight_kp[:], in_=weight.rearrange("(g p t) -> p g t", p=P, t=T))
+        load_shocks(1, 0, 4)
+        load_shocks(2, 0, 4)
+        con_v = contrasts.rearrange("(a r) k -> r a k", r=P)
+        nc.sync.dma_start(out=con_raw[:, 0:2], in_=con_v[:, 0:2])
+        nc.sync.dma_start(out=con_raw[:, 2:4], in_=con_v[:, 2:4])
+        for quad in range(4):
+            nc.sync.dma_start(
+                out=b_scales[32 * quad : 32 * quad + 4].bitcast(I32),
+                in_=basket_scales.rearrange("j s n -> s j n")[4 * quad : 4 * quad + 4].bitcast(I32),
+            )
+        nc.sync.dma_start(out=b_words[:], in_=basket_words.rearrange("j p b -> p j b"))
+
+        sh_wide = {}
+        sh_bank = {}
+        sh_group = {}
+
+        def widen_plain(i, engine):
+            x = work.tile([P, N], BF16, name="xb", bufs=4)
+            sh_wide[i] = x
+            if engine == "scalar":
+                nc.scalar.copy(out=x[:], in_=sh_bytes[:, i, :].bitcast(FP8))
+            else:
+                nc.vector.tensor_copy(out=x[:], in_=sh_bytes[:, i, :].bitcast(FP8))
+
+        def widen_scaled(i):
+            x = work.tile([P, N], BF16, name="xb", bufs=4)
+            sh_wide[i] = x
+            nc.vector.tensor_tensor(out=x[:], in0=sh_bytes[:, i, :].bitcast(FP8), in1=scale_row[:], op=MULT)
+
+        def turn_shocks(i):
+            bank = psum.tile([P, KQ, 2, P], F32, name="tr", bufs=3)
+            sh_bank[i] = bank
+            words = sh_wide[i][:].bitcast(F32)
+            for q in range(KQ):
+                for u in range(2):
+                    nc.tensor.transpose(bank[:, q, u, :], words[:, 256 * q + u : 256 * (q + 1) : 2], ident[:])
+
+        def group_tile(i):
+            if i % 2 == 0:
+                sh_group[i // 2] = work.tile([P, 2, KQ * P * T], BF16, name="xg", bufs=2, align_bytes=64)
+            return sh_group[i // 2][:, i % 2, :]
+
+        def empty_shocks_scaled(i):
+            g = group_tile(i).rearrange("p (q r u e) -> p q r u e", q=KQ, u=2, e=2)
+            b = sh_bank[i][:].rearrange("p q u r -> p (q u r)").bitcast(BF16)
+            b = b.rearrange("p (q u r e) -> p q r u e", q=KQ, u=2, e=2)
+            for q in range(KQ):
+                sc = scale_kp[:, q, :].rearrange("p (u e) -> p u e", u=2).unsqueeze(1).to_broadcast([P, P, 2, 2])
+                nc.vector.tensor_tensor(out=g[:, q], in0=b[:, q], in1=sc, op=MULT)
+
+        def empty_shocks(i):
+            g = group_tile(i).bitcast(F32).rearrange("p (q r u) -> p q r u", q=KQ, u=2)
+            nc.scalar.copy(out=g, in_=sh_bank[i][:].rearrange("p q u r -> p q r u"))
+
+        def quantize_shocks(k):
+            nc.vector.quantize_mx(
+                out=sh_codes[:, 2 * k : 2 * k + 2].rearrange("p i q r -> p (i q r)").bitcast(FP8X4),
+                scales=sh_scales[:, 2 * k : 2 * k + 2].rearrange("p i q r -> p (i q r)"),
+                in_=sh_group[k][:].rearrange("p i c -> p (i c)"),
+            )
+
+        inv_group = {}
+
+        def group_inverse(j, q, engine, c0, c1):
+            if (j, q) not in inv_group:
+                inv_group[j, q] = work.tile([P, KP, T], BF16, name="ig", bufs=2, align_bytes=64)
+            dst = inv_group[j, q][:, c0:c1, :].rearrange("p (c i) t -> p c t i", i=4)
+            src = inv_raw[:, j, q, :, c0:c1].rearrange("p t (c i) -> p c t i", i=4)
+            if engine == "scalar":
+                nc.scalar.copy(out=dst, in_=src)
+            else:
+                nc.vector.tensor_copy(out=dst, in_=src)
+
+        def quantize_inverse(j, q):
+            nc.vector.quantize_mx(
+                out=inv_codes[:, j, q, :].bitcast(FP8X4),
+                scales=inv_scales[:, j, q, :],
+                in_=inv_group[j, q][:].rearrange("p n t -> p (n t)"),
+            )
+
+        con_bank = {}
+        con_group = {}
+
+        def turn_contrasts(g, a0):
+            bank = psum.tile([P, 2, 2, P], F32, name="tr", bufs=3)
+            con_bank[g, a0] = bank
+            for a in range(2):
+                words = con_raw[:, a0 + a, :].bitcast(F32)
+                for u in range(2):
+                    nc.tensor.transpose(bank[:, a, u, :], words[:, 256 * g + u : 256 * (g + 1) : 2], ident[:])
+
+        def empty_contrasts(g, a0):
+            if a0 == 0:
+                con_group[g] = work.tile([P, R * T], BF16, name="cg", bufs=2, align_bytes=64)
+            dst = con_group[g][:].bitcast(F32).rearrange("p (a r u) -> p a r u", r=P, u=2)[:, a0 : a0 + 2]
+            nc.scalar.copy(out=dst, in_=con_bank[g, a0][:].rearrange("p a u r -> p a r u"))
+
+        def quantize_contrasts(g):
+            nc.vector.quantize_mx(out=con_codes[:, g, :].bitcast(FP8X4), scales=con_scales[:, g, :], in_=con_group[g][:])
+
+        mv_bank = {}
+        rel = {}
+        tr_bank = {}
+        priced = {}
+        weighted = {}
+
+        def unit(h, i):
+            return h // 2, BLOCKS[h // 2][0], BLOCKS[h // 2][1], 2 * (h % 2) + i
+
+        def moves(h):
+            for i in range(2):
+                b, g, j, t = unit(h, i)
+                bank = psum.tile([P, KP], F32, name="mm", bufs=3)
+                mv_bank[h, i] = bank
+                for q in range(KQ):
+                    nc.tensor.matmul_mx(
+                        out=bank[:],
+                        lhsT=sh_codes[:, T * g + t, q, :].bitcast(FP8X4),
+                        lhsT_scale=sh_scales[:, T * g + t, q, :],
+                        rhs=inv_codes[:, j, q, :].bitcast(FP8X4),
+                        rhs_scale=inv_scales[:, j, q, :],
+                        start=(q == 0),
+                        stop=(q == KQ - 1),
+                    )
+
+        def relatives(h):
+            for i in range(2):
+                b, g, j, t = unit(h, i)
+                if t == 0:
+                    rel[b] = work.tile([P, T, KP], F32, name="rel", bufs=3)
+                nc.scalar.activation(
+                    out=rel[b][:, t, :].rearrange("p (v m) -> p v m", v=T),
+                    in_=mv_bank[h, i][:].rearrange("p (m v) -> p v m", v=T),
+                    func=EXP,
+                )
+
+        def turn(h):
+            for i in range(2):
+                b, g, j, t = unit(h, i)
+                bank = psum.tile([P, T, P], F32, name="tr", bufs=3)
+                tr_bank[h, i] = bank
+                for v in range(T):
+                    nc.tensor.transpose(bank[:, v, :], rel[b][:, t, P * v : P * (v + 1)], ident[:])
+
+        def price(h):
+            priced[h] = work.tile([P, 2, P, T], BF16, name="pr", bufs=3, align_bytes=64)
+            for i in range(2):
+                b, g, j, t = unit(h, i)
+                nc.vector.tensor_tensor(
+                    out=priced[h][:, i],
+                    in0=tr_bank[h, i][:].rearrange("p v m -> p m v"),
+                    in1=base_kp[:, j, :].unsqueeze(1).to_broadcast([P, P, T]),
+                    op=MULT,
+                )
+
+        def quantize_priced(h):
+            b, g, j, t = unit(h, 0)
+            cols = slice(P * t, P * (t + 2))
+            nc.vector.quantize_mx(
+                out=pr_codes[:, g, j, cols].bitcast(FP8X4),
+                scales=pr_scales[:, g, j, cols],
+                in_=priced[h][:].rearrange("p i m v -> p (i m v)"),
+            )
+
+        def weigh(b, half):
+            g = BLOCKS[b][0]
+            weighted[b, half] = work.tile([P, KP // 2, T], BF16, name="we", bufs=3, align_bytes=64)
+            cols = slice(KP // 2 * half, KP // 2 * (half + 1))
+            nc.vector.tensor_tensor(
+                out=weighted[b, half][:],
+                in0=rel[b][:, :, cols].rearrange("p t n -> p n t"),
+                in1=weight_kp[:, g, :].unsqueeze(1).to_broadcast([P, KP // 2, T]),
+                op=MULT,
+            )
+
+        scaled = {}
+
+        def scale_units(h):
+            for i in range(2):
+                b, g, j, t = unit(h, i)
+                if t == 0:
+                    scaled[b] = work.tile([P, T, KP], BF16, name="sc", bufs=2)
+                nc.scalar.activation(
+                    out=scaled[b][:, t, :],
+                    in_=rel[b][:, t, :],
+                    func=mybir.ActivationFunctionType.Copy,
+                    scale=weight_f32[:, g, t : t + 1],
+                )
+
+        def interleave(b, half):
+            weighted[b, half] = work.tile([P, KP // 2, T], BF16, name="we", bufs=3, align_bytes=64)
+            cols = slice(KP // 2 * half, KP // 2 * (half + 1))
+            nc.vector.tensor_copy(
+                out=weighted[b, half][:].rearrange("p (c i) t -> p c t i", i=4),
+                in_=scaled[b][:, :, cols].rearrange("p t (c i) -> p c t i", i=4),
+            )
+
+        def quantize_weighted(b, half):
+            g, j = BLOCKS[b]
+            cols = slice(KP // 2 * half, KP // 2 * (half + 1))
+            nc.vector.quantize_mx(
+                out=we_codes[:, g, j, cols].bitcast(FP8X4),
+                scales=we_scales[:, g, j, cols],
+                in_=weighted[b, half][:].rearrange("p n t -> p (n t)"),
+            )
+
+        index_v = out_0.rearrange("(g m t) c -> g m t c", m=P, t=T)
+        acc_bank = {}
+
+        def index_mm(g, t):
+            bank = psum.tile([P, C], F32, name="acc", bufs=2)
+            acc_bank[0, g, t] = bank
+            for j in range(NJ):
+                nc.tensor.matmul_mx(
+                    out=bank[:],
+                    lhsT=pr_codes[:, g, j, P * t : P * (t + 1)].bitcast(FP8X4),
+                    lhsT_scale=pr_scales[:, g, j, P * t : P * (t + 1)],
+                    rhs=b_words[:, j, :].bitcast(FP4X4),
+                    rhs_scale=b_scales[:, j, :],
+                    start=(j == 0),
+                    stop=(j == NJ - 1),
+                )
+
+        def index_out(g, t, engine):
+            res = work.tile([P, C], F32, name="res", bufs=8)
+            if engine == "scalar":
+                nc.scalar.copy(out=res[:], in_=acc_bank[0, g, t][:])
+            else:
+                nc.vector.tensor_copy(out=res[:], in_=acc_bank[0, g, t][:])
+            nc.sync.dma_start(out=index_v[g][:, t, :], in_=res[:])
+
+        def contrast_mm(a, j, name, bufs):
+            bank = psum.tile([P, KP], F32, name=name, bufs=bufs)
+            acc_bank[1, a, j] = bank
+            for n, g in enumerate((0, 2, 1)):
+                nc.tensor.matmul_mx(
+                    out=bank[:],
+                    lhsT=con_codes[:, g, P * a : P * (a + 1)].bitcast(FP8X4),
+                    lhsT_scale=con_scales[:, g, P * a : P * (a + 1)],
+                    rhs=we_codes[:, g, j, :].bitcast(FP8X4),
+                    rhs_scale=we_scales[:, g, j, :],
+                    start=(n == 0),
+                    stop=(n == SG - 1),
+                )
+
+        def contrast_out(a, j, engine):
+            res = work.tile([P, KP], F32, name="res", bufs=8)
+            dst = res[:].rearrange("p (m v) -> p m v", v=T)
+            src = acc_bank[1, a, j][:].rearrange("p (v m) -> p m v", v=T)
+            if engine == "scalar":
+                nc.scalar.copy(out=dst, in_=src)
+            else:
+                nc.vector.tensor_copy(out=dst, in_=src)
+            nc.sync.dma_start(out=out_1[P * a : P * (a + 1), KP * j : KP * (j + 1)], in_=res[:])
+
+        widen_plain(0, "vector")
+        widen_plain(1, "scalar")
+        turn_shocks(0)
+        group_inverse(0, 0, "scalar", 0, KP)
+        turn_shocks(1)
+        empty_shocks_scaled(0)
+        empty_shocks_scaled(1)
+        group_inverse(0, 1, "scalar", 0, 3 * KP // 4)
+        group_inverse(0, 1, "vector", 3 * KP // 4, KP)
+        quantize_shocks(0)
+        quantize_inverse(0, 0)
+        widen_plain(2, "scalar")
+        turn_shocks(2)
+        widen_plain(3, "scalar")
+        quantize_inverse(0, 1)
+        moves(0)
+        turn_shocks(3)
+        empty_shocks_scaled(2)
+        empty_shocks_scaled(3)
+        relatives(0)
+        nc.vector.tensor_copy(out=weight_f32[:], in_=weight_kp[:])
+        widen_scaled(4)
+        quantize_shocks(1)
+
+        for h in range(12):
+            if h > 0:
+                moves(h)
+                relatives(h)
+            if h == 0:
+                group_inverse(1, 0, "scalar", 0, KP)
+                group_inverse(1, 1, "scalar", 0, KP)
+                widen_scaled(5)
+                widen_scaled(6)
+                quantize_inverse(1, 0)
+            if h == 1:
+                turn_shocks(4)
+                turn_shocks(5)
+                empty_shocks(4)
+                empty_shocks(5)
+                widen_scaled(7)
+                quantize_inverse(1, 1)
+                quantize_shocks(2)
+            if h == 2:
+                turn_shocks(6)
+                turn_shocks(7)
+                empty_shocks(6)
+                empty_shocks(7)
+                widen_scaled(8)
+                widen_scaled(9)
+                quantize_shocks(3)
+            if h == 3:
+                turn_shocks(8)
+                turn_shocks(9)
+                empty_shocks(8)
+                empty_shocks(9)
+                widen_scaled(10)
+                widen_scaled(11)
+                quantize_shocks(4)
+            if h == 4:
+                turn_shocks(10)
+                turn_shocks(11)
+                empty_shocks(10)
+                empty_shocks(11)
+            if h in (2, 3):
+                weigh(0, h % 2)
+            if h >= 3:
+                scale_units(h - 1)
+            if h >= 4 and h % 2 == 1:
+                interleave(h // 2 - 1, 0)
+                interleave(h // 2 - 1, 1)
+            if h == 4:
+                quantize_shocks(5)
+            if h in (5, 6, 7):
+                turn_contrasts(h - 5, 0)
+                turn_contrasts(h - 5, 2)
+                empty_contrasts(h - 5, 0)
+                empty_contrasts(h - 5, 2)
+            if h >= 1:
+                turn(h - 1)
+                price(h - 1)
+            if h in (2, 3):
+                quantize_weighted(0, h % 2)
+            if h >= 4 and h % 2 == 1:
+                quantize_weighted(h // 2 - 1, 0)
+                quantize_weighted(h // 2 - 1, 1)
+            if h in (5, 6, 7):
+                quantize_contrasts(h - 5)
+            if h >= 1:
+                quantize_priced(h - 1)
+            if h in (5, 6):
+                for t in (0, 1):
+                    index_mm(0, 2 * (h - 5) + t)
+                for t in (0, 1):
+                    index_out(0, 2 * (h - 5) + t, "scalar")
+            if h in (10, 11):
+                for a in (0, 1):
+                    contrast_mm(2 * (h - 10) + a, 0, "acc", 2)
+                for a in (0, 1):
+                    contrast_out(2 * (h - 10) + a, 0, "scalar")
+
+        turn(11)
+        scale_units(11)
+        index_mm(2, 0)
+        index_mm(2, 1)
+        index_out(2, 0, "scalar")
+        index_out(2, 1, "scalar")
+        price(11)
+        interleave(5, 0)
+        interleave(5, 1)
+        quantize_priced(11)
+        quantize_weighted(5, 0)
+        quantize_weighted(5, 1)
+        index_mm(2, 2)
+        index_mm(2, 3)
+        index_out(2, 2, "scalar")
+        index_out(2, 3, "vector")
+        index_mm(1, 0)
+        index_mm(1, 1)
+        index_out(1, 0, "scalar")
+        index_out(1, 1, "vector")
+        for a in range(3):
+            contrast_mm(a, 1, "mm", 3)
+        index_mm(1, 2)
+        index_mm(1, 3)
+        index_out(1, 2, "scalar")
+        contrast_out(0, 1, "vector")
+        contrast_out(1, 1, "scalar")
+        contrast_out(2, 1, "vector")
+        contrast_mm(3, 1, "tr", 3)
+        index_out(1, 3, "scalar")
+        contrast_out(3, 1, "vector")

@@ -16,6 +16,7 @@ FP8X4 = mybir.dt.float8_e4m3fn_x4
 FP4X4 = mybir.dt.float4_e2m1fn_x4
 MULT = mybir.AluOpType.mult
 EXP = mybir.ActivationFunctionType.Exp
+COPY = mybir.ActivationFunctionType.Copy
 
 P = 128
 T = 4
@@ -23,8 +24,11 @@ KP = P * T
 SG = S // KP
 KQ = N // KP
 NJ = N // KP
+HALF = KP // 2
 
 BLOCKS = ((0, 0), (0, 1), (1, 0), (2, 0), (2, 1), (1, 1))
+STEPS = 2 * len(BLOCKS)
+REL_BUFS = 6
 
 
 def tile_ghosh_price_push_s8_kernel(
@@ -34,18 +38,19 @@ def tile_ghosh_price_push_s8_kernel(
     with ExitStack() as ctx:
         keep = ctx.enter_context(tc.tile_pool(name="keep", bufs=1))
         work = ctx.enter_context(tc.tile_pool(name="work", bufs=3))
-        psum = ctx.enter_context(tc.psum_pool(name="psum", bufs=2))
+        psum = ctx.enter_context(tc.psum_pool(name="psum", bufs=1))
+        ctx.enter_context(tc.manual_schedule())
 
-        sh_bytes = keep.tile([P, SG * T, N], U8, name="sh_bytes", align_bytes=64)
+        sh_bytes = [keep.tile([P, 2, N], U8, name="sh_bytes%d" % k, align_bytes=64) for k in range(2 * SG)]
         scale_kp = keep.tile([P, KQ, T], F32, name="scale_kp")
         scale_row = keep.tile([P, N], F32, name="scale_row")
-        inv_raw = keep.tile([P, NJ, KQ, T, KP], BF16, name="inv_raw")
+        inv_raw = {(j, q): keep.tile([P, T, KP], BF16, name="inv_raw%d%d" % (j, q)) for j in range(NJ) for q in range(KQ)}
         base_kp = keep.tile([P, NJ, T], BF16, name="base_kp")
         weight_kp = keep.tile([P, SG, T], BF16, name="weight_kp")
         weight_f32 = keep.tile([P, SG, T], F32, name="weight_f32")
         b_words = keep.tile([P, NJ, 2 * C], U8, name="b_words", align_bytes=64)
         b_scales = keep.tile([P, NJ, C], U8, name="b_scales", align_bytes=64)
-        con_raw = keep.tile([P, T, S], BF16, name="con_raw")
+        con_raw = [keep.tile([P, S], BF16, name="con_raw%d" % a) for a in range(T)]
 
         sh_codes = keep.tile([P, SG * T, KQ, P], U32, name="sh_codes", align_bytes=64)
         sh_scales = keep.tile([P, SG * T, KQ, P], U8, name="sh_scales", align_bytes=64)
@@ -61,103 +66,97 @@ def tile_ghosh_price_push_s8_kernel(
         ident = keep.tile([P, P], F32, name="ident")
         warm = keep.tile([P, 1], F32, name="warm")
 
-        nc.vector.memset(warm[:], 0.0)
-        nc.vector.memset(b_scales[:].rearrange("p j n -> p (j n)").bitcast(I32), 0)
-        nc.scalar.activation(out=warm[:], in_=warm[:], func=EXP)
-        make_identity(nc, ident[:])
-
         shocks_v = shocks_bytes.rearrange("(g m t) k -> g m t k", m=P, t=T)
-
-        def load_shocks(g, t0, t1):
-            nc.sync.dma_start(out=sh_bytes[:, T * g + t0 : T * g + t1, :], in_=shocks_v[g][:, t0:t1, :])
-
         inverse_v = inverse.rearrange("(q p t) n -> q p t n", p=P, t=T)
+        index_v = out_0.rearrange("(g m t) c -> g m t c", m=P, t=T)
+
+        def load_shocks(k):
+            nc.sync.dma_start(out=sh_bytes[k][:], in_=shocks_v[k // 2][:, 2 * (k % 2) : 2 * (k % 2) + 2, :])
 
         def load_inverse(j, q):
-            nc.sync.dma_start(out=inv_raw[:, j, q], in_=inverse_v[q][:, :, KP * j : KP * (j + 1)])
+            nc.sync.dma_start(out=inv_raw[j, q][:], in_=inverse_v[q][:, :, KP * j : KP * (j + 1)])
 
-        nc.sync.dma_start(out=scale_kp[:], in_=shocks_scale.rearrange("o (q p t) -> p (o q) t", p=P, t=T))
-        load_shocks(0, 0, 2)
-        load_inverse(0, 0)
-        load_inverse(0, 1)
-        load_shocks(0, 2, 4)
-        nc.sync.dma_start(out=scale_row[:], in_=shocks_scale.rearrange("o k -> (o k)").partition_broadcast(P))
-        load_inverse(1, 0)
-        load_inverse(1, 1)
-        nc.sync.dma_start(out=base_kp[:], in_=base.rearrange("(j p t) -> p j t", p=P, t=T))
-        nc.sync.dma_start(out=weight_kp[:], in_=weight.rearrange("(g p t) -> p g t", p=P, t=T))
-        load_shocks(1, 0, 4)
-        load_shocks(2, 0, 4)
-        con_v = contrasts.rearrange("(a r) k -> r a k", r=P)
-        nc.sync.dma_start(out=con_raw[:, 0:2], in_=con_v[:, 0:2])
-        nc.sync.dma_start(out=con_raw[:, 2:4], in_=con_v[:, 2:4])
-        for quad in range(4):
-            nc.sync.dma_start(
-                out=b_scales[32 * quad : 32 * quad + 4].bitcast(I32),
-                in_=basket_scales.rearrange("j s n -> s j n")[4 * quad : 4 * quad + 4].bitcast(I32),
+        def load_contrasts(a):
+            nc.sync.dma_start(out=con_raw[a][:], in_=contrasts[P * a : P * (a + 1), :])
+
+        def load_baskets():
+            for quad in range(4):
+                nc.sync.dma_start(
+                    out=b_scales[32 * quad : 32 * quad + 4].bitcast(I32),
+                    in_=basket_scales.rearrange("j s n -> s j n")[4 * quad : 4 * quad + 4].bitcast(I32),
+                )
+            nc.sync.dma_start(out=b_words[:], in_=basket_words.rearrange("j p b -> p j b"))
+
+        def bank_of(number, shape):
+            return psum.tile(shape, F32, name="bank%d" % number)
+
+        def copy_on(engine, out, in_):
+            if engine == "scalar":
+                nc.scalar.copy(out=out, in_=in_)
+            else:
+                nc.vector.tensor_copy(out=out, in_=in_)
+
+        def spread_scales(q, number):
+            bank = bank_of(number, [P, T, P])
+            for t in range(T):
+                nc.tensor.transpose(bank[:, t, :], scale_kp[:, q, t : t + 1].to_broadcast([P, P]), ident[:])
+            nc.scalar.copy(
+                out=scale_row[:, KP * q : KP * (q + 1)].rearrange("p (m t) -> p m t", t=T),
+                in_=bank[:].rearrange("p t m -> p m t"),
             )
-        nc.sync.dma_start(out=b_words[:], in_=basket_words.rearrange("j p b -> p j b"))
 
         sh_wide = {}
         sh_bank = {}
         sh_group = {}
 
-        def widen_plain(i, engine):
-            x = work.tile([P, N], BF16, name="xb", bufs=4)
-            sh_wide[i] = x
-            if engine == "scalar":
-                nc.scalar.copy(out=x[:], in_=sh_bytes[:, i, :].bitcast(FP8))
-            else:
-                nc.vector.tensor_copy(out=x[:], in_=sh_bytes[:, i, :].bitcast(FP8))
+        def widen(i):
+            sh_wide[i] = work.tile([P, N], BF16, name="xb", bufs=4)
+            nc.vector.tensor_tensor(out=sh_wide[i][:], in0=sh_bytes[i // 2][:, i % 2, :].bitcast(FP8), in1=scale_row[:], op=MULT)
 
-        def widen_scaled(i):
-            x = work.tile([P, N], BF16, name="xb", bufs=4)
-            sh_wide[i] = x
-            nc.vector.tensor_tensor(out=x[:], in0=sh_bytes[:, i, :].bitcast(FP8), in1=scale_row[:], op=MULT)
+        def widen_plain(i):
+            sh_wide[i] = work.tile([P, N], BF16, name="xb", bufs=4)
+            nc.vector.tensor_copy(out=sh_wide[i][:], in_=sh_bytes[i // 2][:, i % 2, :].bitcast(FP8))
 
-        def turn_shocks(i):
-            bank = psum.tile([P, KQ, 2, P], F32, name="tr", bufs=3)
-            sh_bank[i] = bank
+        def empty_shocks_scaled(i):
+            sh_group[i] = work.tile([P, KQ * P * T], BF16, name="xg", bufs=4, align_bytes=64)
+            grouped = sh_group[i][:].rearrange("p (q r u e) -> p q r u e", q=KQ, u=2, e=2)
+            halves = sh_bank[i][:].rearrange("p q u r -> p (q u r)").bitcast(BF16)
+            halves = halves.rearrange("p (q u r e) -> p q r u e", q=KQ, u=2, e=2)
+            for q in range(KQ):
+                scales = scale_kp[:, q, :].rearrange("p (u e) -> p u e", u=2).unsqueeze(1).to_broadcast([P, P, 2, 2])
+                nc.vector.tensor_tensor(out=grouped[:, q], in0=halves[:, q], in1=scales, op=MULT)
+
+        def turn_shocks(i, number):
+            sh_bank[i] = bank_of(number, [P, KQ, 2, P])
             words = sh_wide[i][:].bitcast(F32)
             for q in range(KQ):
                 for u in range(2):
-                    nc.tensor.transpose(bank[:, q, u, :], words[:, 256 * q + u : 256 * (q + 1) : 2], ident[:])
-
-        def group_tile(i):
-            if i % 2 == 0:
-                sh_group[i // 2] = work.tile([P, 2, KQ * P * T], BF16, name="xg", bufs=2, align_bytes=64)
-            return sh_group[i // 2][:, i % 2, :]
-
-        def empty_shocks_scaled(i):
-            g = group_tile(i).rearrange("p (q r u e) -> p q r u e", q=KQ, u=2, e=2)
-            b = sh_bank[i][:].rearrange("p q u r -> p (q u r)").bitcast(BF16)
-            b = b.rearrange("p (q u r e) -> p q r u e", q=KQ, u=2, e=2)
-            for q in range(KQ):
-                sc = scale_kp[:, q, :].rearrange("p (u e) -> p u e", u=2).unsqueeze(1).to_broadcast([P, P, 2, 2])
-                nc.vector.tensor_tensor(out=g[:, q], in0=b[:, q], in1=sc, op=MULT)
+                    nc.tensor.transpose(sh_bank[i][:, q, u, :], words[:, 256 * q + u : 256 * (q + 1) : 2], ident[:])
 
         def empty_shocks(i):
-            g = group_tile(i).bitcast(F32).rearrange("p (q r u) -> p q r u", q=KQ, u=2)
-            nc.scalar.copy(out=g, in_=sh_bank[i][:].rearrange("p q u r -> p q r u"))
+            sh_group[i] = work.tile([P, KQ * P * T], BF16, name="xg", bufs=4, align_bytes=64)
+            nc.scalar.copy(
+                out=sh_group[i][:].bitcast(F32).rearrange("p (q r u) -> p q r u", q=KQ, u=2),
+                in_=sh_bank[i][:].rearrange("p q u r -> p q r u"),
+            )
 
-        def quantize_shocks(k):
+        def quantize_shocks(i):
             nc.vector.quantize_mx(
-                out=sh_codes[:, 2 * k : 2 * k + 2].rearrange("p i q r -> p (i q r)").bitcast(FP8X4),
-                scales=sh_scales[:, 2 * k : 2 * k + 2].rearrange("p i q r -> p (i q r)"),
-                in_=sh_group[k][:].rearrange("p i c -> p (i c)"),
+                out=sh_codes[:, i].rearrange("p q r -> p (q r)").bitcast(FP8X4),
+                scales=sh_scales[:, i].rearrange("p q r -> p (q r)"),
+                in_=sh_group[i][:],
             )
 
         inv_group = {}
 
-        def group_inverse(j, q, engine, c0, c1):
+        def group_inverse(j, q, engine, c0=0, c1=KP):
             if (j, q) not in inv_group:
                 inv_group[j, q] = work.tile([P, KP, T], BF16, name="ig", bufs=2, align_bytes=64)
-            dst = inv_group[j, q][:, c0:c1, :].rearrange("p (c i) t -> p c t i", i=4)
-            src = inv_raw[:, j, q, :, c0:c1].rearrange("p t (c i) -> p c t i", i=4)
-            if engine == "scalar":
-                nc.scalar.copy(out=dst, in_=src)
-            else:
-                nc.vector.tensor_copy(out=dst, in_=src)
+            copy_on(
+                engine,
+                inv_group[j, q][:, c0:c1, :].rearrange("p (c i) t -> p c t i", i=4),
+                inv_raw[j, q][:, :, c0:c1].rearrange("p t (c i) -> p c t i", i=4),
+            )
 
         def quantize_inverse(j, q):
             nc.vector.quantize_mx(
@@ -169,138 +168,123 @@ def tile_ghosh_price_push_s8_kernel(
         con_bank = {}
         con_group = {}
 
-        def turn_contrasts(g, a0):
-            bank = psum.tile([P, 2, 2, P], F32, name="tr", bufs=3)
-            con_bank[g, a0] = bank
+        def turn_contrasts(n, number):
+            g, a0 = n // 2, 2 * (n % 2)
+            con_bank[n] = bank_of(number, [P, 2, 2, P])
             for a in range(2):
-                words = con_raw[:, a0 + a, :].bitcast(F32)
+                words = con_raw[a0 + a][:].bitcast(F32)
                 for u in range(2):
-                    nc.tensor.transpose(bank[:, a, u, :], words[:, 256 * g + u : 256 * (g + 1) : 2], ident[:])
+                    nc.tensor.transpose(con_bank[n][:, a, u, :], words[:, 256 * g + u : 256 * (g + 1) : 2], ident[:])
 
-        def empty_contrasts(g, a0):
-            if a0 == 0:
-                con_group[g] = work.tile([P, R * T], BF16, name="cg", bufs=2, align_bytes=64)
-            dst = con_group[g][:].bitcast(F32).rearrange("p (a r u) -> p a r u", r=P, u=2)[:, a0 : a0 + 2]
-            nc.scalar.copy(out=dst, in_=con_bank[g, a0][:].rearrange("p a u r -> p a r u"))
+        def empty_contrasts(n):
+            con_group[n] = work.tile([P, 2 * P * T], BF16, name="xg", bufs=4, align_bytes=64)
+            nc.scalar.copy(
+                out=con_group[n][:].bitcast(F32).rearrange("p (a r u) -> p a r u", a=2, u=2),
+                in_=con_bank[n][:].rearrange("p a u r -> p a r u"),
+            )
 
-        def quantize_contrasts(g):
-            nc.vector.quantize_mx(out=con_codes[:, g, :].bitcast(FP8X4), scales=con_scales[:, g, :], in_=con_group[g][:])
+        def quantize_contrasts(n):
+            g, cols = n // 2, slice(HALF * (n % 2), HALF * (n % 2 + 1))
+            nc.vector.quantize_mx(out=con_codes[:, g, cols].bitcast(FP8X4), scales=con_scales[:, g, cols], in_=con_group[n][:])
 
         mv_bank = {}
         rel = {}
         tr_bank = {}
         priced = {}
+        scaled = {}
         weighted = {}
 
-        def unit(h, i):
-            return h // 2, BLOCKS[h // 2][0], BLOCKS[h // 2][1], 2 * (h % 2) + i
+        def unit(u):
+            return u // T, BLOCKS[u // T][0], BLOCKS[u // T][1], u % T
 
-        def moves(h):
-            for i in range(2):
-                b, g, j, t = unit(h, i)
-                bank = psum.tile([P, KP], F32, name="mm", bufs=3)
-                mv_bank[h, i] = bank
-                for q in range(KQ):
-                    nc.tensor.matmul_mx(
-                        out=bank[:],
-                        lhsT=sh_codes[:, T * g + t, q, :].bitcast(FP8X4),
-                        lhsT_scale=sh_scales[:, T * g + t, q, :],
-                        rhs=inv_codes[:, j, q, :].bitcast(FP8X4),
-                        rhs_scale=inv_scales[:, j, q, :],
-                        start=(q == 0),
-                        stop=(q == KQ - 1),
-                    )
-
-        def relatives(h):
-            for i in range(2):
-                b, g, j, t = unit(h, i)
-                if t == 0:
-                    rel[b] = work.tile([P, T, KP], F32, name="rel", bufs=3)
-                nc.scalar.activation(
-                    out=rel[b][:, t, :].rearrange("p (v m) -> p v m", v=T),
-                    in_=mv_bank[h, i][:].rearrange("p (m v) -> p v m", v=T),
-                    func=EXP,
+        def moves(u):
+            b, g, j, t = unit(u)
+            mv_bank[u] = bank_of(u % 2, [P, KP])
+            for q in range(KQ):
+                nc.tensor.matmul_mx(
+                    out=mv_bank[u][:],
+                    lhsT=sh_codes[:, T * g + t, q, :].bitcast(FP8X4),
+                    lhsT_scale=sh_scales[:, T * g + t, q, :],
+                    rhs=inv_codes[:, j, q, :].bitcast(FP8X4),
+                    rhs_scale=inv_scales[:, j, q, :],
+                    start=(q == 0),
+                    stop=(q == KQ - 1),
                 )
 
-        def turn(h):
-            for i in range(2):
-                b, g, j, t = unit(h, i)
-                bank = psum.tile([P, T, P], F32, name="tr", bufs=3)
-                tr_bank[h, i] = bank
-                for v in range(T):
-                    nc.tensor.transpose(bank[:, v, :], rel[b][:, t, P * v : P * (v + 1)], ident[:])
+        def relatives(u):
+            b, g, j, t = unit(u)
+            if t == 0:
+                rel[b] = work.tile([P, T, KP], F32, name="rel", bufs=REL_BUFS)
+            nc.scalar.activation(
+                out=rel[b][:, t, :].rearrange("p (v m) -> p v m", v=T),
+                in_=mv_bank[u][:].rearrange("p (m v) -> p v m", v=T),
+                func=EXP,
+            )
 
-        def price(h):
-            priced[h] = work.tile([P, 2, P, T], BF16, name="pr", bufs=3, align_bytes=64)
-            for i in range(2):
-                b, g, j, t = unit(h, i)
-                nc.vector.tensor_tensor(
-                    out=priced[h][:, i],
-                    in0=tr_bank[h, i][:].rearrange("p v m -> p m v"),
-                    in1=base_kp[:, j, :].unsqueeze(1).to_broadcast([P, P, T]),
-                    op=MULT,
-                )
+        def turn(u, number):
+            b, g, j, t = unit(u)
+            tr_bank[u] = bank_of(number, [P, T, P])
+            for v in range(T):
+                nc.tensor.transpose(tr_bank[u][:, v, :], rel[b][:, t, P * v : P * (v + 1)], ident[:])
 
-        def quantize_priced(h):
-            b, g, j, t = unit(h, 0)
-            cols = slice(P * t, P * (t + 2))
+        def price(u):
+            b, g, j, t = unit(u)
+            priced[u] = work.tile([P, P, T], BF16, name="pr", bufs=4, align_bytes=64)
+            nc.vector.tensor_tensor(
+                out=priced[u][:],
+                in0=tr_bank[u][:].rearrange("p v m -> p m v"),
+                in1=base_kp[:, j, :].unsqueeze(1).to_broadcast([P, P, T]),
+                op=MULT,
+            )
+
+        def quantize_priced(u):
+            b, g, j, t = unit(u)
+            cols = slice(P * t, P * (t + 1))
             nc.vector.quantize_mx(
                 out=pr_codes[:, g, j, cols].bitcast(FP8X4),
                 scales=pr_scales[:, g, j, cols],
-                in_=priced[h][:].rearrange("p i m v -> p (i m v)"),
+                in_=priced[u][:].rearrange("p m v -> p (m v)"),
             )
 
         def weigh(b, half):
             g = BLOCKS[b][0]
-            weighted[b, half] = work.tile([P, KP // 2, T], BF16, name="we", bufs=3, align_bytes=64)
-            cols = slice(KP // 2 * half, KP // 2 * (half + 1))
+            weighted[b, half] = work.tile([P, HALF, T], BF16, name="we", bufs=3, align_bytes=64)
             nc.vector.tensor_tensor(
-                out=weighted[b, half][:],
-                in0=rel[b][:, :, cols].rearrange("p t n -> p n t"),
-                in1=weight_kp[:, g, :].unsqueeze(1).to_broadcast([P, KP // 2, T]),
+                out=weighted[b, half][:].rearrange("p (c i) t -> p c t i", i=2),
+                in0=rel[b][:, :, HALF * half : HALF * (half + 1)].rearrange("p t (c i) -> p c t i", i=2),
+                in1=weight_kp[:, g, :].unsqueeze(1).unsqueeze(3).to_broadcast([P, HALF // 2, T, 2]),
                 op=MULT,
             )
 
-        scaled = {}
-
-        def scale_units(h):
-            for i in range(2):
-                b, g, j, t = unit(h, i)
-                if t == 0:
-                    scaled[b] = work.tile([P, T, KP], BF16, name="sc", bufs=2)
-                nc.scalar.activation(
-                    out=scaled[b][:, t, :],
-                    in_=rel[b][:, t, :],
-                    func=mybir.ActivationFunctionType.Copy,
-                    scale=weight_f32[:, g, t : t + 1],
-                )
+        def scale_unit(u):
+            b, g, j, t = unit(u)
+            if t == 0:
+                scaled[b] = work.tile([P, T, KP], BF16, name="sc", bufs=4)
+            nc.scalar.activation(out=scaled[b][:, t, :], in_=rel[b][:, t, :], func=COPY, scale=weight_f32[:, g, t : t + 1])
 
         def interleave(b, half):
-            weighted[b, half] = work.tile([P, KP // 2, T], BF16, name="we", bufs=3, align_bytes=64)
-            cols = slice(KP // 2 * half, KP // 2 * (half + 1))
+            weighted[b, half] = work.tile([P, HALF, T], BF16, name="we", bufs=3, align_bytes=64)
             nc.vector.tensor_copy(
                 out=weighted[b, half][:].rearrange("p (c i) t -> p c t i", i=4),
-                in_=scaled[b][:, :, cols].rearrange("p t (c i) -> p c t i", i=4),
+                in_=scaled[b][:, :, HALF * half : HALF * (half + 1)].rearrange("p t (c i) -> p c t i", i=4),
             )
 
         def quantize_weighted(b, half):
             g, j = BLOCKS[b]
-            cols = slice(KP // 2 * half, KP // 2 * (half + 1))
+            cols = slice(HALF * half, HALF * (half + 1))
             nc.vector.quantize_mx(
                 out=we_codes[:, g, j, cols].bitcast(FP8X4),
                 scales=we_scales[:, g, j, cols],
                 in_=weighted[b, half][:].rearrange("p n t -> p (n t)"),
             )
 
-        index_v = out_0.rearrange("(g m t) c -> g m t c", m=P, t=T)
-        acc_bank = {}
+        out_bank = {}
 
-        def index_mm(g, t):
-            bank = psum.tile([P, C], F32, name="acc", bufs=2)
-            acc_bank[0, g, t] = bank
+        def index_mm(g, t, number):
+            out_bank[0, g, t] = bank_of(number, [P, C])
             for j in range(NJ):
                 nc.tensor.matmul_mx(
-                    out=bank[:],
+                    out=out_bank[0, g, t][:],
                     lhsT=pr_codes[:, g, j, P * t : P * (t + 1)].bitcast(FP8X4),
                     lhsT_scale=pr_scales[:, g, j, P * t : P * (t + 1)],
                     rhs=b_words[:, j, :].bitcast(FP4X4),
@@ -311,18 +295,17 @@ def tile_ghosh_price_push_s8_kernel(
 
         def index_out(g, t, engine):
             res = work.tile([P, C], F32, name="res", bufs=8)
-            if engine == "scalar":
-                nc.scalar.copy(out=res[:], in_=acc_bank[0, g, t][:])
-            else:
-                nc.vector.tensor_copy(out=res[:], in_=acc_bank[0, g, t][:])
+            copy_on(engine, res[:], out_bank[0, g, t][:])
             nc.sync.dma_start(out=index_v[g][:, t, :], in_=res[:])
 
-        def contrast_mm(a, j, name, bufs):
-            bank = psum.tile([P, KP], F32, name=name, bufs=bufs)
-            acc_bank[1, a, j] = bank
-            for n, g in enumerate((0, 2, 1)):
+        def contrast_mm(a, j, n0, n1, number=None):
+            order = [g for g, jj in BLOCKS if jj == j]
+            if n0 == 0:
+                out_bank[1, a, j] = bank_of(number, [P, KP])
+            for n in range(n0, n1):
+                g = order[n]
                 nc.tensor.matmul_mx(
-                    out=bank[:],
+                    out=out_bank[1, a, j][:],
                     lhsT=con_codes[:, g, P * a : P * (a + 1)].bitcast(FP8X4),
                     lhsT_scale=con_scales[:, g, P * a : P * (a + 1)],
                     rhs=we_codes[:, g, j, :].bitcast(FP8X4),
@@ -333,142 +316,125 @@ def tile_ghosh_price_push_s8_kernel(
 
         def contrast_out(a, j, engine):
             res = work.tile([P, KP], F32, name="res", bufs=8)
-            dst = res[:].rearrange("p (m v) -> p m v", v=T)
-            src = acc_bank[1, a, j][:].rearrange("p (v m) -> p m v", v=T)
-            if engine == "scalar":
-                nc.scalar.copy(out=dst, in_=src)
-            else:
-                nc.vector.tensor_copy(out=dst, in_=src)
+            copy_on(
+                engine,
+                res[:].rearrange("p (m v) -> p m v", v=T),
+                out_bank[1, a, j][:].rearrange("p (v m) -> p m v", v=T),
+            )
             nc.sync.dma_start(out=out_1[P * a : P * (a + 1), KP * j : KP * (j + 1)], in_=res[:])
 
-        widen_plain(0, "vector")
-        widen_plain(1, "scalar")
-        turn_shocks(0)
-        group_inverse(0, 0, "scalar", 0, KP)
-        turn_shocks(1)
+        nc.vector.memset(warm[:], 0.0)
+        nc.scalar.activation(out=warm[:], in_=warm[:], func=EXP)
+        nc.vector.memset(b_scales[:].rearrange("p j n -> p (j n)").bitcast(I32), 0)
+        make_identity(nc, ident[:])
+        nc.sync.dma_start(out=scale_kp[:], in_=shocks_scale.rearrange("o (q p t) -> p (o q) t", p=P, t=T))
+        load_shocks(0)
+        load_inverse(0, 0)
+        load_inverse(0, 1)
+        load_shocks(1)
+        load_inverse(1, 0)
+        load_contrasts(0)
+        load_contrasts(1)
+        load_shocks(2)
+        load_inverse(1, 1)
+        nc.sync.dma_start(out=base_kp[:], in_=base.rearrange("(j p t) -> p j t", p=P, t=T))
+        nc.sync.dma_start(out=weight_kp[:], in_=weight.rearrange("(g p t) -> p g t", p=P, t=T))
+        load_shocks(3)
+        load_contrasts(2)
+        load_contrasts(3)
+        load_shocks(4)
+        load_shocks(5)
+        load_baskets()
+
+        U = T * len(BLOCKS)
+        PAIRED = 14
+        plan = {}
+
+        def at(step, stage, job, *args):
+            plan.setdefault((step, stage), []).append((job, args))
+
+        for u in range(U):
+            s = u if u < PAIRED else u - u % 2
+            s_turn = u if u < 2 else min(u + 2, PAIRED) if u < PAIRED else s
+            if u >= 2:
+                at(s, "mx", moves, u)
+                at(s, "exp", relatives, u)
+            at(s_turn, "turn", turn, u, (4 if s == PAIRED else 2) + u % 2)
+            at(s_turn + 1, "price", price, u)
+            at(s_turn + 1, "q2" if s_turn < PAIRED else "q0", quantize_priced, u)
+        preps = []
+        for i in range(2, SG * T):
+            s = i - 4 if i < T else 3 * (i - T) // 2
+            at(s, "widen", widen, i)
+            preps.append((s + 1, turn_shocks, empty_shocks, quantize_shocks, i))
+        for n, s in ((0, -2), (2, -1), (4, 0), (1, 6), (3, 9), (5, 12)):
+            preps.append((s, turn_contrasts, empty_contrasts, quantize_contrasts, n))
+        for k, (s, turn_job, empty_job, quantize_job, i) in enumerate(sorted(preps, key=lambda job: job[0])):
+            at(s, "prep", turn_job, i, 4 + k % (4 if s < 3 else 2))
+            at(s + 1, "empty", empty_job, i)
+            at(s + 2, "q0" if s < 2 else "q1", quantize_job, i)
+        at(0, "q2", quantize_inverse, 1, 0)
+        at(1, "scale", group_inverse, 1, 1, "scalar", 0, HALF)
+        at(2, "scale", group_inverse, 1, 1, "scalar", HALF, KP)
+        at(3, "q1", quantize_inverse, 1, 1)
+        at(2, "q2", lambda: nc.vector.tensor_copy(out=weight_f32[:], in_=weight_kp[:]))
+        for b, steps, s_weigh in ((0, (4, 5, 6, 7), 11), (2, (9, 10, 11, 12), 13), (3, (13, 14, 14, 14), 15), (1, (15, 15, 16, 16), 17), (5, (21, 21, 22, 22), 23)):
+            for t in range(T):
+                at(steps[t], "scale2" if steps[t] >= PAIRED and steps[t] % 2 == 0 else "scale", scale_unit, T * b + t)
+            for half in range(2):
+                at(s_weigh, "weigh" if b < 5 else "first", interleave, b, half)
+            for half in range(2):
+                at(s_weigh, "q2" if b < 5 else "first", quantize_weighted, b, half)
+        for b, s in ((4, 19),):
+            for half in range(2):
+                at(s, "weigh", weigh, b, half)
+                at(s, "q2", quantize_weighted, b, half)
+        for t in range(T):
+            at(10 + t, "acc2", index_mm, 0, t, 6 + t % 2)
+            at(11 + t, "out", index_out, 0, t, "scalar")
+            at(20 + t - t % 2, "acc2", index_mm, 2, t, 6 + t % 2)
+            at(21 + t - t % 2, "out", index_out, 2, t, "scalar")
+        for a in range(T):
+            if a < 2:
+                at(14, "acc", contrast_mm, a, 0, 0, 1, 6 + a)
+                at(16, "acc", contrast_mm, a, 0, 1, 2)
+                at(20, "acc", contrast_mm, a, 1, 0, 1, 4 + a)
+            else:
+                at(16, "acc", contrast_mm, a, 0, 0, 2, 2 + a)
+            at(18, "acc", contrast_mm, a, 0, 2, 3)
+            at(19, "out", contrast_out, a, 0, "scalar")
+        for t in range(2):
+            at(23, "acc", index_mm, 1, t, 6 + t)
+            at(24, "out", index_out, 1, t, "scalar")
+            at(23, "acc2", contrast_mm, t, 1, 1, 2)
+        for t in range(2):
+            at(23, "acc2", contrast_mm, t, 1, 2, 3)
+            at(24, "out", contrast_out, t, 1, "scalar")
+            at(24 + t, "acc", index_mm, 1, 2 + t, 2 + t)
+            at(25 + t, "out", index_out, 1, 2 + t, "vector")
+            at(24 + t, "acc2", contrast_mm, 2 + t, 1, 0, 3, t)
+            at(25 + t, "out", contrast_out, 2 + t, 1, "scalar")
+
+        spread_scales(0, 6)
+        spread_scales(1, 7)
+        widen_plain(0)
+        widen_plain(1)
+        turn_shocks(0, 2)
+        group_inverse(0, 0, "vector")
+        turn_shocks(1, 3)
         empty_shocks_scaled(0)
-        empty_shocks_scaled(1)
-        group_inverse(0, 1, "scalar", 0, 3 * KP // 4)
-        group_inverse(0, 1, "vector", 3 * KP // 4, KP)
-        quantize_shocks(0)
         quantize_inverse(0, 0)
-        widen_plain(2, "scalar")
-        turn_shocks(2)
-        widen_plain(3, "scalar")
+        group_inverse(0, 1, "scalar")
+        quantize_shocks(0)
+        empty_shocks_scaled(1)
         quantize_inverse(0, 1)
-        moves(0)
-        turn_shocks(3)
-        empty_shocks_scaled(2)
-        empty_shocks_scaled(3)
-        relatives(0)
-        nc.vector.tensor_copy(out=weight_f32[:], in_=weight_kp[:])
-        widen_scaled(4)
         quantize_shocks(1)
-
-        for h in range(12):
-            if h > 0:
-                moves(h)
-                relatives(h)
-            if h == 0:
-                group_inverse(1, 0, "scalar", 0, KP)
-                group_inverse(1, 1, "scalar", 0, KP)
-                widen_scaled(5)
-                widen_scaled(6)
-                quantize_inverse(1, 0)
-            if h == 1:
-                turn_shocks(4)
-                turn_shocks(5)
-                empty_shocks(4)
-                empty_shocks(5)
-                widen_scaled(7)
-                quantize_inverse(1, 1)
-                quantize_shocks(2)
-            if h == 2:
-                turn_shocks(6)
-                turn_shocks(7)
-                empty_shocks(6)
-                empty_shocks(7)
-                widen_scaled(8)
-                widen_scaled(9)
-                quantize_shocks(3)
-            if h == 3:
-                turn_shocks(8)
-                turn_shocks(9)
-                empty_shocks(8)
-                empty_shocks(9)
-                widen_scaled(10)
-                widen_scaled(11)
-                quantize_shocks(4)
-            if h == 4:
-                turn_shocks(10)
-                turn_shocks(11)
-                empty_shocks(10)
-                empty_shocks(11)
-            if h in (2, 3):
-                weigh(0, h % 2)
-            if h >= 3:
-                scale_units(h - 1)
-            if h >= 4 and h % 2 == 1:
-                interleave(h // 2 - 1, 0)
-                interleave(h // 2 - 1, 1)
-            if h == 4:
-                quantize_shocks(5)
-            if h in (5, 6, 7):
-                turn_contrasts(h - 5, 0)
-                turn_contrasts(h - 5, 2)
-                empty_contrasts(h - 5, 0)
-                empty_contrasts(h - 5, 2)
-            if h >= 1:
-                turn(h - 1)
-                price(h - 1)
-            if h in (2, 3):
-                quantize_weighted(0, h % 2)
-            if h >= 4 and h % 2 == 1:
-                quantize_weighted(h // 2 - 1, 0)
-                quantize_weighted(h // 2 - 1, 1)
-            if h in (5, 6, 7):
-                quantize_contrasts(h - 5)
-            if h >= 1:
-                quantize_priced(h - 1)
-            if h in (5, 6):
-                for t in (0, 1):
-                    index_mm(0, 2 * (h - 5) + t)
-                for t in (0, 1):
-                    index_out(0, 2 * (h - 5) + t, "scalar")
-            if h in (10, 11):
-                for a in (0, 1):
-                    contrast_mm(2 * (h - 10) + a, 0, "acc", 2)
-                for a in (0, 1):
-                    contrast_out(2 * (h - 10) + a, 0, "scalar")
-
-        turn(11)
-        scale_units(11)
-        index_mm(2, 0)
-        index_mm(2, 1)
-        index_out(2, 0, "scalar")
-        index_out(2, 1, "scalar")
-        price(11)
-        interleave(5, 0)
-        interleave(5, 1)
-        quantize_priced(11)
-        quantize_weighted(5, 0)
-        quantize_weighted(5, 1)
-        index_mm(2, 2)
-        index_mm(2, 3)
-        index_out(2, 2, "scalar")
-        index_out(2, 3, "vector")
-        index_mm(1, 0)
-        index_mm(1, 1)
-        index_out(1, 0, "scalar")
-        index_out(1, 1, "vector")
-        for a in range(3):
-            contrast_mm(a, 1, "mm", 3)
-        index_mm(1, 2)
-        index_mm(1, 3)
-        index_out(1, 2, "scalar")
-        contrast_out(0, 1, "vector")
-        contrast_out(1, 1, "scalar")
-        contrast_out(2, 1, "vector")
-        contrast_mm(3, 1, "tr", 3)
-        index_out(1, 3, "scalar")
-        contrast_out(3, 1, "vector")
+        moves(0)
+        moves(1)
+        group_inverse(1, 0, "scalar")
+        relatives(0)
+        relatives(1)
+        for step in range(-2, U + 7):
+            for stage in ("first", "price", "q0", "widen", "q1", "weigh", "q2", "out", "empty", "scale", "mx", "exp", "scale2", "acc", "acc2", "turn", "prep"):
+                for job, args in plan.get((step, stage), []):
+                    job(*args)

@@ -26,7 +26,7 @@ KQ = N // KP
 NJ = N // KP
 HALF = KP // 2
 
-BLOCKS = ((0, 0), (0, 1), (1, 0), (2, 0), (2, 1), (1, 1))
+BLOCKS = tuple((g, j) for g in range(SG) for j in range(NJ))
 STEPS = 2 * len(BLOCKS)
 REL_BUFS = 6
 
@@ -118,7 +118,7 @@ def tile_ghosh_price_push_s8_kernel(
             nc.vector.tensor_copy(out=sh_wide[i][:], in_=sh_bytes[i // 2][:, i % 2, :].bitcast(FP8))
 
         def empty_shocks_scaled(i):
-            sh_group[i] = work.tile([P, KQ * P * T], BF16, name="xg", bufs=4, align_bytes=64)
+            sh_group[i] = work.tile([P, KQ * P * T], BF16, name="xg", bufs=6, align_bytes=64)
             grouped = sh_group[i][:].rearrange("p (q r u e) -> p q r u e", q=KQ, u=2, e=2)
             halves = sh_bank[i][:].rearrange("p q u r -> p (q u r)").bitcast(BF16)
             halves = halves.rearrange("p (q u r e) -> p q r u e", q=KQ, u=2, e=2)
@@ -134,7 +134,7 @@ def tile_ghosh_price_push_s8_kernel(
                     nc.tensor.transpose(sh_bank[i][:, q, u, :], words[:, 256 * q + u : 256 * (q + 1) : 2], ident[:])
 
         def empty_shocks(i):
-            sh_group[i] = work.tile([P, KQ * P * T], BF16, name="xg", bufs=4, align_bytes=64)
+            sh_group[i] = work.tile([P, KQ * P * T], BF16, name="xg", bufs=6, align_bytes=64)
             nc.scalar.copy(
                 out=sh_group[i][:].bitcast(F32).rearrange("p (q r u) -> p q r u", q=KQ, u=2),
                 in_=sh_bank[i][:].rearrange("p q u r -> p q r u"),
@@ -177,7 +177,7 @@ def tile_ghosh_price_push_s8_kernel(
                     nc.tensor.transpose(con_bank[n][:, a, u, :], words[:, 256 * g + u : 256 * (g + 1) : 2], ident[:])
 
         def empty_contrasts(n):
-            con_group[n] = work.tile([P, 2 * P * T], BF16, name="xg", bufs=4, align_bytes=64)
+            con_group[n] = work.tile([P, 2 * P * T], BF16, name="xg", bufs=6, align_bytes=64)
             nc.scalar.copy(
                 out=con_group[n][:].bitcast(F32).rearrange("p (a r u) -> p a r u", a=2, u=2),
                 in_=con_bank[n][:].rearrange("p a u r -> p a r u"),
@@ -335,19 +335,19 @@ def tile_ghosh_price_push_s8_kernel(
         load_inverse(1, 0)
         load_contrasts(0)
         load_contrasts(1)
-        load_shocks(2)
         load_inverse(1, 1)
         nc.sync.dma_start(out=base_kp[:], in_=base.rearrange("(j p t) -> p j t", p=P, t=T))
         nc.sync.dma_start(out=weight_kp[:], in_=weight.rearrange("(g p t) -> p g t", p=P, t=T))
-        load_shocks(3)
+        load_shocks(2)
         load_contrasts(2)
         load_contrasts(3)
+        load_shocks(3)
+        load_baskets()
         load_shocks(4)
         load_shocks(5)
-        load_baskets()
 
         U = T * len(BLOCKS)
-        PAIRED = 14
+        PAIRED = 8
         plan = {}
 
         def at(step, stage, job, *args):
@@ -355,65 +355,71 @@ def tile_ghosh_price_push_s8_kernel(
 
         for u in range(U):
             s = u if u < PAIRED else u - u % 2
-            s_turn = u if u < 2 else min(u + 2, PAIRED) if u < PAIRED else s
+            s_turn = u if u < 2 else min(u + 2, PAIRED) if u < PAIRED else min(s + 2, U - 2)
             if u >= 2:
                 at(s, "mx", moves, u)
                 at(s, "exp", relatives, u)
-            at(s_turn, "turn", turn, u, (4 if s == PAIRED else 2) + u % 2)
-            at(s_turn + 1, "price", price, u)
-            at(s_turn + 1, "q2" if s_turn < PAIRED else "q0", quantize_priced, u)
+            at(s_turn, "turn0" if u in (U - 4, U - 3) else "turn", turn, u, (2 if u < U - 2 else 0) + u % 2)
+            if u < U - 2:
+                at(s_turn + 1, "price", price, u)
+                at(s_turn + 1, "q2" if s_turn < PAIRED else "q0", quantize_priced, u)
         preps = []
-        for i in range(2, SG * T):
-            s = i - 4 if i < T else 3 * (i - T) // 2
-            at(s, "widen", widen, i)
-            preps.append((s + 1, turn_shocks, empty_shocks, quantize_shocks, i))
-        for n, s in ((0, -2), (2, -1), (4, 0), (1, 6), (3, 9), (5, 12)):
-            preps.append((s, turn_contrasts, empty_contrasts, quantize_contrasts, n))
-        for k, (s, turn_job, empty_job, quantize_job, i) in enumerate(sorted(preps, key=lambda job: job[0])):
-            at(s, "prep", turn_job, i, 4 + k % (4 if s < 3 else 2))
+        for i, s in ((2, -2), (3, -1), (4, 1), (5, 2), (6, 4), (7, 5), (8, 6), (9, 7), (10, 9), (11, 11)):
+            at(s, "first" if s > PAIRED else "widen", widen, i)
+            preps.append((s + 1, turn_shocks, empty_shocks, quantize_shocks, i, 2 if s < 7 else 3))
+        for n, s in ((0, -2), (2, 0), (4, 1), (1, 4), (3, 6), (5, 14)):
+            preps.append((s, turn_contrasts, empty_contrasts, quantize_contrasts, n, 3))
+        for k, (s, turn_job, empty_job, quantize_job, i, lag) in enumerate(sorted(preps, key=lambda job: job[0])):
+            at(s, "prep", turn_job, i, 4 + k % (4 if s < 7 else 2))
             at(s + 1, "empty", empty_job, i)
-            at(s + 2, "q0" if s < 2 else "q1", quantize_job, i)
-        at(0, "q2", quantize_inverse, 1, 0)
+            at(s + lag, "first" if s + lag > PAIRED else "q0" if s < 2 and lag == 2 else "q1", quantize_job, i)
+        at(0, "q1", quantize_inverse, 1, 0)
         at(1, "scale", group_inverse, 1, 1, "scalar", 0, HALF)
         at(2, "scale", group_inverse, 1, 1, "scalar", HALF, KP)
-        at(3, "q1", quantize_inverse, 1, 1)
+        at(3, "q0", quantize_inverse, 1, 1)
         at(2, "q2", lambda: nc.vector.tensor_copy(out=weight_f32[:], in_=weight_kp[:]))
-        for b, steps, s_weigh in ((0, (4, 5, 6, 7), 11), (2, (9, 10, 11, 12), 13), (3, (13, 14, 14, 14), 15), (1, (15, 15, 16, 16), 17), (5, (21, 21, 22, 22), 23)):
+        for b, steps in ((0, (4, 5, 7, 8)), (2, (9, 10, 10, 11)), (1, (12, 13, 14, 15)), (4, (16, 17, 18, 18)), (5, (20, 20, 22, 22))):
             for t in range(T):
                 at(steps[t], "scale2" if steps[t] >= PAIRED and steps[t] % 2 == 0 else "scale", scale_unit, T * b + t)
-            for half in range(2):
-                at(s_weigh, "weigh" if b < 5 else "first", interleave, b, half)
-            for half in range(2):
-                at(s_weigh, "q2" if b < 5 else "first", quantize_weighted, b, half)
-        for b, s in ((4, 19),):
-            for half in range(2):
-                at(s, "weigh", weigh, b, half)
-                at(s, "q2", quantize_weighted, b, half)
+        for step, stage, halves in ((11, "weigh", ((0, 0), (0, 1))), (13, "weigh", ((2, 0), (2, 1))), (19, "first", ((4, 0), (4, 1))), (23, "q1", ((5, 0), (5, 1))), (15, "weigh", ((3, 0),)), (17, "weigh", ((3, 1), (1, 0))), (21, "first", ((1, 1),))):
+            for b, half in halves:
+                at(step, stage, weigh if b == 3 else interleave, b, half)
+            for b, half in halves:
+                at(step, "q2" if stage == "weigh" else stage, quantize_weighted, b, half)
+        for t, s in enumerate((8, 10, 10, 12)):
+            at(s, "acc2", index_mm, 0, t, 6 + t % 2)
+            at(s + 1, "out", index_out, 0, t, "scalar")
         for t in range(T):
-            at(10 + t, "acc2", index_mm, 0, t, 6 + t % 2)
-            at(11 + t, "out", index_out, 0, t, "scalar")
-            at(20 + t - t % 2, "acc2", index_mm, 2, t, 6 + t % 2)
-            at(21 + t - t % 2, "out", index_out, 2, t, "scalar")
+            at(16 + t - t % 2, "acc2", index_mm, 1, t, 4 + t % 2)
+            at(17 + t - t % 2, "out", index_out, 1, t, "scalar")
+        at(14, "acc", contrast_mm, 0, 0, 0, 1, 6)
+        at(14, "acc", contrast_mm, 1, 0, 0, 1, 7)
+        at(16, "acc", contrast_mm, 0, 0, 1, 2)
+        at(16, "acc", contrast_mm, 1, 0, 1, 2)
         for a in range(T):
-            if a < 2:
-                at(14, "acc", contrast_mm, a, 0, 0, 1, 6 + a)
-                at(16, "acc", contrast_mm, a, 0, 1, 2)
-                at(20, "acc", contrast_mm, a, 1, 0, 1, 4 + a)
-            else:
-                at(16, "acc", contrast_mm, a, 0, 0, 2, 2 + a)
-            at(18, "acc", contrast_mm, a, 0, 2, 3)
-            at(19, "out", contrast_out, a, 0, "scalar")
+            if a >= 2:
+                at(20, "acc", contrast_mm, a, 0, 0, 2, 2 + a)
+            at(20, "acc2", contrast_mm, a, 0, 2, 3)
+            at(21, "out", contrast_out, a, 0, "scalar")
+        for a in range(2):
+            at(22, "acc", contrast_mm, a, 1, 0, 2, 6 + a)
+        for u in (U - 2, U - 1):
+            at(23, "q2", price, u)
+        for u in (U - 2, U - 1):
+            at(23, "q2", quantize_priced, u)
         for t in range(2):
-            at(23, "acc", index_mm, 1, t, 6 + t)
-            at(24, "out", index_out, 1, t, "scalar")
-            at(23, "acc2", contrast_mm, t, 1, 1, 2)
-        for t in range(2):
-            at(23, "acc2", contrast_mm, t, 1, 2, 3)
-            at(24, "out", contrast_out, t, 1, "scalar")
-            at(24 + t, "acc", index_mm, 1, 2 + t, 2 + t)
-            at(25 + t, "out", index_out, 1, 2 + t, "vector")
-            at(24 + t, "acc2", contrast_mm, 2 + t, 1, 0, 3, t)
-            at(25 + t, "out", contrast_out, 2 + t, 1, "scalar")
+            at(23, "acc", index_mm, 2, t, 2 + t)
+            at(24, "out", index_out, 2, t, "scalar")
+        at(23, "acc", contrast_mm, 2, 1, 0, 2, 4)
+        for a in range(3):
+            at(23, "acc", contrast_mm, a, 1, 2, 3)
+            at(24, "out", contrast_out, a, 1, "vector" if a == 2 else "scalar")
+        at(23, "acc", index_mm, 2, 2, 0)
+        at(24, "out", index_out, 2, 2, "scalar")
+        at(23, "acc", contrast_mm, 3, 1, 0, 3, 5)
+        at(24, "out", contrast_out, 3, 1, "vector")
+        at(23, "acc", index_mm, 2, 3, 1)
+        at(24, "out", index_out, 2, 3, "scalar")
 
         spread_scales(0, 6)
         spread_scales(1, 7)
@@ -434,7 +440,7 @@ def tile_ghosh_price_push_s8_kernel(
         group_inverse(1, 0, "scalar")
         relatives(0)
         relatives(1)
-        for step in range(-2, U + 7):
-            for stage in ("first", "price", "q0", "widen", "q1", "weigh", "q2", "out", "empty", "scale", "mx", "exp", "scale2", "acc", "acc2", "turn", "prep"):
+        for step in range(-2, U + 2):
+            for stage in ("first", "price", "q0", "widen", "q1", "weigh", "q2", "out", "empty", "scale", "mx", "exp", "scale2", "turn0", "acc", "acc2", "turn", "prep"):
                 for job, args in plan.get((step, stage), []):
                     job(*args)

@@ -110,11 +110,11 @@ def tile_ghosh_price_push_s8_kernel(
         sh_group = {}
 
         def widen(i):
-            sh_wide[i] = work.tile([P, N], BF16, name="xb", bufs=4)
+            sh_wide[i] = work.tile([P, N], BF16, name="xb", bufs=5)
             nc.vector.tensor_tensor(out=sh_wide[i][:], in0=sh_bytes[i // 2][:, i % 2, :].bitcast(FP8), in1=scale_row[:], op=MULT)
 
         def widen_plain(i):
-            sh_wide[i] = work.tile([P, N], BF16, name="xb", bufs=4)
+            sh_wide[i] = work.tile([P, N], BF16, name="xb", bufs=5)
             nc.vector.tensor_copy(out=sh_wide[i][:], in_=sh_bytes[i // 2][:, i % 2, :].bitcast(FP8))
 
         def empty_shocks_scaled(i):
@@ -125,6 +125,11 @@ def tile_ghosh_price_push_s8_kernel(
             for q in range(KQ):
                 scales = scale_kp[:, q, :].rearrange("p (u e) -> p u e", u=2).unsqueeze(1).to_broadcast([P, P, 2, 2])
                 nc.vector.tensor_tensor(out=grouped[:, q], in0=halves[:, q], in1=scales, op=MULT)
+
+        def keep_clock(n, number):
+            bank = bank_of(number, [P, KP])
+            for k in range(n):
+                nc.tensor.matmul(bank[:], sh_wide[1][:, 0:P], sh_wide[1][:, 0:KP], start=True, stop=True)
 
         def turn_shocks(i, number):
             sh_bank[i] = bank_of(number, [P, KQ, 2, P])
@@ -258,15 +263,16 @@ def tile_ghosh_price_push_s8_kernel(
 
         def scale_unit(u):
             b, g, j, t = unit(u)
-            if t == 0:
+            if b not in scaled:
                 scaled[b] = work.tile([P, T, KP], BF16, name="sc", bufs=4)
             nc.scalar.activation(out=scaled[b][:, t, :], in_=rel[b][:, t, :], func=COPY, scale=weight_f32[:, g, t : t + 1])
 
-        def interleave(b, half):
+        def interleave(b, half, engine="vector"):
             weighted[b, half] = work.tile([P, HALF, T], BF16, name="we", bufs=3, align_bytes=64)
-            nc.vector.tensor_copy(
-                out=weighted[b, half][:].rearrange("p (c i) t -> p c t i", i=4),
-                in_=scaled[b][:, :, HALF * half : HALF * (half + 1)].rearrange("p t (c i) -> p c t i", i=4),
+            copy_on(
+                engine,
+                weighted[b, half][:].rearrange("p (c i) t -> p c t i", i=4),
+                scaled[b][:, :, HALF * half : HALF * (half + 1)].rearrange("p t (c i) -> p c t i", i=4),
             )
 
         def quantize_weighted(b, half):
@@ -353,10 +359,10 @@ def tile_ghosh_price_push_s8_kernel(
         def at(step, stage, job, *args):
             plan.setdefault((step, stage), []).append((job, args))
 
-        for u in range(U):
+        for u in range(2, U):
             s = u if u < PAIRED else u - u % 2
-            s_turn = u if u < 2 else min(u + 2, PAIRED) if u < PAIRED else min(s + 2, U - 2)
-            if u >= 2:
+            s_turn = min(u + 2, PAIRED) if u < PAIRED else min(s + 2, U - 2)
+            if u >= 4:
                 at(s, "mx", moves, u)
                 at(s, "exp", relatives, u)
             at(s_turn, "turn0" if u in (U - 4, U - 3) else "turn", turn, u, (2 if u < U - 2 else 0) + u % 2)
@@ -364,24 +370,18 @@ def tile_ghosh_price_push_s8_kernel(
                 at(s_turn + 1, "price", price, u)
                 at(s_turn + 1, "q2" if s_turn < PAIRED else "q0", quantize_priced, u)
         preps = []
-        for i, s in ((2, -2), (3, -1), (4, 1), (5, 2), (6, 4), (7, 5), (8, 6), (9, 7), (10, 9), (11, 11)):
+        for i, s in ((6, 4), (7, 5), (8, 6), (9, 7), (10, 9), (11, 11)):
             at(s, "first" if s > PAIRED else "widen", widen, i)
             preps.append((s + 1, turn_shocks, empty_shocks, quantize_shocks, i, 2 if s < 7 else 3))
-        for n, s in ((0, -2), (2, 0), (4, 1), (1, 4), (3, 6), (5, 14)):
+        for n, s in ((1, 4), (3, 6), (5, 14)):
             preps.append((s, turn_contrasts, empty_contrasts, quantize_contrasts, n, 3))
         for k, (s, turn_job, empty_job, quantize_job, i, lag) in enumerate(sorted(preps, key=lambda job: job[0])):
-            at(s, "prep", turn_job, i, 4 + k % (4 if s < 7 else 2))
+            at(s, "prep", turn_job, i, 4 + (k + 3) % (4 if s < 7 else 2))
             at(s + 1, "empty", empty_job, i)
-            at(s + lag, "first" if s + lag > PAIRED else "q0" if s < 2 and lag == 2 else "q1", quantize_job, i)
-        at(0, "q1", quantize_inverse, 1, 0)
-        at(1, "scale", group_inverse, 1, 1, "scalar", 0, HALF)
-        at(2, "scale", group_inverse, 1, 1, "scalar", HALF, KP)
-        at(3, "q0", quantize_inverse, 1, 1)
-        at(2, "q2", lambda: nc.vector.tensor_copy(out=weight_f32[:], in_=weight_kp[:]))
-        for b, steps in ((0, (4, 5, 7, 8)), (2, (9, 10, 10, 11)), (1, (12, 13, 14, 15)), (4, (16, 17, 18, 18)), (5, (20, 20, 22, 22))):
-            for t in range(T):
-                at(steps[t], "scale2" if steps[t] >= PAIRED and steps[t] % 2 == 0 else "scale", scale_unit, T * b + t)
-        for step, stage, halves in ((11, "weigh", ((0, 0), (0, 1))), (13, "weigh", ((2, 0), (2, 1))), (19, "first", ((4, 0), (4, 1))), (23, "q1", ((5, 0), (5, 1))), (15, "weigh", ((3, 0),)), (17, "weigh", ((3, 1), (1, 0))), (21, "first", ((1, 1),))):
+            at(s + lag, "first" if s + lag > PAIRED else "q1", quantize_job, i)
+        for u, step in ((0, 4), (1, 5), (2, 7), (3, 8), (8, 9), (9, 10), (10, 10), (11, 11), (4, 12), (5, 13), (6, 14), (7, 15), (16, 16), (17, 17), (18, 18), (19, 18), (20, 20), (21, 20), (22, 22), (23, 22)):
+            at(step, "scale2" if step >= PAIRED and step % 2 == 0 else "scale", scale_unit, u)
+        for step, stage, halves in ((11, "weigh", ((0, 0), (0, 1))), (13, "weigh", ((2, 0), (2, 1))), (19, "first", ((4, 0), (4, 1))), (15, "weigh", ((3, 0),)), (17, "weigh", ((3, 1), (1, 0))), (21, "first", ((1, 1),)), (23, "q1", ((5, 0), (5, 1)))):
             for b, half in halves:
                 at(step, stage, weigh if b == 3 else interleave, b, half)
             for b, half in halves:
@@ -392,10 +392,9 @@ def tile_ghosh_price_push_s8_kernel(
         for t in range(T):
             at(16 + t - t % 2, "acc2", index_mm, 1, t, 4 + t % 2)
             at(17 + t - t % 2, "out", index_out, 1, t, "scalar")
-        at(14, "acc", contrast_mm, 0, 0, 0, 1, 6)
-        at(14, "acc", contrast_mm, 1, 0, 0, 1, 7)
-        at(16, "acc", contrast_mm, 0, 0, 1, 2)
-        at(16, "acc", contrast_mm, 1, 0, 1, 2)
+        for a in range(2):
+            at(14, "acc", contrast_mm, a, 0, 0, 1, 6 + a)
+            at(16, "acc", contrast_mm, a, 0, 1, 2)
         for a in range(T):
             if a >= 2:
                 at(20, "acc", contrast_mm, a, 0, 0, 2, 2 + a)
@@ -421,6 +420,7 @@ def tile_ghosh_price_push_s8_kernel(
         at(23, "acc", index_mm, 2, 3, 1)
         at(24, "out", index_out, 2, 3, "scalar")
 
+
         spread_scales(0, 6)
         spread_scales(1, 7)
         widen_plain(0)
@@ -428,6 +428,7 @@ def tile_ghosh_price_push_s8_kernel(
         turn_shocks(0, 2)
         group_inverse(0, 0, "vector")
         turn_shocks(1, 3)
+        keep_clock(3, 7)
         empty_shocks_scaled(0)
         quantize_inverse(0, 0)
         group_inverse(0, 1, "scalar")
@@ -440,7 +441,47 @@ def tile_ghosh_price_push_s8_kernel(
         group_inverse(1, 0, "scalar")
         relatives(0)
         relatives(1)
-        for step in range(-2, U + 2):
+        widen(2)
+        turn_contrasts(0, 4)
+        widen(3)
+        empty_contrasts(0)
+        turn_shocks(2, 5)
+        quantize_inverse(1, 0)
+        empty_shocks(2)
+        turn(0, 2)
+        turn_shocks(3, 6)
+        turn_contrasts(2, 7)
+        price(0)
+        quantize_shocks(2)
+        widen(4)
+        quantize_contrasts(0)
+        quantize_priced(0)
+        empty_shocks(3)
+        empty_contrasts(2)
+        group_inverse(1, 1, "scalar", 0, HALF)
+        turn(1, 3)
+        turn_contrasts(4, 4)
+        price(1)
+        quantize_shocks(3)
+        widen(5)
+        quantize_priced(1)
+        nc.vector.tensor_copy(out=weight_f32[:], in_=weight_kp[:])
+        empty_contrasts(4)
+        group_inverse(1, 1, "scalar", HALF, KP)
+        moves(2)
+        relatives(2)
+        turn_shocks(4, 5)
+        quantize_inverse(1, 1)
+        quantize_contrasts(2)
+        empty_shocks(4)
+        moves(3)
+        relatives(3)
+        turn_shocks(5, 6)
+        at(4, "empty", empty_shocks, 5)
+        at(4, "q1", quantize_contrasts, 4)
+        at(4, "q1", quantize_shocks, 4)
+        at(5, "q1", quantize_shocks, 5)
+        for step in range(4, U + 2):
             for stage in ("first", "price", "q0", "widen", "q1", "weigh", "q2", "out", "empty", "scale", "mx", "exp", "scale2", "turn0", "acc", "acc2", "turn", "prep"):
                 for job, args in plan.get((step, stage), []):
                     job(*args)

@@ -28,7 +28,7 @@ HALF = KP // 2
 
 BLOCKS = tuple((g, j) for g in range(SG) for j in range(NJ))
 STEPS = 2 * len(BLOCKS)
-REL_BUFS = 6
+REL_BUFS = 4
 
 
 def tile_ghosh_price_push_s8_kernel(
@@ -117,9 +117,13 @@ def tile_ghosh_price_push_s8_kernel(
             sh_wide[i] = work.tile([P, N], BF16, name="xb", bufs=5)
             nc.vector.tensor_copy(out=sh_wide[i][:], in_=sh_bytes[i // 2][:, i % 2, :].bitcast(FP8))
 
+        def group_half(groups, n):
+            if n // 2 not in groups:
+                groups[n // 2] = work.tile([P, 2, KQ * P * T], BF16, name="xg", bufs=7, align_bytes=64)
+            return groups[n // 2][:, n % 2, :]
+
         def empty_shocks_scaled(i):
-            sh_group[i] = work.tile([P, KQ * P * T], BF16, name="xg", bufs=6, align_bytes=64)
-            grouped = sh_group[i][:].rearrange("p (q r u e) -> p q r u e", q=KQ, u=2, e=2)
+            grouped = group_half(sh_group, i).rearrange("p (q r u e) -> p q r u e", q=KQ, u=2, e=2)
             halves = sh_bank[i][:].rearrange("p q u r -> p (q u r)").bitcast(BF16)
             halves = halves.rearrange("p (q u r e) -> p q r u e", q=KQ, u=2, e=2)
             for q in range(KQ):
@@ -139,17 +143,16 @@ def tile_ghosh_price_push_s8_kernel(
                     nc.tensor.transpose(sh_bank[i][:, q, u, :], words[:, 256 * q + u : 256 * (q + 1) : 2], ident[:])
 
         def empty_shocks(i):
-            sh_group[i] = work.tile([P, KQ * P * T], BF16, name="xg", bufs=6, align_bytes=64)
             nc.scalar.copy(
-                out=sh_group[i][:].bitcast(F32).rearrange("p (q r u) -> p q r u", q=KQ, u=2),
+                out=group_half(sh_group, i).bitcast(F32).rearrange("p (q r u) -> p q r u", q=KQ, u=2),
                 in_=sh_bank[i][:].rearrange("p q u r -> p q r u"),
             )
 
-        def quantize_shocks(i):
+        def quantize_shocks(i0, i1):
             nc.vector.quantize_mx(
-                out=sh_codes[:, i].rearrange("p q r -> p (q r)").bitcast(FP8X4),
-                scales=sh_scales[:, i].rearrange("p q r -> p (q r)"),
-                in_=sh_group[i][:],
+                out=sh_codes[:, i0:i1].rearrange("p i q r -> p (i q r)").bitcast(FP8X4),
+                scales=sh_scales[:, i0:i1].rearrange("p i q r -> p (i q r)"),
+                in_=sh_group[i0 // 2][:, i0 % 2 : i0 % 2 + i1 - i0].rearrange("p i c -> p (i c)"),
             )
 
         inv_group = {}
@@ -182,15 +185,17 @@ def tile_ghosh_price_push_s8_kernel(
                     nc.tensor.transpose(con_bank[n][:, a, u, :], words[:, 256 * g + u : 256 * (g + 1) : 2], ident[:])
 
         def empty_contrasts(n):
-            con_group[n] = work.tile([P, 2 * P * T], BF16, name="xg", bufs=6, align_bytes=64)
             nc.scalar.copy(
-                out=con_group[n][:].bitcast(F32).rearrange("p (a r u) -> p a r u", a=2, u=2),
+                out=group_half(con_group, n).bitcast(F32).rearrange("p (a r u) -> p a r u", a=2, u=2),
                 in_=con_bank[n][:].rearrange("p a u r -> p a r u"),
             )
 
-        def quantize_contrasts(n):
-            g, cols = n // 2, slice(HALF * (n % 2), HALF * (n % 2 + 1))
-            nc.vector.quantize_mx(out=con_codes[:, g, cols].bitcast(FP8X4), scales=con_scales[:, g, cols], in_=con_group[n][:])
+        def quantize_contrasts(g):
+            nc.vector.quantize_mx(
+                out=con_codes[:, g, :].bitcast(FP8X4),
+                scales=con_scales[:, g, :],
+                in_=con_group[g][:].rearrange("p i c -> p (i c)"),
+            )
 
         mv_bank = {}
         rel = {}
@@ -234,30 +239,35 @@ def tile_ghosh_price_push_s8_kernel(
 
         def price(u):
             b, g, j, t = unit(u)
-            priced[u] = work.tile([P, P, T], BF16, name="pr", bufs=4, align_bytes=64)
+            if u % 2 == 0:
+                priced[u // 2] = work.tile([P, 2, P, T], BF16, name="pr", bufs=3, align_bytes=64)
             nc.vector.tensor_tensor(
-                out=priced[u][:],
+                out=priced[u // 2][:, u % 2],
                 in0=tr_bank[u][:].rearrange("p v m -> p m v"),
                 in1=base_kp[:, j, :].unsqueeze(1).to_broadcast([P, P, T]),
                 op=MULT,
             )
 
-        def quantize_priced(u):
-            b, g, j, t = unit(u)
-            cols = slice(P * t, P * (t + 1))
+        def quantize_priced(u0, u1):
+            b, g, j, t = unit(u0)
+            cols = slice(P * t, P * (t + u1 - u0))
             nc.vector.quantize_mx(
                 out=pr_codes[:, g, j, cols].bitcast(FP8X4),
                 scales=pr_scales[:, g, j, cols],
-                in_=priced[u][:].rearrange("p m v -> p (m v)"),
+                in_=priced[u0 // 2][:, u0 % 2 : u0 % 2 + u1 - u0].rearrange("p i m v -> p (i m v)"),
             )
 
-        def weigh(b, half):
+        def weighted_cols(b, c0, c1):
+            if b not in weighted:
+                weighted[b] = work.tile([P, KP, T], BF16, name="we", bufs=3, align_bytes=64)
+            return weighted[b][:, c0:c1, :]
+
+        def weigh(b, c0, c1):
             g = BLOCKS[b][0]
-            weighted[b, half] = work.tile([P, HALF, T], BF16, name="we", bufs=3, align_bytes=64)
             nc.vector.tensor_tensor(
-                out=weighted[b, half][:].rearrange("p (c i) t -> p c t i", i=2),
-                in0=rel[b][:, :, HALF * half : HALF * (half + 1)].rearrange("p t (c i) -> p c t i", i=2),
-                in1=weight_kp[:, g, :].unsqueeze(1).unsqueeze(3).to_broadcast([P, HALF // 2, T, 2]),
+                out=weighted_cols(b, c0, c1).rearrange("p (c i) t -> p c t i", i=2),
+                in0=rel[b][:, :, c0:c1].rearrange("p t (c i) -> p c t i", i=2),
+                in1=weight_kp[:, g, :].unsqueeze(1).unsqueeze(3).to_broadcast([P, (c1 - c0) // 2, T, 2]),
                 op=MULT,
             )
 
@@ -267,21 +277,19 @@ def tile_ghosh_price_push_s8_kernel(
                 scaled[b] = work.tile([P, T, KP], BF16, name="sc", bufs=4)
             nc.scalar.activation(out=scaled[b][:, t, :], in_=rel[b][:, t, :], func=COPY, scale=weight_f32[:, g, t : t + 1])
 
-        def interleave(b, half, engine="vector"):
-            weighted[b, half] = work.tile([P, HALF, T], BF16, name="we", bufs=3, align_bytes=64)
+        def interleave(b, c0, c1, engine="vector"):
             copy_on(
                 engine,
-                weighted[b, half][:].rearrange("p (c i) t -> p c t i", i=4),
-                scaled[b][:, :, HALF * half : HALF * (half + 1)].rearrange("p t (c i) -> p c t i", i=4),
+                weighted_cols(b, c0, c1).rearrange("p (c i) t -> p c t i", i=4),
+                scaled[b][:, :, c0:c1].rearrange("p t (c i) -> p c t i", i=4),
             )
 
-        def quantize_weighted(b, half):
+        def quantize_weighted(b, c0=0, c1=KP):
             g, j = BLOCKS[b]
-            cols = slice(HALF * half, HALF * (half + 1))
             nc.vector.quantize_mx(
-                out=we_codes[:, g, j, cols].bitcast(FP8X4),
-                scales=we_scales[:, g, j, cols],
-                in_=weighted[b, half][:].rearrange("p n t -> p (n t)"),
+                out=we_codes[:, g, j, c0:c1].bitcast(FP8X4),
+                scales=we_scales[:, g, j, c0:c1],
+                in_=weighted[b][:, c0:c1, :].rearrange("p n t -> p (n t)"),
             )
 
         out_bank = {}
@@ -300,7 +308,7 @@ def tile_ghosh_price_push_s8_kernel(
                 )
 
         def index_out(g, t, engine):
-            res = work.tile([P, C], F32, name="res", bufs=8)
+            res = work.tile([P, C], F32, name="res", bufs=6)
             copy_on(engine, res[:], out_bank[0, g, t][:])
             nc.sync.dma_start(out=index_v[g][:, t, :], in_=res[:])
 
@@ -321,7 +329,7 @@ def tile_ghosh_price_push_s8_kernel(
                 )
 
         def contrast_out(a, j, engine):
-            res = work.tile([P, KP], F32, name="res", bufs=8)
+            res = work.tile([P, KP], F32, name="res", bufs=6)
             copy_on(
                 engine,
                 res[:].rearrange("p (m v) -> p m v", v=T),
@@ -368,25 +376,39 @@ def tile_ghosh_price_push_s8_kernel(
             at(s_turn, "turn0" if u in (U - 4, U - 3) else "turn", turn, u, (2 if u < U - 2 else 0) + u % 2)
             if u < U - 2:
                 at(s_turn + 1, "price", price, u)
-                at(s_turn + 1, "q2" if s_turn < PAIRED else "q0", quantize_priced, u)
+                if u % 2:
+                    at(s_turn + 1, "q2", quantize_priced, u - 1, u + 1)
         preps = []
         for i, s in ((6, 4), (7, 5), (8, 6), (9, 7), (10, 9), (11, 11)):
             at(s, "first" if s > PAIRED else "widen", widen, i)
-            preps.append((s + 1, turn_shocks, empty_shocks, quantize_shocks, i, 2 if s < 7 else 3))
+            preps.append((s + 1, turn_shocks, empty_shocks, i))
         for n, s in ((1, 4), (3, 6), (5, 14)):
-            preps.append((s, turn_contrasts, empty_contrasts, quantize_contrasts, n, 3))
-        for k, (s, turn_job, empty_job, quantize_job, i, lag) in enumerate(sorted(preps, key=lambda job: job[0])):
+            preps.append((s, turn_contrasts, empty_contrasts, n))
+        for k, (s, turn_job, empty_job, i) in enumerate(sorted(preps, key=lambda job: job[0])):
             at(s, "prep", turn_job, i, 4 + (k + 3) % (4 if s < 7 else 2))
             at(s + 1, "empty", empty_job, i)
-            at(s + lag, "first" if s + lag > PAIRED else "q1", quantize_job, i)
-        for u, step in ((0, 4), (1, 5), (2, 7), (3, 8), (8, 9), (9, 10), (10, 10), (11, 11), (4, 12), (5, 13), (6, 14), (7, 15), (16, 16), (17, 17), (18, 18), (19, 18), (20, 20), (21, 20), (22, 22), (23, 22)):
+        for u, step in [(u, 4 + n) for n, u in enumerate((0, 1, 2, 3, 8, 9, 10, 11, 4, 5, 6, 7))] + [(12 + n, s) for n, s in enumerate((16, 18, 18, 19))] + [(u, u - u % 2) for u in range(20, U)]:
             at(step, "scale2" if step >= PAIRED and step % 2 == 0 else "scale", scale_unit, u)
-        for step, stage, halves in ((11, "weigh", ((0, 0), (0, 1))), (13, "weigh", ((2, 0), (2, 1))), (19, "first", ((4, 0), (4, 1))), (15, "weigh", ((3, 0),)), (17, "weigh", ((3, 1), (1, 0))), (21, "first", ((1, 1),)), (23, "q1", ((5, 0), (5, 1)))):
-            for b, half in halves:
-                at(step, stage, weigh if b == 3 else interleave, b, half)
-            for b, half in halves:
-                at(step, "q2" if stage == "weigh" else stage, quantize_weighted, b, half)
-        for t, s in enumerate((8, 10, 10, 12)):
+        at(6, "q1", quantize_shocks, 4, 6)
+        at(8, "q1", quantize_shocks, 6, 8)
+        at(11, "q1", quantize_shocks, 8, 10)
+        at(15, "weigh", quantize_shocks, 10, 12)
+        at(7, "q1", quantize_contrasts, 0)
+        at(9, "q1", quantize_contrasts, 1)
+        at(17, "q1", quantize_contrasts, 2)
+        at(11, "weigh", interleave, 0, 0, KP)
+        at(13, "q1", quantize_weighted, 0)
+        at(13, "weigh", interleave, 2, 0, KP)
+        at(15, "q1", quantize_weighted, 2)
+        at(17, "first", interleave, 1, 0, KP)
+        at(17, "weigh", quantize_weighted, 1)
+        at(21, "first", interleave, 3, 0, KP)
+        at(21, "q1", quantize_weighted, 3)
+        at(19, "first", weigh, 4, 0, KP)
+        at(19, "first", price, 16)
+        at(19, "first", quantize_weighted, 4)
+        plan[19, "price"].pop(0)
+        for t, s in enumerate((10, 10, 12, 12)):
             at(s, "acc2", index_mm, 0, t, 6 + t % 2)
             at(s + 1, "out", index_out, 0, t, "scalar")
         for t in range(T):
@@ -394,7 +416,7 @@ def tile_ghosh_price_push_s8_kernel(
             at(17 + t - t % 2, "out", index_out, 1, t, "scalar")
         for a in range(2):
             at(14, "acc", contrast_mm, a, 0, 0, 1, 6 + a)
-            at(16, "acc", contrast_mm, a, 0, 1, 2)
+            at(18, "acc", contrast_mm, a, 0, 1, 2)
         for a in range(T):
             if a >= 2:
                 at(20, "acc", contrast_mm, a, 0, 0, 2, 2 + a)
@@ -402,10 +424,13 @@ def tile_ghosh_price_push_s8_kernel(
             at(21, "out", contrast_out, a, 0, "scalar")
         for a in range(2):
             at(22, "acc", contrast_mm, a, 1, 0, 2, 6 + a)
-        for u in (U - 2, U - 1):
-            at(23, "q2", price, u)
-        for u in (U - 2, U - 1):
-            at(23, "q2", quantize_priced, u)
+        at(22, "scale2", interleave, 5, HALF, KP, "scalar")
+        at(23, "weigh", interleave, 5, 0, HALF)
+        at(23, "weigh", price, U - 2)
+        at(23, "weigh", quantize_weighted, 5)
+        at(23, "weigh", price, U - 1)
+        at(23, "weigh", quantize_priced, U - 2, U - 1)
+        at(23, "weigh", quantize_priced, U - 1, U)
         for t in range(2):
             at(23, "acc", index_mm, 2, t, 2 + t)
             at(24, "out", index_out, 2, t, "scalar")
@@ -426,16 +451,17 @@ def tile_ghosh_price_push_s8_kernel(
         widen_plain(0)
         widen_plain(1)
         turn_shocks(0, 2)
-        group_inverse(0, 0, "vector")
+        group_inverse(0, 0, "vector", 0, 384)
+        group_inverse(0, 0, "scalar", 384, KP)
         turn_shocks(1, 3)
         keep_clock(3, 7)
         empty_shocks_scaled(0)
         quantize_inverse(0, 0)
         group_inverse(0, 1, "scalar")
-        quantize_shocks(0)
+        quantize_shocks(0, 1)
         empty_shocks_scaled(1)
         quantize_inverse(0, 1)
-        quantize_shocks(1)
+        quantize_shocks(1, 2)
         moves(0)
         moves(1)
         group_inverse(1, 0, "scalar")
@@ -452,19 +478,17 @@ def tile_ghosh_price_push_s8_kernel(
         turn_shocks(3, 6)
         turn_contrasts(2, 7)
         price(0)
-        quantize_shocks(2)
+        quantize_shocks(2, 3)
         widen(4)
-        quantize_contrasts(0)
-        quantize_priced(0)
         empty_shocks(3)
         empty_contrasts(2)
         group_inverse(1, 1, "scalar", 0, HALF)
         turn(1, 3)
         turn_contrasts(4, 4)
         price(1)
-        quantize_shocks(3)
+        quantize_shocks(3, 4)
         widen(5)
-        quantize_priced(1)
+        quantize_priced(0, 2)
         nc.vector.tensor_copy(out=weight_f32[:], in_=weight_kp[:])
         empty_contrasts(4)
         group_inverse(1, 1, "scalar", HALF, KP)
@@ -472,16 +496,12 @@ def tile_ghosh_price_push_s8_kernel(
         relatives(2)
         turn_shocks(4, 5)
         quantize_inverse(1, 1)
-        quantize_contrasts(2)
         empty_shocks(4)
         moves(3)
         relatives(3)
         turn_shocks(5, 6)
         at(4, "empty", empty_shocks, 5)
-        at(4, "q1", quantize_contrasts, 4)
-        at(4, "q1", quantize_shocks, 4)
-        at(5, "q1", quantize_shocks, 5)
         for step in range(4, U + 2):
-            for stage in ("first", "price", "q0", "widen", "q1", "weigh", "q2", "out", "empty", "scale", "mx", "exp", "scale2", "turn0", "acc", "acc2", "turn", "prep"):
+            for stage in ("first", "price", "widen", "q1", "q2", "weigh", "out", "empty", "scale", "mx", "exp", "scale2", "turn0", "acc", "acc2", "turn", "prep"):
                 for job, args in plan.get((step, stage), []):
                     job(*args)

@@ -15,6 +15,7 @@ FP8 = mybir.dt.float8_e4m3fn
 FP8X4 = mybir.dt.float8_e4m3fn_x4
 FP4X4 = mybir.dt.float4_e2m1fn_x4
 MULT = mybir.AluOpType.mult
+ADD = mybir.AluOpType.add
 EXP = mybir.ActivationFunctionType.Exp
 COPY = mybir.ActivationFunctionType.Copy
 
@@ -277,6 +278,14 @@ def tile_ghosh_price_push_s8_kernel(
                 scaled[b] = work.tile([P, T, KP], BF16, name="sc", bufs=4)
             nc.scalar.activation(out=scaled[b][:, t, :], in_=rel[b][:, t, :], func=COPY, scale=weight_f32[:, g, t : t + 1])
 
+        def scale_unit_beside(u):
+            b, g, j, t = unit(u)
+            if b not in scaled:
+                scaled[b] = work.tile([P, T, KP], BF16, name="sc", bufs=4)
+            column = work.tile([P, 1], F32, name="wcol", bufs=4)
+            nc.vector.tensor_copy(out=column[:], in_=weight_kp[:, g, t : t + 1])
+            nc.gpsimd.tensor_scalar(out=scaled[b][:, t, :], in0=rel[b][:, t, :], scalar1=column[:], scalar2=0.0, op0=MULT, op1=ADD)
+
         def interleave(b, c0, c1, engine="vector"):
             copy_on(
                 engine,
@@ -347,9 +356,9 @@ def tile_ghosh_price_push_s8_kernel(
         load_inverse(0, 1)
         load_shocks(1)
         load_inverse(1, 0)
+        load_inverse(1, 1)
         load_contrasts(0)
         load_contrasts(1)
-        load_inverse(1, 1)
         nc.sync.dma_start(out=base_kp[:], in_=base.rearrange("(j p t) -> p j t", p=P, t=T))
         nc.sync.dma_start(out=weight_kp[:], in_=weight.rearrange("(g p t) -> p g t", p=P, t=T))
         load_shocks(2)
@@ -361,7 +370,7 @@ def tile_ghosh_price_push_s8_kernel(
         load_shocks(5)
 
         U = T * len(BLOCKS)
-        PAIRED = 8
+        PAIRED = 10
         plan = {}
 
         def at(step, stage, job, *args):
@@ -373,28 +382,29 @@ def tile_ghosh_price_push_s8_kernel(
             if u >= 4:
                 at(s, "mx", moves, u)
                 at(s, "exp", relatives, u)
-            at(s_turn, "turn0" if u in (U - 4, U - 3) else "turn", turn, u, (2 if u < U - 2 else 0) + u % 2)
+            at(s_turn, "turn0" if u in (U - 4, U - 3) else "turn", turn, u, (0 if u >= U - 2 else 6 if u in (4, 5) else 2) + u % 2)
             if u < U - 2:
-                at(s_turn + 1, "price", price, u)
+                at(s_turn + 1 + (u < PAIRED - 2 and u % 2 == 0), "price", price, u)
                 if u % 2:
                     at(s_turn + 1, "q2", quantize_priced, u - 1, u + 1)
         preps = []
-        for i, s in ((6, 4), (7, 5), (8, 6), (9, 7), (10, 9), (11, 11)):
-            at(s, "first" if s > PAIRED else "widen", widen, i)
+        for i, s in ((5, 3), (6, 4), (7, 5), (8, 7), (9, 8), (10, 9), (11, 11)):
+            if i > 5:
+                at(s, "first" if s > PAIRED else "widen", widen, i)
             preps.append((s + 1, turn_shocks, empty_shocks, i))
-        for n, s in ((1, 4), (3, 6), (5, 14)):
+        for n, s in ((1, 7), (3, 12), (5, 14)):
             preps.append((s, turn_contrasts, empty_contrasts, n))
         for k, (s, turn_job, empty_job, i) in enumerate(sorted(preps, key=lambda job: job[0])):
-            at(s, "prep", turn_job, i, 4 + (k + 3) % (4 if s < 7 else 2))
+            at(s, "prep", turn_job, i, 4 + k % 2)
             at(s + 1, "empty", empty_job, i)
-        for u, step in [(u, 4 + n) for n, u in enumerate((0, 1, 2, 3, 8, 9, 10, 11, 4, 5, 6, 7))] + [(12 + n, s) for n, s in enumerate((16, 18, 18, 19))] + [(u, u - u % 2) for u in range(20, U)]:
+        for u, step in ((3, 9), (8, 9), (9, 10), (10, 11), (11, 12), (6, 14), (7, 14), (14, 16), (15, 18), (21, 20), (22, 22), (23, 22)):
             at(step, "scale2" if step >= PAIRED and step % 2 == 0 else "scale", scale_unit, u)
-        at(6, "q1", quantize_shocks, 4, 6)
-        at(8, "q1", quantize_shocks, 6, 8)
+        at(7, "q1", quantize_shocks, 4, 6)
+        at(9, "q1", quantize_shocks, 6, 8)
         at(11, "q1", quantize_shocks, 8, 10)
         at(15, "weigh", quantize_shocks, 10, 12)
-        at(7, "q1", quantize_contrasts, 0)
-        at(9, "q1", quantize_contrasts, 1)
+        at(10, "q1", quantize_contrasts, 0)
+        at(15, "weigh", quantize_contrasts, 1)
         at(17, "q1", quantize_contrasts, 2)
         at(11, "weigh", interleave, 0, 0, KP)
         at(13, "q1", quantize_weighted, 0)
@@ -408,6 +418,8 @@ def tile_ghosh_price_push_s8_kernel(
         at(19, "first", price, 16)
         at(19, "first", quantize_weighted, 4)
         plan[19, "price"].pop(0)
+        for u, step in ((0, 6), (1, 8), (2, 10), (4, 11), (5, 13), (12, 15), (13, 17), (20, 21)):
+            at(step, "beside", scale_unit_beside, u)
         for t, s in enumerate((10, 10, 12, 12)):
             at(s, "acc2", index_mm, 0, t, 6 + t % 2)
             at(s + 1, "out", index_out, 0, t, "scalar")
@@ -451,8 +463,7 @@ def tile_ghosh_price_push_s8_kernel(
         widen_plain(0)
         widen_plain(1)
         turn_shocks(0, 2)
-        group_inverse(0, 0, "vector", 0, 384)
-        group_inverse(0, 0, "scalar", 384, KP)
+        group_inverse(0, 0, "vector")
         turn_shocks(1, 3)
         keep_clock(3, 7)
         empty_shocks_scaled(0)
@@ -470,38 +481,35 @@ def tile_ghosh_price_push_s8_kernel(
         widen(2)
         turn_contrasts(0, 4)
         widen(3)
-        empty_contrasts(0)
         turn_shocks(2, 5)
         quantize_inverse(1, 0)
         empty_shocks(2)
         turn(0, 2)
         turn_shocks(3, 6)
         turn_contrasts(2, 7)
-        price(0)
-        quantize_shocks(2, 3)
+        turn(1, 3)
+        turn_contrasts(4, 5)
         widen(4)
         empty_shocks(3)
-        empty_contrasts(2)
-        group_inverse(1, 1, "scalar", 0, HALF)
-        turn(1, 3)
-        turn_contrasts(4, 4)
-        price(1)
+        quantize_shocks(2, 3)
+        price(0)
         quantize_shocks(3, 4)
+        group_inverse(1, 1, "scalar", 0, 512)
+        moves(2)
+        turn_shocks(4, 6)
+        moves(3)
+        relatives(2)
+        empty_contrasts(0)
+        relatives(3)
+        price(1)
         widen(5)
         quantize_priced(0, 2)
         nc.vector.tensor_copy(out=weight_f32[:], in_=weight_kp[:])
-        empty_contrasts(4)
-        group_inverse(1, 1, "scalar", HALF, KP)
-        moves(2)
-        relatives(2)
-        turn_shocks(4, 5)
         quantize_inverse(1, 1)
-        empty_shocks(4)
-        moves(3)
-        relatives(3)
-        turn_shocks(5, 6)
-        at(4, "empty", empty_shocks, 5)
+        at(4, "empty", empty_contrasts, 2)
+        at(4, "empty", empty_shocks, 4)
+        at(4, "empty", empty_contrasts, 4)
         for step in range(4, U + 2):
-            for stage in ("first", "price", "widen", "q1", "q2", "weigh", "out", "empty", "scale", "mx", "exp", "scale2", "turn0", "acc", "acc2", "turn", "prep"):
+            for stage in ("first", "beside", "price", "widen", "q1", "q2", "weigh", "out", "empty", "scale", "mx", "exp", "scale2", "turn0", "acc", "acc2", "turn", "prep"):
                 for job, args in plan.get((step, stage), []):
                     job(*args)

@@ -22,14 +22,27 @@ COPY = mybir.ActivationFunctionType.Copy
 P = 128
 T = 4
 KP = P * T
+HALF = KP // 2
 SG = S // KP
 KQ = N // KP
 NJ = N // KP
-HALF = KP // 2
-
 BLOCKS = tuple((g, j) for g in range(SG) for j in range(NJ))
-STEPS = 2 * len(BLOCKS)
-REL_BUFS = 4
+UNITS = T * len(BLOCKS)
+LAST = len(BLOCKS) - 1
+DIRECT = LAST - 1
+
+MOVES_BANKS = (0, 1)
+TURN_BANKS = (2, 3)
+PREP_BANKS = (4, 5)
+OUT_BANKS = (6, 7)
+
+HEAD = T
+PAIRED = 10
+TURN_LAG = 2
+FIRST_SCALE = 9
+FIRST_WEIGH = 13
+OPEN_LAG = 3
+WARM_PASSES = 3
 
 
 def tile_ghosh_price_push_s8_kernel(
@@ -106,22 +119,35 @@ def tile_ghosh_price_push_s8_kernel(
                 in_=bank[:].rearrange("p t m -> p m t"),
             )
 
-        sh_wide = {}
-        sh_bank = {}
-        sh_group = {}
+        sh_wide, sh_bank, sh_group, con_bank, con_group = {}, {}, {}, {}, {}
+
+        def wide_tile(i):
+            sh_wide[i] = work.tile([P, N], BF16, name="wide", bufs=5)
+            return sh_wide[i][:]
 
         def widen(i):
-            sh_wide[i] = work.tile([P, N], BF16, name="xb", bufs=5)
-            nc.vector.tensor_tensor(out=sh_wide[i][:], in0=sh_bytes[i // 2][:, i % 2, :].bitcast(FP8), in1=scale_row[:], op=MULT)
+            nc.vector.tensor_tensor(out=wide_tile(i), in0=sh_bytes[i // 2][:, i % 2, :].bitcast(FP8), in1=scale_row[:], op=MULT)
 
-        def widen_plain(i):
-            sh_wide[i] = work.tile([P, N], BF16, name="xb", bufs=5)
-            nc.vector.tensor_copy(out=sh_wide[i][:], in_=sh_bytes[i // 2][:, i % 2, :].bitcast(FP8))
+        def widen_unscaled(i):
+            nc.vector.tensor_copy(out=wide_tile(i), in_=sh_bytes[i // 2][:, i % 2, :].bitcast(FP8))
 
         def group_half(groups, n):
             if n // 2 not in groups:
-                groups[n // 2] = work.tile([P, 2, KQ * P * T], BF16, name="xg", bufs=7, align_bytes=64)
+                groups[n // 2] = work.tile([P, 2, KQ * KP], BF16, name="group", bufs=7, align_bytes=64)
             return groups[n // 2][:, n % 2, :]
+
+        def turn_shocks(i, number):
+            sh_bank[i] = bank_of(number, [P, KQ, 2, P])
+            words = sh_wide[i][:].bitcast(F32)
+            for q in range(KQ):
+                for u in range(2):
+                    nc.tensor.transpose(sh_bank[i][:, q, u, :], words[:, HALF * q + u : HALF * (q + 1) : 2], ident[:])
+
+        def empty_shocks(i):
+            nc.scalar.copy(
+                out=group_half(sh_group, i).bitcast(F32).rearrange("p (q r u) -> p q r u", q=KQ, u=2),
+                in_=sh_bank[i][:].rearrange("p q u r -> p q r u"),
+            )
 
         def empty_shocks_scaled(i):
             grouped = group_half(sh_group, i).rearrange("p (q r u e) -> p q r u e", q=KQ, u=2, e=2)
@@ -131,24 +157,6 @@ def tile_ghosh_price_push_s8_kernel(
                 scales = scale_kp[:, q, :].rearrange("p (u e) -> p u e", u=2).unsqueeze(1).to_broadcast([P, P, 2, 2])
                 nc.vector.tensor_tensor(out=grouped[:, q], in0=halves[:, q], in1=scales, op=MULT)
 
-        def keep_clock(n, number):
-            bank = bank_of(number, [P, KP])
-            for k in range(n):
-                nc.tensor.matmul(bank[:], sh_wide[1][:, 0:P], sh_wide[1][:, 0:KP], start=True, stop=True)
-
-        def turn_shocks(i, number):
-            sh_bank[i] = bank_of(number, [P, KQ, 2, P])
-            words = sh_wide[i][:].bitcast(F32)
-            for q in range(KQ):
-                for u in range(2):
-                    nc.tensor.transpose(sh_bank[i][:, q, u, :], words[:, 256 * q + u : 256 * (q + 1) : 2], ident[:])
-
-        def empty_shocks(i):
-            nc.scalar.copy(
-                out=group_half(sh_group, i).bitcast(F32).rearrange("p (q r u) -> p q r u", q=KQ, u=2),
-                in_=sh_bank[i][:].rearrange("p q u r -> p q r u"),
-            )
-
         def quantize_shocks(i0, i1):
             nc.vector.quantize_mx(
                 out=sh_codes[:, i0:i1].rearrange("p i q r -> p (i q r)").bitcast(FP8X4),
@@ -156,34 +164,13 @@ def tile_ghosh_price_push_s8_kernel(
                 in_=sh_group[i0 // 2][:, i0 % 2 : i0 % 2 + i1 - i0].rearrange("p i c -> p (i c)"),
             )
 
-        inv_group = {}
-
-        def group_inverse(j, q, engine, c0=0, c1=KP):
-            if (j, q) not in inv_group:
-                inv_group[j, q] = work.tile([P, KP, T], BF16, name="ig", bufs=2, align_bytes=64)
-            copy_on(
-                engine,
-                inv_group[j, q][:, c0:c1, :].rearrange("p (c i) t -> p c t i", i=4),
-                inv_raw[j, q][:, :, c0:c1].rearrange("p t (c i) -> p c t i", i=4),
-            )
-
-        def quantize_inverse(j, q):
-            nc.vector.quantize_mx(
-                out=inv_codes[:, j, q, :].bitcast(FP8X4),
-                scales=inv_scales[:, j, q, :],
-                in_=inv_group[j, q][:].rearrange("p n t -> p (n t)"),
-            )
-
-        con_bank = {}
-        con_group = {}
-
         def turn_contrasts(n, number):
             g, a0 = n // 2, 2 * (n % 2)
             con_bank[n] = bank_of(number, [P, 2, 2, P])
             for a in range(2):
                 words = con_raw[a0 + a][:].bitcast(F32)
                 for u in range(2):
-                    nc.tensor.transpose(con_bank[n][:, a, u, :], words[:, 256 * g + u : 256 * (g + 1) : 2], ident[:])
+                    nc.tensor.transpose(con_bank[n][:, a, u, :], words[:, HALF * g + u : HALF * (g + 1) : 2], ident[:])
 
         def empty_contrasts(n):
             nc.scalar.copy(
@@ -198,19 +185,31 @@ def tile_ghosh_price_push_s8_kernel(
                 in_=con_group[g][:].rearrange("p i c -> p (i c)"),
             )
 
-        mv_bank = {}
-        rel = {}
-        tr_bank = {}
-        priced = {}
-        scaled = {}
-        weighted = {}
+        inv_group = {}
+
+        def group_inverse(j, q, engine):
+            inv_group[j, q] = work.tile([P, KP, T], BF16, name="inv_group", bufs=2, align_bytes=64)
+            copy_on(
+                engine,
+                inv_group[j, q][:].rearrange("p (c i) t -> p c t i", i=4),
+                inv_raw[j, q][:].rearrange("p t (c i) -> p c t i", i=4),
+            )
+
+        def quantize_inverse(j, q):
+            nc.vector.quantize_mx(
+                out=inv_codes[:, j, q, :].bitcast(FP8X4),
+                scales=inv_scales[:, j, q, :],
+                in_=inv_group[j, q][:].rearrange("p n t -> p (n t)"),
+            )
+
+        mv_bank, rel, tr_bank, priced, scaled, weighted = {}, {}, {}, {}, {}, {}
 
         def unit(u):
             return u // T, BLOCKS[u // T][0], BLOCKS[u // T][1], u % T
 
         def moves(u):
             b, g, j, t = unit(u)
-            mv_bank[u] = bank_of(u % 2, [P, KP])
+            mv_bank[u] = bank_of(MOVES_BANKS[u % 2], [P, KP])
             for q in range(KQ):
                 nc.tensor.matmul_mx(
                     out=mv_bank[u][:],
@@ -225,7 +224,7 @@ def tile_ghosh_price_push_s8_kernel(
         def relatives(u):
             b, g, j, t = unit(u)
             if t == 0:
-                rel[b] = work.tile([P, T, KP], F32, name="rel", bufs=REL_BUFS)
+                rel[b] = work.tile([P, T, KP], F32, name="rel", bufs=4)
             nc.scalar.activation(
                 out=rel[b][:, t, :].rearrange("p (v m) -> p v m", v=T),
                 in_=mv_bank[u][:].rearrange("p (m v) -> p v m", v=T),
@@ -241,7 +240,7 @@ def tile_ghosh_price_push_s8_kernel(
         def price(u):
             b, g, j, t = unit(u)
             if u % 2 == 0:
-                priced[u // 2] = work.tile([P, 2, P, T], BF16, name="pr", bufs=3, align_bytes=64)
+                priced[u // 2] = work.tile([P, 2, P, T], BF16, name="priced", bufs=3, align_bytes=64)
             nc.vector.tensor_tensor(
                 out=priced[u // 2][:, u % 2],
                 in0=tr_bank[u][:].rearrange("p v m -> p m v"),
@@ -260,54 +259,60 @@ def tile_ghosh_price_push_s8_kernel(
 
         def weighted_cols(b, c0, c1):
             if b not in weighted:
-                weighted[b] = work.tile([P, KP, T], BF16, name="we", bufs=3, align_bytes=64)
+                weighted[b] = work.tile([P, KP, T], BF16, name="weighted", bufs=3, align_bytes=64)
             return weighted[b][:, c0:c1, :]
 
-        def weigh(b, c0, c1):
+        def weigh(b):
             g = BLOCKS[b][0]
             nc.vector.tensor_tensor(
-                out=weighted_cols(b, c0, c1).rearrange("p (c i) t -> p c t i", i=2),
-                in0=rel[b][:, :, c0:c1].rearrange("p t (c i) -> p c t i", i=2),
-                in1=weight_kp[:, g, :].unsqueeze(1).unsqueeze(3).to_broadcast([P, (c1 - c0) // 2, T, 2]),
+                out=weighted_cols(b, 0, KP).rearrange("p (c i) t -> p c t i", i=2),
+                in0=rel[b][:].rearrange("p t (c i) -> p c t i", i=2),
+                in1=weight_kp[:, g, :].unsqueeze(1).unsqueeze(3).to_broadcast([P, HALF, T, 2]),
                 op=MULT,
             )
 
+        def scaled_plane(b, t):
+            if b not in scaled:
+                scaled[b] = work.tile([P, T, KP], BF16, name="scaled", bufs=4)
+            return scaled[b][:, t, :]
+
         def scale_unit(u):
             b, g, j, t = unit(u)
-            if b not in scaled:
-                scaled[b] = work.tile([P, T, KP], BF16, name="sc", bufs=4)
-            nc.scalar.activation(out=scaled[b][:, t, :], in_=rel[b][:, t, :], func=COPY, scale=weight_f32[:, g, t : t + 1])
+            nc.scalar.activation(out=scaled_plane(b, t), in_=rel[b][:, t, :], func=COPY, scale=weight_f32[:, g, t : t + 1])
 
         def scale_unit_beside(u):
             b, g, j, t = unit(u)
-            if b not in scaled:
-                scaled[b] = work.tile([P, T, KP], BF16, name="sc", bufs=4)
-            column = work.tile([P, 1], F32, name="wcol", bufs=4)
+            column = work.tile([P, 1], F32, name="column", bufs=4)
             nc.vector.tensor_copy(out=column[:], in_=weight_kp[:, g, t : t + 1])
-            nc.gpsimd.tensor_scalar(out=scaled[b][:, t, :], in0=rel[b][:, t, :], scalar1=column[:], scalar2=0.0, op0=MULT, op1=ADD)
+            nc.gpsimd.tensor_scalar(
+                out=scaled_plane(b, t), in0=rel[b][:, t, :], scalar1=column[:], scalar2=0.0, op0=MULT, op1=ADD
+            )
 
-        def interleave(b, c0, c1, engine="vector"):
+        def interleave(b, c0=0, c1=KP, engine="vector"):
             copy_on(
                 engine,
                 weighted_cols(b, c0, c1).rearrange("p (c i) t -> p c t i", i=4),
                 scaled[b][:, :, c0:c1].rearrange("p t (c i) -> p c t i", i=4),
             )
 
-        def quantize_weighted(b, c0=0, c1=KP):
+        def quantize_weighted(b):
             g, j = BLOCKS[b]
             nc.vector.quantize_mx(
-                out=we_codes[:, g, j, c0:c1].bitcast(FP8X4),
-                scales=we_scales[:, g, j, c0:c1],
-                in_=weighted[b][:, c0:c1, :].rearrange("p n t -> p (n t)"),
+                out=we_codes[:, g, j, :].bitcast(FP8X4),
+                scales=we_scales[:, g, j, :],
+                in_=weighted[b][:].rearrange("p n t -> p (n t)"),
             )
 
-        out_bank = {}
+        index_bank, contrast_bank = {}, {}
+
+        def result_tile():
+            return work.tile([P, KP], F32, name="result", bufs=6)
 
         def index_mm(g, t, number):
-            out_bank[0, g, t] = bank_of(number, [P, C])
+            index_bank[g, t] = bank_of(number, [P, C])
             for j in range(NJ):
                 nc.tensor.matmul_mx(
-                    out=out_bank[0, g, t][:],
+                    out=index_bank[g, t][:],
                     lhsT=pr_codes[:, g, j, P * t : P * (t + 1)].bitcast(FP8X4),
                     lhsT_scale=pr_scales[:, g, j, P * t : P * (t + 1)],
                     rhs=b_words[:, j, :].bitcast(FP4X4),
@@ -316,35 +321,33 @@ def tile_ghosh_price_push_s8_kernel(
                     stop=(j == NJ - 1),
                 )
 
-        def index_out(g, t, engine):
-            res = work.tile([P, C], F32, name="res", bufs=6)
-            copy_on(engine, res[:], out_bank[0, g, t][:])
-            nc.sync.dma_start(out=index_v[g][:, t, :], in_=res[:])
+        def index_out(g, t):
+            result = result_tile()
+            nc.scalar.copy(out=result[:], in_=index_bank[g, t][:])
+            nc.sync.dma_start(out=index_v[g][:, t, :], in_=result[:])
 
-        def contrast_mm(a, j, n0, n1, number=None):
-            order = [g for g, jj in BLOCKS if jj == j]
-            if n0 == 0:
-                out_bank[1, a, j] = bank_of(number, [P, KP])
-            for n in range(n0, n1):
-                g = order[n]
+        def contrast_mm(a, j, g0, g1, number=None):
+            if g0 == 0:
+                contrast_bank[a, j] = bank_of(number, [P, KP])
+            for g in range(g0, g1):
                 nc.tensor.matmul_mx(
-                    out=out_bank[1, a, j][:],
+                    out=contrast_bank[a, j][:],
                     lhsT=con_codes[:, g, P * a : P * (a + 1)].bitcast(FP8X4),
                     lhsT_scale=con_scales[:, g, P * a : P * (a + 1)],
                     rhs=we_codes[:, g, j, :].bitcast(FP8X4),
                     rhs_scale=we_scales[:, g, j, :],
-                    start=(n == 0),
-                    stop=(n == SG - 1),
+                    start=(g == 0),
+                    stop=(g == SG - 1),
                 )
 
         def contrast_out(a, j, engine):
-            res = work.tile([P, KP], F32, name="res", bufs=6)
+            result = result_tile()
             copy_on(
                 engine,
-                res[:].rearrange("p (m v) -> p m v", v=T),
-                out_bank[1, a, j][:].rearrange("p (v m) -> p m v", v=T),
+                result[:].rearrange("p (m v) -> p m v", v=T),
+                contrast_bank[a, j][:].rearrange("p (v m) -> p m v", v=T),
             )
-            nc.sync.dma_start(out=out_1[P * a : P * (a + 1), KP * j : KP * (j + 1)], in_=res[:])
+            nc.sync.dma_start(out=out_1[P * a : P * (a + 1), KP * j : KP * (j + 1)], in_=result[:])
 
         nc.vector.memset(warm[:], 0.0)
         nc.scalar.activation(out=warm[:], in_=warm[:], func=EXP)
@@ -369,103 +372,16 @@ def tile_ghosh_price_push_s8_kernel(
         load_shocks(4)
         load_shocks(5)
 
-        U = T * len(BLOCKS)
-        PAIRED = 10
-        plan = {}
-
-        def at(step, stage, job, *args):
-            plan.setdefault((step, stage), []).append((job, args))
-
-        for u in range(2, U):
-            s = u if u < PAIRED else u - u % 2
-            s_turn = min(u + 2, PAIRED) if u < PAIRED else min(s + 2, U - 2)
-            if u >= 4:
-                at(s, "mx", moves, u)
-                at(s, "exp", relatives, u)
-            at(s_turn, "turn0" if u in (U - 4, U - 3) else "turn", turn, u, (0 if u >= U - 2 else 6 if u in (4, 5) else 2) + u % 2)
-            if u < U - 2:
-                at(s_turn + 1 + (u < PAIRED - 2 and u % 2 == 0), "price", price, u)
-                if u % 2:
-                    at(s_turn + 1, "q2", quantize_priced, u - 1, u + 1)
-        preps = []
-        for i, s in ((5, 3), (6, 4), (7, 5), (8, 7), (9, 8), (10, 9), (11, 11)):
-            if i > 5:
-                at(s, "first" if s > PAIRED else "widen", widen, i)
-            preps.append((s + 1, turn_shocks, empty_shocks, i))
-        for n, s in ((1, 7), (3, 12), (5, 14)):
-            preps.append((s, turn_contrasts, empty_contrasts, n))
-        for k, (s, turn_job, empty_job, i) in enumerate(sorted(preps, key=lambda job: job[0])):
-            at(s, "prep", turn_job, i, 4 + k % 2)
-            at(s + 1, "empty", empty_job, i)
-        for u, step in ((3, 9), (8, 9), (9, 10), (10, 11), (11, 12), (6, 14), (7, 14), (14, 16), (15, 18), (21, 20), (22, 22), (23, 22)):
-            at(step, "scale2" if step >= PAIRED and step % 2 == 0 else "scale", scale_unit, u)
-        at(7, "q1", quantize_shocks, 4, 6)
-        at(9, "q1", quantize_shocks, 6, 8)
-        at(11, "q1", quantize_shocks, 8, 10)
-        at(15, "weigh", quantize_shocks, 10, 12)
-        at(10, "q1", quantize_contrasts, 0)
-        at(15, "weigh", quantize_contrasts, 1)
-        at(17, "q1", quantize_contrasts, 2)
-        at(11, "weigh", interleave, 0, 0, KP)
-        at(13, "q1", quantize_weighted, 0)
-        at(13, "weigh", interleave, 2, 0, KP)
-        at(15, "q1", quantize_weighted, 2)
-        at(17, "first", interleave, 1, 0, KP)
-        at(17, "weigh", quantize_weighted, 1)
-        at(21, "first", interleave, 3, 0, KP)
-        at(21, "q1", quantize_weighted, 3)
-        at(19, "first", weigh, 4, 0, KP)
-        at(19, "first", price, 16)
-        at(19, "first", quantize_weighted, 4)
-        plan[19, "price"].pop(0)
-        for u, step in ((0, 6), (1, 8), (2, 10), (4, 11), (5, 13), (12, 15), (13, 17), (20, 21)):
-            at(step, "beside", scale_unit_beside, u)
-        for t, s in enumerate((10, 10, 12, 12)):
-            at(s, "acc2", index_mm, 0, t, 6 + t % 2)
-            at(s + 1, "out", index_out, 0, t, "scalar")
-        for t in range(T):
-            at(16 + t - t % 2, "acc2", index_mm, 1, t, 4 + t % 2)
-            at(17 + t - t % 2, "out", index_out, 1, t, "scalar")
-        for a in range(2):
-            at(14, "acc", contrast_mm, a, 0, 0, 1, 6 + a)
-            at(18, "acc", contrast_mm, a, 0, 1, 2)
-        for a in range(T):
-            if a >= 2:
-                at(20, "acc", contrast_mm, a, 0, 0, 2, 2 + a)
-            at(20, "acc2", contrast_mm, a, 0, 2, 3)
-            at(21, "out", contrast_out, a, 0, "scalar")
-        for a in range(2):
-            at(22, "acc", contrast_mm, a, 1, 0, 2, 6 + a)
-        at(22, "scale2", interleave, 5, HALF, KP, "scalar")
-        at(23, "weigh", interleave, 5, 0, HALF)
-        at(23, "weigh", price, U - 2)
-        at(23, "weigh", quantize_weighted, 5)
-        at(23, "weigh", price, U - 1)
-        at(23, "weigh", quantize_priced, U - 2, U - 1)
-        at(23, "weigh", quantize_priced, U - 1, U)
-        for t in range(2):
-            at(23, "acc", index_mm, 2, t, 2 + t)
-            at(24, "out", index_out, 2, t, "scalar")
-        at(23, "acc", contrast_mm, 2, 1, 0, 2, 4)
-        for a in range(3):
-            at(23, "acc", contrast_mm, a, 1, 2, 3)
-            at(24, "out", contrast_out, a, 1, "vector" if a == 2 else "scalar")
-        at(23, "acc", index_mm, 2, 2, 0)
-        at(24, "out", index_out, 2, 2, "scalar")
-        at(23, "acc", contrast_mm, 3, 1, 0, 3, 5)
-        at(24, "out", contrast_out, 3, 1, "vector")
-        at(23, "acc", index_mm, 2, 3, 1)
-        at(24, "out", index_out, 2, 3, "scalar")
-
-
-        spread_scales(0, 6)
-        spread_scales(1, 7)
-        widen_plain(0)
-        widen_plain(1)
-        turn_shocks(0, 2)
+        for q in range(KQ):
+            spread_scales(q, OUT_BANKS[q])
+        widen_unscaled(0)
+        widen_unscaled(1)
+        turn_shocks(0, TURN_BANKS[0])
         group_inverse(0, 0, "vector")
-        turn_shocks(1, 3)
-        keep_clock(3, 7)
+        turn_shocks(1, TURN_BANKS[1])
+        warm_bank = bank_of(OUT_BANKS[1], [P, KP])
+        for k in range(WARM_PASSES):
+            nc.tensor.matmul(warm_bank[:], sh_wide[1][:, 0:P], sh_wide[1][:, 0:KP], start=True, stop=True)
         empty_shocks_scaled(0)
         quantize_inverse(0, 0)
         group_inverse(0, 1, "scalar")
@@ -475,28 +391,29 @@ def tile_ghosh_price_push_s8_kernel(
         quantize_shocks(1, 2)
         moves(0)
         moves(1)
+
         group_inverse(1, 0, "scalar")
         relatives(0)
         relatives(1)
         widen(2)
-        turn_contrasts(0, 4)
+        turn_contrasts(0, PREP_BANKS[0])
         widen(3)
-        turn_shocks(2, 5)
+        turn_shocks(2, PREP_BANKS[1])
         quantize_inverse(1, 0)
         empty_shocks(2)
-        turn(0, 2)
-        turn_shocks(3, 6)
-        turn_contrasts(2, 7)
-        turn(1, 3)
-        turn_contrasts(4, 5)
+        turn(0, TURN_BANKS[0])
+        turn_shocks(3, OUT_BANKS[0])
+        turn_contrasts(2, OUT_BANKS[1])
+        turn(1, TURN_BANKS[1])
+        turn_contrasts(4, PREP_BANKS[1])
         widen(4)
         empty_shocks(3)
         quantize_shocks(2, 3)
         price(0)
         quantize_shocks(3, 4)
-        group_inverse(1, 1, "scalar", 0, 512)
+        group_inverse(1, 1, "scalar")
         moves(2)
-        turn_shocks(4, 6)
+        turn_shocks(4, OUT_BANKS[0])
         moves(3)
         relatives(2)
         empty_contrasts(0)
@@ -506,10 +423,143 @@ def tile_ghosh_price_push_s8_kernel(
         quantize_priced(0, 2)
         nc.vector.tensor_copy(out=weight_f32[:], in_=weight_kp[:])
         quantize_inverse(1, 1)
-        at(4, "empty", empty_contrasts, 2)
-        at(4, "empty", empty_shocks, 4)
-        at(4, "empty", empty_contrasts, 4)
-        for step in range(4, U + 2):
-            for stage in ("first", "beside", "price", "widen", "q1", "q2", "weigh", "out", "empty", "scale", "mx", "exp", "scale2", "turn0", "acc", "acc2", "turn", "prep"):
-                for job, args in plan.get((step, stage), []):
-                    job(*args)
+        empty_contrasts(2)
+        empty_shocks(4)
+        empty_contrasts(4)
+
+        final = UNITS - 2
+        tensor_steps = [s for s in range(HEAD, UNITS) if s < PAIRED or s % 2 == 0]
+        moves_step = [u if u < PAIRED else u - u % 2 for u in range(UNITS)]
+        turn_step = {u: min(moves_step[u] + TURN_LAG, PAIRED if u < PAIRED else final) for u in range(2, UNITS)}
+        price_step = {h: turn_step[2 * h + 1] + 1 for h in range(1, UNITS // 2 - 2)}
+        vector_steps = [HEAD] + sorted(price_step.values())
+        pieces = [[(turn_shocks, empty_shocks, i)] for i in (5, 6, 7)] + [[(turn_contrasts, empty_contrasts, 1)]]
+        pieces += [[(turn_shocks, empty_shocks, i)] for i in (8, 9)]
+        pieces += [[(turn_shocks, empty_shocks, i), (turn_contrasts, empty_contrasts, n)] for i, n in ((10, 3), (11, 5))]
+        prep = dict(zip(tensor_steps, pieces))
+        prep_step = {(job, i): s for s, items in prep.items() for job, empty, i in items}
+        weigh_step = {b: FIRST_WEIGH + 2 * n for n, b in enumerate((0, 2, 1, DIRECT, 3))}
+        to_scale = [T * b + t for b in (0, 2, 1, 3, LAST) for t in range(T)]
+        index_step = {(g, t): max(price_step[T * g + 2] + 1, PAIRED) + t - t % 2 for g in range(SG - 1) for t in range(T)}
+        close_step = weigh_step[DIRECT] + 1
+
+        def next_to_scale(step):
+            return to_scale.pop(0) if to_scale and moves_step[to_scale[0]] <= step else None
+
+        def vector_step_before(step):
+            return max(s for s in vector_steps if s <= step)
+
+        def vector_step_after(step):
+            return min(s for s in vector_steps if s >= step)
+
+        def vector_part(step):
+            blocks = [b for b in weigh_step if weigh_step[b] == step]
+            pairs = [h for h in price_step if price_step[h] == step]
+            first = [(widen, i) for i in range(6, SG * T) if vector_step_before(prep_step[turn_shocks, i]) == step]
+            first += [(weigh if b == DIRECT else interleave, b) for b in blocks]
+            if pairs and DIRECT not in blocks:
+                first.insert(len(first) - 1, (scale_unit_beside, next_to_scale(step - 1)))
+            for job, which in first:
+                job(which)
+            for h in pairs:
+                price(2 * h)
+                if DIRECT in blocks:
+                    quantize_weighted(DIRECT)
+                price(2 * h + 1)
+            rest = [(quantize_weighted, (b,)) for b in blocks if b != DIRECT]
+            for i in range(5, SG * T, 2):
+                if vector_step_after(prep_step[turn_shocks, i] + 2) == step:
+                    rest.append((quantize_shocks, (i - 1, i + 1)))
+            for g in range(SG):
+                if vector_step_after(prep_step[turn_contrasts, 2 * g + 1] + 3) == step:
+                    rest.append((quantize_contrasts, (g,)))
+            rest[1:1] = [(quantize_priced, (2 * h, 2 * h + 2)) for h in pairs]
+            for job, args in rest:
+                job(*args)
+
+        def scale_next(step):
+            u = next_to_scale(step)
+            if u is not None:
+                scale_unit(u)
+
+        def turn_bank(u):
+            if u >= final:
+                return MOVES_BANKS[u % 2]
+            if turn_step[u] < PAIRED and u // 2 % 2 == 0:
+                return OUT_BANKS[u % 2]
+            return TURN_BANKS[u % 2]
+
+        for step in range(HEAD, UNITS - 1):
+            if step in vector_steps:
+                vector_part(step)
+            for g, t in index_step:
+                if index_step[g, t] == step - 1:
+                    index_out(g, t)
+            if step == close_step + 1:
+                for a in range(T):
+                    contrast_out(a, 0, "scalar")
+            for job, empty, i in prep.get(step - 1, []):
+                empty(i)
+            if step >= FIRST_SCALE and (step < PAIRED or step % 2) and len(prep.get(step - 1, [])) < 2:
+                scale_next(step - 1)
+            if step not in tensor_steps:
+                continue
+            units = [u for u in range(UNITS) if moves_step[u] == step]
+            for u in units:
+                moves(u)
+            for u in units:
+                relatives(u)
+            if step >= PAIRED:
+                scale_next(step)
+            turns = [u for u in turn_step if turn_step[u] == step]
+            if step == final:
+                scale_next(step)
+                interleave(LAST, HALF, KP, "scalar")
+                for u in turns[:2]:
+                    turn(u, turn_bank(u))
+                turns = turns[2:]
+            for a in range(2):
+                if step == weigh_step[0] + OPEN_LAG:
+                    contrast_mm(a, 0, 0, 1, OUT_BANKS[a])
+                if step == weigh_step[2] + OPEN_LAG:
+                    contrast_mm(a, 0, 1, 2)
+                if step == close_step:
+                    contrast_mm(2 + a, 0, 0, 2, PREP_BANKS[a])
+                if step == final:
+                    contrast_mm(a, 1, 0, 2, OUT_BANKS[a])
+            if step == close_step:
+                for a in range(T):
+                    contrast_mm(a, 0, 2, 3)
+            for g, t in index_step:
+                if index_step[g, t] == step:
+                    index_mm(g, t, (OUT_BANKS if g == 0 else PREP_BANKS)[t % 2])
+            for u in turns:
+                turn(u, turn_bank(u))
+            for k, (job, empty, i) in enumerate(prep.get(step, [])):
+                job(i, PREP_BANKS[(tensor_steps.index(step) + k) % 2])
+
+        price(final - 2)
+        price(final - 1)
+        quantize_priced(final - 2, final)
+        interleave(LAST, 0, HALF)
+        price(final)
+        quantize_weighted(LAST)
+        price(final + 1)
+        quantize_priced(final, final + 1)
+        quantize_priced(final + 1, final + 2)
+        for t in range(2):
+            index_mm(SG - 1, t, TURN_BANKS[t])
+        contrast_mm(2, 1, 0, 2, PREP_BANKS[0])
+        for a in range(3):
+            contrast_mm(a, 1, 2, 3)
+        index_mm(SG - 1, 2, MOVES_BANKS[0])
+        contrast_mm(3, 1, 0, 3, PREP_BANKS[1])
+        index_mm(SG - 1, 3, MOVES_BANKS[1])
+        for t in range(2):
+            index_out(SG - 1, t)
+        for a in range(2):
+            contrast_out(a, 1, "scalar")
+        contrast_out(2, 1, "vector")
+        index_out(SG - 1, 2)
+        contrast_out(3, 1, "vector")
+        index_out(SG - 1, 3)

@@ -78,7 +78,6 @@ def tile_ghosh_price_push_s8_kernel(
         we_scales = keep.tile([P, SG, NJ, KP], U8, name="we_scales", align_bytes=64)
 
         ident = keep.tile([P, P], F32, name="ident")
-        warm = keep.tile([P, 1], F32, name="warm")
 
         shocks_v = shocks_bytes.rearrange("(g m t) k -> g m t k", m=P, t=T)
         inverse_v = inverse.rearrange("(q p t) n -> q p t n", p=P, t=T)
@@ -349,8 +348,6 @@ def tile_ghosh_price_push_s8_kernel(
             )
             nc.sync.dma_start(out=out_1[P * a : P * (a + 1), KP * j : KP * (j + 1)], in_=result[:])
 
-        nc.vector.memset(warm[:], 0.0)
-        nc.scalar.activation(out=warm[:], in_=warm[:], func=EXP)
         nc.vector.memset(b_scales[:].rearrange("p j n -> p (j n)").bitcast(I32), 0)
         make_identity(nc, ident[:])
         nc.sync.dma_start(out=scale_kp[:], in_=shocks_scale.rearrange("o (q p t) -> p (o q) t", p=P, t=T))

@@ -410,8 +410,8 @@ def tile_ghosh_price_push_s8_kernel(
         quantize_shocks(3, 4)
         group_inverse(1, 1, "scalar")
         moves(2)
-        turn_shocks(4, OUT_BANKS[0])
         moves(3)
+        turn_shocks(4, OUT_BANKS[0])
         relatives(2)
         empty_contrasts(0)
         relatives(3)
@@ -497,7 +497,7 @@ def tile_ghosh_price_push_s8_kernel(
                     contrast_out(a, 0, "scalar")
             for job, empty, i in prep.get(step - 1, []):
                 empty(i)
-            if step >= FIRST_SCALE and (step < PAIRED or step % 2) and len(prep.get(step - 1, [])) < 2:
+            if step >= FIRST_SCALE and (step < PAIRED or step % 2):
                 scale_next(step - 1)
             if step not in tensor_steps:
                 continue
@@ -527,13 +527,16 @@ def tile_ghosh_price_push_s8_kernel(
             if step == close_step:
                 for a in range(T):
                     contrast_mm(a, 0, 2, 3)
-            for g, t in index_step:
-                if index_step[g, t] == step:
-                    index_mm(g, t, (OUT_BANKS if g == 0 else PREP_BANKS)[t % 2])
+            for t in range(T):
+                if index_step[0, t] == step:
+                    index_mm(0, t, OUT_BANKS[t % 2])
             for u in turns:
                 turn(u, turn_bank(u))
             for k, (job, empty, i) in enumerate(prep.get(step, [])):
                 job(i, PREP_BANKS[(tensor_steps.index(step) + k) % 2])
+            for t in range(T):
+                if index_step[1, t] == step:
+                    index_mm(1, t, PREP_BANKS[t % 2])
 
         price(final - 2)
         price(final - 1)

@@ -190,8 +190,8 @@ def tile_ghosh_price_push_s8_kernel(
             inv_group[j, q] = work.tile([P, KP, T], BF16, name="inv_group", bufs=2, align_bytes=64)
             copy_on(
                 engine,
-                inv_group[j, q][:].rearrange("p (c i) t -> p c t i", i=4),
-                inv_raw[j, q][:].rearrange("p t (c i) -> p c t i", i=4),
+                inv_group[j, q][:].rearrange("p (c i) t -> p c t i", i=8),
+                inv_raw[j, q][:].rearrange("p t (c i) -> p c t i", i=8),
             )
 
         def quantize_inverse(j, q):
@@ -290,8 +290,8 @@ def tile_ghosh_price_push_s8_kernel(
         def interleave(b, c0=0, c1=KP, engine="vector"):
             copy_on(
                 engine,
-                weighted_cols(b, c0, c1).rearrange("p (c i) t -> p c t i", i=4),
-                scaled[b][:, :, c0:c1].rearrange("p t (c i) -> p c t i", i=4),
+                weighted_cols(b, c0, c1).rearrange("p (c i) t -> p c t i", i=8),
+                scaled[b][:, :, c0:c1].rearrange("p t (c i) -> p c t i", i=8),
             )
 
         def quantize_weighted(b):

@@ -15,7 +15,6 @@ FP8 = mybir.dt.float8_e4m3fn
 FP8X4 = mybir.dt.float8_e4m3fn_x4
 FP4X4 = mybir.dt.float4_e2m1fn_x4
 MULT = mybir.AluOpType.mult
-ADD = mybir.AluOpType.add
 EXP = mybir.ActivationFunctionType.Exp
 COPY = mybir.ActivationFunctionType.Copy
 
@@ -57,7 +56,6 @@ def tile_ghosh_price_push_s8_kernel(
 
         sh_bytes = [keep.tile([P, 2, N], U8, name="sh_bytes%d" % k, align_bytes=64) for k in range(2 * SG)]
         scale_kp = keep.tile([P, KQ, T], F32, name="scale_kp")
-        scale_row = keep.tile([P, N], F32, name="scale_row")
         inv_raw = {(j, q): keep.tile([P, T, KP], BF16, name="inv_raw%d%d" % (j, q)) for j in range(NJ) for q in range(KQ)}
         base_kp = keep.tile([P, NJ, T], BF16, name="base_kp")
         weight_kp = keep.tile([P, SG, T], BF16, name="weight_kp")
@@ -109,15 +107,6 @@ def tile_ghosh_price_push_s8_kernel(
             else:
                 nc.vector.tensor_copy(out=out, in_=in_)
 
-        def spread_scales(q, number):
-            bank = bank_of(number, [P, T, P])
-            for t in range(T):
-                nc.tensor.transpose(bank[:, t, :], scale_kp[:, q, t : t + 1].to_broadcast([P, P]), ident[:])
-            nc.scalar.copy(
-                out=scale_row[:, KP * q : KP * (q + 1)].rearrange("p (m t) -> p m t", t=T),
-                in_=bank[:].rearrange("p t m -> p m t"),
-            )
-
         sh_wide, sh_bank, sh_group, con_bank, con_group = {}, {}, {}, {}, {}
 
         def wide_tile(i):
@@ -125,10 +114,10 @@ def tile_ghosh_price_push_s8_kernel(
             return sh_wide[i][:]
 
         def widen(i):
-            nc.vector.tensor_tensor(out=wide_tile(i), in0=sh_bytes[i // 2][:, i % 2, :].bitcast(FP8), in1=scale_row[:], op=MULT)
+            nc.scalar.copy(out=wide_tile(i), in_=sh_bytes[i // 2][:, i % 2, :].bitcast(FP8))
 
         def widen_unscaled(i):
-            nc.vector.tensor_copy(out=wide_tile(i), in_=sh_bytes[i // 2][:, i % 2, :].bitcast(FP8))
+            widen(i)
 
         def group_half(groups, n):
             if n // 2 not in groups:
@@ -143,10 +132,7 @@ def tile_ghosh_price_push_s8_kernel(
                     nc.tensor.transpose(sh_bank[i][:, q, u, :], words[:, HALF * q + u : HALF * (q + 1) : 2], ident[:])
 
         def empty_shocks(i):
-            nc.scalar.copy(
-                out=group_half(sh_group, i).bitcast(F32).rearrange("p (q r u) -> p q r u", q=KQ, u=2),
-                in_=sh_bank[i][:].rearrange("p q u r -> p q r u"),
-            )
+            empty_shocks_scaled(i)
 
         def empty_shocks_scaled(i):
             grouped = group_half(sh_group, i).rearrange("p (q r u e) -> p q r u e", q=KQ, u=2, e=2)
@@ -280,12 +266,7 @@ def tile_ghosh_price_push_s8_kernel(
             nc.scalar.activation(out=scaled_plane(b, t), in_=rel[b][:, t, :], func=COPY, scale=weight_f32[:, g, t : t + 1])
 
         def scale_unit_beside(u):
-            b, g, j, t = unit(u)
-            column = work.tile([P, 1], F32, name="column", bufs=4)
-            nc.vector.tensor_copy(out=column[:], in_=weight_kp[:, g, t : t + 1])
-            nc.gpsimd.tensor_scalar(
-                out=scaled_plane(b, t), in0=rel[b][:, t, :], scalar1=column[:], scalar2=0.0, op0=MULT, op1=ADD
-            )
+            scale_unit(u)
 
         def interleave(b, c0=0, c1=KP, engine="vector"):
             copy_on(
@@ -369,8 +350,6 @@ def tile_ghosh_price_push_s8_kernel(
         load_shocks(4)
         load_shocks(5)
 
-        for q in range(KQ):
-            spread_scales(q, OUT_BANKS[q])
         widen_unscaled(0)
         widen_unscaled(1)
         turn_shocks(0, TURN_BANKS[0])

@@ -15,6 +15,7 @@ FP8 = mybir.dt.float8_e4m3fn
 FP8X4 = mybir.dt.float8_e4m3fn_x4
 FP4X4 = mybir.dt.float4_e2m1fn_x4
 MULT = mybir.AluOpType.mult
+ADD = mybir.AluOpType.add
 EXP = mybir.ActivationFunctionType.Exp
 COPY = mybir.ActivationFunctionType.Copy
 
@@ -25,23 +26,10 @@ HALF = KP // 2
 SG = S // KP
 KQ = N // KP
 NJ = N // KP
-BLOCKS = tuple((g, j) for g in range(SG) for j in range(NJ))
-UNITS = T * len(BLOCKS)
-LAST = len(BLOCKS) - 1
-DIRECT = LAST - 1
+TILES = SG * T
+LINE = 8
 
-MOVES_BANKS = (0, 1)
-TURN_BANKS = (2, 3)
-PREP_BANKS = (4, 5)
-OUT_BANKS = (6, 7)
-
-HEAD = T
-PAIRED = 10
-TURN_LAG = 2
-FIRST_SCALE = 9
-FIRST_WEIGH = 13
-OPEN_LAG = 3
-WARM_PASSES = 3
+AHEAD = 3
 
 
 def tile_ghosh_price_push_s8_kernel(
@@ -54,7 +42,13 @@ def tile_ghosh_price_push_s8_kernel(
         psum = ctx.enter_context(tc.psum_pool(name="psum", bufs=1))
         ctx.enter_context(tc.manual_schedule())
 
-        sh_bytes = [keep.tile([P, 2, N], U8, name="sh_bytes%d" % k, align_bytes=64) for k in range(2 * SG)]
+        byte_loads = ((0, 1), (1, 4), (4, 6), (6, 8), (8, 12))
+        sh_bytes = {}
+        for i0, i1 in byte_loads:
+            loaded = keep.tile([P, i1 - i0, N], U8, name="sh_bytes%d" % i0, align_bytes=64)
+            for i in range(i0, i1):
+                sh_bytes[i] = loaded[:, i - i0, :]
+            sh_bytes[i0, i1] = loaded
         scale_kp = keep.tile([P, KQ, T], F32, name="scale_kp")
         inv_raw = {(j, q): keep.tile([P, T, KP], BF16, name="inv_raw%d%d" % (j, q)) for j in range(NJ) for q in range(KQ)}
         base_kp = keep.tile([P, NJ, T], BF16, name="base_kp")
@@ -64,17 +58,16 @@ def tile_ghosh_price_push_s8_kernel(
         b_scales = keep.tile([P, NJ, C], U8, name="b_scales", align_bytes=64)
         con_raw = [keep.tile([P, S], BF16, name="con_raw%d" % a) for a in range(T)]
 
-        sh_codes = keep.tile([P, SG * T, KQ, P], U32, name="sh_codes", align_bytes=64)
-        sh_scales = keep.tile([P, SG * T, KQ, P], U8, name="sh_scales", align_bytes=64)
+        sh_codes = keep.tile([P, TILES, KQ, P], U32, name="sh_codes", align_bytes=64)
+        sh_scales = keep.tile([P, TILES, KQ, P], U8, name="sh_scales", align_bytes=64)
         inv_codes = keep.tile([P, NJ, KQ, KP], U32, name="inv_codes", align_bytes=64)
         inv_scales = keep.tile([P, NJ, KQ, KP], U8, name="inv_scales", align_bytes=64)
         con_codes = keep.tile([P, SG, R], U32, name="con_codes", align_bytes=64)
         con_scales = keep.tile([P, SG, R], U8, name="con_scales", align_bytes=64)
-        pr_codes = keep.tile([P, SG, NJ, KP], U32, name="pr_codes", align_bytes=64)
-        pr_scales = keep.tile([P, SG, NJ, KP], U8, name="pr_scales", align_bytes=64)
+        pr_codes = keep.tile([P, TILES, NJ, P], U32, name="pr_codes", align_bytes=64)
+        pr_scales = keep.tile([P, TILES, NJ, P], U8, name="pr_scales", align_bytes=64)
         we_codes = keep.tile([P, SG, NJ, KP], U32, name="we_codes", align_bytes=64)
         we_scales = keep.tile([P, SG, NJ, KP], U8, name="we_scales", align_bytes=64)
-
         ident = keep.tile([P, P], F32, name="ident")
 
         shocks_v = shocks_bytes.rearrange("(g m t) k -> g m t k", m=P, t=T)
@@ -82,7 +75,8 @@ def tile_ghosh_price_push_s8_kernel(
         index_v = out_0.rearrange("(g m t) c -> g m t c", m=P, t=T)
 
         def load_shocks(k):
-            nc.sync.dma_start(out=sh_bytes[k][:], in_=shocks_v[k // 2][:, 2 * (k % 2) : 2 * (k % 2) + 2, :])
+            i0, i1 = byte_loads[k]
+            nc.sync.dma_start(out=sh_bytes[i0, i1][:], in_=shocks_v[i0 // T][:, i0 % T : i0 % T + i1 - i0, :])
 
         def load_inverse(j, q):
             nc.sync.dma_start(out=inv_raw[j, q][:], in_=inverse_v[q][:, :, KP * j : KP * (j + 1)])
@@ -107,22 +101,26 @@ def tile_ghosh_price_push_s8_kernel(
             else:
                 nc.vector.tensor_copy(out=out, in_=in_)
 
-        sh_wide, sh_bank, sh_group, con_bank, con_group = {}, {}, {}, {}, {}
+        def interleave(engine, grouped, planes):
+            if engine == "gpsimd":
+                nc.gpsimd.tensor_scalar(
+                    out=grouped, in0=planes.rearrange("p t n -> p n t"), scalar1=1.0, scalar2=0.0, op0=MULT, op1=ADD
+                )
+                return
+            copy_on(
+                engine,
+                grouped.rearrange("p (c i) t -> p c t i", i=LINE),
+                planes.rearrange("p t (c i) -> p c t i", i=LINE),
+            )
 
-        def wide_tile(i):
-            sh_wide[i] = work.tile([P, N], BF16, name="wide", bufs=5)
-            return sh_wide[i][:]
+        def quantize(codes, scales, grouped):
+            nc.vector.quantize_mx(out=codes.bitcast(FP8X4), scales=scales, in_=grouped)
 
-        def widen(i):
-            nc.scalar.copy(out=wide_tile(i), in_=sh_bytes[i // 2][:, i % 2, :].bitcast(FP8))
+        sh_wide, sh_bank, sh_group = {}, {}, {}
 
-        def widen_unscaled(i):
-            widen(i)
-
-        def group_half(groups, n):
-            if n // 2 not in groups:
-                groups[n // 2] = work.tile([P, 2, KQ * KP], BF16, name="group", bufs=7, align_bytes=64)
-            return groups[n // 2][:, n % 2, :]
+        def widen(i, engine="scalar"):
+            sh_wide[i] = work.tile([P, N], BF16, name="wide", bufs=3)
+            copy_on(engine, sh_wide[i][:], sh_bytes[i].bitcast(FP8))
 
         def turn_shocks(i, number):
             sh_bank[i] = bank_of(number, [P, KQ, 2, P])
@@ -131,180 +129,157 @@ def tile_ghosh_price_push_s8_kernel(
                 for u in range(2):
                     nc.tensor.transpose(sh_bank[i][:, q, u, :], words[:, HALF * q + u : HALF * (q + 1) : 2], ident[:])
 
-        def empty_shocks(i):
-            empty_shocks_scaled(i)
-
-        def empty_shocks_scaled(i):
-            grouped = group_half(sh_group, i).rearrange("p (q r u e) -> p q r u e", q=KQ, u=2, e=2)
+        def scale_shocks(i):
+            sh_group[i] = work.tile([P, N], BF16, name="sh_group", bufs=4, align_bytes=64)
+            grouped = sh_group[i][:].rearrange("p (q r u e) -> p q r u e", q=KQ, u=2, e=2)
             halves = sh_bank[i][:].rearrange("p q u r -> p (q u r)").bitcast(BF16)
             halves = halves.rearrange("p (q u r e) -> p q r u e", q=KQ, u=2, e=2)
             for q in range(KQ):
                 scales = scale_kp[:, q, :].rearrange("p (u e) -> p u e", u=2).unsqueeze(1).to_broadcast([P, P, 2, 2])
                 nc.vector.tensor_tensor(out=grouped[:, q], in0=halves[:, q], in1=scales, op=MULT)
 
-        def quantize_shocks(i0, i1):
-            nc.vector.quantize_mx(
-                out=sh_codes[:, i0:i1].rearrange("p i q r -> p (i q r)").bitcast(FP8X4),
-                scales=sh_scales[:, i0:i1].rearrange("p i q r -> p (i q r)"),
-                in_=sh_group[i0 // 2][:, i0 % 2 : i0 % 2 + i1 - i0].rearrange("p i c -> p (i c)"),
+        def quantize_shocks(i):
+            quantize(
+                sh_codes[:, i].rearrange("p q r -> p (q r)"), sh_scales[:, i].rearrange("p q r -> p (q r)"), sh_group[i][:]
             )
 
+        con_bank, con_group = {}, {}
+
         def turn_contrasts(n, number):
-            g, a0 = n // 2, 2 * (n % 2)
+            g, a0 = n % SG, 2 * (n // SG)
             con_bank[n] = bank_of(number, [P, 2, 2, P])
             for a in range(2):
                 words = con_raw[a0 + a][:].bitcast(F32)
                 for u in range(2):
                     nc.tensor.transpose(con_bank[n][:, a, u, :], words[:, HALF * g + u : HALF * (g + 1) : 2], ident[:])
 
-        def empty_contrasts(n):
-            nc.scalar.copy(
-                out=group_half(con_group, n).bitcast(F32).rearrange("p (a r u) -> p a r u", a=2, u=2),
-                in_=con_bank[n][:].rearrange("p a u r -> p a r u"),
+        def empty_contrasts(n, engine="scalar"):
+            con_group[n] = work.tile([P, 2 * KP], BF16, name="con_group", bufs=3, align_bytes=64)
+            copy_on(
+                engine,
+                con_group[n][:].bitcast(F32).rearrange("p (a r u) -> p a r u", a=2, u=2),
+                con_bank[n][:].rearrange("p a u r -> p a r u"),
             )
 
-        def quantize_contrasts(g):
-            nc.vector.quantize_mx(
-                out=con_codes[:, g, :].bitcast(FP8X4),
-                scales=con_scales[:, g, :],
-                in_=con_group[g][:].rearrange("p i c -> p (i c)"),
-            )
+        def quantize_contrasts(n):
+            g, cols = n % SG, slice(HALF * (n // SG), HALF * (n // SG + 1))
+            quantize(con_codes[:, g, cols], con_scales[:, g, cols], con_group[n][:])
 
         inv_group = {}
 
-        def group_inverse(j, q, engine):
-            inv_group[j, q] = work.tile([P, KP, T], BF16, name="inv_group", bufs=2, align_bytes=64)
-            copy_on(
-                engine,
-                inv_group[j, q][:].rearrange("p (c i) t -> p c t i", i=8),
-                inv_raw[j, q][:].rearrange("p t (c i) -> p c t i", i=8),
-            )
+        def group_inverse(j, q, engine, c0=0, c1=KP):
+            if (j, q) not in inv_group:
+                inv_group[j, q] = work.tile([P, KP, T], BF16, name="inv_group%d" % (q if j == 0 else 1 - q), bufs=1, align_bytes=64)
+            interleave(engine, inv_group[j, q][:, c0:c1, :], inv_raw[j, q][:, :, c0:c1])
 
         def quantize_inverse(j, q):
-            nc.vector.quantize_mx(
-                out=inv_codes[:, j, q, :].bitcast(FP8X4),
-                scales=inv_scales[:, j, q, :],
-                in_=inv_group[j, q][:].rearrange("p n t -> p (n t)"),
-            )
+            quantize(inv_codes[:, j, q, :], inv_scales[:, j, q, :], inv_group[j, q][:].rearrange("p n t -> p (n t)"))
 
         mv_bank, rel, tr_bank, priced, scaled, weighted = {}, {}, {}, {}, {}, {}
 
-        def unit(u):
-            return u // T, BLOCKS[u // T][0], BLOCKS[u // T][1], u % T
-
-        def moves(u):
-            b, g, j, t = unit(u)
-            mv_bank[u] = bank_of(MOVES_BANKS[u % 2], [P, KP])
+        def moves(i, j, number):
+            mv_bank[i, j] = bank_of(number, [P, KP])
             for q in range(KQ):
                 nc.tensor.matmul_mx(
-                    out=mv_bank[u][:],
-                    lhsT=sh_codes[:, T * g + t, q, :].bitcast(FP8X4),
-                    lhsT_scale=sh_scales[:, T * g + t, q, :],
+                    out=mv_bank[i, j][:],
+                    lhsT=sh_codes[:, i, q, :].bitcast(FP8X4),
+                    lhsT_scale=sh_scales[:, i, q, :],
                     rhs=inv_codes[:, j, q, :].bitcast(FP8X4),
                     rhs_scale=inv_scales[:, j, q, :],
                     start=(q == 0),
                     stop=(q == KQ - 1),
                 )
 
-        def relatives(u):
-            b, g, j, t = unit(u)
-            if t == 0:
-                rel[b] = work.tile([P, T, KP], F32, name="rel", bufs=4)
+        def relatives(i, j):
+            if j == 0:
+                rel[i] = work.tile([P, NJ, KP], F32, name="rel", bufs=12)
             nc.scalar.activation(
-                out=rel[b][:, t, :].rearrange("p (v m) -> p v m", v=T),
-                in_=mv_bank[u][:].rearrange("p (m v) -> p v m", v=T),
+                out=rel[i][:, j, :].rearrange("p (v m) -> p v m", v=T),
+                in_=mv_bank[i, j][:].rearrange("p (m v) -> p v m", v=T),
                 func=EXP,
             )
 
-        def turn(u, number):
-            b, g, j, t = unit(u)
-            tr_bank[u] = bank_of(number, [P, T, P])
+        def turn(i, j, number):
+            tr_bank[i, j] = bank_of(number, [P, T, P])
             for v in range(T):
-                nc.tensor.transpose(tr_bank[u][:, v, :], rel[b][:, t, P * v : P * (v + 1)], ident[:])
+                nc.tensor.transpose(tr_bank[i, j][:, v, :], rel[i][:, j, P * v : P * (v + 1)], ident[:])
 
-        def price(u):
-            b, g, j, t = unit(u)
-            if u % 2 == 0:
-                priced[u // 2] = work.tile([P, 2, P, T], BF16, name="priced", bufs=3, align_bytes=64)
+        def price(i, j):
+            if j == 0:
+                priced[i] = work.tile([P, NJ, P, T], BF16, name="priced", bufs=3, align_bytes=64)
             nc.vector.tensor_tensor(
-                out=priced[u // 2][:, u % 2],
-                in0=tr_bank[u][:].rearrange("p v m -> p m v"),
+                out=priced[i][:, j],
+                in0=tr_bank[i, j][:].rearrange("p v m -> p m v"),
                 in1=base_kp[:, j, :].unsqueeze(1).to_broadcast([P, P, T]),
                 op=MULT,
             )
 
-        def quantize_priced(u0, u1):
-            b, g, j, t = unit(u0)
-            cols = slice(P * t, P * (t + u1 - u0))
-            nc.vector.quantize_mx(
-                out=pr_codes[:, g, j, cols].bitcast(FP8X4),
-                scales=pr_scales[:, g, j, cols],
-                in_=priced[u0 // 2][:, u0 % 2 : u0 % 2 + u1 - u0].rearrange("p i m v -> p (i m v)"),
+        def quantize_priced(i, j0, j1):
+            quantize(
+                pr_codes[:, i, j0:j1].rearrange("p j m -> p (j m)"),
+                pr_scales[:, i, j0:j1].rearrange("p j m -> p (j m)"),
+                priced[i][:, j0:j1].rearrange("p j m v -> p (j m v)"),
             )
 
-        def weighted_cols(b, c0, c1):
-            if b not in weighted:
-                weighted[b] = work.tile([P, KP, T], BF16, name="weighted", bufs=3, align_bytes=64)
-            return weighted[b][:, c0:c1, :]
+        def plane(i, j):
+            if (i // T, j) not in scaled:
+                scaled[i // T, j] = work.tile([P, T, KP], BF16, name="scaled", bufs=5)
+            return scaled[i // T, j][:, i % T, :]
 
-        def weigh(b):
-            g = BLOCKS[b][0]
-            nc.vector.tensor_tensor(
-                out=weighted_cols(b, 0, KP).rearrange("p (c i) t -> p c t i", i=2),
-                in0=rel[b][:].rearrange("p t (c i) -> p c t i", i=2),
-                in1=weight_kp[:, g, :].unsqueeze(1).unsqueeze(3).to_broadcast([P, HALF, T, 2]),
-                op=MULT,
+        def scale_on_scalar(i, j):
+            nc.scalar.activation(
+                out=plane(i, j),
+                in_=rel[i][:, j, :],
+                func=COPY,
+                scale=weight_f32[:, i // T, i % T : i % T + 1],
             )
 
-        def scaled_plane(b, t):
-            if b not in scaled:
-                scaled[b] = work.tile([P, T, KP], BF16, name="scaled", bufs=4)
-            return scaled[b][:, t, :]
+        def scale_on_gpsimd(*units):
+            i0 = min(i for i, j in units)
+            count = max(i for i, j in units) - i0 + 1
+            columns = work.tile([P, count], F32, name="columns", bufs=4)
+            nc.vector.tensor_copy(out=columns[:], in_=weight_kp[:].rearrange("p g t -> p (g t)")[:, i0 : i0 + count])
+            for i, j in units:
+                nc.gpsimd.tensor_scalar(
+                    out=plane(i, j),
+                    in0=rel[i][:, j, :],
+                    scalar1=columns[:, i - i0 : i - i0 + 1],
+                    scalar2=0.0,
+                    op0=MULT,
+                    op1=ADD,
+                )
 
-        def scale_unit(u):
-            b, g, j, t = unit(u)
-            nc.scalar.activation(out=scaled_plane(b, t), in_=rel[b][:, t, :], func=COPY, scale=weight_f32[:, g, t : t + 1])
+        def group_weighted(g, j, engine, c0=0, c1=KP):
+            if (g, j) not in weighted:
+                weighted[g, j] = work.tile([P, KP, T], BF16, name="grouped", bufs=3, align_bytes=64)
+            interleave(engine, weighted[g, j][:, c0:c1, :], scaled[g, j][:, :, c0:c1])
 
-        def scale_unit_beside(u):
-            scale_unit(u)
-
-        def interleave(b, c0=0, c1=KP, engine="vector"):
-            copy_on(
-                engine,
-                weighted_cols(b, c0, c1).rearrange("p (c i) t -> p c t i", i=8),
-                scaled[b][:, :, c0:c1].rearrange("p t (c i) -> p c t i", i=8),
-            )
-
-        def quantize_weighted(b):
-            g, j = BLOCKS[b]
-            nc.vector.quantize_mx(
-                out=we_codes[:, g, j, :].bitcast(FP8X4),
-                scales=we_scales[:, g, j, :],
-                in_=weighted[b][:].rearrange("p n t -> p (n t)"),
-            )
+        def quantize_weighted(g, j):
+            quantize(we_codes[:, g, j, :], we_scales[:, g, j, :], weighted[g, j][:].rearrange("p n t -> p (n t)"))
 
         index_bank, contrast_bank = {}, {}
 
         def result_tile():
             return work.tile([P, KP], F32, name="result", bufs=6)
 
-        def index_mm(g, t, number):
-            index_bank[g, t] = bank_of(number, [P, C])
-            for j in range(NJ):
+        def index_mm(i, number, j0=0, j1=NJ):
+            if j0 == 0:
+                index_bank[i] = bank_of(number, [P, C])
+            for j in range(j0, j1):
                 nc.tensor.matmul_mx(
-                    out=index_bank[g, t][:],
-                    lhsT=pr_codes[:, g, j, P * t : P * (t + 1)].bitcast(FP8X4),
-                    lhsT_scale=pr_scales[:, g, j, P * t : P * (t + 1)],
+                    out=index_bank[i][:],
+                    lhsT=pr_codes[:, i, j, :].bitcast(FP8X4),
+                    lhsT_scale=pr_scales[:, i, j, :],
                     rhs=b_words[:, j, :].bitcast(FP4X4),
                     rhs_scale=b_scales[:, j, :],
                     start=(j == 0),
                     stop=(j == NJ - 1),
                 )
 
-        def index_out(g, t):
+        def index_out(i, engine="scalar"):
             result = result_tile()
-            nc.scalar.copy(out=result[:], in_=index_bank[g, t][:])
-            nc.sync.dma_start(out=index_v[g][:, t, :], in_=result[:])
+            copy_on(engine, result[:], index_bank[i][:])
+            nc.sync.dma_start(out=index_v[i // T][:, i % T, :], in_=result[:])
 
         def contrast_mm(a, j, g0, g1, number=None):
             if g0 == 0:
@@ -320,7 +295,7 @@ def tile_ghosh_price_push_s8_kernel(
                     stop=(g == SG - 1),
                 )
 
-        def contrast_out(a, j, engine):
+        def contrast_out(a, j, engine="scalar"):
             result = result_tile()
             copy_on(
                 engine,
@@ -334,211 +309,247 @@ def tile_ghosh_price_push_s8_kernel(
         nc.sync.dma_start(out=scale_kp[:], in_=shocks_scale.rearrange("o (q p t) -> p (o q) t", p=P, t=T))
         load_shocks(0)
         load_inverse(0, 0)
-        load_inverse(0, 1)
         load_shocks(1)
+        load_inverse(0, 1)
+        load_shocks(2)
         load_inverse(1, 0)
         load_inverse(1, 1)
+        nc.sync.dma_start(out=weight_kp[:], in_=weight.rearrange("(g p t) -> p g t", p=P, t=T))
         load_contrasts(0)
         load_contrasts(1)
-        nc.sync.dma_start(out=base_kp[:], in_=base.rearrange("(j p t) -> p j t", p=P, t=T))
-        nc.sync.dma_start(out=weight_kp[:], in_=weight.rearrange("(g p t) -> p g t", p=P, t=T))
-        load_shocks(2)
+        load_shocks(3)
+        load_shocks(4)
         load_contrasts(2)
         load_contrasts(3)
-        load_shocks(3)
+        nc.sync.dma_start(out=base_kp[:], in_=base.rearrange("(j p t) -> p j t", p=P, t=T))
         load_baskets()
-        load_shocks(4)
-        load_shocks(5)
 
-        widen_unscaled(0)
-        widen_unscaled(1)
-        turn_shocks(0, TURN_BANKS[0])
-        group_inverse(0, 0, "vector")
-        turn_shocks(1, TURN_BANKS[1])
-        warm_bank = bank_of(OUT_BANKS[1], [P, KP])
-        for k in range(WARM_PASSES):
-            nc.tensor.matmul(warm_bank[:], sh_wide[1][:, 0:P], sh_wide[1][:, 0:KP], start=True, stop=True)
-        empty_shocks_scaled(0)
-        quantize_inverse(0, 0)
-        group_inverse(0, 1, "scalar")
-        quantize_shocks(0, 1)
-        empty_shocks_scaled(1)
-        quantize_inverse(0, 1)
-        quantize_shocks(1, 2)
-        moves(0)
-        moves(1)
+        def move(units, banks):
+            for (i, j), number in zip(units, banks):
+                moves(i, j, number)
 
-        group_inverse(1, 0, "scalar")
-        relatives(0)
-        relatives(1)
+        def exps(units):
+            for i, j in units:
+                relatives(i, j)
+
+        def turns(i, banks):
+            for j in range(NJ):
+                turn(i, j, banks[j])
+
+        def prices(i):
+            for j in range(NJ):
+                price(i, j)
+
+        widen(0)
+        turn_shocks(0, 2)
+        widen(1)
+        turn_shocks(1, 3)
         widen(2)
-        turn_contrasts(0, PREP_BANKS[0])
+        turn_shocks(2, 4)
+        group_inverse(0, 0, "vector")
+        scale_shocks(0)
+        group_inverse(0, 1, "scalar", HALF, KP)
+        group_inverse(0, 1, "vector", 0, HALF)
         widen(3)
-        turn_shocks(2, PREP_BANKS[1])
-        quantize_inverse(1, 0)
-        empty_shocks(2)
-        turn(0, TURN_BANKS[0])
-        turn_shocks(3, OUT_BANKS[0])
-        turn_contrasts(2, OUT_BANKS[1])
-        turn(1, TURN_BANKS[1])
-        turn_contrasts(4, PREP_BANKS[1])
         widen(4)
-        empty_shocks(3)
-        quantize_shocks(2, 3)
-        price(0)
-        quantize_shocks(3, 4)
-        group_inverse(1, 1, "scalar")
-        moves(2)
-        moves(3)
-        turn_shocks(4, OUT_BANKS[0])
-        relatives(2)
-        empty_contrasts(0)
-        relatives(3)
-        price(1)
         widen(5)
-        quantize_priced(0, 2)
-        nc.vector.tensor_copy(out=weight_f32[:], in_=weight_kp[:])
+        quantize_inverse(0, 0)
+        quantize_shocks(0)
+        quantize_inverse(0, 1)
+        group_inverse(1, 0, "gpsimd", 0, 320)
+        scale_shocks(1)
+        scale_shocks(2)
+        moves(0, 0, 0)
+        turn_shocks(3, 5)
+        turn_shocks(4, 6)
+        turn_shocks(5, 7)
+        group_inverse(1, 1, "scalar", 0, HALF)
+        relatives(0, 0)
+        group_inverse(1, 1, "scalar", HALF, KP)
+        quantize_shocks(1)
+        scale_on_gpsimd((0, 0))
+        group_inverse(1, 0, "gpsimd", 320, KP)
+        quantize_shocks(2)
+        scale_shocks(3)
+        scale_shocks(4)
+        moves(1, 0, 1)
+        turn_contrasts(0, 2)
+        turn_contrasts(1, 3)
+        relatives(1, 0)
+        widen(6)
+        empty_contrasts(0)
+        moves(2, 0, 0)
+        turn_contrasts(2, 4)
+        turn_shocks(6, 5)
+        relatives(2, 0)
+        widen(7)
+        empty_contrasts(1)
+        quantize_shocks(3)
+        quantize_inverse(1, 0)
         quantize_inverse(1, 1)
+        scale_on_gpsimd((1, 0), (2, 0))
+        quantize_shocks(4)
+        scale_shocks(5)
+        scale_shocks(6)
+        moves(3, 0, 1)
+        turn_shocks(7, 6)
+        relatives(3, 0)
         empty_contrasts(2)
-        empty_shocks(4)
-        empty_contrasts(4)
-
-        final = UNITS - 2
-        tensor_steps = [s for s in range(HEAD, UNITS) if s < PAIRED or s % 2 == 0]
-        moves_step = [u if u < PAIRED else u - u % 2 for u in range(UNITS)]
-        turn_step = {u: min(moves_step[u] + TURN_LAG, PAIRED if u < PAIRED else final) for u in range(2, UNITS)}
-        price_step = {h: turn_step[2 * h + 1] + 1 for h in range(1, UNITS // 2 - 2)}
-        vector_steps = [HEAD] + sorted(price_step.values())
-        pieces = [[(turn_shocks, empty_shocks, i)] for i in (5, 6, 7)] + [[(turn_contrasts, empty_contrasts, 1)]]
-        pieces += [[(turn_shocks, empty_shocks, i)] for i in (8, 9)]
-        pieces += [[(turn_shocks, empty_shocks, i), (turn_contrasts, empty_contrasts, n)] for i, n in ((10, 3), (11, 5))]
-        prep = dict(zip(tensor_steps, pieces))
-        prep_step = {(job, i): s for s, items in prep.items() for job, empty, i in items}
-        weigh_step = {b: FIRST_WEIGH + 2 * n for n, b in enumerate((0, 2, 1, DIRECT, 3))}
-        to_scale = [T * b + t for b in (0, 2, 1, 3, LAST) for t in range(T)]
-        index_step = {(g, t): max(price_step[T * g + 2] + 1, PAIRED) + t - t % 2 for g in range(SG - 1) for t in range(T)}
-        close_step = weigh_step[DIRECT] + 1
-
-        def next_to_scale(step):
-            return to_scale.pop(0) if to_scale and moves_step[to_scale[0]] <= step else None
-
-        def vector_step_before(step):
-            return max(s for s in vector_steps if s <= step)
-
-        def vector_step_after(step):
-            return min(s for s in vector_steps if s >= step)
-
-        def vector_part(step):
-            blocks = [b for b in weigh_step if weigh_step[b] == step]
-            pairs = [h for h in price_step if price_step[h] == step]
-            first = [(widen, i) for i in range(6, SG * T) if vector_step_before(prep_step[turn_shocks, i]) == step]
-            first += [(weigh if b == DIRECT else interleave, b) for b in blocks]
-            if pairs and DIRECT not in blocks:
-                first.insert(len(first) - 1, (scale_unit_beside, next_to_scale(step - 1)))
-            for job, which in first:
-                job(which)
-            for h in pairs:
-                price(2 * h)
-                if DIRECT in blocks:
-                    quantize_weighted(DIRECT)
-                price(2 * h + 1)
-            rest = [(quantize_weighted, (b,)) for b in blocks if b != DIRECT]
-            for i in range(5, SG * T, 2):
-                if vector_step_after(prep_step[turn_shocks, i] + 2) == step:
-                    rest.append((quantize_shocks, (i - 1, i + 1)))
-            for g in range(SG):
-                if vector_step_after(prep_step[turn_contrasts, 2 * g + 1] + 3) == step:
-                    rest.append((quantize_contrasts, (g,)))
-            rest[1:1] = [(quantize_priced, (2 * h, 2 * h + 2)) for h in pairs]
-            for job, args in rest:
-                job(*args)
-
-        def scale_next(step):
-            u = next_to_scale(step)
-            if u is not None:
-                scale_unit(u)
-
-        def turn_bank(u):
-            if u >= final:
-                return MOVES_BANKS[u % 2]
-            if turn_step[u] < PAIRED and u // 2 % 2 == 0:
-                return OUT_BANKS[u % 2]
-            return TURN_BANKS[u % 2]
-
-        for step in range(HEAD, UNITS - 1):
-            if step in vector_steps:
-                vector_part(step)
-            for g, t in index_step:
-                if index_step[g, t] == step - 1:
-                    index_out(g, t)
-            if step == close_step + 1:
-                for a in range(T):
-                    contrast_out(a, 0, "scalar")
-            for job, empty, i in prep.get(step - 1, []):
-                empty(i)
-            if step >= FIRST_SCALE and (step < PAIRED or step % 2):
-                scale_next(step - 1)
-            if step not in tensor_steps:
-                continue
-            units = [u for u in range(UNITS) if moves_step[u] == step]
-            for u in units:
-                moves(u)
-            for u in units:
-                relatives(u)
-            if step >= PAIRED:
-                scale_next(step)
-            turns = [u for u in turn_step if turn_step[u] == step]
-            if step == final:
-                scale_next(step)
-                interleave(LAST, HALF, KP, "scalar")
-                for u in turns[:2]:
-                    turn(u, turn_bank(u))
-                turns = turns[2:]
-            for a in range(2):
-                if step == weigh_step[0] + OPEN_LAG:
-                    contrast_mm(a, 0, 0, 1, OUT_BANKS[a])
-                if step == weigh_step[2] + OPEN_LAG:
-                    contrast_mm(a, 0, 1, 2)
-                if step == close_step:
-                    contrast_mm(2 + a, 0, 0, 2, PREP_BANKS[a])
-                if step == final:
-                    contrast_mm(a, 1, 0, 2, OUT_BANKS[a])
-            if step == close_step:
-                for a in range(T):
-                    contrast_mm(a, 0, 2, 3)
-            for t in range(T):
-                if index_step[0, t] == step:
-                    index_mm(0, t, OUT_BANKS[t % 2])
-            for u in turns:
-                turn(u, turn_bank(u))
-            for k, (job, empty, i) in enumerate(prep.get(step, [])):
-                job(i, PREP_BANKS[(tensor_steps.index(step) + k) % 2])
-            for t in range(T):
-                if index_step[1, t] == step:
-                    index_mm(1, t, PREP_BANKS[t % 2])
-
-        price(final - 2)
-        price(final - 1)
-        quantize_priced(final - 2, final)
-        interleave(LAST, 0, HALF)
-        price(final)
-        quantize_weighted(LAST)
-        price(final + 1)
-        quantize_priced(final, final + 1)
-        quantize_priced(final + 1, final + 2)
-        for t in range(2):
-            index_mm(SG - 1, t, TURN_BANKS[t])
-        contrast_mm(2, 1, 0, 2, PREP_BANKS[0])
-        for a in range(3):
-            contrast_mm(a, 1, 2, 3)
-        index_mm(SG - 1, 2, MOVES_BANKS[0])
-        contrast_mm(3, 1, 0, 3, PREP_BANKS[1])
-        index_mm(SG - 1, 3, MOVES_BANKS[1])
-        for t in range(2):
-            index_out(SG - 1, t)
-        for a in range(2):
-            contrast_out(a, 1, "scalar")
-        contrast_out(2, 1, "vector")
-        index_out(SG - 1, 2)
+        widen(8)
+        widen(9)
+        units = [(0, 1), (1, 1), (2, 1), (3, 1)]
+        move(units, [0, 2, 3, 1])
+        exps(units)
+        turn_shocks(8, 4)
+        turn_shocks(9, 7)
+        widen(10)
+        widen(11)
+        quantize_shocks(5)
+        quantize_contrasts(0)
+        quantize_contrasts(1)
+        scale_on_gpsimd((3, 0), (0, 1))
+        quantize_shocks(6)
+        scale_shocks(7)
+        scale_shocks(8)
+        units = [(4, 0), (5, 0), (4, 1), (5, 1)]
+        move(units, [0, 2, 3, 1])
+        exps(units)
+        turn_shocks(10, 5)
+        turn_shocks(11, 6)
+        nc.vector.tensor_copy(out=weight_f32[:], in_=weight_kp[:])
+        group_weighted(0, 0, "vector")
+        quantize_shocks(7)
+        quantize_contrasts(2)
+        quantize_weighted(0, 0)
+        scale_on_gpsimd((1, 1), (4, 0), (5, 0))
+        quantize_shocks(8)
+        scale_shocks(9)
+        scale_shocks(10)
+        scale_shocks(11)
+        units = [(6, 0), (7, 0), (6, 1), (7, 1)]
+        move(units, [0, 2, 3, 1])
+        exps(units)
+        turns(0, (4, 7))
+        turn_contrasts(3, 5)
+        scale_on_scalar(2, 1)
+        scale_on_scalar(3, 1)
+        quantize_shocks(9)
+        quantize_shocks(10)
+        scale_on_gpsimd((6, 0), (7, 0))
+        quantize_shocks(11)
+        prices(0)
+        empty_contrasts(3, "vector")
+        units = [(8, 0), (9, 0), (8, 1), (9, 1)]
+        move(units, [0, 2, 3, 1])
+        exps(units)
+        turns(1, (4, 7))
+        turn_contrasts(4, 6)
+        group_weighted(1, 0, "scalar", HALF, KP)
+        group_weighted(0, 1, "vector")
+        quantize_priced(0, 0, 2)
+        quantize_contrasts(3)
+        scale_on_gpsimd((8, 0), (9, 0))
+        quantize_weighted(0, 1)
+        prices(1)
+        empty_contrasts(4, "vector")
+        units = [(10, 0), (11, 0), (10, 1), (11, 1)]
+        move(units, [0, 2, 3, 1])
+        index_mm(0, 5)
+        exps(units)
+        turns(2, (4, 7))
+        turn_contrasts(5, 6)
+        scale_on_scalar(10, 0)
+        scale_on_scalar(11, 0)
+        index_out(0)
+        group_weighted(1, 0, "vector", 0, HALF)
+        quantize_priced(1, 0, 2)
+        quantize_contrasts(4)
+        scale_on_gpsimd((4, 1), (5, 1))
+        quantize_weighted(1, 0)
+        prices(2)
+        empty_contrasts(5, "vector")
+        index_mm(1, 5)
+        contrast_mm(0, 0, 0, 1, 0)
+        contrast_mm(1, 0, 0, 1, 2)
+        contrast_mm(0, 0, 1, 2)
+        contrast_mm(1, 0, 1, 2)
+        turns(3, (3, 4))
+        turns(4, (7, 6))
+        group_weighted(2, 0, "scalar")
+        index_out(1)
+        scale_on_scalar(10, 1)
+        scale_on_scalar(11, 1)
+        quantize_priced(2, 0, 2)
+        quantize_contrasts(5)
+        scale_on_gpsimd((6, 1), (7, 1))
+        quantize_weighted(2, 0)
+        prices(3)
+        prices(4)
+        index_mm(2, 5)
+        contrast_mm(0, 0, 2, 3)
+        contrast_mm(1, 0, 2, 3)
+        contrast_mm(2, 0, 0, 3, 1)
+        turns(5, (3, 4))
+        turns(6, (7, 6))
+        index_out(2)
+        contrast_out(0, 0)
+        contrast_out(1, 0)
+        group_weighted(1, 1, "scalar")
+        contrast_out(2, 0)
+        quantize_priced(3, 0, 2)
+        scale_on_gpsimd((8, 1), (9, 1))
+        quantize_priced(4, 0, 2)
+        prices(5)
+        prices(6)
+        contrast_mm(3, 0, 0, 3, 5)
+        index_mm(3, 0)
+        index_mm(4, 2)
+        turns(7, (3, 4))
+        turns(8, (7, 6))
+        contrast_out(3, 0)
+        index_out(3)
+        index_out(4)
+        group_weighted(2, 1, "scalar")
+        quantize_priced(5, 0, 2)
+        quantize_weighted(1, 1)
+        quantize_priced(6, 0, 2)
+        prices(7)
+        prices(8)
+        contrast_mm(0, 1, 0, 2, 1)
+        index_mm(5, 5)
+        index_mm(6, 0)
+        contrast_mm(1, 1, 0, 2, 2)
+        turns(9, (3, 4))
+        turns(10, (7, 6))
+        index_out(5)
+        index_out(6)
+        quantize_priced(7, 0, 2)
+        quantize_weighted(2, 1)
+        quantize_priced(8, 0, 2)
+        prices(9)
+        prices(10)
+        index_mm(7, 5)
+        contrast_mm(0, 1, 2, 3)
+        contrast_mm(1, 1, 2, 3)
+        index_mm(8, 0)
+        turns(11, (3, 4))
+        index_out(7)
+        contrast_out(0, 1)
+        contrast_out(1, 1)
+        index_out(8)
+        quantize_priced(9, 0, 2)
+        price(11, 0)
+        quantize_priced(10, 0, 2)
+        price(11, 1)
+        quantize_priced(11, 0, 1)
+        quantize_priced(11, 1, 2)
+        contrast_mm(2, 1, 0, 3, 7)
+        index_mm(9, 5)
+        contrast_mm(3, 1, 0, 3, 6)
+        index_mm(10, 1)
+        index_mm(11, 2)
+        contrast_out(2, 1)
+        index_out(9)
         contrast_out(3, 1, "vector")
-        index_out(SG - 1, 3)
+        index_out(10)
+        index_out(11, "vector")

@@ -29,7 +29,7 @@ NJ = N // KP
 TILES = SG * T
 LINE = 8
 
-AHEAD = 3
+WARM0 = 4
 
 
 def tile_ghosh_price_push_s8_kernel(
@@ -119,7 +119,7 @@ def tile_ghosh_price_push_s8_kernel(
         sh_wide, sh_bank, sh_group = {}, {}, {}
 
         def widen(i, engine="scalar"):
-            sh_wide[i] = work.tile([P, N], BF16, name="wide", bufs=3)
+            sh_wide[i] = work.tile([P, N], BF16, name="wide", bufs=5)
             copy_on(engine, sh_wide[i][:], sh_bytes[i].bitcast(FP8))
 
         def turn_shocks(i, number):
@@ -129,12 +129,15 @@ def tile_ghosh_price_push_s8_kernel(
                 for u in range(2):
                     nc.tensor.transpose(sh_bank[i][:, q, u, :], words[:, HALF * q + u : HALF * (q + 1) : 2], ident[:])
 
-        def scale_shocks(i):
-            sh_group[i] = work.tile([P, N], BF16, name="sh_group", bufs=4, align_bytes=64)
+        def scale_shocks(i, q0=0, q1=KQ):
+            if q0 == 0 and i == 2:
+                sh_group[i] = work.tile([P, N], BF16, name="handed", bufs=1, align_bytes=64)
+            elif q0 == 0:
+                sh_group[i] = work.tile([P, N], BF16, name="sh_group", bufs=4, align_bytes=64)
             grouped = sh_group[i][:].rearrange("p (q r u e) -> p q r u e", q=KQ, u=2, e=2)
             halves = sh_bank[i][:].rearrange("p q u r -> p (q u r)").bitcast(BF16)
             halves = halves.rearrange("p (q u r e) -> p q r u e", q=KQ, u=2, e=2)
-            for q in range(KQ):
+            for q in range(q0, q1):
                 scales = scale_kp[:, q, :].rearrange("p (u e) -> p u e", u=2).unsqueeze(1).to_broadcast([P, P, 2, 2])
                 nc.vector.tensor_tensor(out=grouped[:, q], in0=halves[:, q], in1=scales, op=MULT)
 
@@ -154,7 +157,7 @@ def tile_ghosh_price_push_s8_kernel(
                     nc.tensor.transpose(con_bank[n][:, a, u, :], words[:, HALF * g + u : HALF * (g + 1) : 2], ident[:])
 
         def empty_contrasts(n, engine="scalar"):
-            con_group[n] = work.tile([P, 2 * KP], BF16, name="con_group", bufs=3, align_bytes=64)
+            con_group[n] = work.tile([P, 2 * KP], BF16, name="con_group", bufs=4, align_bytes=64)
             copy_on(
                 engine,
                 con_group[n][:].bitcast(F32).rearrange("p (a r u) -> p a r u", a=2, u=2),
@@ -169,11 +172,21 @@ def tile_ghosh_price_push_s8_kernel(
 
         def group_inverse(j, q, engine, c0=0, c1=KP):
             if (j, q) not in inv_group:
-                inv_group[j, q] = work.tile([P, KP, T], BF16, name="inv_group%d" % (q if j == 0 else 1 - q), bufs=1, align_bytes=64)
+                inv_group[j, q] = work.tile([P, KP, T], BF16, name="inv_group%d" % (q - j), bufs=1, align_bytes=64)
             interleave(engine, inv_group[j, q][:, c0:c1, :], inv_raw[j, q][:, :, c0:c1])
 
         def quantize_inverse(j, q):
             quantize(inv_codes[:, j, q, :], inv_scales[:, j, q, :], inv_group[j, q][:].rearrange("p n t -> p (n t)"))
+
+        inv_half = {}
+
+        def group_inverse_half(h):
+            inv_half[h] = work.tile([P, HALF, T], BF16, name=("inv_group1", "handed")[h], bufs=1, align_bytes=64)
+            interleave("gpsimd", inv_half[h][:], inv_raw[1, 0][:, :, HALF * h : HALF * (h + 1)])
+
+        def quantize_inverse_half(h):
+            cols = slice(HALF * h, HALF * (h + 1))
+            quantize(inv_codes[:, 1, 0, cols], inv_scales[:, 1, 0, cols], inv_half[h][:].rearrange("p n t -> p (n t)"))
 
         mv_bank, rel, tr_bank, priced, scaled, weighted = {}, {}, {}, {}, {}, {}
 
@@ -192,7 +205,7 @@ def tile_ghosh_price_push_s8_kernel(
 
         def relatives(i, j):
             if j == 0:
-                rel[i] = work.tile([P, NJ, KP], F32, name="rel", bufs=12)
+                rel[i] = work.tile([P, NJ, KP], F32, name="rel", bufs=10)
             nc.scalar.activation(
                 out=rel[i][:, j, :].rearrange("p (v m) -> p v m", v=T),
                 in_=mv_bank[i, j][:].rearrange("p (m v) -> p v m", v=T),
@@ -206,7 +219,7 @@ def tile_ghosh_price_push_s8_kernel(
 
         def price(i, j):
             if j == 0:
-                priced[i] = work.tile([P, NJ, P, T], BF16, name="priced", bufs=3, align_bytes=64)
+                priced[i] = work.tile([P, NJ, P, T], BF16, name="priced", bufs=4, align_bytes=64)
             nc.vector.tensor_tensor(
                 out=priced[i][:, j],
                 in0=tr_bank[i, j][:].rearrange("p v m -> p m v"),
@@ -221,28 +234,28 @@ def tile_ghosh_price_push_s8_kernel(
                 priced[i][:, j0:j1].rearrange("p j m v -> p (j m v)"),
             )
 
-        def plane(i, j):
-            if (i // T, j) not in scaled:
-                scaled[i // T, j] = work.tile([P, T, KP], BF16, name="scaled", bufs=5)
-            return scaled[i // T, j][:, i % T, :]
+        def plane(i, j0, j1):
+            if i // T not in scaled:
+                scaled[i // T] = work.tile([P, T, N], BF16, name="scaled", bufs=3)
+            return scaled[i // T][:, i % T, KP * j0 : KP * j1]
 
         def scale_on_scalar(i, j):
             nc.scalar.activation(
-                out=plane(i, j),
+                out=plane(i, j, j + 1),
                 in_=rel[i][:, j, :],
                 func=COPY,
                 scale=weight_f32[:, i // T, i % T : i % T + 1],
             )
 
         def scale_on_gpsimd(*units):
-            i0 = min(i for i, j in units)
-            count = max(i for i, j in units) - i0 + 1
+            i0 = min(unit[0] for unit in units)
+            count = max(unit[0] for unit in units) - i0 + 1
             columns = work.tile([P, count], F32, name="columns", bufs=4)
             nc.vector.tensor_copy(out=columns[:], in_=weight_kp[:].rearrange("p g t -> p (g t)")[:, i0 : i0 + count])
-            for i, j in units:
+            for i, j0, j1 in units:
                 nc.gpsimd.tensor_scalar(
-                    out=plane(i, j),
-                    in0=rel[i][:, j, :],
+                    out=plane(i, j0, j1),
+                    in0=rel[i][:, j0:j1, :].rearrange("p j c -> p (j c)"),
                     scalar1=columns[:, i - i0 : i - i0 + 1],
                     scalar2=0.0,
                     op0=MULT,
@@ -251,8 +264,8 @@ def tile_ghosh_price_push_s8_kernel(
 
         def group_weighted(g, j, engine, c0=0, c1=KP):
             if (g, j) not in weighted:
-                weighted[g, j] = work.tile([P, KP, T], BF16, name="grouped", bufs=3, align_bytes=64)
-            interleave(engine, weighted[g, j][:, c0:c1, :], scaled[g, j][:, :, c0:c1])
+                weighted[g, j] = work.tile([P, KP, T], BF16, name="grouped%d" % (1 if (g, j) in ((0, 1), (2, 1)) else 2 * (g // 2)), bufs=1, align_bytes=64)
+            interleave(engine, weighted[g, j][:, c0:c1, :], scaled[g][:, :, KP * j + c0 : KP * j + c1])
 
         def quantize_weighted(g, j):
             quantize(we_codes[:, g, j, :], we_scales[:, g, j, :], weighted[g, j][:].rearrange("p n t -> p (n t)"))
@@ -280,6 +293,26 @@ def tile_ghosh_price_push_s8_kernel(
             result = result_tile()
             copy_on(engine, result[:], index_bank[i][:])
             nc.sync.dma_start(out=index_v[i // T][:, i % T, :], in_=result[:])
+
+        def index_half(i, h, number):
+            index_bank[i, h] = bank_of(number, [P, 2, P])
+            for c in range(2):
+                c0 = HALF * h + P * c
+                for j in range(NJ):
+                    nc.tensor.matmul_mx(
+                        out=index_bank[i, h][:, c, :],
+                        lhsT=pr_codes[:, i, j, :].bitcast(FP8X4),
+                        lhsT_scale=pr_scales[:, i, j, :],
+                        rhs=b_words[:, j, 2 * c0 : 2 * (c0 + P)].bitcast(FP4X4),
+                        rhs_scale=b_scales[:, j, c0 : c0 + P],
+                        start=(j == 0),
+                        stop=(j == NJ - 1),
+                    )
+
+        def index_half_out(i, h, engine):
+            result = result_tile()
+            copy_on(engine, result[:, 0:HALF], index_bank[i, h][:].rearrange("p c n -> p (c n)"))
+            nc.sync.dma_start(out=index_v[i // T][:, i % T, HALF * h : HALF * (h + 1)], in_=result[:, 0:HALF])
 
         def contrast_mm(a, j, g0, g1, number=None):
             if g0 == 0:
@@ -309,8 +342,8 @@ def tile_ghosh_price_push_s8_kernel(
         nc.sync.dma_start(out=scale_kp[:], in_=shocks_scale.rearrange("o (q p t) -> p (o q) t", p=P, t=T))
         load_shocks(0)
         load_inverse(0, 0)
-        load_shocks(1)
         load_inverse(0, 1)
+        load_shocks(1)
         load_shocks(2)
         load_inverse(1, 0)
         load_inverse(1, 1)
@@ -340,61 +373,73 @@ def tile_ghosh_price_push_s8_kernel(
             for j in range(NJ):
                 price(i, j)
 
+        def warm(count):
+            if count:
+                bank = bank_of(1, [P, KP])
+                for k in range(count):
+                    nc.tensor.matmul(bank[:], inv_raw[0, 1][:, 0, 0:P], inv_raw[0, 1][:, 0, :], start=True, stop=True)
+
         widen(0)
         turn_shocks(0, 2)
+        warm(WARM0)
+        group_inverse(0, 0, "scalar", HALF, KP)
+        group_inverse(0, 0, "vector", 0, HALF)
+        scale_shocks(0)
+        group_inverse(0, 1, "scalar", HALF, KP)
+        group_inverse(0, 1, "vector", 0, HALF)
         widen(1)
         turn_shocks(1, 3)
         widen(2)
         turn_shocks(2, 4)
-        group_inverse(0, 0, "vector")
-        scale_shocks(0)
-        group_inverse(0, 1, "scalar", HALF, KP)
-        group_inverse(0, 1, "vector", 0, HALF)
         widen(3)
         widen(4)
         widen(5)
         quantize_inverse(0, 0)
         quantize_shocks(0)
         quantize_inverse(0, 1)
-        group_inverse(1, 0, "gpsimd", 0, 320)
-        scale_shocks(1)
-        scale_shocks(2)
+        group_inverse_half(0)
         moves(0, 0, 0)
         turn_shocks(3, 5)
         turn_shocks(4, 6)
+        scale_shocks(1)
+        scale_shocks(2, 0, 1)
+        quantize_shocks(1)
+        moves(1, 0, 1)
         turn_shocks(5, 7)
+        turn_contrasts(0, 2)
         group_inverse(1, 1, "scalar", 0, HALF)
         relatives(0, 0)
         group_inverse(1, 1, "scalar", HALF, KP)
-        quantize_shocks(1)
-        scale_on_gpsimd((0, 0))
-        group_inverse(1, 0, "gpsimd", 320, KP)
-        quantize_shocks(2)
-        scale_shocks(3)
-        scale_shocks(4)
-        moves(1, 0, 1)
-        turn_contrasts(0, 2)
-        turn_contrasts(1, 3)
         relatives(1, 0)
         widen(6)
-        empty_contrasts(0)
+        scale_shocks(2, 1, 2)
+        scale_shocks(3, 0, 1)
+        quantize_shocks(2)
+        group_inverse_half(1)
         moves(2, 0, 0)
+        turn_contrasts(1, 3)
         turn_contrasts(2, 4)
-        turn_shocks(6, 5)
-        relatives(2, 0)
-        widen(7)
-        empty_contrasts(1)
+        scale_shocks(3, 1, 2)
+        scale_shocks(4)
+        scale_shocks(5, 0, 1)
         quantize_shocks(3)
-        quantize_inverse(1, 0)
-        quantize_inverse(1, 1)
-        scale_on_gpsimd((1, 0), (2, 0))
-        quantize_shocks(4)
-        scale_shocks(5)
-        scale_shocks(6)
         moves(3, 0, 1)
+        empty_contrasts(0)
+        widen(7)
+        relatives(2, 0)
+        empty_contrasts(1)
+        turn_shocks(6, 5)
         turn_shocks(7, 6)
         relatives(3, 0)
         empty_contrasts(2)
+        quantize_inverse_half(0)
+        quantize_inverse(1, 1)
+        quantize_inverse_half(1)
+        scale_on_gpsimd((0, 0, 1), (1, 0, 1), (2, 0, 1))
+        quantize_shocks(4)
+        scale_shocks(5, 1, 2)
+        scale_shocks(6)
+        scale_shocks(7, 0, 1)
         widen(8)
         widen(9)
         units = [(0, 1), (1, 1), (2, 1), (3, 1)]
@@ -402,15 +447,18 @@ def tile_ghosh_price_push_s8_kernel(
         exps(units)
         turn_shocks(8, 4)
         turn_shocks(9, 7)
+        turn_contrasts(3, 5)
         widen(10)
         widen(11)
         quantize_shocks(5)
         quantize_contrasts(0)
         quantize_contrasts(1)
-        scale_on_gpsimd((3, 0), (0, 1))
+        scale_on_gpsimd((3, 0, 1), (0, 1, 2), (1, 1, 2))
         quantize_shocks(6)
-        scale_shocks(7)
+        scale_shocks(7, 1, 2)
         scale_shocks(8)
+        empty_contrasts(3, "vector")
+        scale_shocks(9, 0, 1)
         units = [(4, 0), (5, 0), (4, 1), (5, 1)]
         move(units, [0, 2, 3, 1])
         exps(units)
@@ -421,135 +469,132 @@ def tile_ghosh_price_push_s8_kernel(
         quantize_shocks(7)
         quantize_contrasts(2)
         quantize_weighted(0, 0)
-        scale_on_gpsimd((1, 1), (4, 0), (5, 0))
+        scale_on_gpsimd((4, 0, 2), (5, 0, 2))
         quantize_shocks(8)
-        scale_shocks(9)
+        scale_shocks(9, 1, 2)
         scale_shocks(10)
         scale_shocks(11)
         units = [(6, 0), (7, 0), (6, 1), (7, 1)]
         move(units, [0, 2, 3, 1])
         exps(units)
         turns(0, (4, 7))
-        turn_contrasts(3, 5)
+        turn_contrasts(4, 5)
         scale_on_scalar(2, 1)
         scale_on_scalar(3, 1)
         quantize_shocks(9)
         quantize_shocks(10)
-        scale_on_gpsimd((6, 0), (7, 0))
+        scale_on_gpsimd((6, 0, 2))
         quantize_shocks(11)
         prices(0)
-        empty_contrasts(3, "vector")
+        empty_contrasts(4, "vector")
         units = [(8, 0), (9, 0), (8, 1), (9, 1)]
         move(units, [0, 2, 3, 1])
         exps(units)
         turns(1, (4, 7))
-        turn_contrasts(4, 6)
-        group_weighted(1, 0, "scalar", HALF, KP)
-        group_weighted(0, 1, "vector")
-        quantize_priced(0, 0, 2)
+        turn_contrasts(5, 6)
+        group_weighted(0, 1, "scalar", HALF, KP)
         quantize_contrasts(3)
-        scale_on_gpsimd((8, 0), (9, 0))
-        quantize_weighted(0, 1)
+        quantize_contrasts(4)
+        scale_on_gpsimd((7, 0, 2))
+        quantize_priced(0, 0, 2)
         prices(1)
-        empty_contrasts(4, "vector")
+        empty_contrasts(5, "vector")
         units = [(10, 0), (11, 0), (10, 1), (11, 1)]
         move(units, [0, 2, 3, 1])
-        index_mm(0, 5)
         exps(units)
         turns(2, (4, 7))
-        turn_contrasts(5, 6)
+        turns(3, (5, 6))
         scale_on_scalar(10, 0)
         scale_on_scalar(11, 0)
-        index_out(0)
-        group_weighted(1, 0, "vector", 0, HALF)
+        group_weighted(0, 1, "scalar", 0, HALF)
+        group_weighted(1, 0, "vector")
         quantize_priced(1, 0, 2)
-        quantize_contrasts(4)
-        scale_on_gpsimd((4, 1), (5, 1))
+        scale_on_gpsimd((8, 0, 2), (9, 0, 1))
         quantize_weighted(1, 0)
         prices(2)
-        empty_contrasts(5, "vector")
-        index_mm(1, 5)
-        contrast_mm(0, 0, 0, 1, 0)
-        contrast_mm(1, 0, 0, 1, 2)
+        prices(3)
+        index_mm(0, 0)
+        index_mm(1, 2)
+        contrast_mm(0, 0, 0, 1, 3)
+        contrast_mm(1, 0, 0, 1, 1)
         contrast_mm(0, 0, 1, 2)
         contrast_mm(1, 0, 1, 2)
-        turns(3, (3, 4))
-        turns(4, (7, 6))
-        group_weighted(2, 0, "scalar")
+        turns(4, (4, 7))
+        turns(5, (5, 6))
+        index_out(0)
+        group_weighted(2, 0, "scalar", HALF, KP)
         index_out(1)
-        scale_on_scalar(10, 1)
-        scale_on_scalar(11, 1)
         quantize_priced(2, 0, 2)
-        quantize_contrasts(5)
-        scale_on_gpsimd((6, 1), (7, 1))
+        group_weighted(2, 0, "vector", 0, HALF)
+        quantize_priced(3, 0, 2)
+        scale_on_gpsimd((9, 1, 2), (10, 1, 2), (11, 1, 2))
         quantize_weighted(2, 0)
-        prices(3)
         prices(4)
-        index_mm(2, 5)
+        prices(5)
+        index_mm(2, 0)
+        index_mm(3, 2)
         contrast_mm(0, 0, 2, 3)
         contrast_mm(1, 0, 2, 3)
-        contrast_mm(2, 0, 0, 3, 1)
-        turns(5, (3, 4))
-        turns(6, (7, 6))
+        turns(6, (4, 7))
+        turns(7, (5, 6))
         index_out(2)
+        index_out(3)
         contrast_out(0, 0)
         contrast_out(1, 0)
         group_weighted(1, 1, "scalar")
-        contrast_out(2, 0)
-        quantize_priced(3, 0, 2)
-        scale_on_gpsimd((8, 1), (9, 1))
+        quantize_contrasts(5)
         quantize_priced(4, 0, 2)
-        prices(5)
-        prices(6)
-        contrast_mm(3, 0, 0, 3, 5)
-        index_mm(3, 0)
-        index_mm(4, 2)
-        turns(7, (3, 4))
-        turns(8, (7, 6))
-        contrast_out(3, 0)
-        index_out(3)
-        index_out(4)
-        group_weighted(2, 1, "scalar")
         quantize_priced(5, 0, 2)
-        quantize_weighted(1, 1)
-        quantize_priced(6, 0, 2)
+        quantize_weighted(0, 1)
+        group_weighted(2, 1, "gpsimd", 0, 320)
+        prices(6)
         prices(7)
-        prices(8)
-        contrast_mm(0, 1, 0, 2, 1)
-        index_mm(5, 5)
-        index_mm(6, 0)
-        contrast_mm(1, 1, 0, 2, 2)
-        turns(9, (3, 4))
-        turns(10, (7, 6))
+        contrast_mm(2, 0, 0, 3, 3)
+        contrast_mm(3, 0, 0, 3, 1)
+        index_mm(4, 0)
+        index_mm(5, 2)
+        turns(8, (4, 7))
+        turns(9, (5, 6))
+        contrast_out(2, 0)
+        contrast_out(3, 0)
+        index_out(4)
         index_out(5)
-        index_out(6)
+        quantize_priced(6, 0, 2)
+        group_weighted(2, 1, "vector", 320, KP)
         quantize_priced(7, 0, 2)
+        quantize_weighted(1, 1)
         quantize_weighted(2, 1)
-        quantize_priced(8, 0, 2)
+        prices(8)
         prices(9)
-        prices(10)
-        index_mm(7, 5)
-        contrast_mm(0, 1, 2, 3)
-        contrast_mm(1, 1, 2, 3)
-        index_mm(8, 0)
-        turns(11, (3, 4))
+        index_mm(6, 3)
+        index_mm(7, 1)
+        contrast_mm(0, 1, 0, 3, 0)
+        contrast_mm(1, 1, 0, 3, 2)
+        index_out(6)
+        contrast_mm(2, 1, 0, 3, 3)
+        turns(10, (4, 7))
+        turns(11, (5, 6))
         index_out(7)
         contrast_out(0, 1)
         contrast_out(1, 1)
-        index_out(8)
+        contrast_out(2, 1)
+        quantize_priced(8, 0, 2)
         quantize_priced(9, 0, 2)
+        prices(10)
         price(11, 0)
         quantize_priced(10, 0, 2)
         price(11, 1)
         quantize_priced(11, 0, 1)
         quantize_priced(11, 1, 2)
-        contrast_mm(2, 1, 0, 3, 7)
-        index_mm(9, 5)
-        contrast_mm(3, 1, 0, 3, 6)
-        index_mm(10, 1)
-        index_mm(11, 2)
-        contrast_out(2, 1)
+        index_mm(8, 1)
+        index_mm(9, 0)
+        contrast_mm(3, 1, 0, 3, 2)
+        index_mm(10, 3)
+        for h in range(2):
+            index_half(11, h, (4, 7)[h])
+        index_out(8)
         index_out(9)
-        contrast_out(3, 1, "vector")
-        index_out(10)
-        index_out(11, "vector")
+        contrast_out(3, 1)
+        index_out(10, "vector")
+        for h in range(2):
+            index_half_out(11, h, ("scalar", "vector")[h])

@@ -29,7 +29,8 @@ NJ = N // KP
 TILES = SG * T
 LINE = 8
 
-WARM0 = 4
+WARM0 = 3
+WARM1 = 2
 
 
 def tile_ghosh_price_push_s8_kernel(
@@ -42,7 +43,7 @@ def tile_ghosh_price_push_s8_kernel(
         psum = ctx.enter_context(tc.psum_pool(name="psum", bufs=1))
         ctx.enter_context(tc.manual_schedule())
 
-        byte_loads = ((0, 1), (1, 4), (4, 6), (6, 8), (8, 12))
+        byte_loads = ((0, 1), (1, 2), (2, 4), (4, 6), (6, 8), (8, 12))
         sh_bytes = {}
         for i0, i1 in byte_loads:
             loaded = keep.tile([P, i1 - i0, N], U8, name="sh_bytes%d" % i0, align_bytes=64)
@@ -180,9 +181,10 @@ def tile_ghosh_price_push_s8_kernel(
 
         inv_half = {}
 
-        def group_inverse_half(h):
-            inv_half[h] = work.tile([P, HALF, T], BF16, name=("inv_group1", "handed")[h], bufs=1, align_bytes=64)
-            interleave("gpsimd", inv_half[h][:], inv_raw[1, 0][:, :, HALF * h : HALF * (h + 1)])
+        def group_inverse_half(h, engine, c0, c1):
+            if h not in inv_half:
+                inv_half[h] = work.tile([P, HALF, T], BF16, name=("inv_group1", "handed")[h], bufs=1, align_bytes=64)
+            interleave(engine, inv_half[h][:, c0:c1, :], inv_raw[1, 0][:, :, HALF * h + c0 : HALF * h + c1])
 
         def quantize_inverse_half(h):
             cols = slice(HALF * h, HALF * (h + 1))
@@ -264,7 +266,7 @@ def tile_ghosh_price_push_s8_kernel(
 
         def group_weighted(g, j, engine, c0=0, c1=KP):
             if (g, j) not in weighted:
-                weighted[g, j] = work.tile([P, KP, T], BF16, name="grouped%d" % (1 if (g, j) in ((0, 1), (2, 1)) else 2 * (g // 2)), bufs=1, align_bytes=64)
+                weighted[g, j] = work.tile([P, KP, T], BF16, name="grouped%d" % {(0, 0): 0, (0, 1): 1, (1, 0): 2, (2, 0): 0, (1, 1): 2, (2, 1): 1}[g, j], bufs=1, align_bytes=64)
             interleave(engine, weighted[g, j][:, c0:c1, :], scaled[g][:, :, KP * j + c0 : KP * j + c1])
 
         def quantize_weighted(g, j):
@@ -339,19 +341,20 @@ def tile_ghosh_price_push_s8_kernel(
 
         nc.vector.memset(b_scales[:].rearrange("p j n -> p (j n)").bitcast(I32), 0)
         make_identity(nc, ident[:])
-        nc.sync.dma_start(out=scale_kp[:], in_=shocks_scale.rearrange("o (q p t) -> p (o q) t", p=P, t=T))
         load_shocks(0)
         load_inverse(0, 0)
-        load_inverse(0, 1)
+        nc.sync.dma_start(out=scale_kp[:], in_=shocks_scale.rearrange("o (q p t) -> p (o q) t", p=P, t=T))
         load_shocks(1)
+        load_inverse(0, 1)
         load_shocks(2)
+        load_shocks(3)
         load_inverse(1, 0)
         load_inverse(1, 1)
         nc.sync.dma_start(out=weight_kp[:], in_=weight.rearrange("(g p t) -> p g t", p=P, t=T))
         load_contrasts(0)
         load_contrasts(1)
-        load_shocks(3)
         load_shocks(4)
+        load_shocks(5)
         load_contrasts(2)
         load_contrasts(3)
         nc.sync.dma_start(out=base_kp[:], in_=base.rearrange("(j p t) -> p j t", p=P, t=T))
@@ -373,62 +376,64 @@ def tile_ghosh_price_push_s8_kernel(
             for j in range(NJ):
                 price(i, j)
 
-        def warm(count):
+        def warm(count, q):
             if count:
                 bank = bank_of(1, [P, KP])
                 for k in range(count):
-                    nc.tensor.matmul(bank[:], inv_raw[0, 1][:, 0, 0:P], inv_raw[0, 1][:, 0, :], start=True, stop=True)
+                    nc.tensor.matmul(bank[:], inv_raw[0, q][:, 0, 0:P], inv_raw[0, q][:, 0, :], start=True, stop=True)
 
         widen(0)
         turn_shocks(0, 2)
-        warm(WARM0)
+        warm(WARM0, 0)
         group_inverse(0, 0, "scalar", HALF, KP)
         group_inverse(0, 0, "vector", 0, HALF)
         scale_shocks(0)
-        group_inverse(0, 1, "scalar", HALF, KP)
-        group_inverse(0, 1, "vector", 0, HALF)
         widen(1)
         turn_shocks(1, 3)
+        warm(WARM1, 1)
+        group_inverse(0, 1, "scalar", HALF, KP)
+        group_inverse(0, 1, "vector", 0, HALF)
         widen(2)
         turn_shocks(2, 4)
         widen(3)
+        turn_shocks(3, 5)
         widen(4)
         widen(5)
         quantize_inverse(0, 0)
         quantize_shocks(0)
         quantize_inverse(0, 1)
-        group_inverse_half(0)
+        group_inverse_half(0, "gpsimd", 0, 192)
+        group_inverse_half(0, "scalar", 192, HALF)
         moves(0, 0, 0)
-        turn_shocks(3, 5)
         turn_shocks(4, 6)
+        turn_shocks(5, 7)
         scale_shocks(1)
         scale_shocks(2, 0, 1)
         quantize_shocks(1)
         moves(1, 0, 1)
-        turn_shocks(5, 7)
         turn_contrasts(0, 2)
+        turn_contrasts(1, 3)
         group_inverse(1, 1, "scalar", 0, HALF)
         relatives(0, 0)
         group_inverse(1, 1, "scalar", HALF, KP)
-        relatives(1, 0)
         widen(6)
+        relatives(1, 0)
         scale_shocks(2, 1, 2)
         scale_shocks(3, 0, 1)
         quantize_shocks(2)
-        group_inverse_half(1)
+        group_inverse_half(1, "gpsimd", 0, HALF)
         moves(2, 0, 0)
-        turn_contrasts(1, 3)
         turn_contrasts(2, 4)
         scale_shocks(3, 1, 2)
+        turn_shocks(6, 5)
         scale_shocks(4)
         scale_shocks(5, 0, 1)
         quantize_shocks(3)
         moves(3, 0, 1)
-        empty_contrasts(0)
         widen(7)
+        empty_contrasts(0)
         relatives(2, 0)
         empty_contrasts(1)
-        turn_shocks(6, 5)
         turn_shocks(7, 6)
         relatives(3, 0)
         empty_contrasts(2)
@@ -465,10 +470,10 @@ def tile_ghosh_price_push_s8_kernel(
         turn_shocks(10, 5)
         turn_shocks(11, 6)
         nc.vector.tensor_copy(out=weight_f32[:], in_=weight_kp[:])
-        group_weighted(0, 0, "vector")
+        group_weighted(0, 0, "scalar", HALF, KP)
         quantize_shocks(7)
+        group_weighted(0, 0, "vector", 0, HALF)
         quantize_contrasts(2)
-        quantize_weighted(0, 0)
         scale_on_gpsimd((4, 0, 2), (5, 0, 2))
         quantize_shocks(8)
         scale_shocks(9, 1, 2)
@@ -494,9 +499,10 @@ def tile_ghosh_price_push_s8_kernel(
         turn_contrasts(5, 6)
         group_weighted(0, 1, "scalar", HALF, KP)
         quantize_contrasts(3)
+        quantize_priced(0, 0, 2)
         quantize_contrasts(4)
         scale_on_gpsimd((7, 0, 2))
-        quantize_priced(0, 0, 2)
+        quantize_weighted(0, 0)
         prices(1)
         empty_contrasts(5, "vector")
         units = [(10, 0), (11, 0), (10, 1), (11, 1)]
@@ -546,7 +552,8 @@ def tile_ghosh_price_push_s8_kernel(
         quantize_priced(4, 0, 2)
         quantize_priced(5, 0, 2)
         quantize_weighted(0, 1)
-        group_weighted(2, 1, "gpsimd", 0, 320)
+        group_weighted(2, 1, "gpsimd", 0, 288)
+        group_weighted(2, 1, "scalar", 288, KP)
         prices(6)
         prices(7)
         contrast_mm(2, 0, 0, 3, 3)
@@ -560,7 +567,6 @@ def tile_ghosh_price_push_s8_kernel(
         index_out(4)
         index_out(5)
         quantize_priced(6, 0, 2)
-        group_weighted(2, 1, "vector", 320, KP)
         quantize_priced(7, 0, 2)
         quantize_weighted(1, 1)
         quantize_weighted(2, 1)

@@ -43,7 +43,7 @@ def tile_ghosh_price_push_s8_kernel(
         psum = ctx.enter_context(tc.psum_pool(name="psum", bufs=1))
         ctx.enter_context(tc.manual_schedule())
 
-        byte_loads = ((0, 1), (1, 2), (2, 4), (4, 6), (6, 8), (8, 12))
+        byte_loads = ((0, 1), (1, 3), (3, 4), (4, 6), (6, 8), (8, 12))
         sh_bytes = {}
         for i0, i1 in byte_loads:
             loaded = keep.tile([P, i1 - i0, N], U8, name="sh_bytes%d" % i0, align_bytes=64)
@@ -204,6 +204,21 @@ def tile_ghosh_price_push_s8_kernel(
                     start=(q == 0),
                     stop=(q == KQ - 1),
                 )
+
+        def move_passes(units, banks):
+            for (i, j), number in zip(units, banks):
+                mv_bank[i, j] = bank_of(number, [P, KP])
+            for q in (1, 0):
+                for i, j in units:
+                    nc.tensor.matmul_mx(
+                        out=mv_bank[i, j][:],
+                        lhsT=sh_codes[:, i, q, :].bitcast(FP8X4),
+                        lhsT_scale=sh_scales[:, i, q, :],
+                        rhs=inv_codes[:, j, q, :].bitcast(FP8X4),
+                        rhs_scale=inv_scales[:, j, q, :],
+                        start=(q == 1),
+                        stop=(q == 0),
+                    )
 
         def relatives(i, j):
             if j == 0:
@@ -390,11 +405,11 @@ def tile_ghosh_price_push_s8_kernel(
         scale_shocks(0)
         widen(1)
         turn_shocks(1, 3)
+        widen(2)
+        turn_shocks(2, 4)
         warm(WARM1, 1)
         group_inverse(0, 1, "scalar", HALF, KP)
         group_inverse(0, 1, "vector", 0, HALF)
-        widen(2)
-        turn_shocks(2, 4)
         widen(3)
         turn_shocks(3, 5)
         widen(4)
@@ -428,17 +443,17 @@ def tile_ghosh_price_push_s8_kernel(
         turn_shocks(6, 5)
         scale_shocks(4)
         scale_shocks(5, 0, 1)
+        widen(7)
+        turn_shocks(7, 6)
         quantize_shocks(3)
         moves(3, 0, 1)
-        widen(7)
         empty_contrasts(0)
         relatives(2, 0)
         empty_contrasts(1)
-        turn_shocks(7, 6)
-        relatives(3, 0)
         empty_contrasts(2)
-        quantize_inverse_half(0)
+        relatives(3, 0)
         quantize_inverse(1, 1)
+        quantize_inverse_half(0)
         quantize_inverse_half(1)
         scale_on_gpsimd((0, 0, 1), (1, 0, 1), (2, 0, 1))
         quantize_shocks(4)
@@ -448,9 +463,9 @@ def tile_ghosh_price_push_s8_kernel(
         widen(8)
         widen(9)
         units = [(0, 1), (1, 1), (2, 1), (3, 1)]
-        move(units, [0, 2, 3, 1])
+        move_passes(units, [0, 2, 3, 4])
         exps(units)
-        turn_shocks(8, 4)
+        turn_shocks(8, 1)
         turn_shocks(9, 7)
         turn_contrasts(3, 5)
         widen(10)
@@ -465,7 +480,7 @@ def tile_ghosh_price_push_s8_kernel(
         empty_contrasts(3, "vector")
         scale_shocks(9, 0, 1)
         units = [(4, 0), (5, 0), (4, 1), (5, 1)]
-        move(units, [0, 2, 3, 1])
+        move(units, [0, 2, 3, 4])
         exps(units)
         turn_shocks(10, 5)
         turn_shocks(11, 6)
@@ -480,9 +495,9 @@ def tile_ghosh_price_push_s8_kernel(
         scale_shocks(10)
         scale_shocks(11)
         units = [(6, 0), (7, 0), (6, 1), (7, 1)]
-        move(units, [0, 2, 3, 1])
+        move(units, [0, 2, 3, 4])
         exps(units)
-        turns(0, (4, 7))
+        turns(0, (1, 7))
         turn_contrasts(4, 5)
         scale_on_scalar(2, 1)
         scale_on_scalar(3, 1)
@@ -493,22 +508,21 @@ def tile_ghosh_price_push_s8_kernel(
         prices(0)
         empty_contrasts(4, "vector")
         units = [(8, 0), (9, 0), (8, 1), (9, 1)]
-        move(units, [0, 2, 3, 1])
+        move(units, [0, 2, 3, 4])
         exps(units)
-        turns(1, (4, 7))
+        turns(1, (1, 7))
         turn_contrasts(5, 6)
         group_weighted(0, 1, "scalar", HALF, KP)
         quantize_contrasts(3)
         quantize_priced(0, 0, 2)
-        quantize_contrasts(4)
         scale_on_gpsimd((7, 0, 2))
         quantize_weighted(0, 0)
         prices(1)
         empty_contrasts(5, "vector")
         units = [(10, 0), (11, 0), (10, 1), (11, 1)]
-        move(units, [0, 2, 3, 1])
+        move(units, [0, 2, 3, 4])
         exps(units)
-        turns(2, (4, 7))
+        turns(2, (1, 7))
         turns(3, (5, 6))
         scale_on_scalar(10, 0)
         scale_on_scalar(11, 0)
@@ -522,10 +536,10 @@ def tile_ghosh_price_push_s8_kernel(
         index_mm(0, 0)
         index_mm(1, 2)
         contrast_mm(0, 0, 0, 1, 3)
-        contrast_mm(1, 0, 0, 1, 1)
+        contrast_mm(1, 0, 0, 1, 4)
         contrast_mm(0, 0, 1, 2)
         contrast_mm(1, 0, 1, 2)
-        turns(4, (4, 7))
+        turns(4, (1, 7))
         turns(5, (5, 6))
         index_out(0)
         group_weighted(2, 0, "scalar", HALF, KP)
@@ -541,13 +555,14 @@ def tile_ghosh_price_push_s8_kernel(
         index_mm(3, 2)
         contrast_mm(0, 0, 2, 3)
         contrast_mm(1, 0, 2, 3)
-        turns(6, (4, 7))
+        turns(6, (1, 7))
         turns(7, (5, 6))
         index_out(2)
         index_out(3)
         contrast_out(0, 0)
         contrast_out(1, 0)
         group_weighted(1, 1, "scalar")
+        quantize_contrasts(4)
         quantize_contrasts(5)
         quantize_priced(4, 0, 2)
         quantize_priced(5, 0, 2)
@@ -557,10 +572,10 @@ def tile_ghosh_price_push_s8_kernel(
         prices(6)
         prices(7)
         contrast_mm(2, 0, 0, 3, 3)
-        contrast_mm(3, 0, 0, 3, 1)
+        contrast_mm(3, 0, 0, 3, 4)
         index_mm(4, 0)
         index_mm(5, 2)
-        turns(8, (4, 7))
+        turns(8, (1, 7))
         turns(9, (5, 6))
         contrast_out(2, 0)
         contrast_out(3, 0)
@@ -573,12 +588,12 @@ def tile_ghosh_price_push_s8_kernel(
         prices(8)
         prices(9)
         index_mm(6, 3)
-        index_mm(7, 1)
+        index_mm(7, 4)
         contrast_mm(0, 1, 0, 3, 0)
         contrast_mm(1, 1, 0, 3, 2)
         index_out(6)
         contrast_mm(2, 1, 0, 3, 3)
-        turns(10, (4, 7))
+        turns(10, (1, 7))
         turns(11, (5, 6))
         index_out(7)
         contrast_out(0, 1)
@@ -592,12 +607,12 @@ def tile_ghosh_price_push_s8_kernel(
         price(11, 1)
         quantize_priced(11, 0, 1)
         quantize_priced(11, 1, 2)
-        index_mm(8, 1)
+        index_mm(8, 4)
         index_mm(9, 0)
         contrast_mm(3, 1, 0, 3, 2)
         index_mm(10, 3)
         for h in range(2):
-            index_half(11, h, (4, 7)[h])
+            index_half(11, h, (1, 7)[h])
         index_out(8)
         index_out(9)
         contrast_out(3, 1)

@@ -28,9 +28,8 @@ KQ = N // KP
 NJ = N // KP
 TILES = SG * T
 LINE = 8
-
-WARM0 = 3
-WARM1 = 2
+WIDE = 4
+DEPTH = {"sh_group": 4, "con_group": 4, "ga": 1, "gb": 1, "gc": 1, "rel": 10, "priced": 5, "tagged": 4, "scaled": 3, "result": 6}
 
 
 def tile_ghosh_price_push_s8_kernel(
@@ -43,18 +42,10 @@ def tile_ghosh_price_push_s8_kernel(
         psum = ctx.enter_context(tc.psum_pool(name="psum", bufs=1))
         ctx.enter_context(tc.manual_schedule())
 
-        byte_loads = ((0, 1), (1, 3), (3, 4), (4, 6), (6, 8), (8, 12))
-        sh_bytes = {}
-        for i0, i1 in byte_loads:
-            loaded = keep.tile([P, i1 - i0, N], U8, name="sh_bytes%d" % i0, align_bytes=64)
-            for i in range(i0, i1):
-                sh_bytes[i] = loaded[:, i - i0, :]
-            sh_bytes[i0, i1] = loaded
         scale_kp = keep.tile([P, KQ, T], F32, name="scale_kp")
-        inv_raw = {(j, q): keep.tile([P, T, KP], BF16, name="inv_raw%d%d" % (j, q)) for j in range(NJ) for q in range(KQ)}
-        base_kp = keep.tile([P, NJ, T], BF16, name="base_kp")
-        weight_kp = keep.tile([P, SG, T], BF16, name="weight_kp")
-        weight_f32 = keep.tile([P, SG, T], F32, name="weight_f32")
+        base_kp = keep.tile([P, NJ * T], BF16, name="base_kp")
+        weight_kp = keep.tile([P, SG * T], BF16, name="weight_kp")
+        weight_f32 = keep.tile([P, SG * T], F32, name="weight_f32")
         b_words = keep.tile([P, NJ, 2 * C], U8, name="b_words", align_bytes=64)
         b_scales = keep.tile([P, NJ, C], U8, name="b_scales", align_bytes=64)
         con_raw = [keep.tile([P, S], BF16, name="con_raw%d" % a) for a in range(T)]
@@ -75,11 +66,16 @@ def tile_ghosh_price_push_s8_kernel(
         inverse_v = inverse.rearrange("(q p t) n -> q p t n", p=P, t=T)
         index_v = out_0.rearrange("(g m t) c -> g m t c", m=P, t=T)
 
-        def load_shocks(k):
-            i0, i1 = byte_loads[k]
-            nc.sync.dma_start(out=sh_bytes[i0, i1][:], in_=shocks_v[i0 // T][:, i0 % T : i0 % T + i1 - i0, :])
+        sh_bytes, inv_raw = {}, {}
+
+        def load_shocks(i0, i1):
+            loaded = keep.tile([P, i1 - i0, N], U8, name="sh_bytes%d" % i0, align_bytes=64)
+            nc.sync.dma_start(out=loaded[:], in_=shocks_v[i0 // T][:, i0 % T : i0 % T + i1 - i0, :])
+            for i in range(i0, i1):
+                sh_bytes[i] = loaded[:, i - i0, :]
 
         def load_inverse(j, q):
+            inv_raw[j, q] = keep.tile([P, T, KP], BF16, name="inv_raw%d%d" % (j, q))
             nc.sync.dma_start(out=inv_raw[j, q][:], in_=inverse_v[q][:, :, KP * j : KP * (j + 1)])
 
         def load_contrasts(a):
@@ -120,7 +116,7 @@ def tile_ghosh_price_push_s8_kernel(
         sh_wide, sh_bank, sh_group = {}, {}, {}
 
         def widen(i, engine="scalar"):
-            sh_wide[i] = work.tile([P, N], BF16, name="wide", bufs=5)
+            sh_wide[i] = work.tile([P, N], BF16, name="wide", bufs=WIDE)
             copy_on(engine, sh_wide[i][:], sh_bytes[i].bitcast(FP8))
 
         def turn_shocks(i, number):
@@ -130,11 +126,9 @@ def tile_ghosh_price_push_s8_kernel(
                 for u in range(2):
                     nc.tensor.transpose(sh_bank[i][:, q, u, :], words[:, HALF * q + u : HALF * (q + 1) : 2], ident[:])
 
-        def scale_shocks(i, q0=0, q1=KQ):
-            if q0 == 0 and i == 2:
-                sh_group[i] = work.tile([P, N], BF16, name="handed", bufs=1, align_bytes=64)
-            elif q0 == 0:
-                sh_group[i] = work.tile([P, N], BF16, name="sh_group", bufs=4, align_bytes=64)
+        def scale_shocks(i, q0=0, q1=KQ, tag="sh_group"):
+            if q0 == 0:
+                sh_group[i] = work.tile([P, N], BF16, name=tag, bufs=DEPTH[tag], align_bytes=64)
             grouped = sh_group[i][:].rearrange("p (q r u e) -> p q r u e", q=KQ, u=2, e=2)
             halves = sh_bank[i][:].rearrange("p q u r -> p (q u r)").bitcast(BF16)
             halves = halves.rearrange("p (q u r e) -> p q r u e", q=KQ, u=2, e=2)
@@ -157,94 +151,123 @@ def tile_ghosh_price_push_s8_kernel(
                 for u in range(2):
                     nc.tensor.transpose(con_bank[n][:, a, u, :], words[:, HALF * g + u : HALF * (g + 1) : 2], ident[:])
 
-        def empty_contrasts(n, engine="scalar"):
-            con_group[n] = work.tile([P, 2 * KP], BF16, name="con_group", bufs=4, align_bytes=64)
+        def empty_words(grouped, bank, engine):
             copy_on(
                 engine,
-                con_group[n][:].bitcast(F32).rearrange("p (a r u) -> p a r u", a=2, u=2),
-                con_bank[n][:].rearrange("p a u r -> p a r u"),
+                grouped.bitcast(F32).rearrange("p (a r u) -> p a r u", a=2, u=2),
+                bank.rearrange("p a u r -> p a r u"),
             )
+
+        def empty_contrasts(n, engine="scalar"):
+            con_group[n] = work.tile([P, 2 * KP], BF16, name="con_group", bufs=DEPTH["con_group"], align_bytes=64)
+            empty_words(con_group[n][:], con_bank[n][:], engine)
 
         def quantize_contrasts(n):
             g, cols = n % SG, slice(HALF * (n // SG), HALF * (n // SG + 1))
             quantize(con_codes[:, g, cols], con_scales[:, g, cols], con_group[n][:])
 
-        inv_group = {}
+        inv_part = {}
 
-        def group_inverse(j, q, engine, c0=0, c1=KP):
-            if (j, q) not in inv_group:
-                inv_group[j, q] = work.tile([P, KP, T], BF16, name="inv_group%d" % (q - j), bufs=1, align_bytes=64)
-            interleave(engine, inv_group[j, q][:, c0:c1, :], inv_raw[j, q][:, :, c0:c1])
+        def group_inverse(j, q, engine, c0, c1, part=(0, KP), tag=None):
+            if (j, q, part) not in inv_part:
+                tag = tag or "grouped"
+                inv_part[j, q, part] = work.tile([P, part[1] - part[0], T], BF16, name=tag, bufs=DEPTH[tag], align_bytes=64)
+            interleave(engine, inv_part[j, q, part][:, c0 - part[0] : c1 - part[0], :], inv_raw[j, q][:, :, c0:c1])
 
-        def quantize_inverse(j, q):
-            quantize(inv_codes[:, j, q, :], inv_scales[:, j, q, :], inv_group[j, q][:].rearrange("p n t -> p (n t)"))
+        def quantize_inverse(j, q, part=(0, KP)):
+            cols = slice(part[0], part[1])
+            quantize(inv_codes[:, j, q, cols], inv_scales[:, j, q, cols], inv_part[j, q, part][:].rearrange("p n t -> p (n t)"))
 
-        inv_half = {}
+        mv_bank, rel, tr_bank, priced, tagged, scaled, weighted = {}, {}, {}, {}, {}, {}, {}
 
-        def group_inverse_half(h, engine, c0, c1):
-            if h not in inv_half:
-                inv_half[h] = work.tile([P, HALF, T], BF16, name=("inv_group1", "handed")[h], bufs=1, align_bytes=64)
-            interleave(engine, inv_half[h][:, c0:c1, :], inv_raw[1, 0][:, :, HALF * h + c0 : HALF * h + c1])
+        def move_pass(i, j, q, first, last):
+            nc.tensor.matmul_mx(
+                out=mv_bank[i, j][:],
+                lhsT=sh_codes[:, i, q, :].bitcast(FP8X4),
+                lhsT_scale=sh_scales[:, i, q, :],
+                rhs=inv_codes[:, j, q, :].bitcast(FP8X4),
+                rhs_scale=inv_scales[:, j, q, :],
+                start=first,
+                stop=last,
+            )
 
-        def quantize_inverse_half(h):
-            cols = slice(HALF * h, HALF * (h + 1))
-            quantize(inv_codes[:, 1, 0, cols], inv_scales[:, 1, 0, cols], inv_half[h][:].rearrange("p n t -> p (n t)"))
-
-        mv_bank, rel, tr_bank, priced, scaled, weighted = {}, {}, {}, {}, {}, {}
-
-        def moves(i, j, number):
-            mv_bank[i, j] = bank_of(number, [P, KP])
-            for q in range(KQ):
-                nc.tensor.matmul_mx(
-                    out=mv_bank[i, j][:],
-                    lhsT=sh_codes[:, i, q, :].bitcast(FP8X4),
-                    lhsT_scale=sh_scales[:, i, q, :],
-                    rhs=inv_codes[:, j, q, :].bitcast(FP8X4),
-                    rhs_scale=inv_scales[:, j, q, :],
-                    start=(q == 0),
-                    stop=(q == KQ - 1),
-                )
-
-        def move_passes(units, banks):
+        def move(units, banks):
             for (i, j), number in zip(units, banks):
                 mv_bank[i, j] = bank_of(number, [P, KP])
-            for q in (1, 0):
+                for q in range(KQ):
+                    move_pass(i, j, q, q == 0, q == KQ - 1)
+
+        def move_by_pass(units, banks, order=(0, 1)):
+            for (i, j), number in zip(units, banks):
+                mv_bank[i, j] = bank_of(number, [P, KP])
+            for q in order:
                 for i, j in units:
-                    nc.tensor.matmul_mx(
-                        out=mv_bank[i, j][:],
-                        lhsT=sh_codes[:, i, q, :].bitcast(FP8X4),
-                        lhsT_scale=sh_scales[:, i, q, :],
-                        rhs=inv_codes[:, j, q, :].bitcast(FP8X4),
-                        rhs_scale=inv_scales[:, j, q, :],
-                        start=(q == 1),
-                        stop=(q == 0),
-                    )
+                    move_pass(i, j, q, q == order[0], q == order[1])
 
         def relatives(i, j):
             if j == 0:
-                rel[i] = work.tile([P, NJ, KP], F32, name="rel", bufs=10)
+                rel[i] = work.tile([P, NJ, KP], F32, name="rel", bufs=DEPTH["rel"])
             nc.scalar.activation(
                 out=rel[i][:, j, :].rearrange("p (v m) -> p v m", v=T),
                 in_=mv_bank[i, j][:].rearrange("p (m v) -> p v m", v=T),
                 func=EXP,
             )
 
+        def exps(units):
+            for i, j in units:
+                relatives(i, j)
+
         def turn(i, j, number):
             tr_bank[i, j] = bank_of(number, [P, T, P])
             for v in range(T):
                 nc.tensor.transpose(tr_bank[i, j][:, v, :], rel[i][:, j, P * v : P * (v + 1)], ident[:])
 
+        def turns(i, banks):
+            for j in range(NJ):
+                turn(i, j, banks[j])
+
         def price(i, j):
             if j == 0:
-                priced[i] = work.tile([P, NJ, P, T], BF16, name="priced", bufs=4, align_bytes=64)
+                priced[i] = work.tile([P, NJ, P, T], BF16, name="priced", bufs=DEPTH["priced"], align_bytes=64)
             nc.vector.tensor_tensor(
                 out=priced[i][:, j],
                 in0=tr_bank[i, j][:].rearrange("p v m -> p m v"),
-                in1=base_kp[:, j, :].unsqueeze(1).to_broadcast([P, P, T]),
+                in1=base_kp[:, T * j : T * (j + 1)].unsqueeze(1).to_broadcast([P, P, T]),
                 op=MULT,
             )
 
-        def quantize_priced(i, j0, j1):
+        def prices(i):
+            for j in range(NJ):
+                price(i, j)
+
+        base_row = {}
+
+        def spread_base(number):
+            base_row[0] = bank_of(number, [P, 2 * NJ, P])
+            words = base_kp[:].bitcast(F32)
+            for a in range(2 * NJ):
+                nc.tensor.transpose(base_row[0][:, a, :], words[:, a : a + 1].to_broadcast([P, P]), ident[:])
+
+        def price_first(i):
+            tagged[i] = work.tile([P, N], BF16, name="tagged", bufs=DEPTH["tagged"])
+            nc.vector.tensor_tensor(
+                out=tagged[i][:].rearrange("p (a m e) -> p a m e", m=P, e=2),
+                in0=base_row[0][:].rearrange("p a m -> p (a m)").bitcast(BF16).rearrange("p (a m e) -> p a m e", m=P, e=2),
+                in1=rel[i][:].rearrange("p j (u e m) -> p (j u) m e", u=2, e=2),
+                op=MULT,
+            )
+
+        def turn_tagged(i, number):
+            tr_bank[i] = bank_of(number, [P, NJ, 2, P])
+            words = tagged[i][:].bitcast(F32)
+            for a in range(2 * NJ):
+                nc.tensor.transpose(tr_bank[i][:, a // 2, a % 2, :], words[:, P * a : P * (a + 1)], ident[:])
+
+        def empty_tagged(i, engine="scalar"):
+            priced[i] = work.tile([P, NJ, P, T], BF16, name="priced", bufs=DEPTH["priced"], align_bytes=64)
+            empty_words(priced[i][:].rearrange("p j m v -> p (j m v)"), tr_bank[i][:], engine)
+
+        def quantize_priced(i, j0=0, j1=NJ):
             quantize(
                 pr_codes[:, i, j0:j1].rearrange("p j m -> p (j m)"),
                 pr_scales[:, i, j0:j1].rearrange("p j m -> p (j m)"),
@@ -253,36 +276,36 @@ def tile_ghosh_price_push_s8_kernel(
 
         def plane(i, j0, j1):
             if i // T not in scaled:
-                scaled[i // T] = work.tile([P, T, N], BF16, name="scaled", bufs=3)
-            return scaled[i // T][:, i % T, KP * j0 : KP * j1]
+                scaled[i // T] = work.tile([P, NJ, T, KP], BF16, name="scaled", bufs=DEPTH["scaled"])
+            return scaled[i // T][:, j0:j1, i % T, :]
 
-        def scale_on_scalar(i, j):
-            nc.scalar.activation(
-                out=plane(i, j, j + 1),
-                in_=rel[i][:, j, :],
-                func=COPY,
-                scale=weight_f32[:, i // T, i % T : i % T + 1],
+        def weigh_on_scalar(i, j):
+            nc.scalar.activation(out=plane(i, j, j + 1), in_=rel[i][:, j : j + 1, :], func=COPY, scale=weight_f32[:, i : i + 1])
+
+        def weigh_on_vector(i, j):
+            nc.vector.tensor_scalar(
+                out=plane(i, j, j + 1), in0=rel[i][:, j : j + 1, :], scalar1=weight_kp[:, i : i + 1], scalar2=None, op0=MULT
             )
 
-        def scale_on_gpsimd(*units):
+        def weigh_on_gpsimd(*units):
             i0 = min(unit[0] for unit in units)
             count = max(unit[0] for unit in units) - i0 + 1
             columns = work.tile([P, count], F32, name="columns", bufs=4)
-            nc.vector.tensor_copy(out=columns[:], in_=weight_kp[:].rearrange("p g t -> p (g t)")[:, i0 : i0 + count])
+            nc.vector.tensor_copy(out=columns[:], in_=weight_kp[:, i0 : i0 + count])
             for i, j0, j1 in units:
                 nc.gpsimd.tensor_scalar(
                     out=plane(i, j0, j1),
-                    in0=rel[i][:, j0:j1, :].rearrange("p j c -> p (j c)"),
+                    in0=rel[i][:, j0:j1, :],
                     scalar1=columns[:, i - i0 : i - i0 + 1],
                     scalar2=0.0,
                     op0=MULT,
                     op1=ADD,
                 )
 
-        def group_weighted(g, j, engine, c0=0, c1=KP):
+        def group_weighted(g, j, engine, c0=0, c1=KP, tag="grouped"):
             if (g, j) not in weighted:
-                weighted[g, j] = work.tile([P, KP, T], BF16, name="grouped%d" % {(0, 0): 0, (0, 1): 1, (1, 0): 2, (2, 0): 0, (1, 1): 2, (2, 1): 1}[g, j], bufs=1, align_bytes=64)
-            interleave(engine, weighted[g, j][:, c0:c1, :], scaled[g][:, :, KP * j + c0 : KP * j + c1])
+                weighted[g, j] = work.tile([P, KP, T], BF16, name=tag, bufs=DEPTH[tag], align_bytes=64)
+            interleave(engine, weighted[g, j][:, c0:c1, :], scaled[g][:, j, :, c0:c1])
 
         def quantize_weighted(g, j):
             quantize(we_codes[:, g, j, :], we_scales[:, g, j, :], weighted[g, j][:].rearrange("p n t -> p (n t)"))
@@ -290,12 +313,11 @@ def tile_ghosh_price_push_s8_kernel(
         index_bank, contrast_bank = {}, {}
 
         def result_tile():
-            return work.tile([P, KP], F32, name="result", bufs=6)
+            return work.tile([P, KP], F32, name="result", bufs=DEPTH["result"])
 
-        def index_mm(i, number, j0=0, j1=NJ):
-            if j0 == 0:
-                index_bank[i] = bank_of(number, [P, C])
-            for j in range(j0, j1):
+        def index_mm(i, number):
+            index_bank[i] = bank_of(number, [P, C])
+            for j in range(NJ):
                 nc.tensor.matmul_mx(
                     out=index_bank[i][:],
                     lhsT=pr_codes[:, i, j, :].bitcast(FP8X4),
@@ -311,27 +333,7 @@ def tile_ghosh_price_push_s8_kernel(
             copy_on(engine, result[:], index_bank[i][:])
             nc.sync.dma_start(out=index_v[i // T][:, i % T, :], in_=result[:])
 
-        def index_half(i, h, number):
-            index_bank[i, h] = bank_of(number, [P, 2, P])
-            for c in range(2):
-                c0 = HALF * h + P * c
-                for j in range(NJ):
-                    nc.tensor.matmul_mx(
-                        out=index_bank[i, h][:, c, :],
-                        lhsT=pr_codes[:, i, j, :].bitcast(FP8X4),
-                        lhsT_scale=pr_scales[:, i, j, :],
-                        rhs=b_words[:, j, 2 * c0 : 2 * (c0 + P)].bitcast(FP4X4),
-                        rhs_scale=b_scales[:, j, c0 : c0 + P],
-                        start=(j == 0),
-                        stop=(j == NJ - 1),
-                    )
-
-        def index_half_out(i, h, engine):
-            result = result_tile()
-            copy_on(engine, result[:, 0:HALF], index_bank[i, h][:].rearrange("p c n -> p (c n)"))
-            nc.sync.dma_start(out=index_v[i // T][:, i % T, HALF * h : HALF * (h + 1)], in_=result[:, 0:HALF])
-
-        def contrast_mm(a, j, g0, g1, number=None):
+        def contrast_mm(a, j, number, g0=0, g1=SG):
             if g0 == 0:
                 contrast_bank[a, j] = bank_of(number, [P, KP])
             for g in range(g0, g1):
@@ -354,268 +356,247 @@ def tile_ghosh_price_push_s8_kernel(
             )
             nc.sync.dma_start(out=out_1[P * a : P * (a + 1), KP * j : KP * (j + 1)], in_=result[:])
 
+        def warm(count, number, source):
+            bank = bank_of(number, [P, KP])
+            for k in range(count):
+                nc.tensor.matmul(bank[:], source[:, 0, 0:P], source[:, 0, :], start=True, stop=True)
+
         nc.vector.memset(b_scales[:].rearrange("p j n -> p (j n)").bitcast(I32), 0)
         make_identity(nc, ident[:])
-        load_shocks(0)
-        load_inverse(0, 0)
+        load_shocks(0, 1)
         nc.sync.dma_start(out=scale_kp[:], in_=shocks_scale.rearrange("o (q p t) -> p (o q) t", p=P, t=T))
-        load_shocks(1)
+        load_shocks(1, 3)
+        load_inverse(0, 0)
+        load_shocks(3, 4)
         load_inverse(0, 1)
-        load_shocks(2)
-        load_shocks(3)
+        load_shocks(4, 6)
         load_inverse(1, 0)
+        load_shocks(6, 8)
         load_inverse(1, 1)
-        nc.sync.dma_start(out=weight_kp[:], in_=weight.rearrange("(g p t) -> p g t", p=P, t=T))
+        nc.sync.dma_start(out=weight_kp[:].rearrange("p (g t) -> p g t", t=T), in_=weight.rearrange("(g p t) -> p g t", p=P, t=T))
+        nc.sync.dma_start(out=base_kp[:].rearrange("p (j t) -> p j t", t=T), in_=base.rearrange("(j p t) -> p j t", p=P, t=T))
         load_contrasts(0)
         load_contrasts(1)
-        load_shocks(4)
-        load_shocks(5)
+        load_shocks(8, 12)
         load_contrasts(2)
         load_contrasts(3)
-        nc.sync.dma_start(out=base_kp[:], in_=base.rearrange("(j p t) -> p j t", p=P, t=T))
         load_baskets()
 
-        def move(units, banks):
-            for (i, j), number in zip(units, banks):
-                moves(i, j, number)
-
-        def exps(units):
-            for i, j in units:
-                relatives(i, j)
-
-        def turns(i, banks):
-            for j in range(NJ):
-                turn(i, j, banks[j])
-
-        def prices(i):
-            for j in range(NJ):
-                price(i, j)
-
-        def warm(count, q):
-            if count:
-                bank = bank_of(1, [P, KP])
-                for k in range(count):
-                    nc.tensor.matmul(bank[:], inv_raw[0, q][:, 0, 0:P], inv_raw[0, q][:, 0, :], start=True, stop=True)
-
-        widen(0)
-        turn_shocks(0, 2)
-        warm(WARM0, 0)
-        group_inverse(0, 0, "scalar", HALF, KP)
-        group_inverse(0, 0, "vector", 0, HALF)
+        for i in range(3):
+            widen(i)
+            turn_shocks(i, 2 + i)
         scale_shocks(0)
-        widen(1)
-        turn_shocks(1, 3)
-        widen(2)
-        turn_shocks(2, 4)
-        warm(WARM1, 1)
-        group_inverse(0, 1, "scalar", HALF, KP)
-        group_inverse(0, 1, "vector", 0, HALF)
+        scale_shocks(1)
+        group_inverse(0, 0, "gpsimd", 0, HALF, tag="ga")
+        group_inverse(0, 0, "scalar", HALF, KP)
+        warm(2, 1, inv_raw[0, 0])
         widen(3)
         turn_shocks(3, 5)
+        warm(3, 1, inv_raw[0, 1])
+        group_inverse(0, 1, "scalar", HALF, KP, tag="gb")
+        group_inverse(0, 1, "vector", 0, HALF)
         widen(4)
-        widen(5)
-        quantize_inverse(0, 0)
-        quantize_shocks(0)
-        quantize_inverse(0, 1)
-        group_inverse_half(0, "gpsimd", 0, 192)
-        group_inverse_half(0, "scalar", 192, HALF)
-        moves(0, 0, 0)
         turn_shocks(4, 6)
-        turn_shocks(5, 7)
-        scale_shocks(1)
-        scale_shocks(2, 0, 1)
+        widen(5)
+        quantize_shocks(0)
         quantize_shocks(1)
-        moves(1, 0, 1)
-        turn_contrasts(0, 2)
-        turn_contrasts(1, 3)
-        group_inverse(1, 1, "scalar", 0, HALF)
-        relatives(0, 0)
-        group_inverse(1, 1, "scalar", HALF, KP)
+        quantize_inverse(0, 0)
+        quantize_inverse(0, 1)
+        units = [(0, 0), (1, 0)]
+        move_by_pass(units, [0, 1])
+        turn_shocks(5, 7)
+        group_inverse(1, 0, "gpsimd", 0, 384, tag="ga")
+        group_inverse(1, 0, "scalar", 384, KP)
+        scale_shocks(2)
+        scale_shocks(3, tag="gb")
         widen(6)
-        relatives(1, 0)
-        scale_shocks(2, 1, 2)
-        scale_shocks(3, 0, 1)
-        quantize_shocks(2)
-        group_inverse_half(1, "gpsimd", 0, HALF)
-        moves(2, 0, 0)
-        turn_contrasts(2, 4)
-        scale_shocks(3, 1, 2)
-        turn_shocks(6, 5)
-        scale_shocks(4)
-        scale_shocks(5, 0, 1)
+        turn_shocks(6, 2)
         widen(7)
-        turn_shocks(7, 6)
+        turn_shocks(7, 3)
+        exps(units)
         quantize_shocks(3)
-        moves(3, 0, 1)
-        empty_contrasts(0)
-        relatives(2, 0)
-        empty_contrasts(1)
-        empty_contrasts(2)
-        relatives(3, 0)
-        quantize_inverse(1, 1)
-        quantize_inverse_half(0)
-        quantize_inverse_half(1)
-        scale_on_gpsimd((0, 0, 1), (1, 0, 1), (2, 0, 1))
+        group_inverse(1, 1, "gpsimd", 0, 160, tag="gb")
+        quantize_shocks(2)
+        units = [(3, 0), (2, 0)]
+        move(units, [0, 1])
+        turn_contrasts(0, 4)
+        turn_contrasts(1, 5)
+        group_inverse(1, 1, "scalar", 160, KP)
+        scale_shocks(4)
+        quantize_inverse(1, 0)
         quantize_shocks(4)
-        scale_shocks(5, 1, 2)
-        scale_shocks(6)
-        scale_shocks(7, 0, 1)
+        exps(units)
+        weigh_on_gpsimd((0, 0, 1), (1, 0, 1), (3, 0, 1))
+        quantize_inverse(1, 1)
+        empty_contrasts(0)
+        empty_contrasts(1)
         widen(8)
         widen(9)
-        units = [(0, 1), (1, 1), (2, 1), (3, 1)]
-        move_passes(units, [0, 2, 3, 4])
-        exps(units)
-        turn_shocks(8, 1)
-        turn_shocks(9, 7)
-        turn_contrasts(3, 5)
+        scale_shocks(5)
+        scale_shocks(6)
+        units = [(0, 1), (1, 1), (2, 1)]
+        move_by_pass(units, [6, 0, 1])
+        exps(units[:1])
+        move([(4, 0), (3, 1), (4, 1)], [4, 5, 6])
+        exps(units[1:])
+        exps([(4, 0), (3, 1), (4, 1)])
+        quantize_shocks(5)
+        weigh_on_gpsimd((2, 0, 1), (0, 1, 2), (1, 1, 2))
+        quantize_shocks(6)
+        turn_shocks(8, 7)
+        turn_shocks(9, 2)
+        scale_shocks(7)
+        scale_shocks(8)
         widen(10)
         widen(11)
-        quantize_shocks(5)
-        quantize_contrasts(0)
-        quantize_contrasts(1)
-        scale_on_gpsimd((3, 0, 1), (0, 1, 2), (1, 1, 2))
-        quantize_shocks(6)
-        scale_shocks(7, 1, 2)
-        scale_shocks(8)
-        empty_contrasts(3, "vector")
-        scale_shocks(9, 0, 1)
-        units = [(4, 0), (5, 0), (4, 1), (5, 1)]
-        move(units, [0, 2, 3, 4])
+        units = [(5, 0), (6, 0), (5, 1), (6, 1)]
+        move(units, [0, 1, 4, 5])
         exps(units)
-        turn_shocks(10, 5)
-        turn_shocks(11, 6)
-        nc.vector.tensor_copy(out=weight_f32[:], in_=weight_kp[:])
-        group_weighted(0, 0, "scalar", HALF, KP)
         quantize_shocks(7)
-        group_weighted(0, 0, "vector", 0, HALF)
-        quantize_contrasts(2)
-        scale_on_gpsimd((4, 0, 2), (5, 0, 2))
+        group_weighted(0, 0, "vector", tag="ga")
+        weigh_on_gpsimd((2, 1, 2), (3, 1, 2), (4, 0, 2))
         quantize_shocks(8)
-        scale_shocks(9, 1, 2)
+        turn_shocks(10, 3)
+        turn_shocks(11, 7)
+        turn_contrasts(2, 6)
+        scale_shocks(9)
         scale_shocks(10)
         scale_shocks(11)
-        units = [(6, 0), (7, 0), (6, 1), (7, 1)]
-        move(units, [0, 2, 3, 4])
+        empty_contrasts(2)
+        units = [(7, 0), (8, 0), (7, 1), (8, 1)]
+        move(units, [0, 1, 4, 5])
         exps(units)
-        turns(0, (1, 7))
-        turn_contrasts(4, 5)
-        scale_on_scalar(2, 1)
-        scale_on_scalar(3, 1)
         quantize_shocks(9)
         quantize_shocks(10)
-        scale_on_gpsimd((6, 0, 2))
         quantize_shocks(11)
-        prices(0)
-        empty_contrasts(4, "vector")
-        units = [(8, 0), (9, 0), (8, 1), (9, 1)]
-        move(units, [0, 2, 3, 4])
-        exps(units)
-        turns(1, (1, 7))
-        turn_contrasts(5, 6)
-        group_weighted(0, 1, "scalar", HALF, KP)
-        quantize_contrasts(3)
-        quantize_priced(0, 0, 2)
-        scale_on_gpsimd((7, 0, 2))
+        quantize_contrasts(0)
+        weigh_on_gpsimd((5, 0, 1), (6, 0, 1), (7, 0, 1))
         quantize_weighted(0, 0)
+        turns(0, (2, 6))
+        spread_base(3)
+        turn_contrasts(3, 7)
+        prices(0)
+        price_first(4)
+        group_weighted(0, 1, "scalar", 0, HALF, tag="gb")
+        empty_contrasts(3)
+        units = [(9, 0), (10, 0), (9, 1), (11, 0)]
+        move(units, [0, 1, 4, 5])
+        exps(units[:3])
+        group_weighted(1, 0, "scalar", 0, HALF, tag="ga")
+        quantize_priced(0)
+        quantize_contrasts(1)
+        quantize_contrasts(2)
+        turns(1, (2, 6))
+        exps(units[3:])
+        weigh_on_gpsimd((8, 0, 1), (9, 0, 1), (10, 0, 1), (11, 0, 1))
+        quantize_contrasts(3)
+        turn_contrasts(4, 7)
         prices(1)
-        empty_contrasts(5, "vector")
-        units = [(10, 0), (11, 0), (10, 1), (11, 1)]
-        move(units, [0, 2, 3, 4])
-        exps(units)
-        turns(2, (1, 7))
-        turns(3, (5, 6))
-        scale_on_scalar(10, 0)
-        scale_on_scalar(11, 0)
-        group_weighted(0, 1, "scalar", 0, HALF)
-        group_weighted(1, 0, "vector")
-        quantize_priced(1, 0, 2)
-        scale_on_gpsimd((8, 0, 2), (9, 0, 1))
-        quantize_weighted(1, 0)
-        prices(2)
-        prices(3)
-        index_mm(0, 0)
-        index_mm(1, 2)
-        contrast_mm(0, 0, 0, 1, 3)
-        contrast_mm(1, 0, 0, 1, 4)
-        contrast_mm(0, 0, 1, 2)
-        contrast_mm(1, 0, 1, 2)
-        turns(4, (1, 7))
-        turns(5, (5, 6))
+        price_first(5)
+        price_first(6)
+        empty_contrasts(4)
+        units = [(10, 1), (11, 1)]
+        move(units, [0, 1])
+        index_mm(0, 4)
+        relatives(10, 1)
+        group_weighted(1, 0, "scalar", HALF, KP)
+        relatives(11, 1)
+        turn_tagged(4, 5)
+        turn_contrasts(5, 7)
+        turns(2, (2, 6))
+        turn_tagged(5, 0)
+        empty_tagged(4)
         index_out(0)
-        group_weighted(2, 0, "scalar", HALF, KP)
-        index_out(1)
-        quantize_priced(2, 0, 2)
-        group_weighted(2, 0, "vector", 0, HALF)
-        quantize_priced(3, 0, 2)
-        scale_on_gpsimd((9, 1, 2), (10, 1, 2), (11, 1, 2))
+        empty_contrasts(5)
+        empty_tagged(5)
+        quantize_priced(1)
+        quantize_weighted(1, 0)
+        quantize_priced(4)
+        group_weighted(2, 0, "vector", tag="gc")
+        quantize_contrasts(4)
+        quantize_priced(5)
+        quantize_contrasts(5)
+        weigh_on_gpsimd((5, 1, 2), (6, 1, 2), (7, 1, 2))
         quantize_weighted(2, 0)
-        prices(4)
-        prices(5)
-        index_mm(2, 0)
-        index_mm(3, 2)
-        contrast_mm(0, 0, 2, 3)
-        contrast_mm(1, 0, 2, 3)
-        turns(6, (1, 7))
-        turns(7, (5, 6))
-        index_out(2)
-        index_out(3)
+        prices(2)
+        price_first(7)
+        index_mm(1, 1)
+        contrast_mm(0, 0, 5, 0, 2)
+        contrast_mm(1, 0, 4, 0, 2)
+        index_mm(4, 7)
+        turn_tagged(6, 0)
+        index_out(1)
+        index_out(4)
+        empty_tagged(6)
+        index_mm(5, 1)
+        contrast_mm(2, 0, 7, 0, 2)
+        contrast_mm(0, 0, 5, 2, 3)
+        contrast_mm(1, 0, 4, 2, 3)
+        contrast_mm(2, 0, 7, 2, 3)
+        contrast_mm(3, 0, 0)
+        index_out(5)
         contrast_out(0, 0)
         contrast_out(1, 0)
-        group_weighted(1, 1, "scalar")
-        quantize_contrasts(4)
-        quantize_contrasts(5)
-        quantize_priced(4, 0, 2)
-        quantize_priced(5, 0, 2)
-        quantize_weighted(0, 1)
-        group_weighted(2, 1, "gpsimd", 0, 288)
-        group_weighted(2, 1, "scalar", 288, KP)
-        prices(6)
-        prices(7)
-        contrast_mm(2, 0, 0, 3, 3)
-        contrast_mm(3, 0, 0, 3, 4)
-        index_mm(4, 0)
-        index_mm(5, 2)
-        turns(8, (1, 7))
-        turns(9, (5, 6))
+        turns(3, (2, 6))
+        turn_tagged(7, 1)
         contrast_out(2, 0)
+        group_weighted(1, 1, "scalar", 0, HALF, tag="ga")
         contrast_out(3, 0)
-        index_out(4)
-        index_out(5)
-        quantize_priced(6, 0, 2)
-        quantize_priced(7, 0, 2)
-        quantize_weighted(1, 1)
-        quantize_weighted(2, 1)
-        prices(8)
-        prices(9)
-        index_mm(6, 3)
-        index_mm(7, 4)
-        contrast_mm(0, 1, 0, 3, 0)
-        contrast_mm(1, 1, 0, 3, 2)
+        empty_tagged(7)
+        group_weighted(0, 1, "vector", HALF, KP)
+        quantize_priced(6)
+        quantize_priced(2)
+        weigh_on_gpsimd((8, 1, 2), (9, 1, 2), (10, 1, 2))
+        quantize_weighted(0, 1)
+        price_first(8)
+        prices(3)
+        index_mm(6, 5)
+        index_mm(2, 4)
+        contrast_mm(0, 1, 7, 0, 1)
+        contrast_mm(1, 1, 0, 0, 1)
         index_out(6)
-        contrast_mm(2, 1, 0, 3, 3)
-        turns(10, (1, 7))
-        turns(11, (5, 6))
+        index_out(2)
+        turn_tagged(8, 1)
+        turns(9, (3, 5))
+        turns(10, (4, 2))
+        empty_tagged(8)
+        group_weighted(1, 1, "scalar", HALF, KP)
+        weigh_on_vector(11, 1)
+        quantize_priced(7)
+        quantize_priced(3)
+        quantize_priced(8)
+        prices(9)
+        index_mm(7, 6)
+        index_mm(3, 1)
+        index_mm(8, 3)
         index_out(7)
-        contrast_out(0, 1)
-        contrast_out(1, 1)
-        contrast_out(2, 1)
-        quantize_priced(8, 0, 2)
-        quantize_priced(9, 0, 2)
+        group_weighted(2, 1, "scalar", 0, HALF, tag="gb")
+        turns(11, (5, 6))
+        index_out(3)
+        index_out(8)
+        quantize_weighted(1, 1)
+        group_weighted(2, 1, "vector", HALF, KP)
+        quantize_priced(9)
+        quantize_weighted(2, 1)
         prices(10)
         price(11, 0)
-        quantize_priced(10, 0, 2)
+        quantize_priced(10)
         price(11, 1)
         quantize_priced(11, 0, 1)
         quantize_priced(11, 1, 2)
-        index_mm(8, 4)
-        index_mm(9, 0)
-        contrast_mm(3, 1, 0, 3, 2)
-        index_mm(10, 3)
-        for h in range(2):
-            index_half(11, h, (1, 7)[h])
-        index_out(8)
+        contrast_mm(0, 1, 7, 1, 2)
+        contrast_mm(1, 1, 0, 1, 2)
+        index_mm(9, 1)
+        contrast_mm(0, 1, 7, 2, 3)
+        contrast_mm(1, 1, 0, 2, 3)
+        contrast_mm(2, 1, 3)
         index_out(9)
+        contrast_out(0, 1)
+        contrast_out(1, 1)
+        contrast_mm(3, 1, 1)
+        index_mm(10, 4)
+        index_mm(11, 2)
+        contrast_out(2, 1)
         contrast_out(3, 1)
         index_out(10, "vector")
-        for h in range(2):
-            index_half_out(11, h, ("scalar", "vector")[h])
+        index_out(11)

@@ -28,6 +28,7 @@ KQ = N // KP
 NJ = N // KP
 TILES = SG * T
 LINE = 8
+RUN = 4
 WIDE = 4
 DEPTH = {"sh_group": 4, "con_group": 4, "ga": 1, "gb": 1, "gc": 1, "rel": 10, "priced": 5, "tagged": 4, "scaled": 3, "result": 6}
 
@@ -206,10 +207,10 @@ def tile_ghosh_price_push_s8_kernel(
 
         def relatives(i, j):
             if j == 0:
-                rel[i] = work.tile([P, NJ, KP], F32, name="rel", bufs=DEPTH["rel"])
+                rel[i] = work.tile([P, 2, NJ, HALF], F32, name="rel", bufs=DEPTH["rel"])
             nc.scalar.activation(
-                out=rel[i][:, j, :].rearrange("p (v m) -> p v m", v=T),
-                in_=mv_bank[i, j][:].rearrange("p (m v) -> p v m", v=T),
+                out=rel[i][:, :, j, :].rearrange("p e (u m) -> p e u m", u=2),
+                in_=mv_bank[i, j][:].rearrange("p (m u e) -> p e u m", u=2, e=2),
                 func=EXP,
             )
 
@@ -220,7 +221,7 @@ def tile_ghosh_price_push_s8_kernel(
         def turn(i, j, number):
             tr_bank[i, j] = bank_of(number, [P, T, P])
             for v in range(T):
-                nc.tensor.transpose(tr_bank[i, j][:, v, :], rel[i][:, j, P * v : P * (v + 1)], ident[:])
+                nc.tensor.transpose(tr_bank[i, j][:, v, :], rel[i][:, v % 2, j, P * (v // 2) : P * (v // 2 + 1)], ident[:])
 
         def turns(i, banks):
             for j in range(NJ):
@@ -251,9 +252,9 @@ def tile_ghosh_price_push_s8_kernel(
         def price_first(i):
             tagged[i] = work.tile([P, N], BF16, name="tagged", bufs=DEPTH["tagged"])
             nc.vector.tensor_tensor(
-                out=tagged[i][:].rearrange("p (a m e) -> p a m e", m=P, e=2),
-                in0=base_row[0][:].rearrange("p a m -> p (a m)").bitcast(BF16).rearrange("p (a m e) -> p a m e", m=P, e=2),
-                in1=rel[i][:].rearrange("p j (u e m) -> p (j u) m e", u=2, e=2),
+                out=tagged[i][:].rearrange("p (c r e) -> p c e r", r=RUN, e=2),
+                in0=base_row[0][:].rearrange("p a m -> p (a m)").bitcast(BF16).rearrange("p (c r e) -> p c e r", r=RUN, e=2),
+                in1=rel[i][:].rearrange("p e j c -> p e (j c)").rearrange("p e (c r) -> p c e r", r=RUN),
                 op=MULT,
             )
 
@@ -277,14 +278,14 @@ def tile_ghosh_price_push_s8_kernel(
         def plane(i, j0, j1):
             if i // T not in scaled:
                 scaled[i // T] = work.tile([P, NJ, T, KP], BF16, name="scaled", bufs=DEPTH["scaled"])
-            return scaled[i // T][:, j0:j1, i % T, :]
+            return scaled[i // T][:, j0:j1, i % T, :].rearrange("p j (e c) -> p e j c", e=2)
 
         def weigh_on_scalar(i, j):
-            nc.scalar.activation(out=plane(i, j, j + 1), in_=rel[i][:, j : j + 1, :], func=COPY, scale=weight_f32[:, i : i + 1])
+            nc.scalar.activation(out=plane(i, j, j + 1), in_=rel[i][:, :, j : j + 1, :], func=COPY, scale=weight_f32[:, i : i + 1])
 
         def weigh_on_vector(i, j):
             nc.vector.tensor_scalar(
-                out=plane(i, j, j + 1), in0=rel[i][:, j : j + 1, :], scalar1=weight_kp[:, i : i + 1], scalar2=None, op0=MULT
+                out=plane(i, j, j + 1), in0=rel[i][:, :, j : j + 1, :], scalar1=weight_kp[:, i : i + 1], scalar2=None, op0=MULT
             )
 
         def weigh_on_gpsimd(*units):
@@ -295,7 +296,7 @@ def tile_ghosh_price_push_s8_kernel(
             for i, j0, j1 in units:
                 nc.gpsimd.tensor_scalar(
                     out=plane(i, j0, j1),
-                    in0=rel[i][:, j0:j1, :],
+                    in0=rel[i][:, :, j0:j1, :],
                     scalar1=columns[:, i - i0 : i - i0 + 1],
                     scalar2=0.0,
                     op0=MULT,
@@ -351,8 +352,8 @@ def tile_ghosh_price_push_s8_kernel(
             result = result_tile()
             copy_on(
                 engine,
-                result[:].rearrange("p (m v) -> p m v", v=T),
-                contrast_bank[a, j][:].rearrange("p (v m) -> p m v", v=T),
+                result[:].rearrange("p (m u e) -> p m u e", u=2, e=2),
+                contrast_bank[a, j][:].rearrange("p (e u m) -> p m u e", u=2, e=2),
             )
             nc.sync.dma_start(out=out_1[P * a : P * (a + 1), KP * j : KP * (j + 1)], in_=result[:])
 

@@ -357,10 +357,15 @@ def tile_ghosh_price_push_s8_kernel(
             )
             nc.sync.dma_start(out=out_1[P * a : P * (a + 1), KP * j : KP * (j + 1)], in_=result[:])
 
-        def warm(count, number, source):
-            bank = bank_of(number, [P, KP])
+        idle_bank = {}
+
+        def warm(count, columns):
+            if not idle_bank:
+                idle_bank[0] = bank_of(1, [P, KP])
+            bank = idle_bank[0]
+            zeros = b_scales[:].rearrange("p j n -> p (j n)").bitcast(F32)
             for k in range(count):
-                nc.tensor.matmul(bank[:], source[:, 0, 0:P], source[:, 0, :], start=True, stop=True)
+                nc.tensor.matmul(bank[:, 0:columns], zeros[:, 0:P], zeros[:, 0:columns], start=True, stop=True)
 
         nc.vector.memset(b_scales[:].rearrange("p j n -> p (j n)").bitcast(I32), 0)
         make_identity(nc, ident[:])
@@ -381,19 +386,24 @@ def tile_ghosh_price_push_s8_kernel(
         load_shocks(8, 12)
         load_contrasts(2)
         load_contrasts(3)
-        load_baskets()
 
-        for i in range(3):
-            widen(i)
-            turn_shocks(i, 2 + i)
+        warm(2, HALF)
+        widen(0)
+        turn_shocks(0, 2)
+        warm(1, P)
+        widen(1)
+        turn_shocks(1, 3)
+        warm(1, HALF)
+        widen(2)
+        turn_shocks(2, 4)
         scale_shocks(0)
         scale_shocks(1)
         group_inverse(0, 0, "gpsimd", 0, HALF, tag="ga")
         group_inverse(0, 0, "scalar", HALF, KP)
-        warm(2, 1, inv_raw[0, 0])
+        warm(1, P)
         widen(3)
         turn_shocks(3, 5)
-        warm(3, 1, inv_raw[0, 1])
+        warm(1, HALF)
         group_inverse(0, 1, "scalar", HALF, KP, tag="gb")
         group_inverse(0, 1, "vector", 0, HALF)
         widen(4)
@@ -403,6 +413,7 @@ def tile_ghosh_price_push_s8_kernel(
         quantize_shocks(1)
         quantize_inverse(0, 0)
         quantize_inverse(0, 1)
+        load_baskets()
         units = [(0, 0), (1, 0)]
         move_by_pass(units, [0, 1])
         turn_shocks(5, 7)

@@ -313,6 +313,12 @@ def tile_ghosh_price_push_s8_kernel(
 
         index_bank, contrast_bank = {}, {}
 
+        def sums_out(engine, out, in_):
+            if engine == "scalar":
+                nc.scalar.activation(out=out, in_=in_, func=COPY)
+            else:
+                nc.vector.tensor_copy(out=out, in_=in_)
+
         def result_tile():
             return work.tile([P, KP], F32, name="result", bufs=DEPTH["result"])
 
@@ -331,7 +337,7 @@ def tile_ghosh_price_push_s8_kernel(
 
         def index_out(i, engine="scalar"):
             result = result_tile()
-            copy_on(engine, result[:], index_bank[i][:])
+            sums_out(engine, result[:], index_bank[i][:])
             nc.sync.dma_start(out=index_v[i // T][:, i % T, :], in_=result[:])
 
         def contrast_mm(a, j, number, g0=0, g1=SG):
@@ -350,7 +356,7 @@ def tile_ghosh_price_push_s8_kernel(
 
         def contrast_out(a, j, engine="scalar"):
             result = result_tile()
-            copy_on(
+            sums_out(
                 engine,
                 result[:].rearrange("p (m u e) -> p m u e", u=2, e=2),
                 contrast_bank[a, j][:].rearrange("p (e u m) -> p m u e", u=2, e=2),

@@ -30,7 +30,9 @@ TILES = SG * T
 LINE = 8
 RUN = 4
 WIDE = 4
-DEPTH = {"sh_group": 4, "con_group": 4, "ga": 1, "gb": 1, "gc": 1, "rel": 10, "priced": 5, "tagged": 4, "scaled": 3, "result": 6}
+DEPTH = {"sh_group": 3, "con_group": 4, "ga": 1, "gb": 1, "gc": 1, "gx": 1, "rel": 10, "priced": 4, "tagged": 3, "scaled": 3, "result": 6}
+PAIRS = (1,)
+HANDED = {8: "gx"}
 
 
 def tile_ghosh_price_push_s8_kernel(
@@ -121,21 +123,20 @@ def tile_ghosh_price_push_s8_kernel(
             copy_on(engine, sh_wide[i][:], sh_bytes[i].bitcast(FP8))
 
         def turn_shocks(i, number):
-            sh_bank[i] = bank_of(number, [P, KQ, 2, P])
+            sh_bank[i] = bank_of(number, [P, 2, KQ, P])
             words = sh_wide[i][:].bitcast(F32)
             for q in range(KQ):
                 for u in range(2):
-                    nc.tensor.transpose(sh_bank[i][:, q, u, :], words[:, HALF * q + u : HALF * (q + 1) : 2], ident[:])
+                    nc.tensor.transpose(sh_bank[i][:, u, q, :], words[:, HALF * q + u : HALF * (q + 1) : 2], ident[:])
 
         def scale_shocks(i, q0=0, q1=KQ, tag="sh_group"):
             if q0 == 0:
                 sh_group[i] = work.tile([P, N], BF16, name=tag, bufs=DEPTH[tag], align_bytes=64)
             grouped = sh_group[i][:].rearrange("p (q r u e) -> p q r u e", q=KQ, u=2, e=2)
-            halves = sh_bank[i][:].rearrange("p q u r -> p (q u r)").bitcast(BF16)
-            halves = halves.rearrange("p (q u r e) -> p q r u e", q=KQ, u=2, e=2)
-            for q in range(q0, q1):
-                scales = scale_kp[:, q, :].rearrange("p (u e) -> p u e", u=2).unsqueeze(1).to_broadcast([P, P, 2, 2])
-                nc.vector.tensor_tensor(out=grouped[:, q], in0=halves[:, q], in1=scales, op=MULT)
+            halves = sh_bank[i][:].rearrange("p u q r -> p (u q r)").bitcast(BF16)
+            halves = halves.rearrange("p (u q r e) -> p q r u e", q=KQ, u=2, e=2)
+            scales = scale_kp[:, q0:q1, :].rearrange("p q (u e) -> p q u e", u=2).unsqueeze(2).to_broadcast([P, q1 - q0, P, 2, 2])
+            nc.vector.tensor_tensor(out=grouped[:, q0:q1], in0=halves[:, q0:q1], in1=scales, op=MULT)
 
         def quantize_shocks(i):
             quantize(
@@ -179,6 +180,7 @@ def tile_ghosh_price_push_s8_kernel(
             cols = slice(part[0], part[1])
             quantize(inv_codes[:, j, q, cols], inv_scales[:, j, q, cols], inv_part[j, q, part][:].rearrange("p n t -> p (n t)"))
 
+        priced_pair = {}
         mv_bank, rel, tr_bank, priced, tagged, scaled, weighted = {}, {}, {}, {}, {}, {}, {}
 
         def move_pass(i, j, q, first, last):
@@ -227,9 +229,26 @@ def tile_ghosh_price_push_s8_kernel(
             for j in range(NJ):
                 turn(i, j, banks[j])
 
+        def priced_tile(i):
+            if i // 2 not in PAIRS:
+                tag = HANDED.get(i, "priced")
+                single = work.tile([P, NJ, P, T], BF16, name=tag, bufs=DEPTH[tag], align_bytes=64)
+                priced[i] = single[:]
+                return
+            if i // 2 not in priced_pair:
+                priced_pair[i // 2] = work.tile([P, 2, NJ, P, T], BF16, name="pair", bufs=1, align_bytes=64)
+            priced[i] = priced_pair[i // 2][:, i % 2]
+
+        def quantize_pair(i):
+            quantize(
+                pr_codes[:, i : i + 2].rearrange("p i j m -> p (i j m)"),
+                pr_scales[:, i : i + 2].rearrange("p i j m -> p (i j m)"),
+                priced_pair[i // 2][:].rearrange("p i j m v -> p (i j m v)"),
+            )
+
         def price(i, j):
             if j == 0:
-                priced[i] = work.tile([P, NJ, P, T], BF16, name="priced", bufs=DEPTH["priced"], align_bytes=64)
+                priced_tile(i)
             nc.vector.tensor_tensor(
                 out=priced[i][:, j],
                 in0=tr_bank[i, j][:].rearrange("p v m -> p m v"),
@@ -265,8 +284,8 @@ def tile_ghosh_price_push_s8_kernel(
                 nc.tensor.transpose(tr_bank[i][:, a // 2, a % 2, :], words[:, P * a : P * (a + 1)], ident[:])
 
         def empty_tagged(i, engine="scalar"):
-            priced[i] = work.tile([P, NJ, P, T], BF16, name="priced", bufs=DEPTH["priced"], align_bytes=64)
-            empty_words(priced[i][:].rearrange("p j m v -> p (j m v)"), tr_bank[i][:], engine)
+            priced_tile(i)
+            empty_words(priced[i].rearrange("p j m v -> p (j m v)"), tr_bank[i][:], engine)
 
         def quantize_priced(i, j0=0, j1=NJ):
             quantize(
@@ -303,13 +322,14 @@ def tile_ghosh_price_push_s8_kernel(
                     op1=ADD,
                 )
 
-        def group_weighted(g, j, engine, c0=0, c1=KP, tag="grouped"):
-            if (g, j) not in weighted:
-                weighted[g, j] = work.tile([P, KP, T], BF16, name=tag, bufs=DEPTH[tag], align_bytes=64)
-            interleave(engine, weighted[g, j][:, c0:c1, :], scaled[g][:, j, :, c0:c1])
+        def group_weighted(g, j, engine, c0=0, c1=KP, part=(0, KP), tag="grouped"):
+            if (g, j, part) not in weighted:
+                weighted[g, j, part] = work.tile([P, part[1] - part[0], T], BF16, name=tag, bufs=DEPTH[tag], align_bytes=64)
+            interleave(engine, weighted[g, j, part][:, c0 - part[0] : c1 - part[0], :], scaled[g][:, j, :, c0:c1])
 
-        def quantize_weighted(g, j):
-            quantize(we_codes[:, g, j, :], we_scales[:, g, j, :], weighted[g, j][:].rearrange("p n t -> p (n t)"))
+        def quantize_weighted(g, j, part=(0, KP)):
+            cols = slice(part[0], part[1])
+            quantize(we_codes[:, g, j, cols], we_scales[:, g, j, cols], weighted[g, j, part][:].rearrange("p n t -> p (n t)"))
 
         index_bank, contrast_bank = {}, {}
 
@@ -363,6 +383,25 @@ def tile_ghosh_price_push_s8_kernel(
             )
             nc.sync.dma_start(out=out_1[P * a : P * (a + 1), KP * j : KP * (j + 1)], in_=result[:])
 
+        def index_half(i, h, number):
+            index_bank[i, h] = bank_of(number, [P, HALF])
+            cols = slice(HALF * h, HALF * (h + 1))
+            for j in range(NJ):
+                nc.tensor.matmul_mx(
+                    out=index_bank[i, h][:],
+                    lhsT=pr_codes[:, i, j, :].bitcast(FP8X4),
+                    lhsT_scale=pr_scales[:, i, j, :],
+                    rhs=b_words[:, j, KP * h : KP * (h + 1)].bitcast(FP4X4),
+                    rhs_scale=b_scales[:, j, cols],
+                    start=(j == 0),
+                    stop=(j == NJ - 1),
+                )
+
+        def index_half_out(i, h, engine):
+            result = result_tile()
+            sums_out(engine, result[:, 0:HALF], index_bank[i, h][:])
+            nc.sync.dma_start(out=index_v[i // T][:, i % T, HALF * h : HALF * (h + 1)], in_=result[:, 0:HALF])
+
         idle_bank = {}
 
         def warm(count, columns):
@@ -385,13 +424,13 @@ def tile_ghosh_price_push_s8_kernel(
         load_inverse(1, 0)
         load_shocks(6, 8)
         load_inverse(1, 1)
-        nc.sync.dma_start(out=weight_kp[:].rearrange("p (g t) -> p g t", t=T), in_=weight.rearrange("(g p t) -> p g t", p=P, t=T))
-        nc.sync.dma_start(out=base_kp[:].rearrange("p (j t) -> p j t", t=T), in_=base.rearrange("(j p t) -> p j t", p=P, t=T))
         load_contrasts(0)
         load_contrasts(1)
+        nc.sync.dma_start(out=weight_kp[:].rearrange("p (g t) -> p g t", t=T), in_=weight.rearrange("(g p t) -> p g t", p=P, t=T))
         load_shocks(8, 12)
         load_contrasts(2)
         load_contrasts(3)
+        nc.sync.dma_start(out=base_kp[:].rearrange("p (j t) -> p j t", t=T), in_=base.rearrange("(j p t) -> p j t", p=P, t=T))
 
         warm(2, HALF)
         widen(0)
@@ -425,27 +464,28 @@ def tile_ghosh_price_push_s8_kernel(
         turn_shocks(5, 7)
         group_inverse(1, 0, "gpsimd", 0, 384, tag="ga")
         group_inverse(1, 0, "scalar", 384, KP)
-        scale_shocks(2)
-        scale_shocks(3, tag="gb")
+        scale_shocks(2, tag="gx")
+        scale_shocks(3)
         widen(6)
         turn_shocks(6, 2)
         widen(7)
         turn_shocks(7, 3)
         exps(units)
-        quantize_shocks(3)
-        group_inverse(1, 1, "gpsimd", 0, 160, tag="gb")
         quantize_shocks(2)
-        units = [(3, 0), (2, 0)]
+        group_inverse(1, 1, "gpsimd", 0, P, part=(0, P), tag="gx")
+        quantize_shocks(3)
+        units = [(2, 0), (3, 0)]
         move(units, [0, 1])
         turn_contrasts(0, 4)
         turn_contrasts(1, 5)
-        group_inverse(1, 1, "scalar", 160, KP)
+        group_inverse(1, 1, "scalar", P, KP, part=(P, KP), tag="gb")
         scale_shocks(4)
         quantize_inverse(1, 0)
+        quantize_inverse(1, 1, (0, P))
         quantize_shocks(4)
         exps(units)
-        weigh_on_gpsimd((0, 0, 1), (1, 0, 1), (3, 0, 1))
-        quantize_inverse(1, 1)
+        weigh_on_gpsimd((0, 0, 1), (1, 0, 1), (2, 0, 1))
+        quantize_inverse(1, 1, (P, KP))
         empty_contrasts(0)
         empty_contrasts(1)
         widen(8)
@@ -455,13 +495,13 @@ def tile_ghosh_price_push_s8_kernel(
         units = [(0, 1), (1, 1), (2, 1)]
         move_by_pass(units, [6, 0, 1])
         exps(units[:1])
-        move([(4, 0), (3, 1), (4, 1)], [4, 5, 6])
+        move([(4, 0), (3, 1), (4, 1)], [4, 5, 7])
         exps(units[1:])
         exps([(4, 0), (3, 1), (4, 1)])
+        weigh_on_gpsimd((3, 0, 1), (0, 1, 2), (1, 1, 2))
         quantize_shocks(5)
-        weigh_on_gpsimd((2, 0, 1), (0, 1, 2), (1, 1, 2))
         quantize_shocks(6)
-        turn_shocks(8, 7)
+        turn_shocks(8, 6)
         turn_shocks(9, 2)
         scale_shocks(7)
         scale_shocks(8)
@@ -494,7 +534,7 @@ def tile_ghosh_price_push_s8_kernel(
         spread_base(3)
         turn_contrasts(3, 7)
         prices(0)
-        price_first(4)
+        price_first(5)
         group_weighted(0, 1, "scalar", 0, HALF, tag="gb")
         empty_contrasts(3)
         units = [(9, 0), (10, 0), (9, 1), (11, 0)]
@@ -503,117 +543,116 @@ def tile_ghosh_price_push_s8_kernel(
         group_weighted(1, 0, "scalar", 0, HALF, tag="ga")
         quantize_priced(0)
         quantize_contrasts(1)
-        quantize_contrasts(2)
         turns(1, (2, 6))
         exps(units[3:])
         weigh_on_gpsimd((8, 0, 1), (9, 0, 1), (10, 0, 1), (11, 0, 1))
+        quantize_contrasts(2)
         quantize_contrasts(3)
         turn_contrasts(4, 7)
         prices(1)
-        price_first(5)
         price_first(6)
+        price_first(7)
         empty_contrasts(4)
         units = [(10, 1), (11, 1)]
         move(units, [0, 1])
-        index_mm(0, 4)
         relatives(10, 1)
         group_weighted(1, 0, "scalar", HALF, KP)
         relatives(11, 1)
-        turn_tagged(4, 5)
+        turn_tagged(5, 5)
         turn_contrasts(5, 7)
+        index_mm(0, 4)
         turns(2, (2, 6))
-        turn_tagged(5, 0)
-        empty_tagged(4)
+        turn_tagged(6, 0)
+        empty_tagged(5)
         index_out(0)
         empty_contrasts(5)
-        empty_tagged(5)
+        empty_tagged(6)
         quantize_priced(1)
         quantize_weighted(1, 0)
-        quantize_priced(4)
+        quantize_priced(5)
         group_weighted(2, 0, "vector", tag="gc")
         quantize_contrasts(4)
-        quantize_priced(5)
+        quantize_priced(6)
         quantize_contrasts(5)
         weigh_on_gpsimd((5, 1, 2), (6, 1, 2), (7, 1, 2))
         quantize_weighted(2, 0)
-        prices(2)
-        price_first(7)
         index_mm(1, 1)
         contrast_mm(0, 0, 5, 0, 2)
         contrast_mm(1, 0, 4, 0, 2)
-        index_mm(4, 7)
-        turn_tagged(6, 0)
+        index_mm(5, 7)
         index_out(1)
-        index_out(4)
-        empty_tagged(6)
-        index_mm(5, 1)
-        contrast_mm(2, 0, 7, 0, 2)
+        turn_tagged(7, 0)
+        turns(3, (3, 1))
+        index_out(5)
+        empty_tagged(7)
+        prices(2)
+        prices(3)
+        group_weighted(0, 1, "scalar", HALF, KP)
+        index_mm(6, 7)
+        contrast_mm(2, 0, 0, 0, 2)
         contrast_mm(0, 0, 5, 2, 3)
         contrast_mm(1, 0, 4, 2, 3)
-        contrast_mm(2, 0, 7, 2, 3)
-        contrast_mm(3, 0, 0)
-        index_out(5)
+        contrast_mm(2, 0, 0, 2, 3)
+        contrast_mm(3, 0, 2)
+        index_out(6)
         contrast_out(0, 0)
         contrast_out(1, 0)
-        turns(3, (2, 6))
-        turn_tagged(7, 1)
+        turns(4, (6, 3))
+        turns(8, (1, 5))
         contrast_out(2, 0)
         group_weighted(1, 1, "scalar", 0, HALF, tag="ga")
         contrast_out(3, 0)
-        empty_tagged(7)
-        group_weighted(0, 1, "vector", HALF, KP)
-        quantize_priced(6)
-        quantize_priced(2)
+        quantize_priced(7)
+        quantize_pair(2)
         weigh_on_gpsimd((8, 1, 2), (9, 1, 2), (10, 1, 2))
         quantize_weighted(0, 1)
-        price_first(8)
-        prices(3)
-        index_mm(6, 5)
+        prices(4)
+        prices(8)
+        index_mm(7, 7)
         index_mm(2, 4)
-        contrast_mm(0, 1, 7, 0, 1)
-        contrast_mm(1, 1, 0, 0, 1)
-        index_out(6)
-        index_out(2)
-        turn_tagged(8, 1)
-        turns(9, (3, 5))
-        turns(10, (4, 2))
-        empty_tagged(8)
+        contrast_mm(0, 1, 0, 0, 1)
+        contrast_mm(1, 1, 2, 0, 1)
+        index_mm(3, 6)
         group_weighted(1, 1, "scalar", HALF, KP)
-        weigh_on_vector(11, 1)
-        quantize_priced(7)
-        quantize_priced(3)
-        quantize_priced(8)
-        prices(9)
-        index_mm(7, 6)
-        index_mm(3, 1)
-        index_mm(8, 3)
         index_out(7)
-        group_weighted(2, 1, "scalar", 0, HALF, tag="gb")
-        turns(11, (5, 6))
+        index_out(2)
         index_out(3)
-        index_out(8)
+        turns(9, (3, 1))
+        turns(10, (5, 7))
+        weigh_on_vector(11, 1)
+        quantize_priced(4)
+        quantize_priced(8)
+        group_weighted(2, 1, "gpsimd", 0, HALF, part=(0, HALF), tag="gx")
         quantize_weighted(1, 1)
-        group_weighted(2, 1, "vector", HALF, KP)
+        group_weighted(2, 1, "scalar", HALF, KP, part=(HALF, KP), tag="gb")
+        prices(9)
+        index_mm(4, 4)
+        index_mm(8, 6)
+        contrast_mm(0, 1, 0, 1, 2)
+        contrast_mm(1, 1, 2, 1, 2)
+        turns(11, (3, 1))
+        index_out(4)
+        index_out(8)
+        price(10, 0)
         quantize_priced(9)
-        quantize_weighted(2, 1)
-        prices(10)
+        quantize_weighted(2, 1, (HALF, KP))
+        quantize_weighted(2, 1, (0, HALF))
+        price(10, 1)
         price(11, 0)
         quantize_priced(10)
         price(11, 1)
         quantize_priced(11, 0, 1)
         quantize_priced(11, 1, 2)
-        contrast_mm(0, 1, 7, 1, 2)
-        contrast_mm(1, 1, 0, 1, 2)
-        index_mm(9, 1)
-        contrast_mm(0, 1, 7, 2, 3)
-        contrast_mm(1, 1, 0, 2, 3)
-        contrast_mm(2, 1, 3)
+        index_mm(9, 5)
+        contrast_mm(0, 1, 0, 2, 3)
+        contrast_mm(1, 1, 2, 2, 3)
+        contrast_mm(2, 1, 4)
+        contrast_mm(3, 1, 6)
+        index_mm(10, 7)
+        index_mm(11, 3)
         index_out(9)
         contrast_out(0, 1)
         contrast_out(1, 1)
-        contrast_mm(3, 1, 1)
-        index_mm(10, 4)
-        index_mm(11, 2)
         contrast_out(2, 1)
         contrast_out(3, 1)
         index_out(10, "vector")

@@ -29,10 +29,15 @@ NJ = N // KP
 TILES = SG * T
 LINE = 8
 RUN = 4
-WIDE = 4
-DEPTH = {"sh_group": 3, "con_group": 4, "ga": 1, "gb": 1, "gc": 1, "gx": 1, "rel": 10, "priced": 4, "tagged": 3, "scaled": 3, "result": 6}
-PAIRS = (1,)
-HANDED = {8: "gx"}
+
+DEPTH = {
+    "wide": 4, "sh_group": 3, "con_group": 4, "group_a": 1, "group_b": 1, "group_c": 1, "handed": 1,
+    "rel": 10, "priced": 4, "early": 3, "scaled": 3, "columns": 4, "result": 6,
+}
+PAIR = (2, 3)
+HANDED = 8
+SHARE = 384
+WARM_FIRST, WARM_SECOND = 2, 3
 
 
 def tile_ghosh_price_push_s8_kernel(
@@ -48,7 +53,6 @@ def tile_ghosh_price_push_s8_kernel(
         scale_kp = keep.tile([P, KQ, T], F32, name="scale_kp")
         base_kp = keep.tile([P, NJ * T], BF16, name="base_kp")
         weight_kp = keep.tile([P, SG * T], BF16, name="weight_kp")
-        weight_f32 = keep.tile([P, SG * T], F32, name="weight_f32")
         b_words = keep.tile([P, NJ, 2 * C], U8, name="b_words", align_bytes=64)
         b_scales = keep.tile([P, NJ, C], U8, name="b_scales", align_bytes=64)
         con_raw = [keep.tile([P, S], BF16, name="con_raw%d" % a) for a in range(T)]
@@ -118,9 +122,9 @@ def tile_ghosh_price_push_s8_kernel(
 
         sh_wide, sh_bank, sh_group = {}, {}, {}
 
-        def widen(i, engine="scalar"):
-            sh_wide[i] = work.tile([P, N], BF16, name="wide", bufs=WIDE)
-            copy_on(engine, sh_wide[i][:], sh_bytes[i].bitcast(FP8))
+        def widen(i):
+            sh_wide[i] = work.tile([P, N], BF16, name="wide", bufs=DEPTH["wide"])
+            nc.scalar.copy(out=sh_wide[i][:], in_=sh_bytes[i].bitcast(FP8))
 
         def turn_shocks(i, number):
             sh_bank[i] = bank_of(number, [P, 2, KQ, P])
@@ -129,14 +133,15 @@ def tile_ghosh_price_push_s8_kernel(
                 for u in range(2):
                     nc.tensor.transpose(sh_bank[i][:, u, q, :], words[:, HALF * q + u : HALF * (q + 1) : 2], ident[:])
 
-        def scale_shocks(i, q0=0, q1=KQ, tag="sh_group"):
-            if q0 == 0:
-                sh_group[i] = work.tile([P, N], BF16, name=tag, bufs=DEPTH[tag], align_bytes=64)
-            grouped = sh_group[i][:].rearrange("p (q r u e) -> p q r u e", q=KQ, u=2, e=2)
+        def scale_shocks(i, tag="sh_group"):
+            sh_group[i] = work.tile([P, N], BF16, name=tag, bufs=DEPTH[tag], align_bytes=64)
             halves = sh_bank[i][:].rearrange("p u q r -> p (u q r)").bitcast(BF16)
-            halves = halves.rearrange("p (u q r e) -> p q r u e", q=KQ, u=2, e=2)
-            scales = scale_kp[:, q0:q1, :].rearrange("p q (u e) -> p q u e", u=2).unsqueeze(2).to_broadcast([P, q1 - q0, P, 2, 2])
-            nc.vector.tensor_tensor(out=grouped[:, q0:q1], in0=halves[:, q0:q1], in1=scales, op=MULT)
+            nc.vector.tensor_tensor(
+                out=sh_group[i][:].rearrange("p (q r u e) -> p q r u e", q=KQ, u=2, e=2),
+                in0=halves.rearrange("p (u q r e) -> p q r u e", q=KQ, u=2, e=2),
+                in1=scale_kp[:].rearrange("p q (u e) -> p q u e", u=2).unsqueeze(2).to_broadcast([P, KQ, P, 2, 2]),
+                op=MULT,
+            )
 
         def quantize_shocks(i):
             quantize(
@@ -172,7 +177,6 @@ def tile_ghosh_price_push_s8_kernel(
 
         def group_inverse(j, q, engine, c0, c1, part=(0, KP), tag=None):
             if (j, q, part) not in inv_part:
-                tag = tag or "grouped"
                 inv_part[j, q, part] = work.tile([P, part[1] - part[0], T], BF16, name=tag, bufs=DEPTH[tag], align_bytes=64)
             interleave(engine, inv_part[j, q, part][:, c0 - part[0] : c1 - part[0], :], inv_raw[j, q][:, :, c0:c1])
 
@@ -181,31 +185,31 @@ def tile_ghosh_price_push_s8_kernel(
             quantize(inv_codes[:, j, q, cols], inv_scales[:, j, q, cols], inv_part[j, q, part][:].rearrange("p n t -> p (n t)"))
 
         priced_pair = {}
-        mv_bank, rel, tr_bank, priced, tagged, scaled, weighted = {}, {}, {}, {}, {}, {}, {}
+        mv_bank, rel, tr_bank, priced, early, scaled, weighted = {}, {}, {}, {}, {}, {}, {}
 
-        def move_pass(i, j, q, first, last):
+        def move_pass(i, j, q):
             nc.tensor.matmul_mx(
                 out=mv_bank[i, j][:],
                 lhsT=sh_codes[:, i, q, :].bitcast(FP8X4),
                 lhsT_scale=sh_scales[:, i, q, :],
                 rhs=inv_codes[:, j, q, :].bitcast(FP8X4),
                 rhs_scale=inv_scales[:, j, q, :],
-                start=first,
-                stop=last,
+                start=(q == 0),
+                stop=(q == KQ - 1),
             )
 
         def move(units, banks):
             for (i, j), number in zip(units, banks):
                 mv_bank[i, j] = bank_of(number, [P, KP])
                 for q in range(KQ):
-                    move_pass(i, j, q, q == 0, q == KQ - 1)
+                    move_pass(i, j, q)
 
-        def move_by_pass(units, banks, order=(0, 1)):
+        def move_by_pass(units, banks):
             for (i, j), number in zip(units, banks):
                 mv_bank[i, j] = bank_of(number, [P, KP])
-            for q in order:
+            for q in range(KQ):
                 for i, j in units:
-                    move_pass(i, j, q, q == order[0], q == order[1])
+                    move_pass(i, j, q)
 
         def relatives(i, j):
             if j == 0:
@@ -230,20 +234,20 @@ def tile_ghosh_price_push_s8_kernel(
                 turn(i, j, banks[j])
 
         def priced_tile(i):
-            if i // 2 not in PAIRS:
-                tag = HANDED.get(i, "priced")
-                single = work.tile([P, NJ, P, T], BF16, name=tag, bufs=DEPTH[tag], align_bytes=64)
-                priced[i] = single[:]
+            if i in PAIR:
+                if not priced_pair:
+                    priced_pair[0] = work.tile([P, 2, NJ, P, T], BF16, name="pair", bufs=1, align_bytes=64)
+                priced[i] = priced_pair[0][:, i % 2]
                 return
-            if i // 2 not in priced_pair:
-                priced_pair[i // 2] = work.tile([P, 2, NJ, P, T], BF16, name="pair", bufs=1, align_bytes=64)
-            priced[i] = priced_pair[i // 2][:, i % 2]
+            tag = "handed" if i == HANDED else "priced"
+            single = work.tile([P, NJ, P, T], BF16, name=tag, bufs=DEPTH[tag], align_bytes=64)
+            priced[i] = single[:]
 
         def quantize_pair(i):
             quantize(
                 pr_codes[:, i : i + 2].rearrange("p i j m -> p (i j m)"),
                 pr_scales[:, i : i + 2].rearrange("p i j m -> p (i j m)"),
-                priced_pair[i // 2][:].rearrange("p i j m v -> p (i j m v)"),
+                priced_pair[0][:].rearrange("p i j m v -> p (i j m v)"),
             )
 
         def price(i, j):
@@ -268,24 +272,24 @@ def tile_ghosh_price_push_s8_kernel(
             for a in range(2 * NJ):
                 nc.tensor.transpose(base_row[0][:, a, :], words[:, a : a + 1].to_broadcast([P, P]), ident[:])
 
-        def price_first(i):
-            tagged[i] = work.tile([P, N], BF16, name="tagged", bufs=DEPTH["tagged"])
+        def price_early(i):
+            early[i] = work.tile([P, N], BF16, name="early", bufs=DEPTH["early"])
             nc.vector.tensor_tensor(
-                out=tagged[i][:].rearrange("p (c r e) -> p c e r", r=RUN, e=2),
+                out=early[i][:].rearrange("p (c r e) -> p c e r", r=RUN, e=2),
                 in0=base_row[0][:].rearrange("p a m -> p (a m)").bitcast(BF16).rearrange("p (c r e) -> p c e r", r=RUN, e=2),
                 in1=rel[i][:].rearrange("p e j c -> p e (j c)").rearrange("p e (c r) -> p c e r", r=RUN),
                 op=MULT,
             )
 
-        def turn_tagged(i, number):
+        def turn_early(i, number):
             tr_bank[i] = bank_of(number, [P, NJ, 2, P])
-            words = tagged[i][:].bitcast(F32)
+            words = early[i][:].bitcast(F32)
             for a in range(2 * NJ):
                 nc.tensor.transpose(tr_bank[i][:, a // 2, a % 2, :], words[:, P * a : P * (a + 1)], ident[:])
 
-        def empty_tagged(i, engine="scalar"):
+        def empty_early(i):
             priced_tile(i)
-            empty_words(priced[i].rearrange("p j m v -> p (j m v)"), tr_bank[i][:], engine)
+            empty_words(priced[i].rearrange("p j m v -> p (j m v)"), tr_bank[i][:], "scalar")
 
         def quantize_priced(i, j0=0, j1=NJ):
             quantize(
@@ -299,9 +303,6 @@ def tile_ghosh_price_push_s8_kernel(
                 scaled[i // T] = work.tile([P, NJ, T, KP], BF16, name="scaled", bufs=DEPTH["scaled"])
             return scaled[i // T][:, j0:j1, i % T, :].rearrange("p j (e c) -> p e j c", e=2)
 
-        def weigh_on_scalar(i, j):
-            nc.scalar.activation(out=plane(i, j, j + 1), in_=rel[i][:, :, j : j + 1, :], func=COPY, scale=weight_f32[:, i : i + 1])
-
         def weigh_on_vector(i, j):
             nc.vector.tensor_scalar(
                 out=plane(i, j, j + 1), in0=rel[i][:, :, j : j + 1, :], scalar1=weight_kp[:, i : i + 1], scalar2=None, op0=MULT
@@ -310,7 +311,7 @@ def tile_ghosh_price_push_s8_kernel(
         def weigh_on_gpsimd(*units):
             i0 = min(unit[0] for unit in units)
             count = max(unit[0] for unit in units) - i0 + 1
-            columns = work.tile([P, count], F32, name="columns", bufs=4)
+            columns = work.tile([P, count], F32, name="columns", bufs=DEPTH["columns"])
             nc.vector.tensor_copy(out=columns[:], in_=weight_kp[:, i0 : i0 + count])
             for i, j0, j1 in units:
                 nc.gpsimd.tensor_scalar(
@@ -322,7 +323,7 @@ def tile_ghosh_price_push_s8_kernel(
                     op1=ADD,
                 )
 
-        def group_weighted(g, j, engine, c0=0, c1=KP, part=(0, KP), tag="grouped"):
+        def group_weighted(g, j, engine, c0=0, c1=KP, part=(0, KP), tag=None):
             if (g, j, part) not in weighted:
                 weighted[g, j, part] = work.tile([P, part[1] - part[0], T], BF16, name=tag, bufs=DEPTH[tag], align_bytes=64)
             interleave(engine, weighted[g, j, part][:, c0 - part[0] : c1 - part[0], :], scaled[g][:, j, :, c0:c1])
@@ -339,8 +340,12 @@ def tile_ghosh_price_push_s8_kernel(
             else:
                 nc.vector.tensor_copy(out=out, in_=in_)
 
+        stored = []
+
         def result_tile():
-            return work.tile([P, KP], F32, name="result", bufs=DEPTH["result"])
+            tag = "wide" if len(stored) % 2 else "result"
+            stored.append(tag)
+            return work.tile([P, KP], F32, name=tag, bufs=DEPTH[tag])
 
         def index_mm(i, number):
             index_bank[i] = bank_of(number, [P, C])
@@ -383,34 +388,10 @@ def tile_ghosh_price_push_s8_kernel(
             )
             nc.sync.dma_start(out=out_1[P * a : P * (a + 1), KP * j : KP * (j + 1)], in_=result[:])
 
-        def index_half(i, h, number):
-            index_bank[i, h] = bank_of(number, [P, HALF])
-            cols = slice(HALF * h, HALF * (h + 1))
-            for j in range(NJ):
-                nc.tensor.matmul_mx(
-                    out=index_bank[i, h][:],
-                    lhsT=pr_codes[:, i, j, :].bitcast(FP8X4),
-                    lhsT_scale=pr_scales[:, i, j, :],
-                    rhs=b_words[:, j, KP * h : KP * (h + 1)].bitcast(FP4X4),
-                    rhs_scale=b_scales[:, j, cols],
-                    start=(j == 0),
-                    stop=(j == NJ - 1),
-                )
-
-        def index_half_out(i, h, engine):
-            result = result_tile()
-            sums_out(engine, result[:, 0:HALF], index_bank[i, h][:])
-            nc.sync.dma_start(out=index_v[i // T][:, i % T, HALF * h : HALF * (h + 1)], in_=result[:, 0:HALF])
-
-        idle_bank = {}
-
-        def warm(count, columns):
-            if not idle_bank:
-                idle_bank[0] = bank_of(1, [P, KP])
-            bank = idle_bank[0]
-            zeros = b_scales[:].rearrange("p j n -> p (j n)").bitcast(F32)
+        def warm(count, source):
+            bank = bank_of(1, [P, KP])
             for k in range(count):
-                nc.tensor.matmul(bank[:, 0:columns], zeros[:, 0:P], zeros[:, 0:columns], start=True, stop=True)
+                nc.tensor.matmul(bank[:], source[:, 0, 0:P], source[:, 0, :], start=True, stop=True)
 
         nc.vector.memset(b_scales[:].rearrange("p j n -> p (j n)").bitcast(I32), 0)
         make_identity(nc, ident[:])
@@ -432,24 +413,21 @@ def tile_ghosh_price_push_s8_kernel(
         load_contrasts(3)
         nc.sync.dma_start(out=base_kp[:].rearrange("p (j t) -> p j t", t=T), in_=base.rearrange("(j p t) -> p j t", p=P, t=T))
 
-        warm(2, HALF)
         widen(0)
         turn_shocks(0, 2)
-        warm(1, P)
         widen(1)
         turn_shocks(1, 3)
-        warm(1, HALF)
         widen(2)
         turn_shocks(2, 4)
         scale_shocks(0)
         scale_shocks(1)
-        group_inverse(0, 0, "gpsimd", 0, HALF, tag="ga")
+        group_inverse(0, 0, "gpsimd", 0, HALF, tag="group_a")
         group_inverse(0, 0, "scalar", HALF, KP)
-        warm(1, P)
+        warm(WARM_FIRST, inv_raw[0, 0])
         widen(3)
         turn_shocks(3, 5)
-        warm(1, HALF)
-        group_inverse(0, 1, "scalar", HALF, KP, tag="gb")
+        warm(WARM_SECOND, inv_raw[0, 1])
+        group_inverse(0, 1, "scalar", HALF, KP, tag="group_b")
         group_inverse(0, 1, "vector", 0, HALF)
         widen(4)
         turn_shocks(4, 6)
@@ -459,12 +437,13 @@ def tile_ghosh_price_push_s8_kernel(
         quantize_inverse(0, 0)
         quantize_inverse(0, 1)
         load_baskets()
+
         units = [(0, 0), (1, 0)]
         move_by_pass(units, [0, 1])
         turn_shocks(5, 7)
-        group_inverse(1, 0, "gpsimd", 0, 384, tag="ga")
-        group_inverse(1, 0, "scalar", 384, KP)
-        scale_shocks(2, tag="gx")
+        group_inverse(1, 0, "gpsimd", 0, SHARE, tag="group_a")
+        group_inverse(1, 0, "scalar", SHARE, KP)
+        scale_shocks(2, tag="handed")
         scale_shocks(3)
         widen(6)
         turn_shocks(6, 2)
@@ -472,13 +451,14 @@ def tile_ghosh_price_push_s8_kernel(
         turn_shocks(7, 3)
         exps(units)
         quantize_shocks(2)
-        group_inverse(1, 1, "gpsimd", 0, P, part=(0, P), tag="gx")
+        group_inverse(1, 1, "gpsimd", 0, P, part=(0, P), tag="handed")
         quantize_shocks(3)
+
         units = [(2, 0), (3, 0)]
         move(units, [0, 1])
         turn_contrasts(0, 4)
         turn_contrasts(1, 5)
-        group_inverse(1, 1, "scalar", P, KP, part=(P, KP), tag="gb")
+        group_inverse(1, 1, "scalar", P, KP, part=(P, KP), tag="group_b")
         scale_shocks(4)
         quantize_inverse(1, 0)
         quantize_inverse(1, 1, (0, P))
@@ -492,11 +472,13 @@ def tile_ghosh_price_push_s8_kernel(
         widen(9)
         scale_shocks(5)
         scale_shocks(6)
+
         units = [(0, 1), (1, 1), (2, 1)]
         move_by_pass(units, [6, 0, 1])
         exps(units[:1])
         move([(4, 0), (3, 1), (4, 1)], [4, 5, 7])
         exps(units[1:])
+        widen(10)
         exps([(4, 0), (3, 1), (4, 1)])
         weigh_on_gpsimd((3, 0, 1), (0, 1, 2), (1, 1, 2))
         quantize_shocks(5)
@@ -505,24 +487,27 @@ def tile_ghosh_price_push_s8_kernel(
         turn_shocks(9, 2)
         scale_shocks(7)
         scale_shocks(8)
-        widen(10)
         widen(11)
+
         units = [(5, 0), (6, 0), (5, 1), (6, 1)]
-        move(units, [0, 1, 4, 5])
+        move(units[:2], [0, 1])
+        spread_base(3)
+        turn_shocks(10, 6)
+        move(units[2:], [4, 5])
         exps(units)
         quantize_shocks(7)
-        group_weighted(0, 0, "vector", tag="ga")
+        group_weighted(0, 0, "vector", tag="group_a")
         weigh_on_gpsimd((2, 1, 2), (3, 1, 2), (4, 0, 2))
         quantize_shocks(8)
-        turn_shocks(10, 3)
         turn_shocks(11, 7)
-        turn_contrasts(2, 6)
+        turn_contrasts(2, 0)
         scale_shocks(9)
         scale_shocks(10)
         scale_shocks(11)
         empty_contrasts(2)
+
         units = [(7, 0), (8, 0), (7, 1), (8, 1)]
-        move(units, [0, 1, 4, 5])
+        move(units, [1, 2, 4, 5])
         exps(units)
         quantize_shocks(9)
         quantize_shocks(10)
@@ -530,77 +515,80 @@ def tile_ghosh_price_push_s8_kernel(
         quantize_contrasts(0)
         weigh_on_gpsimd((5, 0, 1), (6, 0, 1), (7, 0, 1))
         quantize_weighted(0, 0)
-        turns(0, (2, 6))
-        spread_base(3)
+        turns(0, (6, 0))
         turn_contrasts(3, 7)
         prices(0)
-        price_first(5)
-        group_weighted(0, 1, "scalar", 0, HALF, tag="gb")
+        price_early(5)
+        group_weighted(0, 1, "scalar", 0, HALF, tag="group_b")
         empty_contrasts(3)
+
         units = [(9, 0), (10, 0), (9, 1), (11, 0)]
-        move(units, [0, 1, 4, 5])
+        move(units, [1, 2, 4, 5])
         exps(units[:3])
-        group_weighted(1, 0, "scalar", 0, HALF, tag="ga")
+        group_weighted(1, 0, "scalar", 0, HALF, tag="group_a")
         quantize_priced(0)
         quantize_contrasts(1)
-        turns(1, (2, 6))
+        turns(1, (6, 0))
         exps(units[3:])
         weigh_on_gpsimd((8, 0, 1), (9, 0, 1), (10, 0, 1), (11, 0, 1))
         quantize_contrasts(2)
         quantize_contrasts(3)
         turn_contrasts(4, 7)
         prices(1)
-        price_first(6)
-        price_first(7)
-        empty_contrasts(4)
+        empty_contrasts(4, "vector")
+        price_early(6)
+        price_early(7)
+
         units = [(10, 1), (11, 1)]
-        move(units, [0, 1])
+        move(units, [1, 2])
         relatives(10, 1)
         group_weighted(1, 0, "scalar", HALF, KP)
         relatives(11, 1)
-        turn_tagged(5, 5)
+        turn_early(5, 5)
         turn_contrasts(5, 7)
         index_mm(0, 4)
-        turns(2, (2, 6))
-        turn_tagged(6, 0)
-        empty_tagged(5)
+        turns(2, (6, 0))
+        turn_early(6, 1)
+        empty_early(5)
         index_out(0)
         empty_contrasts(5)
-        empty_tagged(6)
+        empty_early(6)
         quantize_priced(1)
         quantize_weighted(1, 0)
         quantize_priced(5)
-        group_weighted(2, 0, "vector", tag="gc")
+        group_weighted(2, 0, "vector", tag="group_c")
         quantize_contrasts(4)
         quantize_priced(6)
         quantize_contrasts(5)
         weigh_on_gpsimd((5, 1, 2), (6, 1, 2), (7, 1, 2))
         quantize_weighted(2, 0)
-        index_mm(1, 1)
+
+        index_mm(1, 2)
         contrast_mm(0, 0, 5, 0, 2)
         contrast_mm(1, 0, 4, 0, 2)
         index_mm(5, 7)
         index_out(1)
-        turn_tagged(7, 0)
-        turns(3, (3, 1))
+        turn_early(7, 1)
+        turns(3, (3, 2))
         index_out(5)
-        empty_tagged(7)
+        empty_early(7)
         prices(2)
         prices(3)
         group_weighted(0, 1, "scalar", HALF, KP)
+
         index_mm(6, 7)
-        contrast_mm(2, 0, 0, 0, 2)
+        contrast_mm(2, 0, 1, 0, 2)
         contrast_mm(0, 0, 5, 2, 3)
         contrast_mm(1, 0, 4, 2, 3)
-        contrast_mm(2, 0, 0, 2, 3)
-        contrast_mm(3, 0, 2)
+        contrast_mm(2, 0, 1, 2, 3)
+        contrast_mm(3, 0, 6)
         index_out(6)
         contrast_out(0, 0)
         contrast_out(1, 0)
-        turns(4, (6, 3))
-        turns(8, (1, 5))
+        turns(4, (0, 3))
+        turns(8, (2, 5))
         contrast_out(2, 0)
-        group_weighted(1, 1, "scalar", 0, HALF, tag="ga")
+        group_weighted(1, 1, "scalar", 0, HALF, tag="group_a")
         contrast_out(3, 0)
         quantize_priced(7)
         quantize_pair(2)
@@ -608,29 +596,31 @@ def tile_ghosh_price_push_s8_kernel(
         quantize_weighted(0, 1)
         prices(4)
         prices(8)
+
         index_mm(7, 7)
         index_mm(2, 4)
-        contrast_mm(0, 1, 0, 0, 1)
-        contrast_mm(1, 1, 2, 0, 1)
-        index_mm(3, 6)
+        contrast_mm(0, 1, 1, 0, 1)
+        contrast_mm(1, 1, 6, 0, 1)
+        index_mm(3, 0)
         group_weighted(1, 1, "scalar", HALF, KP)
         index_out(7)
         index_out(2)
         index_out(3)
-        turns(9, (3, 1))
+        turns(9, (3, 2))
         turns(10, (5, 7))
         weigh_on_vector(11, 1)
         quantize_priced(4)
         quantize_priced(8)
-        group_weighted(2, 1, "gpsimd", 0, HALF, part=(0, HALF), tag="gx")
+        group_weighted(2, 1, "gpsimd", 0, HALF, part=(0, HALF), tag="handed")
         quantize_weighted(1, 1)
-        group_weighted(2, 1, "scalar", HALF, KP, part=(HALF, KP), tag="gb")
+        group_weighted(2, 1, "scalar", HALF, KP, part=(HALF, KP), tag="group_b")
         prices(9)
+
         index_mm(4, 4)
-        index_mm(8, 6)
-        contrast_mm(0, 1, 0, 1, 2)
-        contrast_mm(1, 1, 2, 1, 2)
-        turns(11, (3, 1))
+        index_mm(8, 0)
+        contrast_mm(0, 1, 1, 1, 2)
+        contrast_mm(1, 1, 6, 1, 2)
+        turns(11, (3, 2))
         index_out(4)
         index_out(8)
         price(10, 0)
@@ -643,11 +633,12 @@ def tile_ghosh_price_push_s8_kernel(
         price(11, 1)
         quantize_priced(11, 0, 1)
         quantize_priced(11, 1, 2)
+
         index_mm(9, 5)
-        contrast_mm(0, 1, 0, 2, 3)
-        contrast_mm(1, 1, 2, 2, 3)
+        contrast_mm(0, 1, 1, 2, 3)
+        contrast_mm(1, 1, 6, 2, 3)
         contrast_mm(2, 1, 4)
-        contrast_mm(3, 1, 6)
+        contrast_mm(3, 1, 0)
         index_mm(10, 7)
         index_mm(11, 3)
         index_out(9)

@@ -31,13 +31,9 @@ LINE = 8
 RUN = 4
 
 DEPTH = {
-    "wide": 4, "sh_group": 3, "con_group": 4, "group_a": 1, "group_b": 1, "group_c": 1, "handed": 1,
-    "rel": 10, "priced": 4, "early": 3, "scaled": 3, "columns": 4, "result": 6,
+    "wide": 4, "sh_group": 4, "con_group": 4, "rel": 3, "priced": 6, "early": 4, "scaled": 1, "columns": 4, "result": 8,
+    "codes": TILES, "scales": TILES, "group_a": 1, "group_b": 1, "group_c": 1, "group_d": 1, "group_e": 1,
 }
-PAIR = (2, 3)
-HANDED = 8
-SHARE = 384
-WARM_FIRST, WARM_SECOND = 2, 3
 
 
 def tile_ghosh_price_push_s8_kernel(
@@ -57,17 +53,15 @@ def tile_ghosh_price_push_s8_kernel(
         b_scales = keep.tile([P, NJ, C], U8, name="b_scales", align_bytes=64)
         con_raw = [keep.tile([P, S], BF16, name="con_raw%d" % a) for a in range(T)]
 
-        sh_codes = keep.tile([P, TILES, KQ, P], U32, name="sh_codes", align_bytes=64)
-        sh_scales = keep.tile([P, TILES, KQ, P], U8, name="sh_scales", align_bytes=64)
         inv_codes = keep.tile([P, NJ, KQ, KP], U32, name="inv_codes", align_bytes=64)
         inv_scales = keep.tile([P, NJ, KQ, KP], U8, name="inv_scales", align_bytes=64)
-        con_codes = keep.tile([P, SG, R], U32, name="con_codes", align_bytes=64)
-        con_scales = keep.tile([P, SG, R], U8, name="con_scales", align_bytes=64)
-        pr_codes = keep.tile([P, TILES, NJ, P], U32, name="pr_codes", align_bytes=64)
-        pr_scales = keep.tile([P, TILES, NJ, P], U8, name="pr_scales", align_bytes=64)
+        con_codes = keep.tile([P, SG * R], U32, name="con_codes", align_bytes=64)
+        con_scales = keep.tile([P, SG * R], U8, name="con_scales", align_bytes=64)
         we_codes = keep.tile([P, SG, NJ, KP], U32, name="we_codes", align_bytes=64)
         we_scales = keep.tile([P, SG, NJ, KP], U8, name="we_scales", align_bytes=64)
         ident = keep.tile([P, P], F32, name="ident")
+        ident_bf = keep.tile([P, P], BF16, name="ident_bf")
+        ones = keep.tile([P, 1], F32, name="ones")
 
         shocks_v = shocks_bytes.rearrange("(g m t) k -> g m t k", m=P, t=T)
         inverse_v = inverse.rearrange("(q p t) n -> q p t n", p=P, t=T)
@@ -88,6 +82,9 @@ def tile_ghosh_price_push_s8_kernel(
         def load_contrasts(a):
             nc.sync.dma_start(out=con_raw[a][:], in_=contrasts[P * a : P * (a + 1), :])
 
+        def load_factors(tile, vector):
+            nc.sync.dma_start(out=tile[:].rearrange("p (g t) -> p g t", t=T), in_=vector.rearrange("(g p t) -> p g t", p=P, t=T))
+
         def load_baskets():
             for quad in range(4):
                 nc.sync.dma_start(
@@ -98,6 +95,9 @@ def tile_ghosh_price_push_s8_kernel(
 
         def bank_of(number, shape):
             return psum.tile(shape, F32, name="bank%d" % number)
+
+        def buffer(tag, shape, dtype):
+            return work.tile(shape, dtype, name=tag, bufs=DEPTH[tag], align_bytes=64)
 
         def copy_on(engine, out, in_):
             if engine == "scalar":
@@ -120,43 +120,70 @@ def tile_ghosh_price_push_s8_kernel(
         def quantize(codes, scales, grouped):
             nc.vector.quantize_mx(out=codes.bitcast(FP8X4), scales=scales, in_=grouped)
 
-        sh_wide, sh_bank, sh_group = {}, {}, {}
+        def tile_codes():
+            return buffer("codes", [P, 2, P], U32), buffer("scales", [P, 2, P], U8)
 
-        def widen(i):
-            sh_wide[i] = work.tile([P, N], BF16, name="wide", bufs=DEPTH["wide"])
-            nc.scalar.copy(out=sh_wide[i][:], in_=sh_bytes[i].bitcast(FP8))
+        def quantize_tile(pair, grouped):
+            quantize(pair[0][:].rearrange("p q r -> p (q r)"), pair[1][:].rearrange("p q r -> p (q r)"), grouped)
 
-        def turn_shocks(i, number):
-            sh_bank[i] = bank_of(number, [P, 2, KQ, P])
+        sh_wide, sh_bank, sh_group, sh_mx = {}, {}, {}, {}
+
+        def widen(i, q0=0, q1=KQ):
+            if i not in sh_wide:
+                sh_wide[i] = buffer("wide", [P, N], BF16)
+            nc.scalar.copy(out=sh_wide[i][:, KP * q0 : KP * q1], in_=sh_bytes[i][:, KP * q0 : KP * q1].bitcast(FP8))
+
+        sorted_parts = {}
+
+        def widen_sorted(i, q0=0, q1=KQ):
+            if i not in sh_wide:
+                sh_wide[i] = buffer("wide", [P, N], BF16)
+            for q in range(q0, q1):
+                sorted_parts[i, q] = (HALF * q0 + P * (q - q0), P * (q1 - q0))
+            nc.vector.tensor_scalar(
+                out=sh_wide[i][:, KP * q0 : KP * q1].rearrange("p (u w e) -> p w u e", u=2, e=2),
+                in0=sh_bytes[i][:, KP * q0 : KP * q1].bitcast(FP8).rearrange("p (w u e) -> p w u e", u=2, e=2),
+                scalar1=ones[:],
+                scalar2=None,
+                op0=MULT,
+            )
+
+        def turn_shocks(i, number, q0=0, q1=KQ):
+            sh_bank[i, q0] = bank_of(number, [P, 2, q1 - q0, P])
             words = sh_wide[i][:].bitcast(F32)
-            for q in range(KQ):
+            for q in range(q0, q1):
                 for u in range(2):
-                    nc.tensor.transpose(sh_bank[i][:, u, q, :], words[:, HALF * q + u : HALF * (q + 1) : 2], ident[:])
+                    if (i, q) in sorted_parts:
+                        first = sorted_parts[i, q][0] + u * sorted_parts[i, q][1]
+                        part = words[:, first : first + P]
+                    else:
+                        part = words[:, HALF * q + u : HALF * (q + 1) : 2]
+                    nc.tensor.transpose(sh_bank[i, q0][:, u, q - q0, :], part, ident[:])
 
-        def scale_shocks(i, tag="sh_group"):
-            sh_group[i] = work.tile([P, N], BF16, name=tag, bufs=DEPTH[tag], align_bytes=64)
-            halves = sh_bank[i][:].rearrange("p u q r -> p (u q r)").bitcast(BF16)
+        def scale_shocks(i, q0=0, q1=KQ, tag="sh_group"):
+            if i not in sh_group:
+                sh_group[i] = buffer(tag, [P, N], BF16)
+            halves = sh_bank[i, q0][:].rearrange("p u q r -> p (u q r)").bitcast(BF16)
             nc.vector.tensor_tensor(
-                out=sh_group[i][:].rearrange("p (q r u e) -> p q r u e", q=KQ, u=2, e=2),
-                in0=halves.rearrange("p (u q r e) -> p q r u e", q=KQ, u=2, e=2),
-                in1=scale_kp[:].rearrange("p q (u e) -> p q u e", u=2).unsqueeze(2).to_broadcast([P, KQ, P, 2, 2]),
+                out=sh_group[i][:, KP * q0 : KP * q1].rearrange("p (q r u e) -> p q r u e", r=P, u=2, e=2),
+                in0=halves.rearrange("p (u q r e) -> p q r u e", r=P, u=2, e=2),
+                in1=scale_kp[:, q0:q1].rearrange("p q (u e) -> p q u e", u=2).unsqueeze(2).to_broadcast([P, q1 - q0, P, 2, 2]),
                 op=MULT,
             )
 
         def quantize_shocks(i):
-            quantize(
-                sh_codes[:, i].rearrange("p q r -> p (q r)"), sh_scales[:, i].rearrange("p q r -> p (q r)"), sh_group[i][:]
-            )
+            sh_mx[i] = tile_codes()
+            quantize_tile(sh_mx[i], sh_group[i][:])
 
         con_bank, con_group = {}, {}
 
         def turn_contrasts(n, number):
-            g, a0 = n % SG, 2 * (n // SG)
             con_bank[n] = bank_of(number, [P, 2, 2, P])
-            for a in range(2):
-                words = con_raw[a0 + a][:].bitcast(F32)
+            for h in range(2):
+                a, g = divmod(2 * n + h, SG)
+                words = con_raw[a][:].bitcast(F32)
                 for u in range(2):
-                    nc.tensor.transpose(con_bank[n][:, a, u, :], words[:, HALF * g + u : HALF * (g + 1) : 2], ident[:])
+                    nc.tensor.transpose(con_bank[n][:, h, u, :], words[:, HALF * g + u : HALF * (g + 1) : 2], ident[:])
 
         def empty_words(grouped, bank, engine):
             copy_on(
@@ -166,56 +193,52 @@ def tile_ghosh_price_push_s8_kernel(
             )
 
         def empty_contrasts(n, engine="scalar"):
-            con_group[n] = work.tile([P, 2 * KP], BF16, name="con_group", bufs=DEPTH["con_group"], align_bytes=64)
+            con_group[n] = buffer("con_group", [P, 2 * KP], BF16)
             empty_words(con_group[n][:], con_bank[n][:], engine)
 
         def quantize_contrasts(n):
-            g, cols = n % SG, slice(HALF * (n // SG), HALF * (n // SG + 1))
-            quantize(con_codes[:, g, cols], con_scales[:, g, cols], con_group[n][:])
+            cols = slice(HALF * n, HALF * (n + 1))
+            quantize(con_codes[:, cols], con_scales[:, cols], con_group[n][:])
 
         inv_part = {}
 
         def group_inverse(j, q, engine, c0, c1, part=(0, KP), tag=None):
             if (j, q, part) not in inv_part:
-                inv_part[j, q, part] = work.tile([P, part[1] - part[0], T], BF16, name=tag, bufs=DEPTH[tag], align_bytes=64)
+                inv_part[j, q, part] = buffer(tag, [P, part[1] - part[0], T], BF16)
             interleave(engine, inv_part[j, q, part][:, c0 - part[0] : c1 - part[0], :], inv_raw[j, q][:, :, c0:c1])
 
         def quantize_inverse(j, q, part=(0, KP)):
             cols = slice(part[0], part[1])
             quantize(inv_codes[:, j, q, cols], inv_scales[:, j, q, cols], inv_part[j, q, part][:].rearrange("p n t -> p (n t)"))
 
-        priced_pair = {}
-        mv_bank, rel, tr_bank, priced, early, scaled, weighted = {}, {}, {}, {}, {}, {}, {}
+        mv_bank, tr_bank, priced, early, scaled, weighted, pr_mx = {}, {}, {}, {}, {}, {}, {}
 
-        def move_pass(i, j, q):
+        def move_pass(i, j, q, number=None):
+            if number is not None:
+                mv_bank[i, j] = bank_of(number, [P, KP])
             nc.tensor.matmul_mx(
                 out=mv_bank[i, j][:],
-                lhsT=sh_codes[:, i, q, :].bitcast(FP8X4),
-                lhsT_scale=sh_scales[:, i, q, :],
+                lhsT=sh_mx[i][0][:, q, :].bitcast(FP8X4),
+                lhsT_scale=sh_mx[i][1][:, q, :],
                 rhs=inv_codes[:, j, q, :].bitcast(FP8X4),
                 rhs_scale=inv_scales[:, j, q, :],
-                start=(q == 0),
-                stop=(q == KQ - 1),
+                start=number is not None,
+                stop=number is None,
             )
 
         def move(units, banks):
             for (i, j), number in zip(units, banks):
-                mv_bank[i, j] = bank_of(number, [P, KP])
-                for q in range(KQ):
-                    move_pass(i, j, q)
+                move_pass(i, j, 0, number)
+                move_pass(i, j, 1)
 
-        def move_by_pass(units, banks):
-            for (i, j), number in zip(units, banks):
-                mv_bank[i, j] = bank_of(number, [P, KP])
-            for q in range(KQ):
-                for i, j in units:
-                    move_pass(i, j, q)
+        rel = [keep.tile([P, NJ, T, KP], F32, name="rel%d" % g) for g in range(SG)]
+
+        def unit_rel(i, j):
+            return rel[i // T][:, j, i % T, :]
 
         def relatives(i, j):
-            if j == 0:
-                rel[i] = work.tile([P, 2, NJ, HALF], F32, name="rel", bufs=DEPTH["rel"])
             nc.scalar.activation(
-                out=rel[i][:, :, j, :].rearrange("p e (u m) -> p e u m", u=2),
+                out=unit_rel(i, j).rearrange("p (e u m) -> p e u m", e=2, u=2),
                 in_=mv_bank[i, j][:].rearrange("p (m u e) -> p e u m", u=2, e=2),
                 func=EXP,
             )
@@ -227,34 +250,21 @@ def tile_ghosh_price_push_s8_kernel(
         def turn(i, j, number):
             tr_bank[i, j] = bank_of(number, [P, T, P])
             for v in range(T):
-                nc.tensor.transpose(tr_bank[i, j][:, v, :], rel[i][:, v % 2, j, P * (v // 2) : P * (v // 2 + 1)], ident[:])
+                c0 = HALF * (v % 2) + P * (v // 2)
+                nc.tensor.transpose(tr_bank[i, j][:, v, :], unit_rel(i, j)[:, c0 : c0 + P], ident[:])
 
         def turns(i, banks):
             for j in range(NJ):
                 turn(i, j, banks[j])
 
-        def priced_tile(i):
-            if i in PAIR:
-                if not priced_pair:
-                    priced_pair[0] = work.tile([P, 2, NJ, P, T], BF16, name="pair", bufs=1, align_bytes=64)
-                priced[i] = priced_pair[0][:, i % 2]
-                return
-            tag = "handed" if i == HANDED else "priced"
-            single = work.tile([P, NJ, P, T], BF16, name=tag, bufs=DEPTH[tag], align_bytes=64)
-            priced[i] = single[:]
-
-        def quantize_pair(i):
-            quantize(
-                pr_codes[:, i : i + 2].rearrange("p i j m -> p (i j m)"),
-                pr_scales[:, i : i + 2].rearrange("p i j m -> p (i j m)"),
-                priced_pair[0][:].rearrange("p i j m v -> p (i j m v)"),
-            )
+        def priced_tile(i, tag="priced"):
+            if i not in priced:
+                priced[i] = buffer(tag, [P, NJ, P, T], BF16)
+            return priced[i]
 
         def price(i, j):
-            if j == 0:
-                priced_tile(i)
             nc.vector.tensor_tensor(
-                out=priced[i][:, j],
+                out=priced_tile(i)[:, j],
                 in0=tr_bank[i, j][:].rearrange("p v m -> p m v"),
                 in1=base_kp[:, T * j : T * (j + 1)].unsqueeze(1).to_broadcast([P, P, T]),
                 op=MULT,
@@ -264,69 +274,91 @@ def tile_ghosh_price_push_s8_kernel(
             for j in range(NJ):
                 price(i, j)
 
-        base_row = {}
+        consts = {}
 
         def spread_base(number):
-            base_row[0] = bank_of(number, [P, 2 * NJ, P])
+            consts["base"] = bank_of(number, [P, 2 * NJ, P])
             words = base_kp[:].bitcast(F32)
             for a in range(2 * NJ):
-                nc.tensor.transpose(base_row[0][:, a, :], words[:, a : a + 1].to_broadcast([P, P]), ident[:])
+                nc.tensor.transpose(consts["base"][:, a, :], words[:, a : a + 1].to_broadcast([P, P]), ident[:])
+
+        def place_weights(number):
+            consts["weight"] = bank_of(number, [P, TILES])
+            nc.tensor.matmul(consts["weight"][:], ident_bf[:], weight_kp[:], start=True, stop=True)
 
         def price_early(i):
-            early[i] = work.tile([P, N], BF16, name="early", bufs=DEPTH["early"])
-            nc.vector.tensor_tensor(
-                out=early[i][:].rearrange("p (c r e) -> p c e r", r=RUN, e=2),
-                in0=base_row[0][:].rearrange("p a m -> p (a m)").bitcast(BF16).rearrange("p (c r e) -> p c e r", r=RUN, e=2),
-                in1=rel[i][:].rearrange("p e j c -> p e (j c)").rearrange("p e (c r) -> p c e r", r=RUN),
-                op=MULT,
-            )
+            early[i] = buffer("early", [P, NJ, KP], BF16)
+            row = consts["base"][:].rearrange("p a m -> p (a m)").bitcast(BF16)
+            for j in range(NJ):
+                nc.vector.tensor_tensor(
+                    out=early[i][:, j].rearrange("p (c r e) -> p c e r", r=RUN, e=2),
+                    in0=row[:, KP * j : KP * (j + 1)].rearrange("p (c r e) -> p c e r", r=RUN, e=2),
+                    in1=unit_rel(i, j).rearrange("p (e c r) -> p c e r", r=RUN, e=2),
+                    op=MULT,
+                )
 
         def turn_early(i, number):
             tr_bank[i] = bank_of(number, [P, NJ, 2, P])
-            words = early[i][:].bitcast(F32)
+            words = early[i][:].rearrange("p j n -> p (j n)").bitcast(F32)
             for a in range(2 * NJ):
                 nc.tensor.transpose(tr_bank[i][:, a // 2, a % 2, :], words[:, P * a : P * (a + 1)], ident[:])
 
-        def empty_early(i):
-            priced_tile(i)
-            empty_words(priced[i].rearrange("p j m v -> p (j m v)"), tr_bank[i][:], "scalar")
+        def empty_early(i, engine="scalar"):
+            empty_words(priced_tile(i)[:].rearrange("p j m v -> p (j m v)"), tr_bank[i][:], engine)
 
-        def quantize_priced(i, j0=0, j1=NJ):
-            quantize(
-                pr_codes[:, i, j0:j1].rearrange("p j m -> p (j m)"),
-                pr_scales[:, i, j0:j1].rearrange("p j m -> p (j m)"),
-                priced[i][:, j0:j1].rearrange("p j m v -> p (j m v)"),
-            )
+        def quantize_priced(i):
+            pr_mx[i] = tile_codes()
+            quantize_tile(pr_mx[i], priced[i][:].rearrange("p j m v -> p (j m v)"))
 
-        def plane(i, j0, j1):
-            if i // T not in scaled:
-                scaled[i // T] = work.tile([P, NJ, T, KP], BF16, name="scaled", bufs=DEPTH["scaled"])
-            return scaled[i // T][:, j0:j1, i % T, :].rearrange("p j (e c) -> p e j c", e=2)
+        def planes(g):
+            if g not in scaled:
+                scaled[g] = buffer("scaled", [P, NJ, T, KP], BF16)
+            return scaled[g]
 
-        def weigh_on_vector(i, j):
-            nc.vector.tensor_scalar(
-                out=plane(i, j, j + 1), in0=rel[i][:, :, j : j + 1, :], scalar1=weight_kp[:, i : i + 1], scalar2=None, op0=MULT
-            )
+        def weight_columns(i0, count):
+            columns = buffer("columns", [P, count], F32)
+            nc.vector.tensor_copy(out=columns[:], in_=weight_kp[:, i0 : i0 + count])
+            return columns
 
         def weigh_on_gpsimd(*units):
             i0 = min(unit[0] for unit in units)
-            count = max(unit[0] for unit in units) - i0 + 1
-            columns = work.tile([P, count], F32, name="columns", bufs=DEPTH["columns"])
-            nc.vector.tensor_copy(out=columns[:], in_=weight_kp[:, i0 : i0 + count])
+            columns = weight_columns(i0, max(unit[0] for unit in units) - i0 + 1)
             for i, j0, j1 in units:
                 nc.gpsimd.tensor_scalar(
-                    out=plane(i, j0, j1),
-                    in0=rel[i][:, :, j0:j1, :],
+                    out=planes(i // T)[:, j0:j1, i % T, :],
+                    in0=rel[i // T][:, j0:j1, i % T, :],
                     scalar1=columns[:, i - i0 : i - i0 + 1],
                     scalar2=0.0,
                     op0=MULT,
                     op1=ADD,
                 )
 
-        def group_weighted(g, j, engine, c0=0, c1=KP, part=(0, KP), tag=None):
+        def weighted_part(g, j, part, tag):
             if (g, j, part) not in weighted:
-                weighted[g, j, part] = work.tile([P, part[1] - part[0], T], BF16, name=tag, bufs=DEPTH[tag], align_bytes=64)
-            interleave(engine, weighted[g, j, part][:, c0 - part[0] : c1 - part[0], :], scaled[g][:, j, :, c0:c1])
+                weighted[g, j, part] = buffer(tag, [P, part[1] - part[0], T], BF16)
+            return weighted[g, j, part]
+
+        def group_weighted(g, j, engine, c0=0, c1=KP, part=(0, KP), tag=None):
+            interleave(engine, weighted_part(g, j, part, tag)[:, c0 - part[0] : c1 - part[0], :], scaled[g][:, j, :, c0:c1])
+
+        def weigh_grouped(engine, weights, g, j, c0, c1, tag):
+            count = (c1 - c0) // RUN
+            grouped = weighted_part(g, j, (0, KP), tag)[:, c0:c1, :].rearrange("p (c r) t -> p c t r", r=RUN)
+            values = rel[g][:, j, :, c0:c1].rearrange("p t (c r) -> p c t r", r=RUN)
+            factors = weights.unsqueeze(1).unsqueeze(3).to_broadcast([P, count, T, RUN])
+            if engine == "gpsimd":
+                nc.gpsimd.tensor_tensor(out=grouped, in0=values, in1=factors, op=MULT)
+            else:
+                nc.vector.tensor_tensor(out=grouped, in0=factors, in1=values, op=MULT)
+
+        def fuse_on_gpsimd(*parts):
+            g0 = min(part[0] for part in parts)
+            columns = weight_columns(T * g0, T * (max(part[0] for part in parts) - g0 + 1))
+            for g, j, c0, c1, tag in parts:
+                weigh_grouped("gpsimd", columns[:, T * (g - g0) : T * (g - g0 + 1)], g, j, c0, c1, tag)
+
+        def fuse_on_vector(g, j, c0, c1, tag):
+            weigh_grouped("vector", consts["weight"][:, T * g : T * (g + 1)], g, j, c0, c1, tag)
 
         def quantize_weighted(g, j, part=(0, KP)):
             cols = slice(part[0], part[1])
@@ -340,20 +372,13 @@ def tile_ghosh_price_push_s8_kernel(
             else:
                 nc.vector.tensor_copy(out=out, in_=in_)
 
-        stored = []
-
-        def result_tile():
-            tag = "wide" if len(stored) % 2 else "result"
-            stored.append(tag)
-            return work.tile([P, KP], F32, name=tag, bufs=DEPTH[tag])
-
         def index_mm(i, number):
             index_bank[i] = bank_of(number, [P, C])
             for j in range(NJ):
                 nc.tensor.matmul_mx(
                     out=index_bank[i][:],
-                    lhsT=pr_codes[:, i, j, :].bitcast(FP8X4),
-                    lhsT_scale=pr_scales[:, i, j, :],
+                    lhsT=pr_mx[i][0][:, j, :].bitcast(FP8X4),
+                    lhsT_scale=pr_mx[i][1][:, j, :],
                     rhs=b_words[:, j, :].bitcast(FP4X4),
                     rhs_scale=b_scales[:, j, :],
                     start=(j == 0),
@@ -361,7 +386,7 @@ def tile_ghosh_price_push_s8_kernel(
                 )
 
         def index_out(i, engine="scalar"):
-            result = result_tile()
+            result = buffer("result", [P, KP], F32)
             sums_out(engine, result[:], index_bank[i][:])
             nc.sync.dma_start(out=index_v[i // T][:, i % T, :], in_=result[:])
 
@@ -371,8 +396,8 @@ def tile_ghosh_price_push_s8_kernel(
             for g in range(g0, g1):
                 nc.tensor.matmul_mx(
                     out=contrast_bank[a, j][:],
-                    lhsT=con_codes[:, g, P * a : P * (a + 1)].bitcast(FP8X4),
-                    lhsT_scale=con_scales[:, g, P * a : P * (a + 1)],
+                    lhsT=con_codes[:, P * (SG * a + g) : P * (SG * a + g + 1)].bitcast(FP8X4),
+                    lhsT_scale=con_scales[:, P * (SG * a + g) : P * (SG * a + g + 1)],
                     rhs=we_codes[:, g, j, :].bitcast(FP8X4),
                     rhs_scale=we_scales[:, g, j, :],
                     start=(g == 0),
@@ -380,7 +405,7 @@ def tile_ghosh_price_push_s8_kernel(
                 )
 
         def contrast_out(a, j, engine="scalar"):
-            result = result_tile()
+            result = buffer("result", [P, KP], F32)
             sums_out(
                 engine,
                 result[:].rearrange("p (m u e) -> p m u e", u=2, e=2),
@@ -388,263 +413,242 @@ def tile_ghosh_price_push_s8_kernel(
             )
             nc.sync.dma_start(out=out_1[P * a : P * (a + 1), KP * j : KP * (j + 1)], in_=result[:])
 
-        def warm(count, source):
-            bank = bank_of(1, [P, KP])
+        def warm(count, number, source):
+            bank = bank_of(number, [P, KP])
             for k in range(count):
-                nc.tensor.matmul(bank[:], source[:, 0, 0:P], source[:, 0, :], start=True, stop=True)
+                nc.tensor.matmul(bank[:], source[:, 0:P], source[:, 0:KP], start=True, stop=True)
 
         nc.vector.memset(b_scales[:].rearrange("p j n -> p (j n)").bitcast(I32), 0)
+        nc.vector.memset(ones[:], 1.0)
         make_identity(nc, ident[:])
+        make_identity(nc, ident_bf[:])
         load_shocks(0, 1)
         nc.sync.dma_start(out=scale_kp[:], in_=shocks_scale.rearrange("o (q p t) -> p (o q) t", p=P, t=T))
-        load_shocks(1, 3)
+        load_shocks(1, 2)
+        load_shocks(2, 4)
         load_inverse(0, 0)
-        load_shocks(3, 4)
         load_inverse(0, 1)
-        load_shocks(4, 6)
-        load_inverse(1, 0)
-        load_shocks(6, 8)
+        load_shocks(4, 8)
         load_inverse(1, 1)
-        load_contrasts(0)
-        load_contrasts(1)
-        nc.sync.dma_start(out=weight_kp[:].rearrange("p (g t) -> p g t", t=T), in_=weight.rearrange("(g p t) -> p g t", p=P, t=T))
+        load_inverse(1, 0)
+        load_factors(weight_kp, weight)
         load_shocks(8, 12)
-        load_contrasts(2)
-        load_contrasts(3)
-        nc.sync.dma_start(out=base_kp[:].rearrange("p (j t) -> p j t", t=T), in_=base.rearrange("(j p t) -> p j t", p=P, t=T))
+        load_factors(base_kp, base)
+        for a in range(T):
+            load_contrasts(a)
 
-        widen(0)
-        turn_shocks(0, 2)
-        widen(1)
-        turn_shocks(1, 3)
-        widen(2)
-        turn_shocks(2, 4)
-        scale_shocks(0)
+        widen_sorted(0, 0, 1)
+        widen(0, 1, 2)
+        turn_shocks(0, 0, 0, 1)
+        turn_shocks(0, 1, 1, 2)
+        widen_sorted(1)
+        turn_shocks(1, 2)
+        for i in (2, 3):
+            widen(i)
+            turn_shocks(i, i + 1)
+        scale_shocks(0, 0, 1)
+        scale_shocks(0, 1, 2)
         scale_shocks(1)
+        scale_shocks(2, tag="group_c")
+        scale_shocks(3)
         group_inverse(0, 0, "gpsimd", 0, HALF, tag="group_a")
         group_inverse(0, 0, "scalar", HALF, KP)
-        warm(WARM_FIRST, inv_raw[0, 0])
-        widen(3)
-        turn_shocks(3, 5)
-        warm(WARM_SECOND, inv_raw[0, 1])
-        group_inverse(0, 1, "scalar", HALF, KP, tag="group_b")
-        group_inverse(0, 1, "vector", 0, HALF)
+        warm(3, 7, inv_raw[0, 0][:, 0])
+        group_inverse(0, 1, "gpsimd", 0, HALF, tag="group_b")
+        group_inverse(0, 1, "scalar", HALF, KP)
         widen(4)
-        turn_shocks(4, 6)
         widen(5)
-        quantize_shocks(0)
-        quantize_shocks(1)
+        turn_shocks(4, 0)
+        warm(1, 7, inv_raw[0, 1][:, 0])
+        turn_shocks(5, 1)
         quantize_inverse(0, 0)
+        quantize_shocks(0)
         quantize_inverse(0, 1)
+        quantize_shocks(1)
+        quantize_shocks(2)
+        group_inverse(1, 0, "gpsimd", 0, 384, tag="group_c")
+        quantize_shocks(3)
         load_baskets()
 
-        units = [(0, 0), (1, 0)]
-        move_by_pass(units, [0, 1])
-        turn_shocks(5, 7)
-        group_inverse(1, 0, "gpsimd", 0, SHARE, tag="group_a")
-        group_inverse(1, 0, "scalar", SHARE, KP)
-        scale_shocks(2, tag="handed")
-        scale_shocks(3)
+        units = [(0, 0), (1, 0), (2, 0), (3, 0)]
+        move(units, [5, 6, 7, 2])
         widen(6)
-        turn_shocks(6, 2)
+        group_inverse(1, 1, "scalar", 0, KP, tag="group_d")
         widen(7)
-        turn_shocks(7, 3)
+        group_inverse(1, 0, "scalar", 384, KP)
+        turn_shocks(6, 3)
+        turn_shocks(7, 4)
         exps(units)
-        quantize_shocks(2)
-        group_inverse(1, 1, "gpsimd", 0, P, part=(0, P), tag="handed")
-        quantize_shocks(3)
-
-        units = [(2, 0), (3, 0)]
-        move(units, [0, 1])
-        turn_contrasts(0, 4)
-        turn_contrasts(1, 5)
-        group_inverse(1, 1, "scalar", P, KP, part=(P, KP), tag="group_b")
         scale_shocks(4)
+        scale_shocks(5)
+        quantize_inverse(1, 1)
         quantize_inverse(1, 0)
-        quantize_inverse(1, 1, (0, P))
+        fuse_on_gpsimd((0, 0, 0, 352, "group_a"))
         quantize_shocks(4)
-        exps(units)
-        weigh_on_gpsimd((0, 0, 1), (1, 0, 1), (2, 0, 1))
-        quantize_inverse(1, 1, (P, KP))
-        empty_contrasts(0)
-        empty_contrasts(1)
+        quantize_shocks(5)
+
+        move_pass(0, 1, 1, 0)
+        move_pass(1, 1, 1, 1)
+        move_pass(2, 1, 1, 5)
+        move_pass(0, 1, 0)
+        move_pass(1, 1, 0)
+        move_pass(2, 1, 0)
+        move([(3, 1)], [6])
         widen(8)
         widen(9)
-        scale_shocks(5)
-        scale_shocks(6)
-
-        units = [(0, 1), (1, 1), (2, 1)]
-        move_by_pass(units, [6, 0, 1])
-        exps(units[:1])
-        move([(4, 0), (3, 1), (4, 1)], [4, 5, 7])
-        exps(units[1:])
         widen(10)
-        exps([(4, 0), (3, 1), (4, 1)])
-        weigh_on_gpsimd((3, 0, 1), (0, 1, 2), (1, 1, 2))
-        quantize_shocks(5)
-        quantize_shocks(6)
-        turn_shocks(8, 6)
+        scale_shocks(6)
+        turn_shocks(8, 7)
         turn_shocks(9, 2)
+        turn_shocks(10, 3)
+        exps([(0, 1), (1, 1), (2, 1), (3, 1)])
         scale_shocks(7)
         scale_shocks(8)
-        widen(11)
-
-        units = [(5, 0), (6, 0), (5, 1), (6, 1)]
-        move(units[:2], [0, 1])
-        spread_base(3)
-        turn_shocks(10, 6)
-        move(units[2:], [4, 5])
-        exps(units)
+        quantize_shocks(6)
+        fuse_on_gpsimd((0, 0, 352, KP, None), (0, 1, 0, 192, "group_b"))
         quantize_shocks(7)
-        group_weighted(0, 0, "vector", tag="group_a")
-        weigh_on_gpsimd((2, 1, 2), (3, 1, 2), (4, 0, 2))
         quantize_shocks(8)
-        turn_shocks(11, 7)
-        turn_contrasts(2, 0)
+
+        units = [(4, 0), (4, 1), (5, 0), (5, 1)]
+        move(units, [4, 0, 1, 5])
+        widen(11)
         scale_shocks(9)
+        turn_shocks(11, 6)
+        spread_base(7)
+        turn_contrasts(0, 2)
+        exps(units)
+        empty_contrasts(0)
         scale_shocks(10)
         scale_shocks(11)
-        empty_contrasts(2)
-
-        units = [(7, 0), (8, 0), (7, 1), (8, 1)]
-        move(units, [1, 2, 4, 5])
-        exps(units)
         quantize_shocks(9)
         quantize_shocks(10)
         quantize_shocks(11)
-        quantize_contrasts(0)
-        weigh_on_gpsimd((5, 0, 1), (6, 0, 1), (7, 0, 1))
-        quantize_weighted(0, 0)
-        turns(0, (6, 0))
-        turn_contrasts(3, 7)
-        prices(0)
-        price_early(5)
-        group_weighted(0, 1, "scalar", 0, HALF, tag="group_b")
-        empty_contrasts(3)
 
-        units = [(9, 0), (10, 0), (9, 1), (11, 0)]
-        move(units, [1, 2, 4, 5])
-        exps(units[:3])
-        group_weighted(1, 0, "scalar", 0, HALF, tag="group_a")
-        quantize_priced(0)
+        units = [(6, 0), (7, 0), (6, 1), (7, 1)]
+        move(units, [4, 0, 1, 5])
+        turn_contrasts(1, 3)
+        turn_contrasts(2, 6)
+        turn_contrasts(3, 2)
+        exps(units)
+        fuse_on_gpsimd((1, 0, 0, 352, "group_c"))
+        quantize_weighted(0, 0)
+        for n in (1, 2, 3):
+            empty_contrasts(n)
+        for i in (0, 1, 2):
+            price_early(i)
+
+        units = [(8, 0), (9, 0), (10, 0), (11, 0)]
+        move(units, [4, 0, 1, 5])
+        place_weights(2)
+        turn_early(0, 3)
+        turn_early(1, 6)
+        exps(units)
+        turn_early(2, 4)
+        quantize_contrasts(0)
         quantize_contrasts(1)
-        turns(1, (6, 0))
-        exps(units[3:])
-        weigh_on_gpsimd((8, 0, 1), (9, 0, 1), (10, 0, 1), (11, 0, 1))
+        fuse_on_gpsimd((1, 0, 352, KP, None), (0, 1, 192, KP, None))
         quantize_contrasts(2)
         quantize_contrasts(3)
-        turn_contrasts(4, 7)
-        prices(1)
-        empty_contrasts(4, "vector")
-        price_early(6)
-        price_early(7)
+        for i in (0, 1, 2):
+            empty_early(i)
+        fuse_on_vector(1, 1, 0, KP, "group_a")
+        fuse_on_vector(2, 0, 0, KP, "group_d")
 
-        units = [(10, 1), (11, 1)]
-        move(units, [1, 2])
-        relatives(10, 1)
-        group_weighted(1, 0, "scalar", HALF, KP)
-        relatives(11, 1)
-        turn_early(5, 5)
-        turn_contrasts(5, 7)
-        index_mm(0, 4)
-        turns(2, (6, 0))
-        turn_early(6, 1)
-        empty_early(5)
-        index_out(0)
+        units = [(8, 1), (9, 1), (10, 1), (11, 1)]
+        move(units, [0, 1, 5, 3])
+        turn_contrasts(4, 6)
+        turn_contrasts(5, 4)
+        exps(units)
+        turns(3, (0, 1))
+        empty_contrasts(4)
         empty_contrasts(5)
-        empty_early(6)
+        quantize_priced(0)
         quantize_priced(1)
         quantize_weighted(1, 0)
-        quantize_priced(5)
-        group_weighted(2, 0, "vector", tag="group_c")
-        quantize_contrasts(4)
-        quantize_priced(6)
-        quantize_contrasts(5)
-        weigh_on_gpsimd((5, 1, 2), (6, 1, 2), (7, 1, 2))
         quantize_weighted(2, 0)
-
-        index_mm(1, 2)
-        contrast_mm(0, 0, 5, 0, 2)
-        contrast_mm(1, 0, 4, 0, 2)
-        index_mm(5, 7)
-        index_out(1)
-        turn_early(7, 1)
-        turns(3, (3, 2))
-        index_out(5)
-        empty_early(7)
-        prices(2)
+        quantize_priced(2)
+        quantize_contrasts(4)
+        quantize_contrasts(5)
+        weigh_on_gpsimd((8, 1, 2), (9, 1, 2), (10, 1, 2), (11, 1, 2))
+        quantize_weighted(0, 1)
+        price_early(4)
+        price_early(5)
         prices(3)
-        group_weighted(0, 1, "scalar", HALF, KP)
 
-        index_mm(6, 7)
-        contrast_mm(2, 0, 1, 0, 2)
-        contrast_mm(0, 0, 5, 2, 3)
-        contrast_mm(1, 0, 4, 2, 3)
-        contrast_mm(2, 0, 1, 2, 3)
-        contrast_mm(3, 0, 6)
-        index_out(6)
+        index_mm(0, 2)
+        index_mm(1, 5)
+        contrast_mm(0, 0, 3)
+        index_out(0)
+        index_out(1)
+        contrast_mm(1, 0, 2)
+        index_mm(2, 5)
+        contrast_mm(2, 0, 6)
+        contrast_mm(3, 0, 4)
         contrast_out(0, 0)
         contrast_out(1, 0)
-        turns(4, (0, 3))
-        turns(8, (2, 5))
+        index_out(2)
+        turn_early(4, 3)
+        turn_early(5, 2)
         contrast_out(2, 0)
-        group_weighted(1, 1, "scalar", 0, HALF, tag="group_a")
+        turns(8, (5, 6))
         contrast_out(3, 0)
-        quantize_priced(7)
-        quantize_pair(2)
-        weigh_on_gpsimd((8, 1, 2), (9, 1, 2), (10, 1, 2))
-        quantize_weighted(0, 1)
-        prices(4)
+        empty_early(4)
+        empty_early(5)
+        group_weighted(2, 1, "scalar", tag="group_c")
+        quantize_weighted(1, 1)
+        quantize_priced(3)
+        quantize_priced(4)
+        quantize_priced(5)
+        price_early(6)
+        price_early(7)
         prices(8)
 
-        index_mm(7, 7)
-        index_mm(2, 4)
-        contrast_mm(0, 1, 1, 0, 1)
-        contrast_mm(1, 1, 6, 0, 1)
-        index_mm(3, 0)
-        group_weighted(1, 1, "scalar", HALF, KP)
-        index_out(7)
-        index_out(2)
+        contrast_mm(0, 1, 4, 0, 2)
+        contrast_mm(1, 1, 0, 0, 2)
+        index_mm(3, 1)
+        index_mm(4, 3)
+        index_mm(5, 2)
         index_out(3)
-        turns(9, (3, 2))
-        turns(10, (5, 7))
-        weigh_on_vector(11, 1)
-        quantize_priced(4)
-        quantize_priced(8)
-        group_weighted(2, 1, "gpsimd", 0, HALF, part=(0, HALF), tag="handed")
-        quantize_weighted(1, 1)
-        group_weighted(2, 1, "scalar", HALF, KP, part=(HALF, KP), tag="group_b")
-        prices(9)
-
-        index_mm(4, 4)
-        index_mm(8, 0)
-        contrast_mm(0, 1, 1, 1, 2)
-        contrast_mm(1, 1, 6, 1, 2)
-        turns(11, (3, 2))
         index_out(4)
-        index_out(8)
-        price(10, 0)
-        quantize_priced(9)
-        quantize_weighted(2, 1, (HALF, KP))
-        quantize_weighted(2, 1, (0, HALF))
-        price(10, 1)
-        price(11, 0)
-        quantize_priced(10)
-        price(11, 1)
-        quantize_priced(11, 0, 1)
-        quantize_priced(11, 1, 2)
+        turn_early(6, 1)
+        turn_early(7, 3)
+        index_out(5)
+        empty_early(6)
+        empty_early(7)
+        quantize_weighted(2, 1)
+        quantize_priced(8)
+        quantize_priced(6)
+        quantize_priced(7)
+        price_early(9)
 
-        index_mm(9, 5)
-        contrast_mm(0, 1, 1, 2, 3)
-        contrast_mm(1, 1, 6, 2, 3)
-        contrast_mm(2, 1, 4)
-        contrast_mm(3, 1, 0)
-        index_mm(10, 7)
-        index_mm(11, 3)
-        index_out(9)
+        contrast_mm(2, 1, 5, 0, 2)
+        contrast_mm(0, 1, 4, 2, 3)
+        contrast_mm(1, 1, 0, 2, 3)
+        contrast_mm(2, 1, 5, 2, 3)
+        index_mm(8, 6)
+        index_mm(6, 2)
+        turns(10, (1, 3))
         contrast_out(0, 1)
         contrast_out(1, 1)
+        turn_early(9, 4)
         contrast_out(2, 1)
+        index_out(8)
+        empty_early(9)
+        index_out(6)
+        prices(10)
+        turns(11, (7, 0))
+        prices(11)
+        quantize_priced(10)
+        quantize_priced(9)
+        quantize_priced(11)
+
+        index_mm(7, 5)
+        contrast_mm(3, 1, 6)
+        index_mm(10, 2)
+        index_mm(9, 1)
+        index_mm(11, 3)
+        index_out(7)
         contrast_out(3, 1)
-        index_out(10, "vector")
+        index_out(10)
+        index_out(9, "vector")
         index_out(11)

@@ -29,6 +29,7 @@ NJ = N // KP
 TILES = SG * T
 LINE = 8
 RUN = 4
+PAIR = 2
 
 DEPTH = {
     "wide": 4, "sh_group": 4, "con_group": 4, "rel": 3, "priced": 6, "early": 4, "scaled": 1, "columns": 4, "result": 8,
@@ -342,10 +343,10 @@ def tile_ghosh_price_push_s8_kernel(
             interleave(engine, weighted_part(g, j, part, tag)[:, c0 - part[0] : c1 - part[0], :], scaled[g][:, j, :, c0:c1])
 
         def weigh_grouped(engine, weights, g, j, c0, c1, tag):
-            count = (c1 - c0) // RUN
-            grouped = weighted_part(g, j, (0, KP), tag)[:, c0:c1, :].rearrange("p (c r) t -> p c t r", r=RUN)
-            values = rel[g][:, j, :, c0:c1].rearrange("p t (c r) -> p c t r", r=RUN)
-            factors = weights.unsqueeze(1).unsqueeze(3).to_broadcast([P, count, T, RUN])
+            count = (c1 - c0) // PAIR
+            grouped = weighted_part(g, j, (0, KP), tag)[:, c0:c1, :].rearrange("p (c r) t -> p c t r", r=PAIR)
+            values = rel[g][:, j, :, c0:c1].rearrange("p t (c r) -> p c t r", r=PAIR)
+            factors = weights.unsqueeze(1).unsqueeze(3).to_broadcast([P, count, T, PAIR])
             if engine == "gpsimd":
                 nc.gpsimd.tensor_tensor(out=grouped, in0=values, in1=factors, op=MULT)
             else:

@@ -28,12 +28,11 @@ KQ = N // KP
 NJ = N // KP
 TILES = SG * T
 LINE = 8
-RUN = 4
 PAIR = 2
 
 DEPTH = {
-    "wide": 4, "sh_group": 4, "con_group": 4, "rel": 3, "priced": 6, "early": 4, "scaled": 1, "columns": 4, "result": 8,
-    "codes": TILES, "scales": TILES, "group_a": 1, "group_b": 1, "group_c": 1, "group_d": 1, "group_e": 1,
+    "wide": 4, "sh_group": 3, "con_group": 2, "priced": 4, "early": 4, "scaled": 2, "columns": 4, "result": 9,
+    "codes": TILES // 2, "scales": TILES // 2, "group_a": 1, "group_b": 1, "group_c": 1, "group_d": 1,
 }
 
 
@@ -121,11 +120,16 @@ def tile_ghosh_price_push_s8_kernel(
         def quantize(codes, scales, grouped):
             nc.vector.quantize_mx(out=codes.bitcast(FP8X4), scales=scales, in_=grouped)
 
-        def tile_codes():
-            return buffer("codes", [P, 2, P], U32), buffer("scales", [P, 2, P], U8)
-
-        def quantize_tile(pair, grouped):
-            quantize(pair[0][:].rearrange("p q r -> p (q r)"), pair[1][:].rearrange("p q r -> p (q r)"), grouped)
+        def quantize_tiles(mx, grouped, i0, i1):
+            k = i0 // 2
+            if k not in mx:
+                mx[k] = (buffer("codes", [P, 2, 2, P], U32), buffer("scales", [P, 2, 2, P], U8))
+            part = slice(i0 - 2 * k, i1 - 2 * k)
+            quantize(
+                mx[k][0][:, part].rearrange("p i q r -> p (i q r)"),
+                mx[k][1][:, part].rearrange("p i q r -> p (i q r)"),
+                grouped[k][:, part].rearrange("p i n -> p (i n)"),
+            )
 
         sh_wide, sh_bank, sh_group, sh_mx = {}, {}, {}, {}
 
@@ -161,20 +165,19 @@ def tile_ghosh_price_push_s8_kernel(
                         part = words[:, HALF * q + u : HALF * (q + 1) : 2]
                     nc.tensor.transpose(sh_bank[i, q0][:, u, q - q0, :], part, ident[:])
 
-        def scale_shocks(i, q0=0, q1=KQ, tag="sh_group"):
-            if i not in sh_group:
-                sh_group[i] = buffer(tag, [P, N], BF16)
+        def scale_shocks(i, q0=0, q1=KQ):
+            if i // 2 not in sh_group:
+                sh_group[i // 2] = buffer("sh_group", [P, 2, N], BF16)
             halves = sh_bank[i, q0][:].rearrange("p u q r -> p (u q r)").bitcast(BF16)
             nc.vector.tensor_tensor(
-                out=sh_group[i][:, KP * q0 : KP * q1].rearrange("p (q r u e) -> p q r u e", r=P, u=2, e=2),
+                out=sh_group[i // 2][:, i % 2, KP * q0 : KP * q1].rearrange("p (q r u e) -> p q r u e", r=P, u=2, e=2),
                 in0=halves.rearrange("p (u q r e) -> p q r u e", r=P, u=2, e=2),
                 in1=scale_kp[:, q0:q1].rearrange("p q (u e) -> p q u e", u=2).unsqueeze(2).to_broadcast([P, q1 - q0, P, 2, 2]),
                 op=MULT,
             )
 
-        def quantize_shocks(i):
-            sh_mx[i] = tile_codes()
-            quantize_tile(sh_mx[i], sh_group[i][:])
+        def quantize_shocks(i0, count=1):
+            quantize_tiles(sh_mx, sh_group, i0, i0 + count)
 
         con_bank, con_group = {}, {}
 
@@ -194,12 +197,13 @@ def tile_ghosh_price_push_s8_kernel(
             )
 
         def empty_contrasts(n, engine="scalar"):
-            con_group[n] = buffer("con_group", [P, 2 * KP], BF16)
-            empty_words(con_group[n][:], con_bank[n][:], engine)
+            if n % 2 == 0:
+                con_group[n // 2] = buffer("con_group", [P, 2, 2 * KP], BF16)
+            empty_words(con_group[n // 2][:, n % 2], con_bank[n][:], engine)
 
-        def quantize_contrasts(n):
-            cols = slice(HALF * n, HALF * (n + 1))
-            quantize(con_codes[:, cols], con_scales[:, cols], con_group[n][:])
+        def quantize_contrasts(k):
+            cols = slice(KP * k, KP * (k + 1))
+            quantize(con_codes[:, cols], con_scales[:, cols], con_group[k][:].rearrange("p h n -> p (h n)"))
 
         inv_part = {}
 
@@ -219,8 +223,8 @@ def tile_ghosh_price_push_s8_kernel(
                 mv_bank[i, j] = bank_of(number, [P, KP])
             nc.tensor.matmul_mx(
                 out=mv_bank[i, j][:],
-                lhsT=sh_mx[i][0][:, q, :].bitcast(FP8X4),
-                lhsT_scale=sh_mx[i][1][:, q, :],
+                lhsT=sh_mx[i // 2][0][:, i % 2, q, :].bitcast(FP8X4),
+                lhsT_scale=sh_mx[i // 2][1][:, i % 2, q, :],
                 rhs=inv_codes[:, j, q, :].bitcast(FP8X4),
                 rhs_scale=inv_scales[:, j, q, :],
                 start=number is not None,
@@ -259,13 +263,13 @@ def tile_ghosh_price_push_s8_kernel(
                 turn(i, j, banks[j])
 
         def priced_tile(i, tag="priced"):
-            if i not in priced:
-                priced[i] = buffer(tag, [P, NJ, P, T], BF16)
-            return priced[i]
+            if i // 2 not in priced:
+                priced[i // 2] = buffer(tag, [P, 2, N], BF16)
+            return priced[i // 2][:, i % 2]
 
         def price(i, j):
             nc.vector.tensor_tensor(
-                out=priced_tile(i)[:, j],
+                out=priced_tile(i)[:, KP * j : KP * (j + 1)].rearrange("p (m v) -> p m v", v=T),
                 in0=tr_bank[i, j][:].rearrange("p v m -> p m v"),
                 in1=base_kp[:, T * j : T * (j + 1)].unsqueeze(1).to_broadcast([P, P, T]),
                 op=MULT,
@@ -287,16 +291,22 @@ def tile_ghosh_price_push_s8_kernel(
             consts["weight"] = bank_of(number, [P, TILES])
             nc.tensor.matmul(consts["weight"][:], ident_bf[:], weight_kp[:], start=True, stop=True)
 
+        def price_before(engine, i, row, tag):
+            early[i] = buffer(tag, [P, NJ, KP], BF16)
+            out = early[i][:].rearrange("p j (c e) -> p j c e", e=2)
+            row = row.rearrange("p (j c e) -> p j c e", j=NJ, e=2)
+            values = rel[i // T][:, :, i % T, :].rearrange("p j (e c) -> p j c e", e=2)
+            engine.tensor_tensor(out=out, in0=row, in1=values, op=MULT)
+
         def price_early(i):
-            early[i] = buffer("early", [P, NJ, KP], BF16)
-            row = consts["base"][:].rearrange("p a m -> p (a m)").bitcast(BF16)
-            for j in range(NJ):
-                nc.vector.tensor_tensor(
-                    out=early[i][:, j].rearrange("p (c r e) -> p c e r", r=RUN, e=2),
-                    in0=row[:, KP * j : KP * (j + 1)].rearrange("p (c r e) -> p c e r", r=RUN, e=2),
-                    in1=unit_rel(i, j).rearrange("p (e c r) -> p c e r", r=RUN, e=2),
-                    op=MULT,
-                )
+            price_before(nc.vector, i, consts["base"][:].rearrange("p a m -> p (a m)").bitcast(BF16), "early")
+
+        def keep_base():
+            consts["row"] = keep.tile([P, N], BF16, name="base_row")
+            nc.scalar.copy(out=consts["row"][:], in_=consts["base"][:].rearrange("p a m -> p (a m)").bitcast(BF16))
+
+        def price_early_on_gpsimd(i, tag):
+            price_before(nc.gpsimd, i, consts["row"][:], tag)
 
         def turn_early(i, number):
             tr_bank[i] = bank_of(number, [P, NJ, 2, P])
@@ -304,35 +314,31 @@ def tile_ghosh_price_push_s8_kernel(
             for a in range(2 * NJ):
                 nc.tensor.transpose(tr_bank[i][:, a // 2, a % 2, :], words[:, P * a : P * (a + 1)], ident[:])
 
-        def empty_early(i, engine="scalar"):
-            empty_words(priced_tile(i)[:].rearrange("p j m v -> p (j m v)"), tr_bank[i][:], engine)
+        def empty_early(i, engine="scalar", tag="priced"):
+            empty_words(priced_tile(i, tag), tr_bank[i][:], engine)
 
-        def quantize_priced(i):
-            pr_mx[i] = tile_codes()
-            quantize_tile(pr_mx[i], priced[i][:].rearrange("p j m v -> p (j m v)"))
+        def quantize_priced(i0, count=1):
+            quantize_tiles(pr_mx, priced, i0, i0 + count)
 
-        def planes(g):
-            if g not in scaled:
-                scaled[g] = buffer("scaled", [P, NJ, T, KP], BF16)
-            return scaled[g]
+        def planes(g, j):
+            if (g, j) not in scaled:
+                scaled[g, j] = buffer("scaled", [P, T, KP], BF16)
+            return scaled[g, j]
 
         def weight_columns(i0, count):
             columns = buffer("columns", [P, count], F32)
             nc.vector.tensor_copy(out=columns[:], in_=weight_kp[:, i0 : i0 + count])
             return columns
 
-        def weigh_on_gpsimd(*units):
-            i0 = min(unit[0] for unit in units)
-            columns = weight_columns(i0, max(unit[0] for unit in units) - i0 + 1)
-            for i, j0, j1 in units:
-                nc.gpsimd.tensor_scalar(
-                    out=planes(i // T)[:, j0:j1, i % T, :],
-                    in0=rel[i // T][:, j0:j1, i % T, :],
-                    scalar1=columns[:, i - i0 : i - i0 + 1],
-                    scalar2=0.0,
-                    op0=MULT,
-                    op1=ADD,
-                )
+        def weigh(columns, i0, i, j):
+            nc.gpsimd.tensor_scalar(
+                out=planes(i // T, j)[:, i % T, :],
+                in0=unit_rel(i, j),
+                scalar1=columns[:, i - i0 : i - i0 + 1],
+                scalar2=0.0,
+                op0=MULT,
+                op1=ADD,
+            )
 
         def weighted_part(g, j, part, tag):
             if (g, j, part) not in weighted:
@@ -340,7 +346,7 @@ def tile_ghosh_price_push_s8_kernel(
             return weighted[g, j, part]
 
         def group_weighted(g, j, engine, c0=0, c1=KP, part=(0, KP), tag=None):
-            interleave(engine, weighted_part(g, j, part, tag)[:, c0 - part[0] : c1 - part[0], :], scaled[g][:, j, :, c0:c1])
+            interleave(engine, weighted_part(g, j, part, tag)[:, c0 - part[0] : c1 - part[0], :], scaled[g, j][:, :, c0:c1])
 
         def weigh_grouped(engine, weights, g, j, c0, c1, tag):
             count = (c1 - c0) // PAIR
@@ -352,11 +358,14 @@ def tile_ghosh_price_push_s8_kernel(
             else:
                 nc.vector.tensor_tensor(out=grouped, in0=factors, in1=values, op=MULT)
 
-        def fuse_on_gpsimd(*parts):
-            g0 = min(part[0] for part in parts)
-            columns = weight_columns(T * g0, T * (max(part[0] for part in parts) - g0 + 1))
+        def on_gpsimd(parts, units):
+            groups = [part[0] for part in parts] + [i // T for i, j in units]
+            i0 = T * min(groups)
+            columns = weight_columns(i0, T * (max(groups) + 1) - i0)
             for g, j, c0, c1, tag in parts:
-                weigh_grouped("gpsimd", columns[:, T * (g - g0) : T * (g - g0 + 1)], g, j, c0, c1, tag)
+                weigh_grouped("gpsimd", columns[:, T * g - i0 : T * (g + 1) - i0], g, j, c0, c1, tag)
+            for i, j in units:
+                weigh(columns, i0, i, j)
 
         def fuse_on_vector(g, j, c0, c1, tag):
             weigh_grouped("vector", consts["weight"][:, T * g : T * (g + 1)], g, j, c0, c1, tag)
@@ -378,8 +387,8 @@ def tile_ghosh_price_push_s8_kernel(
             for j in range(NJ):
                 nc.tensor.matmul_mx(
                     out=index_bank[i][:],
-                    lhsT=pr_mx[i][0][:, j, :].bitcast(FP8X4),
-                    lhsT_scale=pr_mx[i][1][:, j, :],
+                    lhsT=pr_mx[i // 2][0][:, i % 2, j, :].bitcast(FP8X4),
+                    lhsT_scale=pr_mx[i // 2][1][:, i % 2, j, :],
                     rhs=b_words[:, j, :].bitcast(FP4X4),
                     rhs_scale=b_scales[:, j, :],
                     start=(j == 0),
@@ -391,18 +400,22 @@ def tile_ghosh_price_push_s8_kernel(
             sums_out(engine, result[:], index_bank[i][:])
             nc.sync.dma_start(out=index_v[i // T][:, i % T, :], in_=result[:])
 
-        def contrast_mm(a, j, number, g0=0, g1=SG):
-            if g0 == 0:
+        summed = {}
+
+        def contrast_mm(a, j, number, groups=range(SG)):
+            if (a, j) not in summed:
                 contrast_bank[a, j] = bank_of(number, [P, KP])
-            for g in range(g0, g1):
+                summed[a, j] = []
+            for g in groups:
+                summed[a, j].append(g)
                 nc.tensor.matmul_mx(
                     out=contrast_bank[a, j][:],
                     lhsT=con_codes[:, P * (SG * a + g) : P * (SG * a + g + 1)].bitcast(FP8X4),
                     lhsT_scale=con_scales[:, P * (SG * a + g) : P * (SG * a + g + 1)],
                     rhs=we_codes[:, g, j, :].bitcast(FP8X4),
                     rhs_scale=we_scales[:, g, j, :],
-                    start=(g == 0),
-                    stop=(g == SG - 1),
+                    start=len(summed[a, j]) == 1,
+                    stop=len(summed[a, j]) == SG,
                 )
 
         def contrast_out(a, j, engine="scalar"):
@@ -450,25 +463,22 @@ def tile_ghosh_price_push_s8_kernel(
         scale_shocks(0, 0, 1)
         scale_shocks(0, 1, 2)
         scale_shocks(1)
-        scale_shocks(2, tag="group_c")
+        scale_shocks(2)
         scale_shocks(3)
         group_inverse(0, 0, "gpsimd", 0, HALF, tag="group_a")
         group_inverse(0, 0, "scalar", HALF, KP)
-        warm(3, 7, inv_raw[0, 0][:, 0])
+        warm(4, 7, inv_raw[0, 0][:, 0])
         group_inverse(0, 1, "gpsimd", 0, HALF, tag="group_b")
         group_inverse(0, 1, "scalar", HALF, KP)
         widen(4)
         widen(5)
         turn_shocks(4, 0)
-        warm(1, 7, inv_raw[0, 1][:, 0])
         turn_shocks(5, 1)
         quantize_inverse(0, 0)
-        quantize_shocks(0)
+        quantize_shocks(0, 2)
         quantize_inverse(0, 1)
-        quantize_shocks(1)
-        quantize_shocks(2)
-        group_inverse(1, 0, "gpsimd", 0, 384, tag="group_c")
-        quantize_shocks(3)
+        group_inverse(1, 0, "gpsimd", 0, 384, tag="group_b")
+        quantize_shocks(2, 2)
         load_baskets()
 
         units = [(0, 0), (1, 0), (2, 0), (3, 0)]
@@ -484,9 +494,8 @@ def tile_ghosh_price_push_s8_kernel(
         scale_shocks(5)
         quantize_inverse(1, 1)
         quantize_inverse(1, 0)
-        fuse_on_gpsimd((0, 0, 0, 352, "group_a"))
-        quantize_shocks(4)
-        quantize_shocks(5)
+        on_gpsimd([(0, 0, 0, 320, "group_a")], [])
+        quantize_shocks(4, 2)
 
         move_pass(0, 1, 1, 0)
         move_pass(1, 1, 1, 1)
@@ -505,9 +514,8 @@ def tile_ghosh_price_push_s8_kernel(
         exps([(0, 1), (1, 1), (2, 1), (3, 1)])
         scale_shocks(7)
         scale_shocks(8)
-        quantize_shocks(6)
-        fuse_on_gpsimd((0, 0, 352, KP, None), (0, 1, 0, 192, "group_b"))
-        quantize_shocks(7)
+        quantize_shocks(6, 2)
+        on_gpsimd([(0, 0, 320, KP, None)], [(0, 1)])
         quantize_shocks(8)
 
         units = [(4, 0), (4, 1), (5, 0), (5, 1)]
@@ -518,12 +526,12 @@ def tile_ghosh_price_push_s8_kernel(
         spread_base(7)
         turn_contrasts(0, 2)
         exps(units)
+        keep_base()
         empty_contrasts(0)
         scale_shocks(10)
         scale_shocks(11)
         quantize_shocks(9)
-        quantize_shocks(10)
-        quantize_shocks(11)
+        quantize_shocks(10, 2)
 
         units = [(6, 0), (7, 0), (6, 1), (7, 1)]
         move(units, [4, 0, 1, 5])
@@ -531,7 +539,7 @@ def tile_ghosh_price_push_s8_kernel(
         turn_contrasts(2, 6)
         turn_contrasts(3, 2)
         exps(units)
-        fuse_on_gpsimd((1, 0, 0, 352, "group_c"))
+        on_gpsimd([(1, 0, 0, 320, "group_c")], [])
         quantize_weighted(0, 0)
         for n in (1, 2, 3):
             empty_contrasts(n)
@@ -540,116 +548,118 @@ def tile_ghosh_price_push_s8_kernel(
 
         units = [(8, 0), (9, 0), (10, 0), (11, 0)]
         move(units, [4, 0, 1, 5])
-        place_weights(2)
         turn_early(0, 3)
         turn_early(1, 6)
+        turn_early(2, 2)
         exps(units)
-        turn_early(2, 4)
         quantize_contrasts(0)
+        on_gpsimd([(1, 0, 320, KP, None)], [])
         quantize_contrasts(1)
-        fuse_on_gpsimd((1, 0, 352, KP, None), (0, 1, 192, KP, None))
-        quantize_contrasts(2)
-        quantize_contrasts(3)
         for i in (0, 1, 2):
             empty_early(i)
-        fuse_on_vector(1, 1, 0, KP, "group_a")
-        fuse_on_vector(2, 0, 0, KP, "group_d")
+        price_early(3)
+        price_early(4)
+        on_gpsimd([], [(1, 1), (2, 1), (3, 1)])
+        quantize_priced(0, 2)
 
         units = [(8, 1), (9, 1), (10, 1), (11, 1)]
-        move(units, [0, 1, 5, 3])
-        turn_contrasts(4, 6)
-        turn_contrasts(5, 4)
+        move(units, [4, 0, 1, 5])
+        place_weights(3)
+        fuse_on_vector(2, 0, 0, KP, "group_d")
         exps(units)
-        turns(3, (0, 1))
+        turn_contrasts(4, 6)
+        turn_contrasts(5, 2)
+        turn_early(3, 4)
+        turn_early(4, 0)
         empty_contrasts(4)
         empty_contrasts(5)
-        quantize_priced(0)
-        quantize_priced(1)
+        empty_early(3)
+        empty_early(4)
         quantize_weighted(1, 0)
         quantize_weighted(2, 0)
-        quantize_priced(2)
-        quantize_contrasts(4)
-        quantize_contrasts(5)
-        weigh_on_gpsimd((8, 1, 2), (9, 1, 2), (10, 1, 2), (11, 1, 2))
-        quantize_weighted(0, 1)
-        price_early(4)
+        quantize_priced(2, 2)
+        quantize_priced(4)
+        on_gpsimd([], [(8, 1), (9, 1), (10, 1), (11, 1)])
+        quantize_contrasts(2)
         price_early(5)
-        prices(3)
+        fuse_on_vector(1, 1, 0, KP, "group_a")
 
-        index_mm(0, 2)
+        index_mm(0, 1)
         index_mm(1, 5)
-        contrast_mm(0, 0, 3)
+        for g in range(SG):
+            contrast_mm(0, 0, 6, [g])
+            contrast_mm(1, 0, 2, [g])
+        index_mm(2, 4)
+        index_mm(3, 0)
         index_out(0)
         index_out(1)
-        contrast_mm(1, 0, 2)
-        index_mm(2, 5)
-        contrast_mm(2, 0, 6)
-        contrast_mm(3, 0, 4)
+        contrast_mm(2, 0, 1)
+        contrast_mm(3, 0, 5)
         contrast_out(0, 0)
+        group_weighted(0, 1, "scalar", 0, HALF, tag="group_b")
         contrast_out(1, 0)
+        index_mm(4, 6)
         index_out(2)
-        turn_early(4, 3)
-        turn_early(5, 2)
-        contrast_out(2, 0)
-        turns(8, (5, 6))
-        contrast_out(3, 0)
-        empty_early(4)
+        index_out(3)
+        group_weighted(0, 1, "scalar", HALF, KP)
+        turn_early(5, 4)
+        turns(8, (2, 0))
         empty_early(5)
-        group_weighted(2, 1, "scalar", tag="group_c")
+        contrast_out(2, 0)
+        contrast_out(3, 0)
+        index_out(4)
         quantize_weighted(1, 1)
-        quantize_priced(3)
-        quantize_priced(4)
+        quantize_weighted(0, 1)
+        price_early_on_gpsimd(9, "group_b")
         quantize_priced(5)
+        group_weighted(2, 1, "scalar", tag="group_c")
+        prices(8)
         price_early(6)
         price_early(7)
-        prices(8)
 
-        contrast_mm(0, 1, 4, 0, 2)
-        contrast_mm(1, 1, 0, 0, 2)
-        index_mm(3, 1)
-        index_mm(4, 3)
-        index_mm(5, 2)
-        index_out(3)
-        index_out(4)
-        turn_early(6, 1)
-        turn_early(7, 3)
+        contrast_mm(0, 1, 3, [1])
+        contrast_mm(1, 1, 1, [1])
+        contrast_mm(0, 1, 3, [0])
+        contrast_mm(1, 1, 1, [0])
+        index_mm(5, 4)
+        contrast_mm(2, 1, 5, [1, 0])
+        turns(10, (2, 0))
+        turn_early(6, 6)
         index_out(5)
+        turn_early(9, 4)
+        turn_early(7, 7)
         empty_early(6)
+        empty_early(9)
         empty_early(7)
         quantize_weighted(2, 1)
-        quantize_priced(8)
         quantize_priced(6)
+        quantize_priced(8, 2)
         quantize_priced(7)
-        price_early(9)
+        prices(10)
 
-        contrast_mm(2, 1, 5, 0, 2)
-        contrast_mm(0, 1, 4, 2, 3)
-        contrast_mm(1, 1, 0, 2, 3)
-        contrast_mm(2, 1, 5, 2, 3)
-        index_mm(8, 6)
-        index_mm(6, 2)
-        turns(10, (1, 3))
+        contrast_mm(0, 1, 3, [2])
+        contrast_mm(1, 1, 1, [2])
+        contrast_mm(2, 1, 5, [2])
+        index_mm(6, 6)
         contrast_out(0, 1)
         contrast_out(1, 1)
-        turn_early(9, 4)
+        turns(11, (4, 7))
         contrast_out(2, 1)
-        index_out(8)
-        empty_early(9)
         index_out(6)
-        prices(10)
-        turns(11, (7, 0))
-        prices(11)
+        price(11, 0)
         quantize_priced(10)
-        quantize_priced(9)
+        price(11, 1)
         quantize_priced(11)
 
-        index_mm(7, 5)
-        contrast_mm(3, 1, 6)
-        index_mm(10, 2)
+        index_mm(8, 3)
         index_mm(9, 1)
-        index_mm(11, 3)
+        index_mm(7, 5)
+        contrast_mm(3, 1, 2)
+        index_mm(10, 0)
+        index_mm(11, 6)
+        index_out(8)
+        index_out(9)
         index_out(7)
-        contrast_out(3, 1)
+        contrast_out(3, 1, "vector")
         index_out(10)
-        index_out(9, "vector")
-        index_out(11)
+        index_out(11, "vector")

@@ -27,11 +27,12 @@ SG = S // KP
 KQ = N // KP
 NJ = N // KP
 TILES = SG * T
+GROUP_BYTES = 4 * NJ * T * KP
 LINE = 8
 PAIR = 2
 
 DEPTH = {
-    "wide": 4, "sh_group": 3, "con_group": 2, "priced": 4, "early": 4, "scaled": 2, "columns": 4, "result": 9,
+    "wide": 7, "sh_group": 3, "con_group": 2, "priced": 4, "early": 4, "scaled": 2, "columns": 4, "result": 6,
     "codes": TILES // 2, "scales": TILES // 2, "group_a": 1, "group_b": 1, "group_c": 1, "group_d": 1,
 }
 
@@ -43,6 +44,7 @@ def tile_ghosh_price_push_s8_kernel(
     with ExitStack() as ctx:
         keep = ctx.enter_context(tc.tile_pool(name="keep", bufs=1))
         work = ctx.enter_context(tc.tile_pool(name="work", bufs=3))
+        shared = ctx.enter_context(tc.tile_pool(name="shared", bufs=1))
         psum = ctx.enter_context(tc.psum_pool(name="psum", bufs=1))
         ctx.enter_context(tc.manual_schedule())
 
@@ -236,7 +238,7 @@ def tile_ghosh_price_push_s8_kernel(
                 move_pass(i, j, 0, number)
                 move_pass(i, j, 1)
 
-        rel = [keep.tile([P, NJ, T, KP], F32, name="rel%d" % g) for g in range(SG)]
+        rel = [shared.tile([P, NJ, T, KP], F32, name="rel%d" % g, offset=GROUP_BYTES * g) for g in range(SG)]
 
         def unit_rel(i, j):
             return rel[i // T][:, j, i % T, :]
@@ -382,6 +384,18 @@ def tile_ghosh_price_push_s8_kernel(
             else:
                 nc.vector.tensor_copy(out=out, in_=in_)
 
+        stored = []
+
+        def result_tile():
+            k = len(stored)
+            stored.append(k)
+            shelf, slot = divmod(k, NJ * T + 6)
+            if slot >= NJ * T:
+                single = buffer("result", [P, KP], F32)
+                return single[:]
+            placed = shared.tile([P, KP], F32, name="placed%d" % k, offset=GROUP_BYTES * shelf + 4 * KP * slot)
+            return placed[:]
+
         def index_mm(i, number):
             index_bank[i] = bank_of(number, [P, C])
             for j in range(NJ):
@@ -396,9 +410,26 @@ def tile_ghosh_price_push_s8_kernel(
                 )
 
         def index_out(i, engine="scalar"):
-            result = buffer("result", [P, KP], F32)
-            sums_out(engine, result[:], index_bank[i][:])
-            nc.sync.dma_start(out=index_v[i // T][:, i % T, :], in_=result[:])
+            result = result_tile()
+            sums_out(engine, result, index_bank[i][:])
+            nc.sync.dma_start(out=index_v[i // T][:, i % T, :], in_=result)
+
+        def index_by_halves(i, banks):
+            result = result_tile()
+            for number, engine, c0 in zip(banks, ("scalar", "vector"), (0, HALF)):
+                bank = bank_of(number, [P, HALF])
+                for j in range(NJ):
+                    nc.tensor.matmul_mx(
+                        out=bank[:],
+                        lhsT=pr_mx[i // 2][0][:, i % 2, j, :].bitcast(FP8X4),
+                        lhsT_scale=pr_mx[i // 2][1][:, i % 2, j, :],
+                        rhs=b_words[:, j, 2 * c0 : 2 * (c0 + HALF)].bitcast(FP4X4),
+                        rhs_scale=b_scales[:, j, c0 : c0 + HALF],
+                        start=(j == 0),
+                        stop=(j == NJ - 1),
+                    )
+                sums_out(engine, result[:, c0 : c0 + HALF], bank[:])
+                nc.sync.dma_start(out=index_v[i // T][:, i % T, c0 : c0 + HALF], in_=result[:, c0 : c0 + HALF])
 
         summed = {}
 
@@ -419,13 +450,13 @@ def tile_ghosh_price_push_s8_kernel(
                 )
 
         def contrast_out(a, j, engine="scalar"):
-            result = buffer("result", [P, KP], F32)
+            result = result_tile()
             sums_out(
                 engine,
-                result[:].rearrange("p (m u e) -> p m u e", u=2, e=2),
+                result.rearrange("p (m u e) -> p m u e", u=2, e=2),
                 contrast_bank[a, j][:].rearrange("p (e u m) -> p m u e", u=2, e=2),
             )
-            nc.sync.dma_start(out=out_1[P * a : P * (a + 1), KP * j : KP * (j + 1)], in_=result[:])
+            nc.sync.dma_start(out=out_1[P * a : P * (a + 1), KP * j : KP * (j + 1)], in_=result)
 
         def warm(count, number, source):
             bank = bank_of(number, [P, KP])
@@ -435,7 +466,6 @@ def tile_ghosh_price_push_s8_kernel(
         nc.vector.memset(b_scales[:].rearrange("p j n -> p (j n)").bitcast(I32), 0)
         nc.vector.memset(ones[:], 1.0)
         make_identity(nc, ident[:])
-        make_identity(nc, ident_bf[:])
         load_shocks(0, 1)
         nc.sync.dma_start(out=scale_kp[:], in_=shocks_scale.rearrange("o (q p t) -> p (o q) t", p=P, t=T))
         load_shocks(1, 2)
@@ -453,9 +483,10 @@ def tile_ghosh_price_push_s8_kernel(
 
         widen_sorted(0, 0, 1)
         widen(0, 1, 2)
+        nc.scalar.copy(out=ident_bf[:], in_=ident[:])
         turn_shocks(0, 0, 0, 1)
         turn_shocks(0, 1, 1, 2)
-        widen_sorted(1)
+        widen(1)
         turn_shocks(1, 2)
         for i in (2, 3):
             widen(i)
@@ -465,11 +496,11 @@ def tile_ghosh_price_push_s8_kernel(
         scale_shocks(1)
         scale_shocks(2)
         scale_shocks(3)
-        group_inverse(0, 0, "gpsimd", 0, HALF, tag="group_a")
-        group_inverse(0, 0, "scalar", HALF, KP)
+        group_inverse(0, 0, "gpsimd", 0, 232, tag="group_a")
+        group_inverse(0, 0, "scalar", 232, KP)
         warm(4, 7, inv_raw[0, 0][:, 0])
-        group_inverse(0, 1, "gpsimd", 0, HALF, tag="group_b")
-        group_inverse(0, 1, "scalar", HALF, KP)
+        group_inverse(0, 1, "gpsimd", 0, 232, tag="group_b")
+        group_inverse(0, 1, "scalar", 232, KP)
         widen(4)
         widen(5)
         turn_shocks(4, 0)
@@ -486,15 +517,15 @@ def tile_ghosh_price_push_s8_kernel(
         widen(6)
         group_inverse(1, 1, "scalar", 0, KP, tag="group_d")
         widen(7)
-        group_inverse(1, 0, "scalar", 384, KP)
         turn_shocks(6, 3)
         turn_shocks(7, 4)
         exps(units)
         scale_shocks(4)
         scale_shocks(5)
+        group_inverse(1, 0, "vector", 384, KP)
         quantize_inverse(1, 1)
         quantize_inverse(1, 0)
-        on_gpsimd([(0, 0, 0, 320, "group_a")], [])
+        on_gpsimd([(0, 0, 0, 288, "group_a")], [])
         quantize_shocks(4, 2)
 
         move_pass(0, 1, 1, 0)
@@ -515,7 +546,7 @@ def tile_ghosh_price_push_s8_kernel(
         scale_shocks(7)
         scale_shocks(8)
         quantize_shocks(6, 2)
-        on_gpsimd([(0, 0, 320, KP, None)], [(0, 1)])
+        on_gpsimd([(0, 0, 288, KP, None)], [(0, 1)])
         quantize_shocks(8)
 
         units = [(4, 0), (4, 1), (5, 0), (5, 1)]
@@ -539,7 +570,7 @@ def tile_ghosh_price_push_s8_kernel(
         turn_contrasts(2, 6)
         turn_contrasts(3, 2)
         exps(units)
-        on_gpsimd([(1, 0, 0, 320, "group_c")], [])
+        on_gpsimd([(1, 0, 0, 304, "group_c")], [])
         quantize_weighted(0, 0)
         for n in (1, 2, 3):
             empty_contrasts(n)
@@ -553,7 +584,7 @@ def tile_ghosh_price_push_s8_kernel(
         turn_early(2, 2)
         exps(units)
         quantize_contrasts(0)
-        on_gpsimd([(1, 0, 320, KP, None)], [])
+        on_gpsimd([(1, 0, 304, KP, None)], [])
         quantize_contrasts(1)
         for i in (0, 1, 2):
             empty_early(i)
@@ -579,9 +610,10 @@ def tile_ghosh_price_push_s8_kernel(
         quantize_weighted(2, 0)
         quantize_priced(2, 2)
         quantize_priced(4)
-        on_gpsimd([], [(8, 1), (9, 1), (10, 1), (11, 1)])
+        on_gpsimd([(2, 1, 0, 384, "group_c")], [])
         quantize_contrasts(2)
         price_early(5)
+        fuse_on_vector(2, 1, 384, KP, None)
         fuse_on_vector(1, 1, 0, KP, "group_a")
 
         index_mm(0, 1)
@@ -608,58 +640,49 @@ def tile_ghosh_price_push_s8_kernel(
         contrast_out(2, 0)
         contrast_out(3, 0)
         index_out(4)
+        quantize_weighted(2, 1)
         quantize_weighted(1, 1)
         quantize_weighted(0, 1)
         price_early_on_gpsimd(9, "group_b")
         quantize_priced(5)
-        group_weighted(2, 1, "scalar", tag="group_c")
         prices(8)
         price_early(6)
         price_early(7)
 
-        contrast_mm(0, 1, 3, [1])
-        contrast_mm(1, 1, 1, [1])
-        contrast_mm(0, 1, 3, [0])
-        contrast_mm(1, 1, 1, [0])
-        index_mm(5, 4)
-        contrast_mm(2, 1, 5, [1, 0])
-        turns(10, (2, 0))
-        turn_early(6, 6)
+        for g in (2, 1, 0):
+            contrast_mm(0, 1, 3, [g])
+            contrast_mm(1, 1, 4, [g])
+        index_mm(5, 1)
+        contrast_mm(2, 1, 5)
+        contrast_mm(3, 1, 6)
+        contrast_out(0, 1)
+        contrast_out(1, 1)
         index_out(5)
+        contrast_out(2, 1)
+        contrast_out(3, 1)
+        turns(10, (2, 0))
+        turn_early(6, 3)
         turn_early(9, 4)
-        turn_early(7, 7)
+        turn_early(7, 1)
+        turns(11, (7, 5))
         empty_early(6)
         empty_early(9)
         empty_early(7)
-        quantize_weighted(2, 1)
-        quantize_priced(6)
-        quantize_priced(8, 2)
-        quantize_priced(7)
+        quantize_priced(8)
         prices(10)
-
-        contrast_mm(0, 1, 3, [2])
-        contrast_mm(1, 1, 1, [2])
-        contrast_mm(2, 1, 5, [2])
-        index_mm(6, 6)
-        contrast_out(0, 1)
-        contrast_out(1, 1)
-        turns(11, (4, 7))
-        contrast_out(2, 1)
-        index_out(6)
+        quantize_priced(6)
+        quantize_priced(9)
         price(11, 0)
+        quantize_priced(7)
         quantize_priced(10)
         price(11, 1)
         quantize_priced(11)
 
-        index_mm(8, 3)
-        index_mm(9, 1)
-        index_mm(7, 5)
-        contrast_mm(3, 1, 2)
+        index_mm(8, 6)
+        index_mm(6, 3)
+        index_mm(9, 4)
+        index_mm(7, 2)
         index_mm(10, 0)
-        index_mm(11, 6)
-        index_out(8)
-        index_out(9)
-        index_out(7)
-        contrast_out(3, 1, "vector")
-        index_out(10)
-        index_out(11, "vector")
+        for i in (8, 6, 9, 7, 10):
+            index_out(i)
+        index_by_halves(11, (1, 7))

@@ -322,6 +322,10 @@ def tile_ghosh_price_push_s8_kernel(
         def quantize_priced(i0, count=1):
             quantize_tiles(pr_mx, priced, i0, i0 + count)
 
+        def quantize_priced_half(i, j):
+            codes, scales = pr_mx[i // 2]
+            quantize(codes[:, i % 2, j], scales[:, i % 2, j], priced[i // 2][:, i % 2, KP * j : KP * (j + 1)])
+
         def planes(g, j):
             if (g, j) not in scaled:
                 scaled[g, j] = buffer("scaled", [P, T, KP], BF16)
@@ -414,21 +418,26 @@ def tile_ghosh_price_push_s8_kernel(
             sums_out(engine, result, index_bank[i][:])
             nc.sync.dma_start(out=index_v[i // T][:, i % T, :], in_=result)
 
-        def index_by_halves(i, banks):
+        half_bank = {}
+
+        def index_halves_mm(i, j, banks):
+            for number, c0 in zip(banks, (0, HALF)):
+                if j == 0:
+                    half_bank[c0] = bank_of(number, [P, HALF])
+                nc.tensor.matmul_mx(
+                    out=half_bank[c0][:],
+                    lhsT=pr_mx[i // 2][0][:, i % 2, j, :].bitcast(FP8X4),
+                    lhsT_scale=pr_mx[i // 2][1][:, i % 2, j, :],
+                    rhs=b_words[:, j, 2 * c0 : 2 * (c0 + HALF)].bitcast(FP4X4),
+                    rhs_scale=b_scales[:, j, c0 : c0 + HALF],
+                    start=(j == 0),
+                    stop=(j == NJ - 1),
+                )
+
+        def index_halves_out(i):
             result = result_tile()
-            for number, engine, c0 in zip(banks, ("scalar", "vector"), (0, HALF)):
-                bank = bank_of(number, [P, HALF])
-                for j in range(NJ):
-                    nc.tensor.matmul_mx(
-                        out=bank[:],
-                        lhsT=pr_mx[i // 2][0][:, i % 2, j, :].bitcast(FP8X4),
-                        lhsT_scale=pr_mx[i // 2][1][:, i % 2, j, :],
-                        rhs=b_words[:, j, 2 * c0 : 2 * (c0 + HALF)].bitcast(FP4X4),
-                        rhs_scale=b_scales[:, j, c0 : c0 + HALF],
-                        start=(j == 0),
-                        stop=(j == NJ - 1),
-                    )
-                sums_out(engine, result[:, c0 : c0 + HALF], bank[:])
+            for engine, c0 in (("scalar", 0), ("vector", HALF)):
+                sums_out(engine, result[:, c0 : c0 + HALF], half_bank[c0][:])
                 nc.sync.dma_start(out=index_v[i // T][:, i % T, c0 : c0 + HALF], in_=result[:, c0 : c0 + HALF])
 
         summed = {}
@@ -467,7 +476,7 @@ def tile_ghosh_price_push_s8_kernel(
         nc.vector.memset(ones[:], 1.0)
         make_identity(nc, ident[:])
         load_shocks(0, 1)
-        nc.sync.dma_start(out=scale_kp[:], in_=shocks_scale.rearrange("o (q p t) -> p (o q) t", p=P, t=T))
+        nc.scalar.dma_start(out=scale_kp[:], in_=shocks_scale.rearrange("o (q p t) -> p (o q) t", p=P, t=T))
         load_shocks(1, 2)
         load_shocks(2, 4)
         load_inverse(0, 0)
@@ -525,7 +534,7 @@ def tile_ghosh_price_push_s8_kernel(
         group_inverse(1, 0, "vector", 384, KP)
         quantize_inverse(1, 1)
         quantize_inverse(1, 0)
-        on_gpsimd([(0, 0, 0, 288, "group_a")], [])
+        on_gpsimd([(0, 0, 0, 336, "group_a")], [])
         quantize_shocks(4, 2)
 
         move_pass(0, 1, 1, 0)
@@ -546,7 +555,7 @@ def tile_ghosh_price_push_s8_kernel(
         scale_shocks(7)
         scale_shocks(8)
         quantize_shocks(6, 2)
-        on_gpsimd([(0, 0, 288, KP, None)], [(0, 1)])
+        on_gpsimd([(0, 0, 336, KP, None)], [(0, 1), (1, 1)])
         quantize_shocks(8)
 
         units = [(4, 0), (4, 1), (5, 0), (5, 1)]
@@ -570,7 +579,7 @@ def tile_ghosh_price_push_s8_kernel(
         turn_contrasts(2, 6)
         turn_contrasts(3, 2)
         exps(units)
-        on_gpsimd([(1, 0, 0, 304, "group_c")], [])
+        on_gpsimd([(1, 0, 0, 320, "group_c")], [])
         quantize_weighted(0, 0)
         for n in (1, 2, 3):
             empty_contrasts(n)
@@ -584,19 +593,20 @@ def tile_ghosh_price_push_s8_kernel(
         turn_early(2, 2)
         exps(units)
         quantize_contrasts(0)
-        on_gpsimd([(1, 0, 304, KP, None)], [])
+        on_gpsimd([(1, 0, 320, KP, None)], [])
         quantize_contrasts(1)
         for i in (0, 1, 2):
             empty_early(i)
         price_early(3)
         price_early(4)
-        on_gpsimd([], [(1, 1), (2, 1), (3, 1)])
-        quantize_priced(0, 2)
 
         units = [(8, 1), (9, 1), (10, 1), (11, 1)]
-        move(units, [4, 0, 1, 5])
+        move(units[:2], [4, 0])
         place_weights(3)
-        fuse_on_vector(2, 0, 0, KP, "group_d")
+        move(units[2:], [1, 5])
+        on_gpsimd([(2, 0, 432, KP, "group_d")], [(2, 1), (3, 1)])
+        quantize_priced(0, 2)
+        fuse_on_vector(2, 0, 0, 432, None)
         exps(units)
         turn_contrasts(4, 6)
         turn_contrasts(5, 2)
@@ -610,11 +620,11 @@ def tile_ghosh_price_push_s8_kernel(
         quantize_weighted(2, 0)
         quantize_priced(2, 2)
         quantize_priced(4)
-        on_gpsimd([(2, 1, 0, 384, "group_c")], [])
+        on_gpsimd([(2, 1, 0, 416, "group_c")], [])
         quantize_contrasts(2)
         price_early(5)
-        fuse_on_vector(2, 1, 384, KP, None)
         fuse_on_vector(1, 1, 0, KP, "group_a")
+        fuse_on_vector(2, 1, 416, KP, None)
 
         index_mm(0, 1)
         index_mm(1, 5)
@@ -630,18 +640,18 @@ def tile_ghosh_price_push_s8_kernel(
         contrast_out(0, 0)
         group_weighted(0, 1, "scalar", 0, HALF, tag="group_b")
         contrast_out(1, 0)
-        index_mm(4, 6)
         index_out(2)
         index_out(3)
         group_weighted(0, 1, "scalar", HALF, KP)
         turn_early(5, 4)
         turns(8, (2, 0))
+        index_mm(4, 6)
         empty_early(5)
         contrast_out(2, 0)
         contrast_out(3, 0)
         index_out(4)
-        quantize_weighted(2, 1)
         quantize_weighted(1, 1)
+        quantize_weighted(2, 1)
         quantize_weighted(0, 1)
         price_early_on_gpsimd(9, "group_b")
         quantize_priced(5)
@@ -649,7 +659,7 @@ def tile_ghosh_price_push_s8_kernel(
         price_early(6)
         price_early(7)
 
-        for g in (2, 1, 0):
+        for g in (1, 2, 0):
             contrast_mm(0, 1, 3, [g])
             contrast_mm(1, 1, 4, [g])
         index_mm(5, 1)
@@ -676,13 +686,16 @@ def tile_ghosh_price_push_s8_kernel(
         quantize_priced(7)
         quantize_priced(10)
         price(11, 1)
-        quantize_priced(11)
+        quantize_priced_half(11, 0)
+        quantize_priced_half(11, 1)
 
         index_mm(8, 6)
         index_mm(6, 3)
         index_mm(9, 4)
         index_mm(7, 2)
         index_mm(10, 0)
+        index_halves_mm(11, 0, (1, 7))
+        index_halves_mm(11, 1, (1, 7))
         for i in (8, 6, 9, 7, 10):
             index_out(i)
-        index_by_halves(11, (1, 7))
+        index_halves_out(11)

@@ -476,7 +476,7 @@ def tile_ghosh_price_push_s8_kernel(
         nc.vector.memset(ones[:], 1.0)
         make_identity(nc, ident[:])
         load_shocks(0, 1)
-        nc.scalar.dma_start(out=scale_kp[:], in_=shocks_scale.rearrange("o (q p t) -> p (o q) t", p=P, t=T))
+        nc.sync.dma_start(out=scale_kp[:], in_=shocks_scale.rearrange("o (q p t) -> p (o q) t", p=P, t=T))
         load_shocks(1, 2)
         load_shocks(2, 4)
         load_inverse(0, 0)

@@ -32,7 +32,7 @@ LINE = 8
 PAIR = 2
 
 DEPTH = {
-    "wide": 7, "sh_group": 3, "con_group": 2, "priced": 4, "early": 4, "scaled": 2, "columns": 4, "result": 6,
+    "wide": 7, "sh_group": 2, "group_e": 1, "group_f": 1, "con_group": 2, "priced": 4, "early": 4, "columns": 4, "result": 6,
     "codes": TILES // 2, "scales": TILES // 2, "group_a": 1, "group_b": 1, "group_c": 1, "group_d": 1,
 }
 
@@ -167,9 +167,9 @@ def tile_ghosh_price_push_s8_kernel(
                         part = words[:, HALF * q + u : HALF * (q + 1) : 2]
                     nc.tensor.transpose(sh_bank[i, q0][:, u, q - q0, :], part, ident[:])
 
-        def scale_shocks(i, q0=0, q1=KQ):
+        def scale_shocks(i, q0=0, q1=KQ, tag="sh_group"):
             if i // 2 not in sh_group:
-                sh_group[i // 2] = buffer("sh_group", [P, 2, N], BF16)
+                sh_group[i // 2] = buffer(tag, [P, 2, N], BF16)
             halves = sh_bank[i, q0][:].rearrange("p u q r -> p (u q r)").bitcast(BF16)
             nc.vector.tensor_tensor(
                 out=sh_group[i // 2][:, i % 2, KP * q0 : KP * q1].rearrange("p (q r u e) -> p q r u e", r=P, u=2, e=2),
@@ -198,9 +198,9 @@ def tile_ghosh_price_push_s8_kernel(
                 bank.rearrange("p a u r -> p a r u"),
             )
 
-        def empty_contrasts(n, engine="scalar"):
+        def empty_contrasts(n, engine="scalar", tag="con_group"):
             if n % 2 == 0:
-                con_group[n // 2] = buffer("con_group", [P, 2, 2 * KP], BF16)
+                con_group[n // 2] = buffer(tag, [P, 2, 2 * KP], BF16)
             empty_words(con_group[n // 2][:, n % 2], con_bank[n][:], engine)
 
         def quantize_contrasts(k):
@@ -326,9 +326,9 @@ def tile_ghosh_price_push_s8_kernel(
             codes, scales = pr_mx[i // 2]
             quantize(codes[:, i % 2, j], scales[:, i % 2, j], priced[i // 2][:, i % 2, KP * j : KP * (j + 1)])
 
-        def planes(g, j):
+        def planes(g, j, tag=None):
             if (g, j) not in scaled:
-                scaled[g, j] = buffer("scaled", [P, T, KP], BF16)
+                scaled[g, j] = buffer(tag, [P, T, KP], BF16)
             return scaled[g, j]
 
         def weight_columns(i0, count):
@@ -336,9 +336,9 @@ def tile_ghosh_price_push_s8_kernel(
             nc.vector.tensor_copy(out=columns[:], in_=weight_kp[:, i0 : i0 + count])
             return columns
 
-        def weigh(columns, i0, i, j):
+        def weigh(columns, i0, i, j, tag=None):
             nc.gpsimd.tensor_scalar(
-                out=planes(i // T, j)[:, i % T, :],
+                out=planes(i // T, j, tag)[:, i % T, :],
                 in0=unit_rel(i, j),
                 scalar1=columns[:, i - i0 : i - i0 + 1],
                 scalar2=0.0,
@@ -476,8 +476,8 @@ def tile_ghosh_price_push_s8_kernel(
         nc.vector.memset(ones[:], 1.0)
         make_identity(nc, ident[:])
         load_shocks(0, 1)
-        nc.sync.dma_start(out=scale_kp[:], in_=shocks_scale.rearrange("o (q p t) -> p (o q) t", p=P, t=T))
         load_shocks(1, 2)
+        nc.sync.dma_start(out=scale_kp[:], in_=shocks_scale.rearrange("o (q p t) -> p (o q) t", p=P, t=T))
         load_shocks(2, 4)
         load_inverse(0, 0)
         load_inverse(0, 1)
@@ -526,15 +526,16 @@ def tile_ghosh_price_push_s8_kernel(
         widen(6)
         group_inverse(1, 1, "scalar", 0, KP, tag="group_d")
         widen(7)
+        group_inverse(1, 0, "scalar", 384, KP)
         turn_shocks(6, 3)
         turn_shocks(7, 4)
         exps(units)
         scale_shocks(4)
         scale_shocks(5)
-        group_inverse(1, 0, "vector", 384, KP)
         quantize_inverse(1, 1)
         quantize_inverse(1, 0)
-        on_gpsimd([(0, 0, 0, 336, "group_a")], [])
+        weights = weight_columns(0, TILES)
+        weigh_grouped("gpsimd", weights[:, 0:T], 0, 0, 0, 312, "group_b")
         quantize_shocks(4, 2)
 
         move_pass(0, 1, 1, 0)
@@ -547,7 +548,7 @@ def tile_ghosh_price_push_s8_kernel(
         widen(8)
         widen(9)
         widen(10)
-        scale_shocks(6)
+        scale_shocks(6, tag="group_e")
         turn_shocks(8, 7)
         turn_shocks(9, 2)
         turn_shocks(10, 3)
@@ -555,7 +556,8 @@ def tile_ghosh_price_push_s8_kernel(
         scale_shocks(7)
         scale_shocks(8)
         quantize_shocks(6, 2)
-        on_gpsimd([(0, 0, 336, KP, None)], [(0, 1), (1, 1)])
+        weigh(weights, 0, 0, 1, "group_e")
+        weigh_grouped("gpsimd", weights[:, 0:T], 0, 0, 312, KP, None)
         quantize_shocks(8)
 
         units = [(4, 0), (4, 1), (5, 0), (5, 1)]
@@ -568,7 +570,7 @@ def tile_ghosh_price_push_s8_kernel(
         exps(units)
         keep_base()
         empty_contrasts(0)
-        scale_shocks(10)
+        scale_shocks(10, tag="group_f")
         scale_shocks(11)
         quantize_shocks(9)
         quantize_shocks(10, 2)
@@ -579,7 +581,7 @@ def tile_ghosh_price_push_s8_kernel(
         turn_contrasts(2, 6)
         turn_contrasts(3, 2)
         exps(units)
-        on_gpsimd([(1, 0, 0, 320, "group_c")], [])
+        weigh_grouped("gpsimd", weights[:, T : 2 * T], 1, 0, 0, 304, "group_f")
         quantize_weighted(0, 0)
         for n in (1, 2, 3):
             empty_contrasts(n)
@@ -593,7 +595,7 @@ def tile_ghosh_price_push_s8_kernel(
         turn_early(2, 2)
         exps(units)
         quantize_contrasts(0)
-        on_gpsimd([(1, 0, 320, KP, None)], [])
+        on_gpsimd([(1, 0, 304, KP, None)], [])
         quantize_contrasts(1)
         for i in (0, 1, 2):
             empty_early(i)
@@ -604,27 +606,27 @@ def tile_ghosh_price_push_s8_kernel(
         move(units[:2], [4, 0])
         place_weights(3)
         move(units[2:], [1, 5])
-        on_gpsimd([(2, 0, 432, KP, "group_d")], [(2, 1), (3, 1)])
+        on_gpsimd([], [(1, 1), (2, 1), (3, 1)])
         quantize_priced(0, 2)
-        fuse_on_vector(2, 0, 0, 432, None)
+        fuse_on_vector(2, 0, 0, KP, "group_d")
         exps(units)
         turn_contrasts(4, 6)
         turn_contrasts(5, 2)
         turn_early(3, 4)
         turn_early(4, 0)
-        empty_contrasts(4)
+        empty_contrasts(4, tag="group_c")
         empty_contrasts(5)
         empty_early(3)
         empty_early(4)
         quantize_weighted(1, 0)
         quantize_weighted(2, 0)
         quantize_priced(2, 2)
-        quantize_priced(4)
-        on_gpsimd([(2, 1, 0, 416, "group_c")], [])
         quantize_contrasts(2)
+        weigh_grouped("gpsimd", weights[:, 2 * T :], 2, 1, 0, 400, "group_c")
+        quantize_priced(4)
         price_early(5)
         fuse_on_vector(1, 1, 0, KP, "group_a")
-        fuse_on_vector(2, 1, 416, KP, None)
+        fuse_on_vector(2, 1, 400, KP, None)
 
         index_mm(0, 1)
         index_mm(1, 5)

@@ -32,7 +32,7 @@ LINE = 8
 PAIR = 2
 
 DEPTH = {
-    "wide": 7, "sh_group": 2, "group_e": 1, "group_f": 1, "con_group": 2, "priced": 4, "early": 4, "columns": 4, "result": 6,
+    "wide": 6, "wide_pair": 2, "sh_group": 2, "group_e": 1, "group_f": 1, "con_group": 2, "priced": 4, "early": 4, "columns": 4, "result": 6,
     "codes": TILES // 2, "scales": TILES // 2, "group_a": 1, "group_b": 1, "group_c": 1, "group_d": 1,
 }
 
@@ -63,19 +63,22 @@ def tile_ghosh_price_push_s8_kernel(
         we_scales = keep.tile([P, SG, NJ, KP], U8, name="we_scales", align_bytes=64)
         ident = keep.tile([P, P], F32, name="ident")
         ident_bf = keep.tile([P, P], BF16, name="ident_bf")
+        base_rows = keep.tile([P, N], BF16, name="base_rows")
         ones = keep.tile([P, 1], F32, name="ones")
 
         shocks_v = shocks_bytes.rearrange("(g m t) k -> g m t k", m=P, t=T)
         inverse_v = inverse.rearrange("(q p t) n -> q p t n", p=P, t=T)
         index_v = out_0.rearrange("(g m t) c -> g m t c", m=P, t=T)
 
-        sh_bytes, inv_raw = {}, {}
+        sh_bytes, sh_pair, inv_raw = {}, {}, {}
 
         def load_shocks(i0, i1):
             loaded = keep.tile([P, i1 - i0, N], U8, name="sh_bytes%d" % i0, align_bytes=64)
             nc.sync.dma_start(out=loaded[:], in_=shocks_v[i0 // T][:, i0 % T : i0 % T + i1 - i0, :])
             for i in range(i0, i1):
                 sh_bytes[i] = loaded[:, i - i0, :]
+            for i in range(i0, i1 - 1):
+                sh_pair[i] = loaded[:, i - i0 : i - i0 + 2, :].rearrange("p i k -> p (i k)")
 
         def load_inverse(j, q):
             inv_raw[j, q] = keep.tile([P, T, KP], BF16, name="inv_raw%d%d" % (j, q))
@@ -139,6 +142,11 @@ def tile_ghosh_price_push_s8_kernel(
             if i not in sh_wide:
                 sh_wide[i] = buffer("wide", [P, N], BF16)
             nc.scalar.copy(out=sh_wide[i][:, KP * q0 : KP * q1], in_=sh_bytes[i][:, KP * q0 : KP * q1].bitcast(FP8))
+
+        def widen_pair(i):
+            pair = buffer("wide_pair", [P, 2, N], BF16)
+            nc.scalar.copy(out=pair[:].rearrange("p i k -> p (i k)"), in_=sh_pair[i].bitcast(FP8))
+            sh_wide[i], sh_wide[i + 1] = pair[:, 0], pair[:, 1]
 
         sorted_parts = {}
 
@@ -303,12 +311,15 @@ def tile_ghosh_price_push_s8_kernel(
         def price_early(i):
             price_before(nc.vector, i, consts["base"][:].rearrange("p a m -> p (a m)").bitcast(BF16), "early")
 
-        def keep_base():
-            consts["row"] = keep.tile([P, N], BF16, name="base_row")
-            nc.scalar.copy(out=consts["row"][:], in_=consts["base"][:].rearrange("p a m -> p (a m)").bitcast(BF16))
-
         def price_early_on_gpsimd(i, tag):
-            price_before(nc.gpsimd, i, consts["row"][:], tag)
+            early[i] = buffer(tag, [P, NJ, KP], BF16)
+            for j in range(NJ):
+                nc.gpsimd.tensor_tensor(
+                    out=early[i][:, j].rearrange("p (u m e) -> p u m e", u=2, e=2),
+                    in0=base_rows[:, KP * j : KP * (j + 1)].rearrange("p (m u e) -> p u m e", u=2, e=2),
+                    in1=unit_rel(i, j).rearrange("p (e u m) -> p u m e", u=2, e=2),
+                    op=MULT,
+                )
 
         def turn_early(i, number):
             tr_bank[i] = bank_of(number, [P, NJ, 2, P])
@@ -345,6 +356,9 @@ def tile_ghosh_price_push_s8_kernel(
                 op0=MULT,
                 op1=ADD,
             )
+
+        def weigh_on_scalar(columns, i, j):
+            nc.scalar.activation(out=planes(i // T, j)[:, i % T, :], in_=unit_rel(i, j), func=COPY, scale=columns[:, i : i + 1])
 
         def weighted_part(g, j, part, tag):
             if (g, j, part) not in weighted:
@@ -520,6 +534,7 @@ def tile_ghosh_price_push_s8_kernel(
         group_inverse(1, 0, "gpsimd", 0, 384, tag="group_b")
         quantize_shocks(2, 2)
         load_baskets()
+        nc.sync.dma_start(out=base_rows[:], in_=base.partition_broadcast(P))
 
         units = [(0, 0), (1, 0), (2, 0), (3, 0)]
         move(units, [5, 6, 7, 2])
@@ -535,7 +550,7 @@ def tile_ghosh_price_push_s8_kernel(
         quantize_inverse(1, 1)
         quantize_inverse(1, 0)
         weights = weight_columns(0, TILES)
-        weigh_grouped("gpsimd", weights[:, 0:T], 0, 0, 0, 312, "group_b")
+        weigh_grouped("gpsimd", weights[:, 0:T], 0, 0, 0, 272, "group_b")
         quantize_shocks(4, 2)
 
         move_pass(0, 1, 1, 0)
@@ -557,7 +572,7 @@ def tile_ghosh_price_push_s8_kernel(
         scale_shocks(8)
         quantize_shocks(6, 2)
         weigh(weights, 0, 0, 1, "group_e")
-        weigh_grouped("gpsimd", weights[:, 0:T], 0, 0, 312, KP, None)
+        weigh_grouped("gpsimd", weights[:, 0:T], 0, 0, 272, KP, None)
         quantize_shocks(8)
 
         units = [(4, 0), (4, 1), (5, 0), (5, 1)]
@@ -568,7 +583,6 @@ def tile_ghosh_price_push_s8_kernel(
         spread_base(7)
         turn_contrasts(0, 2)
         exps(units)
-        keep_base()
         empty_contrasts(0)
         scale_shocks(10, tag="group_f")
         scale_shocks(11)
@@ -594,30 +608,29 @@ def tile_ghosh_price_push_s8_kernel(
         turn_early(1, 6)
         turn_early(2, 2)
         exps(units)
+        turns(4, (4, 0))
         quantize_contrasts(0)
         on_gpsimd([(1, 0, 304, KP, None)], [])
         quantize_contrasts(1)
         for i in (0, 1, 2):
             empty_early(i)
         price_early(3)
-        price_early(4)
+        prices(4)
 
         units = [(8, 1), (9, 1), (10, 1), (11, 1)]
-        move(units[:2], [4, 0])
+        move(units[:2], [1, 5])
         place_weights(3)
-        move(units[2:], [1, 5])
+        move(units[2:], [6, 2])
         on_gpsimd([], [(1, 1), (2, 1), (3, 1)])
         quantize_priced(0, 2)
         fuse_on_vector(2, 0, 0, KP, "group_d")
         exps(units)
-        turn_contrasts(4, 6)
-        turn_contrasts(5, 2)
-        turn_early(3, 4)
-        turn_early(4, 0)
+        turn_contrasts(4, 4)
+        turn_contrasts(5, 0)
+        turn_early(3, 1)
         empty_contrasts(4, tag="group_c")
         empty_contrasts(5)
         empty_early(3)
-        empty_early(4)
         quantize_weighted(1, 0)
         quantize_weighted(2, 0)
         quantize_priced(2, 2)
@@ -628,26 +641,26 @@ def tile_ghosh_price_push_s8_kernel(
         fuse_on_vector(1, 1, 0, KP, "group_a")
         fuse_on_vector(2, 1, 400, KP, None)
 
-        index_mm(0, 1)
-        index_mm(1, 5)
+        index_mm(0, 5)
+        index_mm(1, 6)
         for g in range(SG):
-            contrast_mm(0, 0, 6, [g])
-            contrast_mm(1, 0, 2, [g])
-        index_mm(2, 4)
-        index_mm(3, 0)
+            contrast_mm(0, 0, 2, [g])
+            contrast_mm(1, 0, 4, [g])
+        index_mm(2, 0)
+        index_mm(3, 1)
         index_out(0)
         index_out(1)
-        contrast_mm(2, 0, 1)
-        contrast_mm(3, 0, 5)
+        contrast_mm(2, 0, 5)
+        contrast_mm(3, 0, 6)
         contrast_out(0, 0)
         group_weighted(0, 1, "scalar", 0, HALF, tag="group_b")
         contrast_out(1, 0)
         index_out(2)
         index_out(3)
         group_weighted(0, 1, "scalar", HALF, KP)
-        turn_early(5, 4)
-        turns(8, (2, 0))
-        index_mm(4, 6)
+        turn_early(5, 0)
+        turns(8, (4, 1))
+        index_mm(4, 2)
         empty_early(5)
         contrast_out(2, 0)
         contrast_out(3, 0)
@@ -663,20 +676,20 @@ def tile_ghosh_price_push_s8_kernel(
 
         for g in (1, 2, 0):
             contrast_mm(0, 1, 3, [g])
-            contrast_mm(1, 1, 4, [g])
-        index_mm(5, 1)
-        contrast_mm(2, 1, 5)
-        contrast_mm(3, 1, 6)
+            contrast_mm(1, 1, 0, [g])
+        index_mm(5, 5)
+        contrast_mm(2, 1, 6)
+        contrast_mm(3, 1, 2)
         contrast_out(0, 1)
         contrast_out(1, 1)
         index_out(5)
         contrast_out(2, 1)
         contrast_out(3, 1)
-        turns(10, (2, 0))
+        turns(10, (4, 1))
         turn_early(6, 3)
-        turn_early(9, 4)
-        turn_early(7, 1)
-        turns(11, (7, 5))
+        turn_early(9, 0)
+        turn_early(7, 5)
+        turns(11, (7, 6))
         empty_early(6)
         empty_early(9)
         empty_early(7)
@@ -691,13 +704,13 @@ def tile_ghosh_price_push_s8_kernel(
         quantize_priced_half(11, 0)
         quantize_priced_half(11, 1)
 
-        index_mm(8, 6)
+        index_mm(8, 2)
         index_mm(6, 3)
-        index_mm(9, 4)
-        index_mm(7, 2)
-        index_mm(10, 0)
-        index_halves_mm(11, 0, (1, 7))
-        index_halves_mm(11, 1, (1, 7))
+        index_mm(9, 0)
+        index_mm(7, 4)
+        index_mm(10, 1)
+        index_halves_mm(11, 0, (5, 7))
+        index_halves_mm(11, 1, (5, 7))
         for i in (8, 6, 9, 7, 10):
             index_out(i)
         index_halves_out(11)

@@ -28,13 +28,20 @@ KQ = N // KP
 NJ = N // KP
 TILES = SG * T
 GROUP_BYTES = 4 * NJ * T * KP
+BANKS = 8
 LINE = 8
 PAIR = 2
 
 DEPTH = {
-    "wide": 6, "wide_pair": 2, "sh_group": 2, "group_e": 1, "group_f": 1, "con_group": 2, "priced": 4, "early": 4, "columns": 4, "result": 6,
+    "wide": 7, "sh_group": 2, "group_e": 1, "group_f": 1, "con_group": 2, "priced": 4, "early": 4, "columns": 4, "result": 6,
     "codes": TILES // 2, "scales": TILES // 2, "group_a": 1, "group_b": 1, "group_c": 1, "group_d": 1,
 }
+HEAD_SHARE = 232
+SECOND_SHARE = 384
+FUSED_00 = 272
+FUSED_10 = 320
+FUSED_21 = 320
+WARM_UPS = 4
 
 
 def tile_ghosh_price_push_s8_kernel(
@@ -63,22 +70,20 @@ def tile_ghosh_price_push_s8_kernel(
         we_scales = keep.tile([P, SG, NJ, KP], U8, name="we_scales", align_bytes=64)
         ident = keep.tile([P, P], F32, name="ident")
         ident_bf = keep.tile([P, P], BF16, name="ident_bf")
-        base_rows = keep.tile([P, N], BF16, name="base_rows")
         ones = keep.tile([P, 1], F32, name="ones")
+        base_rows = keep.tile([P, N], BF16, name="base_rows")
 
         shocks_v = shocks_bytes.rearrange("(g m t) k -> g m t k", m=P, t=T)
         inverse_v = inverse.rearrange("(q p t) n -> q p t n", p=P, t=T)
         index_v = out_0.rearrange("(g m t) c -> g m t c", m=P, t=T)
 
-        sh_bytes, sh_pair, inv_raw = {}, {}, {}
+        sh_bytes, inv_raw = {}, {}
 
         def load_shocks(i0, i1):
             loaded = keep.tile([P, i1 - i0, N], U8, name="sh_bytes%d" % i0, align_bytes=64)
             nc.sync.dma_start(out=loaded[:], in_=shocks_v[i0 // T][:, i0 % T : i0 % T + i1 - i0, :])
             for i in range(i0, i1):
                 sh_bytes[i] = loaded[:, i - i0, :]
-            for i in range(i0, i1 - 1):
-                sh_pair[i] = loaded[:, i - i0 : i - i0 + 2, :].rearrange("p i k -> p (i k)")
 
         def load_inverse(j, q):
             inv_raw[j, q] = keep.tile([P, T, KP], BF16, name="inv_raw%d%d" % (j, q))
@@ -98,17 +103,17 @@ def tile_ghosh_price_push_s8_kernel(
                 )
             nc.sync.dma_start(out=b_words[:], in_=basket_words.rearrange("j p b -> p j b"))
 
-        def bank_of(number, shape):
-            return psum.tile(shape, F32, name="bank%d" % number)
+        free_banks, held = list(range(BANKS)), {}
+
+        def take_bank(use, shape):
+            held[use] = free_banks.pop(0)
+            return psum.tile(shape, F32, name="bank%d" % held[use])
+
+        def give_back(use):
+            free_banks.append(held.pop(use))
 
         def buffer(tag, shape, dtype):
             return work.tile(shape, dtype, name=tag, bufs=DEPTH[tag], align_bytes=64)
-
-        def copy_on(engine, out, in_):
-            if engine == "scalar":
-                nc.scalar.copy(out=out, in_=in_)
-            else:
-                nc.vector.tensor_copy(out=out, in_=in_)
 
         def interleave(engine, grouped, planes):
             if engine == "gpsimd":
@@ -116,10 +121,9 @@ def tile_ghosh_price_push_s8_kernel(
                     out=grouped, in0=planes.rearrange("p t n -> p n t"), scalar1=1.0, scalar2=0.0, op0=MULT, op1=ADD
                 )
                 return
-            copy_on(
-                engine,
-                grouped.rearrange("p (c i) t -> p c t i", i=LINE),
-                planes.rearrange("p t (c i) -> p c t i", i=LINE),
+            nc.scalar.copy(
+                out=grouped.rearrange("p (c i) t -> p c t i", i=LINE),
+                in_=planes.rearrange("p t (c i) -> p c t i", i=LINE),
             )
 
         def quantize(codes, scales, grouped):
@@ -143,37 +147,26 @@ def tile_ghosh_price_push_s8_kernel(
                 sh_wide[i] = buffer("wide", [P, N], BF16)
             nc.scalar.copy(out=sh_wide[i][:, KP * q0 : KP * q1], in_=sh_bytes[i][:, KP * q0 : KP * q1].bitcast(FP8))
 
-        def widen_pair(i):
-            pair = buffer("wide_pair", [P, 2, N], BF16)
-            nc.scalar.copy(out=pair[:].rearrange("p i k -> p (i k)"), in_=sh_pair[i].bitcast(FP8))
-            sh_wide[i], sh_wide[i + 1] = pair[:, 0], pair[:, 1]
-
-        sorted_parts = {}
-
-        def widen_sorted(i, q0=0, q1=KQ):
-            if i not in sh_wide:
-                sh_wide[i] = buffer("wide", [P, N], BF16)
-            for q in range(q0, q1):
-                sorted_parts[i, q] = (HALF * q0 + P * (q - q0), P * (q1 - q0))
+        def widen_first():
+            sh_wide[0] = buffer("wide", [P, N], BF16)
             nc.vector.tensor_scalar(
-                out=sh_wide[i][:, KP * q0 : KP * q1].rearrange("p (u w e) -> p w u e", u=2, e=2),
-                in0=sh_bytes[i][:, KP * q0 : KP * q1].bitcast(FP8).rearrange("p (w u e) -> p w u e", u=2, e=2),
+                out=sh_wide[0][:, 0:KP].rearrange("p (u w e) -> p w u e", u=2, e=2),
+                in0=sh_bytes[0][:, 0:KP].bitcast(FP8).rearrange("p (w u e) -> p w u e", u=2, e=2),
                 scalar1=ones[:],
                 scalar2=None,
                 op0=MULT,
             )
 
-        def turn_shocks(i, number, q0=0, q1=KQ):
-            sh_bank[i, q0] = bank_of(number, [P, 2, q1 - q0, P])
+        def turn_shocks(i, q0=0, q1=KQ):
+            sh_bank[i, q0] = take_bank(("shocks", i, q0), [P, 2, q1 - q0, P])
             words = sh_wide[i][:].bitcast(F32)
             for q in range(q0, q1):
                 for u in range(2):
-                    if (i, q) in sorted_parts:
-                        first = sorted_parts[i, q][0] + u * sorted_parts[i, q][1]
-                        part = words[:, first : first + P]
+                    if (i, q) == (0, 0):
+                        source = words[:, P * u : P * (u + 1)]
                     else:
-                        part = words[:, HALF * q + u : HALF * (q + 1) : 2]
-                    nc.tensor.transpose(sh_bank[i, q0][:, u, q - q0, :], part, ident[:])
+                        source = words[:, HALF * q + u : HALF * (q + 1) : 2]
+                    nc.tensor.transpose(sh_bank[i, q0][:, u, q - q0, :], source, ident[:])
 
         def scale_shocks(i, q0=0, q1=KQ, tag="sh_group"):
             if i // 2 not in sh_group:
@@ -185,65 +178,66 @@ def tile_ghosh_price_push_s8_kernel(
                 in1=scale_kp[:, q0:q1].rearrange("p q (u e) -> p q u e", u=2).unsqueeze(2).to_broadcast([P, q1 - q0, P, 2, 2]),
                 op=MULT,
             )
+            give_back(("shocks", i, q0))
 
         def quantize_shocks(i0, count=1):
             quantize_tiles(sh_mx, sh_group, i0, i0 + count)
 
         con_bank, con_group = {}, {}
 
-        def turn_contrasts(n, number):
-            con_bank[n] = bank_of(number, [P, 2, 2, P])
+        def turn_contrasts(n):
+            con_bank[n] = take_bank(("contrasts", n), [P, 2, 2, P])
             for h in range(2):
                 a, g = divmod(2 * n + h, SG)
                 words = con_raw[a][:].bitcast(F32)
                 for u in range(2):
                     nc.tensor.transpose(con_bank[n][:, h, u, :], words[:, HALF * g + u : HALF * (g + 1) : 2], ident[:])
 
-        def empty_words(grouped, bank, engine):
-            copy_on(
-                engine,
-                grouped.bitcast(F32).rearrange("p (a r u) -> p a r u", a=2, u=2),
-                bank.rearrange("p a u r -> p a r u"),
+        def empty_words(grouped, bank):
+            nc.scalar.copy(
+                out=grouped.bitcast(F32).rearrange("p (a r u) -> p a r u", a=2, u=2),
+                in_=bank.rearrange("p a u r -> p a r u"),
             )
 
-        def empty_contrasts(n, engine="scalar", tag="con_group"):
+        def empty_contrasts(n, tag="con_group"):
             if n % 2 == 0:
                 con_group[n // 2] = buffer(tag, [P, 2, 2 * KP], BF16)
-            empty_words(con_group[n // 2][:, n % 2], con_bank[n][:], engine)
+            empty_words(con_group[n // 2][:, n % 2], con_bank[n][:])
+            give_back(("contrasts", n))
 
         def quantize_contrasts(k):
             cols = slice(KP * k, KP * (k + 1))
             quantize(con_codes[:, cols], con_scales[:, cols], con_group[k][:].rearrange("p h n -> p (h n)"))
 
-        inv_part = {}
+        inv_group = {}
 
-        def group_inverse(j, q, engine, c0, c1, part=(0, KP), tag=None):
-            if (j, q, part) not in inv_part:
-                inv_part[j, q, part] = buffer(tag, [P, part[1] - part[0], T], BF16)
-            interleave(engine, inv_part[j, q, part][:, c0 - part[0] : c1 - part[0], :], inv_raw[j, q][:, :, c0:c1])
+        def group_inverse(j, q, engine, c0, c1, tag=None):
+            if (j, q) not in inv_group:
+                inv_group[j, q] = buffer(tag, [P, KP, T], BF16)
+            interleave(engine, inv_group[j, q][:, c0:c1, :], inv_raw[j, q][:, :, c0:c1])
 
-        def quantize_inverse(j, q, part=(0, KP)):
-            cols = slice(part[0], part[1])
-            quantize(inv_codes[:, j, q, cols], inv_scales[:, j, q, cols], inv_part[j, q, part][:].rearrange("p n t -> p (n t)"))
+        def quantize_inverse(j, q):
+            quantize(inv_codes[:, j, q, :], inv_scales[:, j, q, :], inv_group[j, q][:].rearrange("p n t -> p (n t)"))
 
         mv_bank, tr_bank, priced, early, scaled, weighted, pr_mx = {}, {}, {}, {}, {}, {}, {}
 
-        def move_pass(i, j, q, number=None):
-            if number is not None:
-                mv_bank[i, j] = bank_of(number, [P, KP])
+        def move_pass(i, j, q):
+            opens = (i, j) not in mv_bank
+            if opens:
+                mv_bank[i, j] = take_bank(("moves", i, j), [P, KP])
             nc.tensor.matmul_mx(
                 out=mv_bank[i, j][:],
                 lhsT=sh_mx[i // 2][0][:, i % 2, q, :].bitcast(FP8X4),
                 lhsT_scale=sh_mx[i // 2][1][:, i % 2, q, :],
                 rhs=inv_codes[:, j, q, :].bitcast(FP8X4),
                 rhs_scale=inv_scales[:, j, q, :],
-                start=number is not None,
-                stop=number is None,
+                start=opens,
+                stop=not opens,
             )
 
-        def move(units, banks):
-            for (i, j), number in zip(units, banks):
-                move_pass(i, j, 0, number)
+        def move(units):
+            for i, j in units:
+                move_pass(i, j, 0)
                 move_pass(i, j, 1)
 
         rel = [shared.tile([P, NJ, T, KP], F32, name="rel%d" % g, offset=GROUP_BYTES * g) for g in range(SG)]
@@ -257,24 +251,25 @@ def tile_ghosh_price_push_s8_kernel(
                 in_=mv_bank[i, j][:].rearrange("p (m u e) -> p e u m", u=2, e=2),
                 func=EXP,
             )
+            give_back(("moves", i, j))
 
         def exps(units):
             for i, j in units:
                 relatives(i, j)
 
-        def turn(i, j, number):
-            tr_bank[i, j] = bank_of(number, [P, T, P])
+        def turn(i, j):
+            tr_bank[i, j] = take_bank(("relatives", i, j), [P, T, P])
             for v in range(T):
                 c0 = HALF * (v % 2) + P * (v // 2)
                 nc.tensor.transpose(tr_bank[i, j][:, v, :], unit_rel(i, j)[:, c0 : c0 + P], ident[:])
 
-        def turns(i, banks):
+        def turns(i):
             for j in range(NJ):
-                turn(i, j, banks[j])
+                turn(i, j)
 
-        def priced_tile(i, tag="priced"):
+        def priced_tile(i):
             if i // 2 not in priced:
-                priced[i // 2] = buffer(tag, [P, 2, N], BF16)
+                priced[i // 2] = buffer("priced", [P, 2, N], BF16)
             return priced[i // 2][:, i % 2]
 
         def price(i, j):
@@ -284,6 +279,7 @@ def tile_ghosh_price_push_s8_kernel(
                 in1=base_kp[:, T * j : T * (j + 1)].unsqueeze(1).to_broadcast([P, P, T]),
                 op=MULT,
             )
+            give_back(("relatives", i, j))
 
         def prices(i):
             for j in range(NJ):
@@ -291,44 +287,47 @@ def tile_ghosh_price_push_s8_kernel(
 
         consts = {}
 
-        def spread_base(number):
-            consts["base"] = bank_of(number, [P, 2 * NJ, P])
+        def spread_base():
+            consts["base"] = take_bank("base", [P, 2 * NJ, P])
             words = base_kp[:].bitcast(F32)
             for a in range(2 * NJ):
                 nc.tensor.transpose(consts["base"][:, a, :], words[:, a : a + 1].to_broadcast([P, P]), ident[:])
 
-        def place_weights(number):
-            consts["weight"] = bank_of(number, [P, TILES])
+        def place_weights():
+            consts["weight"] = take_bank("weight", [P, TILES])
             nc.tensor.matmul(consts["weight"][:], ident_bf[:], weight_kp[:], start=True, stop=True)
 
-        def price_before(engine, i, row, tag):
-            early[i] = buffer(tag, [P, NJ, KP], BF16)
-            out = early[i][:].rearrange("p j (c e) -> p j c e", e=2)
-            row = row.rearrange("p (j c e) -> p j c e", j=NJ, e=2)
-            values = rel[i // T][:, :, i % T, :].rearrange("p j (e c) -> p j c e", e=2)
-            engine.tensor_tensor(out=out, in0=row, in1=values, op=MULT)
+        def early_tile(i, tag):
+            if i not in early:
+                early[i] = buffer(tag, [P, NJ, KP], BF16)
+            return early[i]
 
-        def price_early(i):
-            price_before(nc.vector, i, consts["base"][:].rearrange("p a m -> p (a m)").bitcast(BF16), "early")
+        def price_early(i, j0=0, j1=NJ):
+            row = consts["base"][:].rearrange("p a m -> p (a m)").bitcast(BF16)
+            nc.vector.tensor_tensor(
+                out=early_tile(i, "early")[:, j0:j1].rearrange("p j (c e) -> p j c e", e=2),
+                in0=row.rearrange("p (j c e) -> p j c e", j=NJ, e=2)[:, j0:j1],
+                in1=rel[i // T][:, j0:j1, i % T, :].rearrange("p j (e c) -> p j c e", e=2),
+                op=MULT,
+            )
 
-        def price_early_on_gpsimd(i, tag):
-            early[i] = buffer(tag, [P, NJ, KP], BF16)
-            for j in range(NJ):
-                nc.gpsimd.tensor_tensor(
-                    out=early[i][:, j].rearrange("p (u m e) -> p u m e", u=2, e=2),
-                    in0=base_rows[:, KP * j : KP * (j + 1)].rearrange("p (m u e) -> p u m e", u=2, e=2),
-                    in1=unit_rel(i, j).rearrange("p (e u m) -> p u m e", u=2, e=2),
-                    op=MULT,
-                )
+        def price_early_on_gpsimd(i, j, tag="early"):
+            nc.gpsimd.tensor_tensor(
+                out=early_tile(i, tag)[:, j].rearrange("p (u m e) -> p u m e", u=2, e=2),
+                in0=base_rows[:, KP * j : KP * (j + 1)].rearrange("p (m u e) -> p u m e", u=2, e=2),
+                in1=unit_rel(i, j).rearrange("p (e u m) -> p u m e", u=2, e=2),
+                op=MULT,
+            )
 
-        def turn_early(i, number):
-            tr_bank[i] = bank_of(number, [P, NJ, 2, P])
+        def turn_early(i):
+            tr_bank[i] = take_bank(("early", i), [P, NJ, 2, P])
             words = early[i][:].rearrange("p j n -> p (j n)").bitcast(F32)
             for a in range(2 * NJ):
                 nc.tensor.transpose(tr_bank[i][:, a // 2, a % 2, :], words[:, P * a : P * (a + 1)], ident[:])
 
-        def empty_early(i, engine="scalar", tag="priced"):
-            empty_words(priced_tile(i, tag), tr_bank[i][:], engine)
+        def empty_early(i):
+            empty_words(priced_tile(i), tr_bank[i][:])
+            give_back(("early", i))
 
         def quantize_priced(i0, count=1):
             quantize_tiles(pr_mx, priced, i0, i0 + count)
@@ -337,62 +336,47 @@ def tile_ghosh_price_push_s8_kernel(
             codes, scales = pr_mx[i // 2]
             quantize(codes[:, i % 2, j], scales[:, i % 2, j], priced[i // 2][:, i % 2, KP * j : KP * (j + 1)])
 
-        def planes(g, j, tag=None):
-            if (g, j) not in scaled:
-                scaled[g, j] = buffer(tag, [P, T, KP], BF16)
-            return scaled[g, j]
-
         def weight_columns(i0, count):
             columns = buffer("columns", [P, count], F32)
             nc.vector.tensor_copy(out=columns[:], in_=weight_kp[:, i0 : i0 + count])
             return columns
 
-        def weigh(columns, i0, i, j, tag=None):
+        def weigh(columns, i, j, tag=None):
+            if (i // T, j) not in scaled:
+                scaled[i // T, j] = buffer(tag, [P, T, KP], BF16)
             nc.gpsimd.tensor_scalar(
-                out=planes(i // T, j, tag)[:, i % T, :],
+                out=scaled[i // T, j][:, i % T, :],
                 in0=unit_rel(i, j),
-                scalar1=columns[:, i - i0 : i - i0 + 1],
+                scalar1=columns[:, i : i + 1],
                 scalar2=0.0,
                 op0=MULT,
                 op1=ADD,
             )
 
-        def weigh_on_scalar(columns, i, j):
-            nc.scalar.activation(out=planes(i // T, j)[:, i % T, :], in_=unit_rel(i, j), func=COPY, scale=columns[:, i : i + 1])
+        def sheet(g, j, tag):
+            if (g, j) not in weighted:
+                weighted[g, j] = buffer(tag, [P, KP, T], BF16)
+            return weighted[g, j]
 
-        def weighted_part(g, j, part, tag):
-            if (g, j, part) not in weighted:
-                weighted[g, j, part] = buffer(tag, [P, part[1] - part[0], T], BF16)
-            return weighted[g, j, part]
+        def group_weighted(g, j, c0, c1, tag=None):
+            interleave("scalar", sheet(g, j, tag)[:, c0:c1, :], scaled[g, j][:, :, c0:c1])
 
-        def group_weighted(g, j, engine, c0=0, c1=KP, part=(0, KP), tag=None):
-            interleave(engine, weighted_part(g, j, part, tag)[:, c0 - part[0] : c1 - part[0], :], scaled[g, j][:, :, c0:c1])
-
-        def weigh_grouped(engine, weights, g, j, c0, c1, tag):
-            count = (c1 - c0) // PAIR
-            grouped = weighted_part(g, j, (0, KP), tag)[:, c0:c1, :].rearrange("p (c r) t -> p c t r", r=PAIR)
+        def fused_operands(four_weights, g, j, c0, c1, tag):
+            grouped = sheet(g, j, tag)[:, c0:c1, :].rearrange("p (c r) t -> p c t r", r=PAIR)
             values = rel[g][:, j, :, c0:c1].rearrange("p t (c r) -> p c t r", r=PAIR)
-            factors = weights.unsqueeze(1).unsqueeze(3).to_broadcast([P, count, T, PAIR])
-            if engine == "gpsimd":
-                nc.gpsimd.tensor_tensor(out=grouped, in0=values, in1=factors, op=MULT)
-            else:
-                nc.vector.tensor_tensor(out=grouped, in0=factors, in1=values, op=MULT)
+            factors = four_weights.unsqueeze(1).unsqueeze(3).to_broadcast([P, (c1 - c0) // PAIR, T, PAIR])
+            return grouped, values, factors
 
-        def on_gpsimd(parts, units):
-            groups = [part[0] for part in parts] + [i // T for i, j in units]
-            i0 = T * min(groups)
-            columns = weight_columns(i0, T * (max(groups) + 1) - i0)
-            for g, j, c0, c1, tag in parts:
-                weigh_grouped("gpsimd", columns[:, T * g - i0 : T * (g + 1) - i0], g, j, c0, c1, tag)
-            for i, j in units:
-                weigh(columns, i0, i, j)
+        def fuse_on_gpsimd(four_weights, g, j, c0, c1, tag=None):
+            grouped, values, factors = fused_operands(four_weights, g, j, c0, c1, tag)
+            nc.gpsimd.tensor_tensor(out=grouped, in0=values, in1=factors, op=MULT)
 
-        def fuse_on_vector(g, j, c0, c1, tag):
-            weigh_grouped("vector", consts["weight"][:, T * g : T * (g + 1)], g, j, c0, c1, tag)
+        def fuse_on_vector(g, j, c0, c1, tag=None):
+            grouped, values, factors = fused_operands(consts["weight"][:, T * g : T * (g + 1)], g, j, c0, c1, tag)
+            nc.vector.tensor_tensor(out=grouped, in0=factors, in1=values, op=MULT)
 
-        def quantize_weighted(g, j, part=(0, KP)):
-            cols = slice(part[0], part[1])
-            quantize(we_codes[:, g, j, cols], we_scales[:, g, j, cols], weighted[g, j, part][:].rearrange("p n t -> p (n t)"))
+        def quantize_weighted(g, j):
+            quantize(we_codes[:, g, j, :], we_scales[:, g, j, :], weighted[g, j][:].rearrange("p n t -> p (n t)"))
 
         index_bank, contrast_bank = {}, {}
 
@@ -407,15 +391,15 @@ def tile_ghosh_price_push_s8_kernel(
         def result_tile():
             k = len(stored)
             stored.append(k)
-            shelf, slot = divmod(k, NJ * T + 6)
+            shelf, slot = divmod(k, NJ * T + DEPTH["result"])
             if slot >= NJ * T:
                 single = buffer("result", [P, KP], F32)
                 return single[:]
             placed = shared.tile([P, KP], F32, name="placed%d" % k, offset=GROUP_BYTES * shelf + 4 * KP * slot)
             return placed[:]
 
-        def index_mm(i, number):
-            index_bank[i] = bank_of(number, [P, C])
+        def index_mm(i):
+            index_bank[i] = take_bank(("index", i), [P, C])
             for j in range(NJ):
                 nc.tensor.matmul_mx(
                     out=index_bank[i][:],
@@ -430,14 +414,15 @@ def tile_ghosh_price_push_s8_kernel(
         def index_out(i, engine="scalar"):
             result = result_tile()
             sums_out(engine, result, index_bank[i][:])
+            give_back(("index", i))
             nc.sync.dma_start(out=index_v[i // T][:, i % T, :], in_=result)
 
         half_bank = {}
 
-        def index_halves_mm(i, j, banks):
-            for number, c0 in zip(banks, (0, HALF)):
+        def index_halves_mm(i, j):
+            for c0 in (0, HALF):
                 if j == 0:
-                    half_bank[c0] = bank_of(number, [P, HALF])
+                    half_bank[c0] = take_bank(("index", i, c0), [P, HALF])
                 nc.tensor.matmul_mx(
                     out=half_bank[c0][:],
                     lhsT=pr_mx[i // 2][0][:, i % 2, j, :].bitcast(FP8X4),
@@ -456,9 +441,9 @@ def tile_ghosh_price_push_s8_kernel(
 
         summed = {}
 
-        def contrast_mm(a, j, number, groups=range(SG)):
+        def contrast_mm(a, j, groups=range(SG)):
             if (a, j) not in summed:
-                contrast_bank[a, j] = bank_of(number, [P, KP])
+                contrast_bank[a, j] = take_bank(("contrast", a, j), [P, KP])
                 summed[a, j] = []
             for g in groups:
                 summed[a, j].append(g)
@@ -472,19 +457,21 @@ def tile_ghosh_price_push_s8_kernel(
                     stop=len(summed[a, j]) == SG,
                 )
 
-        def contrast_out(a, j, engine="scalar"):
+        def contrast_out(a, j):
             result = result_tile()
             sums_out(
-                engine,
+                "scalar",
                 result.rearrange("p (m u e) -> p m u e", u=2, e=2),
                 contrast_bank[a, j][:].rearrange("p (e u m) -> p m u e", u=2, e=2),
             )
+            give_back(("contrast", a, j))
             nc.sync.dma_start(out=out_1[P * a : P * (a + 1), KP * j : KP * (j + 1)], in_=result)
 
-        def warm(count, number, source):
-            bank = bank_of(number, [P, KP])
-            for k in range(count):
+        def warm(source):
+            bank = take_bank("warm", [P, KP])
+            for k in range(WARM_UPS):
                 nc.tensor.matmul(bank[:], source[:, 0:P], source[:, 0:KP], start=True, stop=True)
+            give_back("warm")
 
         nc.vector.memset(b_scales[:].rearrange("p j n -> p (j n)").bitcast(I32), 0)
         nc.vector.memset(ones[:], 1.0)
@@ -504,84 +491,84 @@ def tile_ghosh_price_push_s8_kernel(
         for a in range(T):
             load_contrasts(a)
 
-        widen_sorted(0, 0, 1)
+        widen_first()
         widen(0, 1, 2)
-        nc.scalar.copy(out=ident_bf[:], in_=ident[:])
-        turn_shocks(0, 0, 0, 1)
-        turn_shocks(0, 1, 1, 2)
+        nc.vector.tensor_copy(out=ident_bf[:], in_=ident[:])
+        turn_shocks(0, 0, 1)
+        turn_shocks(0, 1, 2)
         widen(1)
-        turn_shocks(1, 2)
+        turn_shocks(1)
         for i in (2, 3):
             widen(i)
-            turn_shocks(i, i + 1)
+            turn_shocks(i)
         scale_shocks(0, 0, 1)
         scale_shocks(0, 1, 2)
         scale_shocks(1)
         scale_shocks(2)
         scale_shocks(3)
-        group_inverse(0, 0, "gpsimd", 0, 232, tag="group_a")
-        group_inverse(0, 0, "scalar", 232, KP)
-        warm(4, 7, inv_raw[0, 0][:, 0])
-        group_inverse(0, 1, "gpsimd", 0, 232, tag="group_b")
-        group_inverse(0, 1, "scalar", 232, KP)
+        group_inverse(0, 0, "gpsimd", 0, HEAD_SHARE, tag="group_a")
+        group_inverse(0, 0, "scalar", HEAD_SHARE, KP)
+        warm(inv_raw[0, 0][:, 0])
+        group_inverse(0, 1, "gpsimd", 0, HEAD_SHARE, tag="group_b")
+        group_inverse(0, 1, "scalar", HEAD_SHARE, KP)
         widen(4)
         widen(5)
-        turn_shocks(4, 0)
-        turn_shocks(5, 1)
+        turn_shocks(4)
+        turn_shocks(5)
         quantize_inverse(0, 0)
         quantize_shocks(0, 2)
         quantize_inverse(0, 1)
-        group_inverse(1, 0, "gpsimd", 0, 384, tag="group_b")
+        group_inverse(1, 0, "gpsimd", 0, SECOND_SHARE, tag="group_b")
         quantize_shocks(2, 2)
         load_baskets()
         nc.sync.dma_start(out=base_rows[:], in_=base.partition_broadcast(P))
 
         units = [(0, 0), (1, 0), (2, 0), (3, 0)]
-        move(units, [5, 6, 7, 2])
+        move(units)
         widen(6)
         group_inverse(1, 1, "scalar", 0, KP, tag="group_d")
         widen(7)
-        group_inverse(1, 0, "scalar", 384, KP)
-        turn_shocks(6, 3)
-        turn_shocks(7, 4)
-        exps(units)
+        group_inverse(1, 0, "scalar", SECOND_SHARE, KP)
+        turn_shocks(6)
+        turn_shocks(7)
         scale_shocks(4)
         scale_shocks(5)
+        exps(units)
         quantize_inverse(1, 1)
         quantize_inverse(1, 0)
         weights = weight_columns(0, TILES)
-        weigh_grouped("gpsimd", weights[:, 0:T], 0, 0, 0, 272, "group_b")
+        fuse_on_gpsimd(weights[:, 0:T], 0, 0, 0, FUSED_00, "group_b")
         quantize_shocks(4, 2)
 
-        move_pass(0, 1, 1, 0)
-        move_pass(1, 1, 1, 1)
-        move_pass(2, 1, 1, 5)
+        move_pass(0, 1, 1)
+        move_pass(1, 1, 1)
+        move_pass(2, 1, 1)
         move_pass(0, 1, 0)
         move_pass(1, 1, 0)
         move_pass(2, 1, 0)
-        move([(3, 1)], [6])
+        move([(3, 1)])
         widen(8)
         widen(9)
         widen(10)
         scale_shocks(6, tag="group_e")
-        turn_shocks(8, 7)
-        turn_shocks(9, 2)
-        turn_shocks(10, 3)
-        exps([(0, 1), (1, 1), (2, 1), (3, 1)])
+        turn_shocks(8)
+        turn_shocks(9)
+        turn_shocks(10)
         scale_shocks(7)
+        exps([(0, 1), (1, 1), (2, 1), (3, 1)])
         scale_shocks(8)
         quantize_shocks(6, 2)
-        weigh(weights, 0, 0, 1, "group_e")
-        weigh_grouped("gpsimd", weights[:, 0:T], 0, 0, 272, KP, None)
+        weigh(weights, 0, 1, "group_e")
+        fuse_on_gpsimd(weights[:, 0:T], 0, 0, FUSED_00, KP)
         quantize_shocks(8)
 
         units = [(4, 0), (4, 1), (5, 0), (5, 1)]
-        move(units, [4, 0, 1, 5])
+        move(units)
         widen(11)
         scale_shocks(9)
-        turn_shocks(11, 6)
-        spread_base(7)
-        turn_contrasts(0, 2)
+        turn_shocks(11)
+        spread_base()
+        turn_contrasts(0)
         exps(units)
         empty_contrasts(0)
         scale_shocks(10, tag="group_f")
@@ -590,127 +577,127 @@ def tile_ghosh_price_push_s8_kernel(
         quantize_shocks(10, 2)
 
         units = [(6, 0), (7, 0), (6, 1), (7, 1)]
-        move(units, [4, 0, 1, 5])
-        turn_contrasts(1, 3)
-        turn_contrasts(2, 6)
-        turn_contrasts(3, 2)
+        move(units)
+        turn_contrasts(1)
+        turn_contrasts(2)
+        turn_contrasts(3)
         exps(units)
-        weigh_grouped("gpsimd", weights[:, T : 2 * T], 1, 0, 0, 304, "group_f")
+        fuse_on_gpsimd(weights[:, T : 2 * T], 1, 0, 0, FUSED_10, "group_f")
         quantize_weighted(0, 0)
         for n in (1, 2, 3):
             empty_contrasts(n)
         for i in (0, 1, 2):
             price_early(i)
 
-        units = [(8, 0), (9, 0), (10, 0), (11, 0)]
-        move(units, [4, 0, 1, 5])
-        turn_early(0, 3)
-        turn_early(1, 6)
-        turn_early(2, 2)
-        exps(units)
-        turns(4, (4, 0))
+        units = [(i, j) for j in range(NJ) for i in range(8, 12)]
+        move(units[:4])
+        exps(units[:2])
+        move(units[4:6])
+        exps(units[2:4])
+        place_weights()
+        exps(units[4:6])
+        move(units[6:])
+        turn_contrasts(4)
+        turn_early(0)
+        exps(units[6:])
+        turn_early(1)
         quantize_contrasts(0)
-        on_gpsimd([(1, 0, 304, KP, None)], [])
+        group_1_weights = weight_columns(T, T)
+        fuse_on_gpsimd(group_1_weights[:, 0:T], 1, 0, FUSED_10, KP)
         quantize_contrasts(1)
-        for i in (0, 1, 2):
-            empty_early(i)
         price_early(3)
-        prices(4)
-
-        units = [(8, 1), (9, 1), (10, 1), (11, 1)]
-        move(units[:2], [1, 5])
-        place_weights(3)
-        move(units[2:], [6, 2])
-        on_gpsimd([], [(1, 1), (2, 1), (3, 1)])
-        quantize_priced(0, 2)
-        fuse_on_vector(2, 0, 0, KP, "group_d")
-        exps(units)
-        turn_contrasts(4, 4)
-        turn_contrasts(5, 0)
-        turn_early(3, 1)
+        fuse_on_vector(2, 0, 0, HALF, "group_d")
         empty_contrasts(4, tag="group_c")
-        empty_contrasts(5)
-        empty_early(3)
+        empty_early(0)
+        turns(4)
+        empty_early(1)
+        turn_early(2)
+        turn_early(3)
+        empty_early(2)
+        turn_contrasts(5)
+        group_0_weights = weight_columns(0, T)
+        for i in (1, 2, 3):
+            weigh(group_0_weights, i, 1)
         quantize_weighted(1, 0)
+        fuse_on_vector(2, 0, HALF, KP)
+        prices(4)
+        empty_early(3)
+        empty_contrasts(5)
+        for a in (0, 1, 2):
+            contrast_mm(a, 0, [0, 1])
         quantize_weighted(2, 0)
+        quantize_priced(0, 2)
         quantize_priced(2, 2)
         quantize_contrasts(2)
-        weigh_grouped("gpsimd", weights[:, 2 * T :], 2, 1, 0, 400, "group_c")
+        fuse_on_gpsimd(weights[:, 2 * T :], 2, 1, 0, FUSED_21, "group_c")
         quantize_priced(4)
-        price_early(5)
         fuse_on_vector(1, 1, 0, KP, "group_a")
-        fuse_on_vector(2, 1, 400, KP, None)
-
-        index_mm(0, 5)
-        index_mm(1, 6)
-        for g in range(SG):
-            contrast_mm(0, 0, 2, [g])
-            contrast_mm(1, 0, 4, [g])
-        index_mm(2, 0)
-        index_mm(3, 1)
-        index_out(0)
-        index_out(1)
-        contrast_mm(2, 0, 5)
-        contrast_mm(3, 0, 6)
+        fuse_on_vector(2, 1, FUSED_21, KP)
+        group_weighted(0, 1, 0, HALF, "group_b")
+        contrast_mm(0, 0, [2])
+        contrast_mm(1, 0, [2])
+        index_mm(0)
+        index_mm(1)
+        index_mm(2)
         contrast_out(0, 0)
-        group_weighted(0, 1, "scalar", 0, HALF, tag="group_b")
         contrast_out(1, 0)
-        index_out(2)
-        index_out(3)
-        group_weighted(0, 1, "scalar", HALF, KP)
-        turn_early(5, 0)
-        turns(8, (4, 1))
-        index_mm(4, 2)
-        empty_early(5)
+        index_mm(3)
+        contrast_mm(2, 0, [2])
+        contrast_mm(3, 0)
+        for i in range(4):
+            index_out(i)
+        group_weighted(0, 1, HALF, KP)
+        turns(8)
+        turns(10)
+        give_back("weight")
+        index_mm(4)
         contrast_out(2, 0)
         contrast_out(3, 0)
         index_out(4)
         quantize_weighted(1, 1)
         quantize_weighted(2, 1)
+        price_early_on_gpsimd(9, 0, "group_c")
+        price_early_on_gpsimd(9, 1)
         quantize_weighted(0, 1)
-        price_early_on_gpsimd(9, "group_b")
-        quantize_priced(5)
-        prices(8)
+        price_early(5)
         price_early(6)
-        price_early(7)
-
-        for g in (1, 2, 0):
-            contrast_mm(0, 1, 3, [g])
-            contrast_mm(1, 1, 0, [g])
-        index_mm(5, 5)
-        contrast_mm(2, 1, 6)
-        contrast_mm(3, 1, 2)
+        price_early(7, 0, 1)
+        price_early_on_gpsimd(7, 1)
+        contrast_mm(0, 1, [1, 2])
+        contrast_mm(1, 1, [1, 2])
+        contrast_mm(0, 1, [0])
+        contrast_mm(1, 1, [0])
+        contrast_mm(2, 1)
         contrast_out(0, 1)
+        contrast_mm(3, 1)
         contrast_out(1, 1)
-        index_out(5)
         contrast_out(2, 1)
+        give_back("base")
+        turn_early(5)
+        turn_early(6)
+        turn_early(9)
         contrast_out(3, 1)
-        turns(10, (4, 1))
-        turn_early(6, 3)
-        turn_early(9, 0)
-        turn_early(7, 5)
-        turns(11, (7, 6))
+        prices(8)
+        turns(11)
+        turn_early(7)
+        empty_early(5)
         empty_early(6)
         empty_early(9)
         empty_early(7)
+        price(10, 0)
         quantize_priced(8)
-        prices(10)
+        quantize_priced(5)
         quantize_priced(6)
+        price(10, 1)
         quantize_priced(9)
-        price(11, 0)
         quantize_priced(7)
         quantize_priced(10)
-        price(11, 1)
+        prices(11)
         quantize_priced_half(11, 0)
         quantize_priced_half(11, 1)
-
-        index_mm(8, 2)
-        index_mm(6, 3)
-        index_mm(9, 0)
-        index_mm(7, 4)
-        index_mm(10, 1)
-        index_halves_mm(11, 0, (5, 7))
-        index_halves_mm(11, 1, (5, 7))
-        for i in (8, 6, 9, 7, 10):
+        for i in (8, 5, 6, 9, 7, 10):
+            index_mm(i)
             index_out(i)
+        index_halves_mm(11, 0)
+        index_halves_mm(11, 1)
         index_halves_out(11)

from contextlib import ExitStack

import concourse.mybir as mybir
from concourse.masks import make_identity

S, N, C, R = 1536, 1024, 512, 512
FLOPS = 2 * (S * N * N + S * N * C + R * S * N)

F32 = mybir.dt.float32
BF16 = mybir.dt.bfloat16
I32 = mybir.dt.int32
U32 = mybir.dt.uint32
U8 = mybir.dt.uint8
FP8 = mybir.dt.float8_e4m3fn
FP8X4 = mybir.dt.float8_e4m3fn_x4
FP4X4 = mybir.dt.float4_e2m1fn_x4
MULT = mybir.AluOpType.mult
ADD = mybir.AluOpType.add
EXP = mybir.ActivationFunctionType.Exp
COPY = mybir.ActivationFunctionType.Copy

P = 128
T = 4
KP = P * T
HALF = KP // 2
SG = S // KP
KQ = N // KP
NJ = N // KP
TILES = SG * T
GROUP_BYTES = 4 * NJ * T * KP
BANKS = 8
LINE = 8
PAIR = 2

DEPTH = {
    "wide": 7, "sh_group": 2, "group_e": 1, "group_f": 1, "con_group": 2, "priced": 4, "early": 4, "columns": 4, "result": 6,
    "codes": TILES // 2, "scales": TILES // 2, "group_a": 1, "group_b": 1, "group_c": 1, "group_d": 1,
}
HEAD_SHARE = 232
SECOND_SHARE = 384
FUSED_00 = 272
FUSED_10 = 320
FUSED_21 = 320
WARM_UPS = 4


def tile_ghosh_price_push_s8_kernel(
    tc, shocks_bytes, shocks_scale, inverse, base, weight, basket_words, basket_scales, contrasts, out_0, out_1
):
    nc = tc.nc
    with ExitStack() as ctx:
        keep = ctx.enter_context(tc.tile_pool(name="keep", bufs=1))
        work = ctx.enter_context(tc.tile_pool(name="work", bufs=3))
        shared = ctx.enter_context(tc.tile_pool(name="shared", bufs=1))
        psum = ctx.enter_context(tc.psum_pool(name="psum", bufs=1))
        ctx.enter_context(tc.manual_schedule())

        scale_kp = keep.tile([P, KQ, T], F32, name="scale_kp")
        base_kp = keep.tile([P, NJ * T], BF16, name="base_kp")
        weight_kp = keep.tile([P, SG * T], BF16, name="weight_kp")
        b_words = keep.tile([P, NJ, 2 * C], U8, name="b_words", align_bytes=64)
        b_scales = keep.tile([P, NJ, C], U8, name="b_scales", align_bytes=64)
        con_raw = [keep.tile([P, S], BF16, name="con_raw%d" % a) for a in range(T)]

        inv_codes = keep.tile([P, NJ, KQ, KP], U32, name="inv_codes", align_bytes=64)
        inv_scales = keep.tile([P, NJ, KQ, KP], U8, name="inv_scales", align_bytes=64)
        con_codes = keep.tile([P, SG * R], U32, name="con_codes", align_bytes=64)
        con_scales = keep.tile([P, SG * R], U8, name="con_scales", align_bytes=64)
        we_codes = keep.tile([P, SG, NJ, KP], U32, name="we_codes", align_bytes=64)
        we_scales = keep.tile([P, SG, NJ, KP], U8, name="we_scales", align_bytes=64)
        ident = keep.tile([P, P], F32, name="ident")
        ident_bf = keep.tile([P, P], BF16, name="ident_bf")
        ones = keep.tile([P, 1], F32, name="ones")
        base_rows = keep.tile([P, N], BF16, name="base_rows")

        shocks_v = shocks_bytes.rearrange("(g m t) k -> g m t k", m=P, t=T)
        inverse_v = inverse.rearrange("(q p t) n -> q p t n", p=P, t=T)
        index_v = out_0.rearrange("(g m t) c -> g m t c", m=P, t=T)

        sh_bytes, inv_raw = {}, {}

        def load_shocks(i0, i1):
            loaded = keep.tile([P, i1 - i0, N], U8, name="sh_bytes%d" % i0, align_bytes=64)
            nc.sync.dma_start(out=loaded[:], in_=shocks_v[i0 // T][:, i0 % T : i0 % T + i1 - i0, :])
            for i in range(i0, i1):
                sh_bytes[i] = loaded[:, i - i0, :]

        def load_inverse(j, q):
            inv_raw[j, q] = keep.tile([P, T, KP], BF16, name="inv_raw%d%d" % (j, q))
            nc.sync.dma_start(out=inv_raw[j, q][:], in_=inverse_v[q][:, :, KP * j : KP * (j + 1)])

        def load_contrasts(a):
            nc.sync.dma_start(out=con_raw[a][:], in_=contrasts[P * a : P * (a + 1), :])

        def load_factors(tile, vector):
            nc.sync.dma_start(out=tile[:].rearrange("p (g t) -> p g t", t=T), in_=vector.rearrange("(g p t) -> p g t", p=P, t=T))

        def load_baskets():
            for quad in range(4):
                nc.sync.dma_start(
                    out=b_scales[32 * quad : 32 * quad + 4].bitcast(I32),
                    in_=basket_scales.rearrange("j s n -> s j n")[4 * quad : 4 * quad + 4].bitcast(I32),
                )
            nc.sync.dma_start(out=b_words[:], in_=basket_words.rearrange("j p b -> p j b"))

        free_banks, held = list(range(BANKS)), {}

        def take_bank(use, shape):
            held[use] = free_banks.pop(0)
            return psum.tile(shape, F32, name="bank%d" % held[use])

        def give_back(use):
            free_banks.append(held.pop(use))

        def buffer(tag, shape, dtype):
            return work.tile(shape, dtype, name=tag, bufs=DEPTH[tag], align_bytes=64)

        def interleave(engine, grouped, planes):
            if engine == "gpsimd":
                nc.gpsimd.tensor_scalar(
                    out=grouped, in0=planes.rearrange("p t n -> p n t"), scalar1=1.0, scalar2=0.0, op0=MULT, op1=ADD
                )
                return
            nc.scalar.copy(
                out=grouped.rearrange("p (c i) t -> p c t i", i=LINE),
                in_=planes.rearrange("p t (c i) -> p c t i", i=LINE),
            )

        def quantize(codes, scales, grouped):
            nc.vector.quantize_mx(out=codes.bitcast(FP8X4), scales=scales, in_=grouped)

        def quantize_tiles(mx, grouped, i0, i1):
            k = i0 // 2
            if k not in mx:
                mx[k] = (buffer("codes", [P, 2, 2, P], U32), buffer("scales", [P, 2, 2, P], U8))
            part = slice(i0 - 2 * k, i1 - 2 * k)
            quantize(
                mx[k][0][:, part].rearrange("p i q r -> p (i q r)"),
                mx[k][1][:, part].rearrange("p i q r -> p (i q r)"),
                grouped[k][:, part].rearrange("p i n -> p (i n)"),
            )

        sh_wide, sh_bank, sh_group, sh_mx = {}, {}, {}, {}

        def widen(i, q0=0, q1=KQ):
            if i not in sh_wide:
                sh_wide[i] = buffer("wide", [P, N], BF16)
            nc.scalar.copy(out=sh_wide[i][:, KP * q0 : KP * q1], in_=sh_bytes[i][:, KP * q0 : KP * q1].bitcast(FP8))

        def widen_first():
            sh_wide[0] = buffer("wide", [P, N], BF16)
            nc.vector.tensor_scalar(
                out=sh_wide[0][:, 0:KP].rearrange("p (u w e) -> p w u e", u=2, e=2),
                in0=sh_bytes[0][:, 0:KP].bitcast(FP8).rearrange("p (w u e) -> p w u e", u=2, e=2),
                scalar1=ones[:],
                scalar2=None,
                op0=MULT,
            )

        def turn_shocks(i, q0=0, q1=KQ):
            sh_bank[i, q0] = take_bank(("shocks", i, q0), [P, 2, q1 - q0, P])
            words = sh_wide[i][:].bitcast(F32)
            for q in range(q0, q1):
                for u in range(2):
                    if (i, q) == (0, 0):
                        source = words[:, P * u : P * (u + 1)]
                    else:
                        source = words[:, HALF * q + u : HALF * (q + 1) : 2]
                    nc.tensor.transpose(sh_bank[i, q0][:, u, q - q0, :], source, ident[:])

        def scale_shocks(i, q0=0, q1=KQ, tag="sh_group"):
            if i // 2 not in sh_group:
                sh_group[i // 2] = buffer(tag, [P, 2, N], BF16)
            halves = sh_bank[i, q0][:].rearrange("p u q r -> p (u q r)").bitcast(BF16)
            nc.vector.tensor_tensor(
                out=sh_group[i // 2][:, i % 2, KP * q0 : KP * q1].rearrange("p (q r u e) -> p q r u e", r=P, u=2, e=2),
                in0=halves.rearrange("p (u q r e) -> p q r u e", r=P, u=2, e=2),
                in1=scale_kp[:, q0:q1].rearrange("p q (u e) -> p q u e", u=2).unsqueeze(2).to_broadcast([P, q1 - q0, P, 2, 2]),
                op=MULT,
            )
            give_back(("shocks", i, q0))

        def quantize_shocks(i0, count=1):
            quantize_tiles(sh_mx, sh_group, i0, i0 + count)

        con_bank, con_group = {}, {}

        def turn_contrasts(n):
            con_bank[n] = take_bank(("contrasts", n), [P, 2, 2, P])
            for h in range(2):
                a, g = divmod(2 * n + h, SG)
                words = con_raw[a][:].bitcast(F32)
                for u in range(2):
                    nc.tensor.transpose(con_bank[n][:, h, u, :], words[:, HALF * g + u : HALF * (g + 1) : 2], ident[:])

        def empty_words(grouped, bank):
            nc.scalar.copy(
                out=grouped.bitcast(F32).rearrange("p (a r u) -> p a r u", a=2, u=2),
                in_=bank.rearrange("p a u r -> p a r u"),
            )

        def empty_contrasts(n, tag="con_group"):
            if n % 2 == 0:
                con_group[n // 2] = buffer(tag, [P, 2, 2 * KP], BF16)
            empty_words(con_group[n // 2][:, n % 2], con_bank[n][:])
            give_back(("contrasts", n))

        def quantize_contrasts(k):
            cols = slice(KP * k, KP * (k + 1))
            quantize(con_codes[:, cols], con_scales[:, cols], con_group[k][:].rearrange("p h n -> p (h n)"))

        inv_group = {}

        def group_inverse(j, q, engine, c0, c1, tag=None):
            if (j, q) not in inv_group:
                inv_group[j, q] = buffer(tag, [P, KP, T], BF16)
            interleave(engine, inv_group[j, q][:, c0:c1, :], inv_raw[j, q][:, :, c0:c1])

        def quantize_inverse(j, q):
            quantize(inv_codes[:, j, q, :], inv_scales[:, j, q, :], inv_group[j, q][:].rearrange("p n t -> p (n t)"))

        mv_bank, tr_bank, priced, early, scaled, weighted, pr_mx = {}, {}, {}, {}, {}, {}, {}

        def move_pass(i, j, q):
            opens = (i, j) not in mv_bank
            if opens:
                mv_bank[i, j] = take_bank(("moves", i, j), [P, KP])
            nc.tensor.matmul_mx(
                out=mv_bank[i, j][:],
                lhsT=sh_mx[i // 2][0][:, i % 2, q, :].bitcast(FP8X4),
                lhsT_scale=sh_mx[i // 2][1][:, i % 2, q, :],
                rhs=inv_codes[:, j, q, :].bitcast(FP8X4),
                rhs_scale=inv_scales[:, j, q, :],
                start=opens,
                stop=not opens,
            )

        def move(units):
            for i, j in units:
                move_pass(i, j, 0)
                move_pass(i, j, 1)

        rel = [shared.tile([P, NJ, T, KP], F32, name="rel%d" % g, offset=GROUP_BYTES * g) for g in range(SG)]

        def unit_rel(i, j):
            return rel[i // T][:, j, i % T, :]

        def relatives(i, j):
            nc.scalar.activation(
                out=unit_rel(i, j).rearrange("p (e u m) -> p e u m", e=2, u=2),
                in_=mv_bank[i, j][:].rearrange("p (m u e) -> p e u m", u=2, e=2),
                func=EXP,
            )
            give_back(("moves", i, j))

        def exps(units):
            for i, j in units:
                relatives(i, j)

        def turn(i, j):
            tr_bank[i, j] = take_bank(("relatives", i, j), [P, T, P])
            for v in range(T):
                c0 = HALF * (v % 2) + P * (v // 2)
                nc.tensor.transpose(tr_bank[i, j][:, v, :], unit_rel(i, j)[:, c0 : c0 + P], ident[:])

        def turns(i):
            for j in range(NJ):
                turn(i, j)

        def priced_tile(i):
            if i // 2 not in priced:
                priced[i // 2] = buffer("priced", [P, 2, N], BF16)
            return priced[i // 2][:, i % 2]

        def price(i, j):
            nc.vector.tensor_tensor(
                out=priced_tile(i)[:, KP * j : KP * (j + 1)].rearrange("p (m v) -> p m v", v=T),
                in0=tr_bank[i, j][:].rearrange("p v m -> p m v"),
                in1=base_kp[:, T * j : T * (j + 1)].unsqueeze(1).to_broadcast([P, P, T]),
                op=MULT,
            )
            give_back(("relatives", i, j))

        def prices(i):
            for j in range(NJ):
                price(i, j)

        consts = {}

        def spread_base():
            consts["base"] = take_bank("base", [P, 2 * NJ, P])
            words = base_kp[:].bitcast(F32)
            for a in range(2 * NJ):
                nc.tensor.transpose(consts["base"][:, a, :], words[:, a : a + 1].to_broadcast([P, P]), ident[:])

        def place_weights():
            consts["weight"] = take_bank("weight", [P, TILES])
            nc.tensor.matmul(consts["weight"][:], ident_bf[:], weight_kp[:], start=True, stop=True)

        def early_tile(i, tag):
            if i not in early:
                early[i] = buffer(tag, [P, NJ, KP], BF16)
            return early[i]

        def price_early(i, j0=0, j1=NJ):
            row = consts["base"][:].rearrange("p a m -> p (a m)").bitcast(BF16)
            nc.vector.tensor_tensor(
                out=early_tile(i, "early")[:, j0:j1].rearrange("p j (c e) -> p j c e", e=2),
                in0=row.rearrange("p (j c e) -> p j c e", j=NJ, e=2)[:, j0:j1],
                in1=rel[i // T][:, j0:j1, i % T, :].rearrange("p j (e c) -> p j c e", e=2),
                op=MULT,
            )

        def price_early_on_gpsimd(i, j, tag="early"):
            nc.gpsimd.tensor_tensor(
                out=early_tile(i, tag)[:, j].rearrange("p (u m e) -> p u m e", u=2, e=2),
                in0=base_rows[:, KP * j : KP * (j + 1)].rearrange("p (m u e) -> p u m e", u=2, e=2),
                in1=unit_rel(i, j).rearrange("p (e u m) -> p u m e", u=2, e=2),
                op=MULT,
            )

        def turn_early(i):
            tr_bank[i] = take_bank(("early", i), [P, NJ, 2, P])
            words = early[i][:].rearrange("p j n -> p (j n)").bitcast(F32)
            for a in range(2 * NJ):
                nc.tensor.transpose(tr_bank[i][:, a // 2, a % 2, :], words[:, P * a : P * (a + 1)], ident[:])

        def empty_early(i):
            empty_words(priced_tile(i), tr_bank[i][:])
            give_back(("early", i))

        def quantize_priced(i0, count=1):
            quantize_tiles(pr_mx, priced, i0, i0 + count)

        def quantize_priced_half(i, j):
            codes, scales = pr_mx[i // 2]
            quantize(codes[:, i % 2, j], scales[:, i % 2, j], priced[i // 2][:, i % 2, KP * j : KP * (j + 1)])

        def weight_columns(i0, count):
            columns = buffer("columns", [P, count], F32)
            nc.vector.tensor_copy(out=columns[:], in_=weight_kp[:, i0 : i0 + count])
            return columns

        def weigh(columns, i, j, tag=None):
            if (i // T, j) not in scaled:
                scaled[i // T, j] = buffer(tag, [P, T, KP], BF16)
            nc.gpsimd.tensor_scalar(
                out=scaled[i // T, j][:, i % T, :],
                in0=unit_rel(i, j),
                scalar1=columns[:, i : i + 1],
                scalar2=0.0,
                op0=MULT,
                op1=ADD,
            )

        def sheet(g, j, tag):
            if (g, j) not in weighted:
                weighted[g, j] = buffer(tag, [P, KP, T], BF16)
            return weighted[g, j]

        def group_weighted(g, j, c0, c1, tag=None):
            interleave("scalar", sheet(g, j, tag)[:, c0:c1, :], scaled[g, j][:, :, c0:c1])

        def fused_operands(four_weights, g, j, c0, c1, tag):
            grouped = sheet(g, j, tag)[:, c0:c1, :].rearrange("p (c r) t -> p c t r", r=PAIR)
            values = rel[g][:, j, :, c0:c1].rearrange("p t (c r) -> p c t r", r=PAIR)
            factors = four_weights.unsqueeze(1).unsqueeze(3).to_broadcast([P, (c1 - c0) // PAIR, T, PAIR])
            return grouped, values, factors

        def fuse_on_gpsimd(four_weights, g, j, c0, c1, tag=None):
            grouped, values, factors = fused_operands(four_weights, g, j, c0, c1, tag)
            nc.gpsimd.tensor_tensor(out=grouped, in0=values, in1=factors, op=MULT)

        def fuse_on_vector(g, j, c0, c1, tag=None):
            grouped, values, factors = fused_operands(consts["weight"][:, T * g : T * (g + 1)], g, j, c0, c1, tag)
            nc.vector.tensor_tensor(out=grouped, in0=factors, in1=values, op=MULT)

        def quantize_weighted(g, j):
            quantize(we_codes[:, g, j, :], we_scales[:, g, j, :], weighted[g, j][:].rearrange("p n t -> p (n t)"))

        index_bank, contrast_bank = {}, {}

        def sums_out(engine, out, in_):
            if engine == "scalar":
                nc.scalar.activation(out=out, in_=in_, func=COPY)
            else:
                nc.vector.tensor_copy(out=out, in_=in_)

        stored = []

        def result_tile():
            k = len(stored)
            stored.append(k)
            shelf, slot = divmod(k, NJ * T + DEPTH["result"])
            if slot >= NJ * T:
                single = buffer("result", [P, KP], F32)
                return single[:]
            placed = shared.tile([P, KP], F32, name="placed%d" % k, offset=GROUP_BYTES * shelf + 4 * KP * slot)
            return placed[:]

        def index_mm(i):
            index_bank[i] = take_bank(("index", i), [P, C])
            for j in range(NJ):
                nc.tensor.matmul_mx(
                    out=index_bank[i][:],
                    lhsT=pr_mx[i // 2][0][:, i % 2, j, :].bitcast(FP8X4),
                    lhsT_scale=pr_mx[i // 2][1][:, i % 2, j, :],
                    rhs=b_words[:, j, :].bitcast(FP4X4),
                    rhs_scale=b_scales[:, j, :],
                    start=(j == 0),
                    stop=(j == NJ - 1),
                )

        def index_out(i, engine="scalar"):
            result = result_tile()
            sums_out(engine, result, index_bank[i][:])
            give_back(("index", i))
            nc.sync.dma_start(out=index_v[i // T][:, i % T, :], in_=result)

        half_bank = {}

        def index_halves_mm(i, j):
            for c0 in (0, HALF):
                if j == 0:
                    half_bank[c0] = take_bank(("index", i, c0), [P, HALF])
                nc.tensor.matmul_mx(
                    out=half_bank[c0][:],
                    lhsT=pr_mx[i // 2][0][:, i % 2, j, :].bitcast(FP8X4),
                    lhsT_scale=pr_mx[i // 2][1][:, i % 2, j, :],
                    rhs=b_words[:, j, 2 * c0 : 2 * (c0 + HALF)].bitcast(FP4X4),
                    rhs_scale=b_scales[:, j, c0 : c0 + HALF],
                    start=(j == 0),
                    stop=(j == NJ - 1),
                )

        def index_halves_out(i):
            result = result_tile()
            for engine, c0 in (("scalar", 0), ("vector", HALF)):
                sums_out(engine, result[:, c0 : c0 + HALF], half_bank[c0][:])
                nc.sync.dma_start(out=index_v[i // T][:, i % T, c0 : c0 + HALF], in_=result[:, c0 : c0 + HALF])

        summed = {}

        def contrast_mm(a, j, groups=range(SG)):
            if (a, j) not in summed:
                contrast_bank[a, j] = take_bank(("contrast", a, j), [P, KP])
                summed[a, j] = []
            for g in groups:
                summed[a, j].append(g)
                nc.tensor.matmul_mx(
                    out=contrast_bank[a, j][:],
                    lhsT=con_codes[:, P * (SG * a + g) : P * (SG * a + g + 1)].bitcast(FP8X4),
                    lhsT_scale=con_scales[:, P * (SG * a + g) : P * (SG * a + g + 1)],
                    rhs=we_codes[:, g, j, :].bitcast(FP8X4),
                    rhs_scale=we_scales[:, g, j, :],
                    start=len(summed[a, j]) == 1,
                    stop=len(summed[a, j]) == SG,
                )

        def contrast_out(a, j):
            result = result_tile()
            sums_out(
                "scalar",
                result.rearrange("p (m u e) -> p m u e", u=2, e=2),
                contrast_bank[a, j][:].rearrange("p (e u m) -> p m u e", u=2, e=2),
            )
            give_back(("contrast", a, j))
            nc.sync.dma_start(out=out_1[P * a : P * (a + 1), KP * j : KP * (j + 1)], in_=result)

        def warm(source):
            bank = take_bank("warm", [P, KP])
            for k in range(WARM_UPS):
                nc.tensor.matmul(bank[:], source[:, 0:P], source[:, 0:KP], start=True, stop=True)
            give_back("warm")

        nc.vector.memset(b_scales[:].rearrange("p j n -> p (j n)").bitcast(I32), 0)
        nc.vector.memset(ones[:], 1.0)
        make_identity(nc, ident[:])
        load_shocks(0, 1)
        load_shocks(1, 2)
        nc.sync.dma_start(out=scale_kp[:], in_=shocks_scale.rearrange("o (q p t) -> p (o q) t", p=P, t=T))
        load_shocks(2, 4)
        load_inverse(0, 0)
        load_inverse(0, 1)
        load_shocks(4, 8)
        load_inverse(1, 1)
        load_inverse(1, 0)
        load_factors(weight_kp, weight)
        load_shocks(8, 12)
        load_factors(base_kp, base)
        for a in range(T):
            load_contrasts(a)

        widen_first()
        widen(0, 1, 2)
        nc.vector.tensor_copy(out=ident_bf[:], in_=ident[:])
        turn_shocks(0, 0, 1)
        turn_shocks(0, 1, 2)
        widen(1)
        turn_shocks(1)
        for i in (2, 3):
            widen(i)
            turn_shocks(i)
        scale_shocks(0, 0, 1)
        scale_shocks(0, 1, 2)
        scale_shocks(1)
        scale_shocks(2)
        scale_shocks(3)
        group_inverse(0, 0, "gpsimd", 0, HEAD_SHARE, tag="group_a")
        group_inverse(0, 0, "scalar", HEAD_SHARE, KP)
        warm(inv_raw[0, 0][:, 0])
        group_inverse(0, 1, "gpsimd", 0, HEAD_SHARE, tag="group_b")
        group_inverse(0, 1, "scalar", HEAD_SHARE, KP)
        widen(4)
        widen(5)
        turn_shocks(4)
        turn_shocks(5)
        quantize_inverse(0, 0)
        quantize_shocks(0, 2)
        quantize_inverse(0, 1)
        group_inverse(1, 0, "gpsimd", 0, SECOND_SHARE, tag="group_b")
        quantize_shocks(2, 2)
        load_baskets()
        nc.sync.dma_start(out=base_rows[:], in_=base.partition_broadcast(P))

        units = [(0, 0), (1, 0), (2, 0), (3, 0)]
        move(units)
        widen(6)
        group_inverse(1, 1, "scalar", 0, KP, tag="group_d")
        widen(7)
        group_inverse(1, 0, "scalar", SECOND_SHARE, KP)
        turn_shocks(6)
        turn_shocks(7)
        scale_shocks(4)
        scale_shocks(5)
        exps(units)
        quantize_inverse(1, 1)
        quantize_inverse(1, 0)
        weights = weight_columns(0, TILES)
        fuse_on_gpsimd(weights[:, 0:T], 0, 0, 0, FUSED_00, "group_b")
        quantize_shocks(4, 2)

        move_pass(0, 1, 1)
        move_pass(1, 1, 1)
        move_pass(2, 1, 1)
        move_pass(0, 1, 0)
        move_pass(1, 1, 0)
        move_pass(2, 1, 0)
        move([(3, 1)])
        widen(8)
        widen(9)
        widen(10)
        scale_shocks(6, tag="group_e")
        turn_shocks(8)
        turn_shocks(9)
        turn_shocks(10)
        scale_shocks(7)
        exps([(0, 1), (1, 1), (2, 1), (3, 1)])
        scale_shocks(8)
        quantize_shocks(6, 2)
        weigh(weights, 0, 1, "group_e")
        fuse_on_gpsimd(weights[:, 0:T], 0, 0, FUSED_00, KP)
        quantize_shocks(8)

        units = [(4, 0), (4, 1), (5, 0), (5, 1)]
        move(units)
        widen(11)
        scale_shocks(9)
        turn_shocks(11)
        spread_base()
        turn_contrasts(0)
        exps(units)
        empty_contrasts(0)
        scale_shocks(10, tag="group_f")
        scale_shocks(11)
        quantize_shocks(9)
        quantize_shocks(10, 2)

        units = [(6, 0), (7, 0), (6, 1), (7, 1)]
        move(units)
        turn_contrasts(1)
        turn_contrasts(2)
        turn_contrasts(3)
        exps(units)
        fuse_on_gpsimd(weights[:, T : 2 * T], 1, 0, 0, FUSED_10, "group_f")
        quantize_weighted(0, 0)
        for n in (1, 2, 3):
            empty_contrasts(n)
        for i in (0, 1, 2):
            price_early(i)

        units = [(i, j) for j in range(NJ) for i in range(8, 12)]
        move(units[:4])
        exps(units[:2])
        move(units[4:6])
        exps(units[2:4])
        place_weights()
        exps(units[4:6])
        move(units[6:])
        turn_contrasts(4)
        turn_early(0)
        exps(units[6:])
        turn_early(1)
        quantize_contrasts(0)
        group_1_weights = weight_columns(T, T)
        fuse_on_gpsimd(group_1_weights[:, 0:T], 1, 0, FUSED_10, KP)
        quantize_contrasts(1)
        price_early(3)
        fuse_on_vector(2, 0, 0, HALF, "group_d")
        empty_contrasts(4, tag="group_c")
        empty_early(0)
        turns(4)
        empty_early(1)
        turn_early(2)
        turn_early(3)
        empty_early(2)
        turn_contrasts(5)
        group_0_weights = weight_columns(0, T)
        for i in (1, 2, 3):
            weigh(group_0_weights, i, 1)
        quantize_weighted(1, 0)
        fuse_on_vector(2, 0, HALF, KP)
        prices(4)
        empty_early(3)
        empty_contrasts(5)
        for a in (0, 1, 2):
            contrast_mm(a, 0, [0, 1])
        quantize_weighted(2, 0)
        quantize_priced(0, 2)
        quantize_priced(2, 2)
        quantize_contrasts(2)
        fuse_on_gpsimd(weights[:, 2 * T :], 2, 1, 0, FUSED_21, "group_c")
        quantize_priced(4)
        fuse_on_vector(1, 1, 0, KP, "group_a")
        fuse_on_vector(2, 1, FUSED_21, KP)
        group_weighted(0, 1, 0, HALF, "group_b")
        contrast_mm(0, 0, [2])
        contrast_mm(1, 0, [2])
        index_mm(0)
        index_mm(1)
        index_mm(2)
        contrast_out(0, 0)
        contrast_out(1, 0)
        index_mm(3)
        contrast_mm(2, 0, [2])
        contrast_mm(3, 0)
        for i in range(4):
            index_out(i)
        group_weighted(0, 1, HALF, KP)
        turns(8)
        turns(10)
        give_back("weight")
        index_mm(4)
        contrast_out(2, 0)
        contrast_out(3, 0)
        index_out(4)
        quantize_weighted(1, 1)
        quantize_weighted(2, 1)
        price_early_on_gpsimd(9, 0, "group_c")
        price_early_on_gpsimd(9, 1)
        quantize_weighted(0, 1)
        price_early(5)
        price_early(6)
        price_early(7, 0, 1)
        price_early_on_gpsimd(7, 1)
        contrast_mm(0, 1, [1, 2])
        contrast_mm(1, 1, [1, 2])
        contrast_mm(0, 1, [0])
        contrast_mm(1, 1, [0])
        contrast_mm(2, 1)
        contrast_out(0, 1)
        contrast_mm(3, 1)
        contrast_out(1, 1)
        contrast_out(2, 1)
        give_back("base")
        turn_early(5)
        turn_early(6)
        turn_early(9)
        contrast_out(3, 1)
        prices(8)
        turns(11)
        turn_early(7)
        empty_early(5)
        empty_early(6)
        empty_early(9)
        empty_early(7)
        price(10, 0)
        quantize_priced(8)
        quantize_priced(5)
        quantize_priced(6)
        price(10, 1)
        quantize_priced(9)
        quantize_priced(7)
        quantize_priced(10)
        prices(11)
        quantize_priced_half(11, 0)
        quantize_priced_half(11, 1)
        for i in (8, 5, 6, 9, 7, 10):
            index_mm(i)
            index_out(i)
        index_halves_mm(11, 0)
        index_halves_mm(11, 1)
        index_halves_out(11)
